import numpy as np, ml_dtypes
CORES = [9,25,41,57]
N = 4
BF = ml_dtypes.bfloat16
def gentries(a):
    return np.ascontiguousarray(a.reshape(8, 16, -1).transpose(0, 2, 1)).reshape(8, -1)
def gtable(e):
    e = np.asarray(e); return np.ascontiguousarray(e.reshape(8, -1, 16).transpose(0, 2, 1)).reshape(128, -1).astype(np.int32)
W, L, S, ST = 4096, 256, 16, 5
def parts(rng):
    x = rng.integers(0, 64, (N, 8, 16, W)); v = rng.integers(0, W, (N, 8, L, S)); c = rng.integers(0, W, (N, 8, L, S))
    n = np.where(rng.random((N, 8, L)) < 0.4, rng.integers(0, 4, (N, 8, L)), rng.integers(4, S + 1, (N, 8, L)))
    return x, v, c, n, rng.integers(220, 460, (N, 8)), rng.integers(0, 256, (N, 8, 16))
def pack(x, v, c, n, th, w):
    return {"xc": np.ascontiguousarray(x.reshape(N, 128, W)).astype(np.float32).astype(BF), "vl": np.stack([gtable(a.reshape(8, -1)) for a in v]), "cl": np.stack([gtable(a.reshape(8, -1)) for a in c]),
            "ln": np.ascontiguousarray(n).astype(np.int32), "th": np.ascontiguousarray(th.reshape(N, 8, 1)).astype(np.int32), "wt": np.ascontiguousarray(w.reshape(N, 128, 1)).astype(np.int32)}
def setup_inputs(rng):
    return pack(*parts(rng))
def setup_inputs_ties(rng):
    x, v, c, n, th, w = parts(rng)
    x = np.repeat(8 * rng.integers(0, 8, (N, 8, 1, W)), 16, axis=2); up = rng.integers(0, 3, (N, 8, W)) * (rng.random((N, 8, W)) < 0.4)
    x = x + up[:, :, None, :] * (np.arange(16)[:, None] == rng.integers(0, 16, (N, 8, 1, W)))
    o = np.argsort(rng.random((N, 8)), axis=1); j = o >> 1; less = np.where(rng.random((N, 8)) < 0.6, rng.integers(0, 2, (N, 8)), rng.integers(0, 32, (N, 8)))
    th = np.maximum(128 * j - less, 0); s = np.arange(S)
    for r in range(N):
        z = 128 * int(rng.integers(4, 7))
        for g, e in ((int(np.argmin(o[r])), 0), (int(np.argmax(o[r])), 1)):
            th[r, g] = z + e
            x[r, g, :, 0] = 0; x[r, g, :, 1] = 56; x[r, g, :, 2] = z >> 4; x[r, g, int(rng.integers(0, 16)), 2] += 1
            v[r, g, 1::2] = np.where(s < 2, 0, 2); c[r, g, 1::2] = np.where(s < 1, 1, 2); n[r, g, 1::2] = rng.integers(4, S + 1, L // 2)
    q = int(rng.integers(0, N)); a = (q - 1) % N; b = (q - 2) % N
    n[a] = np.where(n[a] >= 4, rng.integers(4, 6, (8, L)), n[a])
    n[q] = rng.integers(0, 4, (8, L)); p = rng.permutation(8 * L)[:31]; one = rng.integers(0, W, (31, 1))
    n[q, p // L, p % L] = 4; v[q, p // L, p % L] = one; c[q, p // L, p % L] = one; th[q] = 128 * rng.integers(1, 4, 8) - 16
    x[b, :, :, 16:40:3] = 0; x[b, :, :, 17:40:3] = 56; x[b, :, :, 18:40:3] = 63; x[b, :, :, 64:128] = 8 * rng.integers(0, 2, (8, 1, 64))
    f0 = 16 + 3 * (np.arange(L // 4)[:, None] & 7); far = rng.integers(64, 128, (8, L // 4, S)); e = rng.integers(128, W, (8, L // 4, S))
    v[b, :, ::4] = np.where(s == 0, e, np.where((s == 1) | (s >= S - 3), f0 + 2, np.where(s == 2, f0 + 1, far)))
    c[b, :, ::4] = np.where(s == 0, f0 + 2, np.where((s == 1) | (s == S - 3), f0, rng.integers(128, W, far.shape)))
    n[b, :, ::4] = S
    return pack(x, v, c, n, th, w)
def setup_inputs_alike(rng):
    x, v, c, n, th, w = parts(rng)
    few = np.array([0, W - 1, W // 2, 3, W - 2, 17])
    v[:, ::2] = few[rng.integers(0, 6, (N, 4, L, S))]; v[:, 1::2, :, 0] = few[rng.integers(0, 6, (N, 4, L))]
    w[:, ::2] = 0; th[:, ::2] = rng.integers(0, 260, (N, 4)); th[:, 1::2] = rng.integers(150, 500, (N, 4))
    o = rng.permutation(4); shutting = 2 * int(o[0]); taking = 2 * int(o[1]); growing = 1 + 2 * int(rng.integers(0, 4))
    n[:, growing] = rng.integers(4, S + 1, (N, L)); v[:, growing, :, 0] = few[int(rng.integers(0, 6))]; th[:, growing] = 0
    n[:, shutting] = rng.integers(ST + 3, S + 1, (N, L)); th[:, shutting] = 1008
    rest = np.where(rng.random((N, L)) < 0.8, 0, rng.integers(1, 4, (N, L)))
    n[:, taking] = np.where(np.arange(N)[:, None] % 2 == 0, rng.integers(ST + 3, S + 1, (N, L)), rest); th[:, taking] = 1008
    return pack(x, v, c, n, th, w)
def setup_inputs_corners(rng):
    x, v, c, n, th, w = parts(rng)
    lo = (W - 1) * rng.integers(0, 2, (N, 8, 1)); hi = W - 1 - lo
    x[..., 0] = np.where(lo == 0, 0, 63); x[..., W - 1] = np.where(lo == 0, 63, 0)
    n = rng.choice(np.array([0, 1, 2, 3, 4, 5, S - 1, S]), (N, 8, L)); kind = rng.integers(0, 5, (N, 8, L))
    for g, i in ((0, 0), (7, L - 1)):
        n[0, g, i] = S; kind[0, g, i] = 0; n[1, g, i] = 0
    n[N - 1, 7, L - 2] = S; kind[N - 1, 7, L - 2] = 1
    s = np.arange(S); q = np.maximum(n, 4)[..., None]; kd = kind[..., None]; A = lo[..., None]; H = hi[..., None]
    v0 = np.where((s < 2) | (s == q - 1), H, A); v1 = np.where((s == q - 3) | (s == q - 2), H, A); v2 = np.where(s >= q - 3, H, A)
    one = rng.integers(0, W, (N, 8, L, 1))
    v = np.where(kd == 0, v0, np.where(kd == 1, v1, np.where(kd == 2, v2, np.where(kd == 3, one, v))))
    c = np.where(kd < 3, A, np.where(kd == 3, one, c))
    v = np.where(s < n[..., None], v, (W - 1) * rng.integers(0, 2, v.shape)); c = np.where(s < n[..., None], c, (W - 1) * rng.integers(0, 2, c.shape))
    return pack(x, v, c, n, np.array([0, 5, 500, 900])[np.argsort(rng.random((N, 8)), axis=1) >> 1], w)
def setup_inputs_ends(rng):
    x, v, c, n, th, w = parts(rng)
    e = 63 * rng.integers(0, 2, (N, 8, 1)); e[N - 1, 7] = 0
    x = 63 * rng.integers(0, 2, (N, 8, 16, W)); x[..., 0] = e; x[..., W - 1] = 63 - e
    for j in range(1, 17):
        for col in (j, W - 1 - j):
            x[..., col] = 63 - e; x[:, :, j - 1, col] = np.abs(62 - e[..., 0])
    v = np.where(rng.random(v.shape) < 0.75, (W - 1) * rng.integers(0, 2, v.shape), v); c = np.where(rng.random(c.shape) < 0.75, (W - 1) * rng.integers(0, 2, c.shape), c)
    kind = rng.integers(0, 3, (N, 8, L)); kind[..., 0] = 1; kind[..., L - 1] = 1; kind[..., 1] = 2; kind[..., L - 2] = 2
    k1 = kind == 1; k2 = kind == 2; v[k1 | k2] = W - 1; c[k1] = W - 1
    c = np.where(k2[..., None], (W - 1) * rng.integers(0, 2, c.shape), c)
    near = rng.integers(1, 17, (N, 8, L)); near = np.where(rng.random((N, 8, L)) < 0.5, near, W - 1 - near)
    v[..., 0] = np.where(k1, near, v[..., 0]); c[..., 0] = np.where(k1, 0, c[..., 0]); c[..., S - 3] = np.where(k1 | k2, 0, c[..., S - 3])
    v[..., S - 1] = np.where(k1, (W - 1) * rng.integers(0, 2, (N, 8, L)), v[..., S - 1]); v[N - 1, 7, L - 1, S - 1] = 0
    n = np.where(rng.random((N, 8, L)) < 0.7, S, 0); n[..., 0] = S; n[..., 1] = S; n[..., 2] = 0; n[..., L - 2] = S; n[..., L - 1] = S; n[0, :, L - 1] = 0
    th = 1008 * (np.argsort(rng.random((N, 8)), axis=1) & 1)
    if th[N - 1, 7] > 0: th[N - 1] = 1008 - th[N - 1]
    w = 255 * rng.integers(0, 2, (N, 8, 16)); w[:, 7] = 255; w[:, 0] = 0
    return pack(x, v, c, n, th, w)
def setup_inputs_spread(rng):
    x, v, c, n, th, w = parts(rng)
    x = np.minimum((np.exp2(6.1 * rng.random((N, 8, 1, W))) * rng.random((N, 8, 16, W))).astype(np.int64), 63)
    po = rng.choice(np.array([1.0, 2.0, 4.0]), (N, 8, 1, 1)); v = np.minimum((W * rng.random(v.shape) ** po).astype(np.int64), W - 1); c = np.minimum((W * rng.random(c.shape) ** po[:, ::-1]).astype(np.int64), W - 1)
    n = np.minimum(((S + 1) * rng.random((N, 8, L)) ** rng.choice(np.array([0.5, 1.0, 2.0]), (N, 8, 1))).astype(np.int64), S)
    th = np.minimum(np.exp2(10 * rng.random((N, 8))).astype(np.int64) - 1, 1008); w = np.minimum(np.exp2(8.05 * rng.random((N, 8, 16))).astype(np.int64) - 1, 255)
    return pack(x, v, c, n, th, w)
def check_inputs(d):
    bad = []
    for k, lo, hi in (("xc", 0, 63), ("vl", 0, W - 1), ("cl", 0, W - 1), ("ln", 0, S), ("th", 0, 1008), ("wt", 0, 255)):
        a = np.asarray(d[k]).astype(np.float64)
        if not (np.min(a) >= lo and np.max(a) <= hi): bad.append("range of " + k)
    a = np.asarray(d["xc"]).astype(np.float64)
    if not np.all(np.floor(a) == a): bad.append("xc is not whole")
    return bad
def reference(xc, vl, cl, ln, th, wt):
    X = np.ascontiguousarray(xc.astype(np.float32).astype(np.int32).reshape(N, 8, 16, W).transpose(0, 1, 3, 2))
    V = np.stack([gentries(q) for q in vl]).astype(np.int32).reshape(N, 8, L, S); C = np.stack([gentries(q) for q in cl]).astype(np.int32).reshape(N, 8, L, S)
    n = ln.astype(np.int64).reshape(N, 8, L); lim = th.astype(np.int64).reshape(N, 8, 1, 1); w = wt.astype(np.int64).reshape(N, 8, 1, 16)
    a = np.arange(N)[:, None, None, None]; b = np.arange(8)[None, :, None, None]; s = np.arange(S); shut = np.zeros(N, np.int64)
    for t in range(ST):
        XV = X[a, b, V]; XC = X[a, b, C]; live = n >= 4
        bend = np.add.reduce(np.abs(XV[:, :, :, :-1] + XV[:, :, :, 1:] - 2 * XC[:, :, :, :-1]), axis=-1, dtype=np.int32)
        k = np.argmax(np.where(s[:-1] <= n[..., None] - 3, bend, -1), axis=3)[..., None]
        Vk = np.take_along_axis(V, k, 3); Vn = np.take_along_axis(V, k + 1, 3); Ck = np.take_along_axis(C, k, 3)
        y = np.clip(X[a, b, Vk] + X[a, b, Vn] - X[a, b, Ck], 0, 63)
        dist = np.add.reduce(np.abs(XV - y), axis=-1, dtype=np.int32)
        fit = (s >= k + 2) & (s <= n[..., None] - 1) & (dist <= lim + shut[:, None, None, None]) & live[..., None]
        close = np.any(fit, axis=3); m = np.argmax(fit, axis=3)[..., None]; grow = live & ~close
        size = np.where(close[..., None], m - k - 1, 0)
        ix = np.minimum(k + 1 + s, S - 1); keep = s < size
        PV = np.where(keep, np.take_along_axis(V, ix, 3), 0); PC = np.where(keep, np.take_along_axis(C, ix, 3), 0)
        y = y[:, :, :, 0]; u = np.add.reduce(w * y, axis=-1) & (W - 1)
        h = (((u * u) >> 5) + 37 * Vk[..., 0].astype(np.int64)) & (W - 1)
        src = np.minimum(np.where(s <= k, s, s + size - grow[..., None].astype(np.int64)), S - 1)
        V2 = np.take_along_axis(V, src, 3); C2 = np.take_along_axis(C, src, 3); new = grow[..., None] & (s == k + 1)
        V2 = np.where(new, h[..., None], V2); C2 = np.where(new, Vk, np.where(live[..., None] & (s == k), Vn, C2))
        n2 = np.minimum(n + grow.astype(np.int64), S) - size[..., 0]
        for i in range(L - 1, -1, -1):
            p, q = np.nonzero(grow[:, :, i]); X[p, q, h[p, q, i]] = y[p, q, i]
        d = 1 + t % (N - 1)
        came = np.roll(size, d, axis=0)[..., 0]; yin = np.roll(y, d, axis=0); lin = np.roll(live, d, axis=0)
        take = ~live & (came > n)
        V = np.where(take[..., None], np.roll(PV, d, axis=0), V2); C = np.where(take[..., None], np.roll(PC, d, axis=0), C2); n = np.where(take, came, n2)
        V = np.where(s < n[..., None], V, 0).astype(np.int32); C = np.where(s < n[..., None], C, 0).astype(np.int32)
        has = lin & (n >= 1); old = X.copy()
        for i in range(L - 1, -1, -1):
            p, q = np.nonzero(has[:, :, i]); z = V[p, q, i, 0]; X[p, q, z] = (old[p, q, z] + yin[p, q, i]) >> 1
        shut = np.add.reduce(close.astype(np.int64).reshape(N, -1), axis=1) & 31
    return {"yx": np.ascontiguousarray(X.transpose(0, 1, 3, 2)).reshape(N, 128, W).astype(np.float32).astype(BF), "yv": np.stack([gtable(q.reshape(8, -1)) for q in V]).astype(np.float32),
            "yc": np.stack([gtable(q.reshape(8, -1)) for q in C]).astype(np.float32), "yn": n.astype(np.float32)}

@@ -1,0 +1,724 @@
+from concourse.mybir import AluOpType, AxisListType, ActivationFunctionType
+
+OP = AluOpType
+AF = ActivationFunctionType
+W, L, S, ST = 4096, 256, 16, 5
+BIG = 8388608.0
+F32, BF, I32, U16 = "float32", "bfloat16", "int32", "uint16"
+
+MEASURE = ("gc0 ss0 dd0 gv1 ab0 ky0 ss1 gc1 dd1 pk0 ee0 gv2 ab1 ky1 ss2 gc2 dd2 pk1 ds0 ee1 "
+           "gv3 ab2 ky2 ss3 gc3 dd3 pk2 ds1 ee2 ab3 ky3 pk3 ds2 ee3 ds3")
+CYC, GATHER, SCATTER, WAKE, SLACK = 0.001, 1.5, 3.8, 0.18, 0.02
+BETA = 0.03
+SCRATCH = {"X": ("sbuf", [128, W + L], BF)}
+ALIAS = {}
+
+
+def _pack(buf, names, cols, d):
+    names = names.split()
+    for k, n in enumerate(names):
+        ALIAS[n] = (buf, k * cols, cols, d)
+    SCRATCH[buf] = ("sbuf", [128, len(names) * cols], d)
+
+
+def _add(names, cols, d):
+    for n in names.split():
+        SCRATCH[n] = ("sbuf", [128, cols], d)
+
+
+for _c in range(4):
+    _add("GV%d SS%d GC%d" % (_c, _c, _c), 1024, BF)
+_add("AB0 AB1 EE0 EE1", 1024, BF)
+_pack("VNC", "V N C", 256, F32)
+_add("VCB CIN2 CT1 CT2 DG", 256, F32)
+_pack("MF", "PW m1 m2 m3 m4 m5 m6 m7 m8 m9 KS LM RS MP CT3 QC Hx f1 f2 SO VCA kb s6B zb xB NKB VKB TKb kthB mthB MXB kqB ngB nlB KVs TB nC oC "
+      "m1' m2' m3' m4' m5' m6' m7' m8' m9' Hx' f1' f2' zb'", 256, F32)
+_add("SK SM IV IC iw LNI", 256, I32)
+_add("Pb Vg VL B3 Y Yn SYs GYs BL BL2 Pa Pr g1 g2", 256, BF)
+_add("LST", 768, U16)
+_pack("RR", "Ru Ru'", 256, U16)
+_pack("EQQ", "EQ EQ'", 2176, BF)
+_pack("PLF", "nn V0 live kp2 H2 Z0 Z1 close grow rest MXe TR hp s1 s2 s3 s4 s5 s6 s7 s8 s9 zL take kqe mth kth x Tl "
+      "s1' s2' s3' s4' s5' s6' s7' s8' s9' hp' zL' has", 16, F32)
+_pack("PLI", "KA KB UI HI K37 MX VM", 16, I32)
+_pack("PLU", "o16 off16 z16 bcA bc15", 16, U16)
+_add("bcY", 64, U16)
+_pack("COF", "pcF pmF p4F btF thm lim cs1 e1 e2 wF ws", 1, F32)
+_pack("COI", "pcI pmI p4I btI cI", 1, I32)
+_add("WI THI", 1, I32)
+_add("mq mg mm blkF onesF G8 IdF", 128, F32)
+_pack("IDS", "Ident In1 In2 Ibig Im256 Im4k ones blk blk8k", 128, BF)
+_add("LQ1 LQk LQh LW", 2048, BF)
+_add("CR", 64, BF)
+_add("cc", 64, F32)
+_add("LNF THF", 256, F32)
+_add("G8T", 8, F32)
+_add("bcI", 64, I32)
+for _t in range(ST):
+    _add("rL%d" % _t, 768, F32)
+    _add("rP%d rY%d" % (_t, _t), 256, BF)
+    _add("rB%d" % _t, 48, F32)
+_add("SB", 48, F32)
+for _b in range(8):
+    SCRATCH["pb%d" % _b] = ("psum", [128, 512], F32)
+
+SEMAPHORES = ["sV", "sS", "sT", "sG", "lR", "lP", "lY", "lB"]
+SEMAPHORES += ["a%s%d" % (m, t) for m in "RPYB" for t in range(ST)]
+SEMAPHORES += ["d%d" % k for k in range(24)]
+
+
+def rank_program(g, core, T, topo):
+    rank = T.rank_of(core)
+    if rank is None:
+        return
+    queues = {"V": g.vector, "S": g.scalar, "T": g.tensor, "G": g, "Y": g.sync}
+    count = {}
+    known = {q: {} for q in queues}
+    clock = {}
+    recs = {}
+    ndma = [0]
+
+    par = [0]
+
+    def v(name, lo=0, hi=None, step=1, p=None):
+        if par[0] and name + "'" in ALIAS:
+            name += "'"
+        if name in ALIAS:
+            name, at, width, _d = ALIAS[name]
+            hi = at + (width if hi is None else hi)
+            lo += at
+        hi = SCRATCH[name][1][1] if hi is None else hi
+        t = T[name]
+        sl = slice(lo, hi, step) if step != 1 else slice(lo, hi)
+        return (t[:, sl] if p is None else t[0:p, sl], [(name, lo, hi)], (hi - lo + step - 1) // step, False)
+
+    def ind(win, off):
+        return (win[0].indirect(off[0]), win[1] + off[1], off[2] * 16, True)
+
+    def need(q, reads, writes):
+        toks = []
+        for acc, wr in [(a, False) for a in reads] + [(a, True) for a in writes]:
+            name, lo, hi = acc
+            bank = name.startswith("pb")
+            for (l2, h2, tok, q2, w2) in recs.get(name, []):
+                if bank and q2 != q:
+                    toks.append(tok)
+                elif lo < h2 and l2 < hi and (wr or w2):
+                    if q2 == q and q == "T":
+                        continue
+                    toks.append(tok)
+        return toks
+
+    def wait(q, toks):
+        best = {}
+        for s, n in toks:
+            best[s] = max(best.get(s, 0), n)
+        kn = known[q]
+        todo = sorted(best.items(), key=lambda a: -len(clock.get(a, {})))
+        for s, n in todo:
+            if kn.get(s, 0) >= n:
+                continue
+            if any(clock.get((s2, n2), {}).get(s, 0) >= n for s2, n2 in todo if s2 != s and kn.get(s2, 0) < n2):
+                continue
+            queues[q].wait_ge(T.sem[s], n)
+            for s3, n3 in clock.get((s, n), {}).items():
+                kn[s3] = max(kn.get(s3, 0), n3)
+            kn[s] = max(kn.get(s, 0), n)
+
+    def record(q, tok, reads, writes):
+        for acc, wr in [(a, False) for a in reads] + [(a, True) for a in writes]:
+            name, lo, hi = acc
+            old = recs.get(name, [])
+            if name.startswith("pb"):
+                old = [r for r in old if r[3] == q]
+            if wr:
+                old = [r for r in old if not (lo <= r[0] and r[1] <= hi)]
+            else:
+                old = [r for r in old if r[4] or r[3] != q or (r[0], r[1]) != (lo, hi)]
+            old.append((lo, hi, tok, q, wr))
+            recs[name] = old
+
+    def bump(q, sem, n):
+        count[sem] = count.get(sem, 0) + n
+        tok = (sem, count[sem])
+        clock[tok] = dict(known[q])
+        return tok
+
+    OPS = []
+
+    def add(q, emit, reads, writes, cost, lat=0.0, after=()):
+        OPS.append([q, emit, [a for x in reads for a in x[1]], [a for x in writes for a in x[1]], cost, lat, list(after)])
+        return len(OPS) - 1
+
+    def op(q, fn, reads, writes, cost=0.06):
+        def emit(rd, wr):
+            wait(q, need(q, rd, wr))
+            sem = "s" + q
+            fn(queues[q]).then_inc(T.sem[sem], 1)
+            record(q, bump(q, sem, 1), rd, wr)
+        return add(q, emit, reads, writes, cost)
+
+    def dma(q, out, in_, reads=(), writes=()):
+        sem = "d%d" % ndma[0]
+        ndma[0] += 1
+
+        def emit(rd, wr):
+            wait(q, need(q, rd, wr))
+            queues[q].dma_start(out, in_).then_inc(T.sem[sem], 16)
+            record(q + "d", bump(q, sem, 16), rd, wr)
+        return add(q, emit, reads, writes, 0.1, 5.0 if writes and writes[0][1][0][0] == "X" else 2.2)
+
+    def order():
+        seen, deps, succ = {}, [], [[] for _ in OPS]
+        for i, o in enumerate(OPS):
+            q, dp = o[0], {}
+            for j in o[6]:
+                dp[j] = 1
+            for acc, wr in [(a, 0) for a in o[2]] + [(a, 1) for a in o[3]]:
+                name, lo, hi = acc
+                bank = name.startswith("pb")
+                if bank and seen.get(name) and seen[name][0][3] != q:
+                    seen[name, "before"] = seen.pop(name)
+                for r in seen.get((name, "before"), []):
+                    dp[r[2]] = 1
+                for (l2, h2, j, q2, w2) in seen.get(name, []):
+                    if bank and q == "T":
+                        dp[j] = max(dp.get(j, 0), 0)
+                    elif lo < h2 and l2 < hi and (wr or w2):
+                        dp[j] = 1
+            for acc, wr in [(a, 0) for a in o[2]] + [(a, 1) for a in o[3]]:
+                name, lo, hi = acc
+                old = seen.get(name, [])
+                if wr:
+                    old = [r for r in old if not (lo <= r[0] and r[1] <= hi)]
+                seen[name] = old + [(lo, hi, i, q, wr)]
+            dp.pop(i, None)
+            deps.append(dp)
+            for j in dp:
+                succ[j].append(i)
+        n = len(OPS)
+        prio = [0.0] * n
+        for i in range(n - 1, -1, -1):
+            prio[i] = OPS[i][4] + OPS[i][5] + max([prio[j] + (WAKE if deps[j][i] else -OPS[i][4]) for j in succ[i]] or [0.0])
+        left = [len(dp) for dp in deps]
+        start, fin = [0.0] * n, [0.0] * n
+        free, ready, out = {}, {}, []
+
+        def push(i):
+            r = 0.0
+            for j, k in deps[i].items():
+                r = max(r, fin[j] + WAKE if k else start[j])
+            ready.setdefault(OPS[i][0], []).append((r, BETA * i - prio[i], i))
+        for i in range(n):
+            if left[i] == 0:
+                push(i)
+        while len(out) < n:
+            best = None
+            for q, lst in ready.items():
+                if lst:
+                    t0 = max(free.get(q, 0.0), min(lst)[0])
+                    p, i, r = min((c[1], c[2], c) for c in lst if c[0] <= t0 + SLACK)
+                    st = max(t0, r[0])
+                    if best is None or st < best[0]:
+                        best = (st, q, i, r)
+            st, q, i, r = best
+            ready[q].remove(r)
+            start[i] = st
+            fin[i] = st + OPS[i][4] + OPS[i][5]
+            free[q] = st + OPS[i][4]
+            out.append(i)
+            for j in succ[i]:
+                left[j] -= 1
+                if left[j] == 0:
+                    push(j)
+        return out
+
+    def vcost(out, a, b=None):
+        views = [x for x in (out, a, b) if x is not None]
+        if out[3]:
+            return 0.06 + SCATTER * CYC * out[2]
+        if any(x[3] for x in views):
+            return 0.06 + GATHER * CYC * out[2]
+        n = max(out[2], a[2])
+        psum = any(x[1][0][0].startswith("pb") for x in views[1:])
+        small = all(SCRATCH[x[1][0][0]][2] in (BF, U16) for x in views)
+        if b is not None:
+            n *= 1 if psum else 2
+        elif small:
+            n *= 0.5
+        return max(64, n) * CYC
+
+    def tt(out, a, b, o):
+        op("V", lambda e: e.tensor_tensor(out[0], a[0], b[0], o), [a, b], [out], vcost(out, a, b))
+
+    def ts(out, a, s1, o0, s2=None, o1=None):
+        rd = [a] + [x for x in (s1, s2) if isinstance(x, tuple)]
+        x1 = s1[0] if isinstance(s1, tuple) else s1
+        x2 = s2[0] if isinstance(s2, tuple) else s2
+        if o1 is None:
+            op("V", lambda e: e.tensor_scalar(out[0], a[0], x1, None, o0), rd, [out], vcost(out, a))
+        else:
+            op("V", lambda e: e.tensor_scalar(out[0], a[0], x1, x2, o0, o1), rd, [out], vcost(out, a))
+
+    def cp(out, a):
+        op("V", lambda e: e.tensor_copy(out[0], a[0]), [a], [out], vcost(out, a))
+
+    def act(out, a, f=AF.Copy, scale=1.0, bias=0.0):
+        c = (0.07 + GATHER * CYC * out[2]) if a[3] else 0.06 + CYC * max(64, out[2])
+        op("S", lambda e: e.activation(out[0], a[0], f, bias=bias, scale=scale), [a], [out], c)
+
+    def mm(out, l, r, start, stop):
+        c = max(64, r[2]) * CYC * (4 if SCRATCH[r[1][0][0]][2] == F32 else 1)
+        op("T", lambda e: e.matmul(out[0], l[0], r[0], start, stop), [l, r], [out], c)
+
+    def scan(out, d0, d1, o0, o1):
+        op("V", lambda e: e.tensor_tensor_scan(out[0], d0[0], d1[0], 0.0, o0, o1), [d0, d1], [out], max(64, out[2]) * CYC)
+
+    def tr(out, a):
+        op("V", lambda e: e.transpose(out[0], a[0]), [a], [out], vcost(out, a))
+
+    def fill(out, c):
+        op("V", lambda e: e.memset(out[0], c), [], [out])
+
+    def iota(out, pat, base, cm):
+        if SCRATCH[out[1][0][0]][2] == I32:
+            op("G", lambda e: e.iota(out[0], pat, base, cm), [], [out], 0.13 + 2 * CYC * out[2])
+        else:
+            op("G", lambda e: e.iota(out[0], pat, base, cm, allow_small_or_imprecise_dtypes=True), [], [out], 0.13 + 2 * CYC * out[2])
+
+    def bc(x):
+        return ind(x, v("bcA"))
+
+    def wide(dst, x, scale=1.0, bias=0.0):
+        act(v(dst), bc(v(x)), AF.Copy if (scale, bias) == (1.0, 0.0) else AF.Identity, scale, bias)
+
+    def line(dst, x, scale, bias):
+        act(dst, x, AF.Identity, scale, bias)
+
+    def last(name, a0=0, a1=16):
+        return v(name, a0 * 16 + 15, a1 * 16, 16)
+
+    half = W // 2
+    dma("Y", T.IV[:], T.vl[:], [], [v("IV")])
+    dma("S", T.IC[:], T.cl[:], [], [v("IC")])
+    dma("Y", T.X[:, 0:half], T.xc[:, 0:half], [], [v("X", 0, half)])
+    dma("S", T.X[:, half:W], T.xc[:, half:W], [], [v("X", half, W)])
+    dma("Y", T.LNI[0:8, :], T.ln[:], [], [v("LNI")])
+    dma("S", T.WI[:], T.wt[:], [], [v("WI")])
+    dma("Y", T.THI[0:8, :], T.th[:], [], [v("THI")])
+
+    iota(v("pcI"), [[0, 1]], 0, 1)
+    iota(v("MP"), [[0, 8], [1, 2], [0, 16]], 0, 0)
+    iota(v("iw", 0, 16), [[1, 16]], 0, 0)
+    iota(v("iw", 16, 32), [[16, 16]], 15, 0)
+    iota(v("QC"), [[0, 16], [1, 16]], 0, 0)
+    iota(v("mg"), [[1, 8], [0, 16]], 0, 0)
+    iota(v("mq"), [[0, 8], [1, 16]], 0, 0)
+    iota(v("mm"), [[1, 128]], 0, 0)
+    iota(v("cc"), [[1, 64]], 0, 0)
+    iota(v("bcI"), [[16, 4], [0, 16]], 0, 0)
+    iota(v("f2", 0, 16), [[16, 16]], W + 2, 0)
+    ts(v("pmI"), v("pcI"), 15, OP.bitwise_and)
+    ts(v("p4I"), v("pcI"), 4, OP.arith_shift_right)
+    ts(v("btI"), v("p4I"), 1, OP.bitwise_and)
+    for a, b in (("pcF", "pcI"), ("pmF", "pmI"), ("p4F", "p4I"), ("btF", "btI")):
+        cp(v(a), v(b))
+    ts(v("MP"), v("MP"), v("btF"), OP.is_equal)
+    cp(v("bcA"), v("iw", 0, 16))
+    cp(v("bc15"), v("iw", 16, 32))
+
+    def conv(src, dst):
+        act(v("CIN2", 0, 240), v(src, 16, 256))
+        act(v("CIN2", 240, 256), v(src, 0, 16))
+        tr(v("CT1"), v(src))
+        tr(v("CT2"), v("CIN2"))
+        act(v("pb6", 16, 256), v("CT2", 0, 240))
+        act(v("pb6", 0, 16), v("CT2", 240, 256))
+        tt(v("pb5", 0, 256), v("CT1"), v("pb6", 0, 256), OP.subtract)
+        tt(v("m9"), v("pb5", 0, 256), v("MP"), OP.mult)
+        tt(v(dst), v("m9"), v("pb6", 0, 256), OP.add)
+
+    ts(v("m1"), v("IV"), 4096.0, OP.mult)
+    tt(v("VCA"), v("m1"), v("IC"), OP.add)
+    conv("VCA", "VCB")
+    cp(v("iw"), v("VCB"))
+    ts(v("IV"), v("iw"), 12, OP.arith_shift_right)
+    cp(v("LST", 0, 256), v("IV"))
+    ts(v("IC"), v("iw"), 4095, OP.bitwise_and)
+    cp(v("LST", 256, 511), v("IV", 1, 256))
+    cp(v("LST", 511, 512), v("IV", 255, 256))
+    cp(v("LST", 512, 768), v("IC"))
+
+    def consts1():
+        cp(v("V"), v("IV"))
+        cp(v("C"), v("IC"))
+        cp(v("N", 0, 255), v("V", 1, 256))
+        cp(v("N", 255, 256), v("V", 255, 256))
+        ts(v("V0"), v("V", 0, 256, 16), 2.0, OP.add)
+        ts(v("DG"), v("QC"), v("pmF"), OP.is_equal)
+        ts(v("RS"), v("QC"), 0.0, OP.is_gt)
+        op("V", lambda e: e.tensor_scalar(T.G8[0:8, :], T.mg[0:8, :], v("pcF", p=8)[0], None, OP.is_equal), [v("mg"), v("pcF")], [v("G8")])
+        op("V", lambda e: e.tensor_copy(T.LNF[0:8, :], T.LNI[0:8, :]), [v("LNI")], [v("LNF")])
+        op("V", lambda e: e.tensor_copy(T.THF[0:8, 0:1], T.THI[0:8, :]), [v("THI")], [v("THF")])
+        op("T", lambda e: e.matmul(T.pb0[:, 0:256], T.G8[0:8, :], T.LNF[0:8, :], True, True), [v("G8"), v("LNF")], [v("pb0", 0, 256)])
+        op("T", lambda e: e.matmul(T.pb1[:, 0:1], T.G8[0:8, :], T.THF[0:8, 0:1], True, True), [v("G8"), v("THF")], [v("pb1", 0, 1)])
+        cp(v("pb7", 0, 256), v("QC"))
+        tt(v("f1"), v("pb0", 0, 256), v("DG"), OP.mult)
+        scan(v("f2"), v("RS"), v("f1"), OP.mult, OP.add)
+        cp(v("nn"), last("f2"))
+        ts(v("thm"), v("pb1", 0, 1), 0.5, OP.mult, -8192.0, OP.add)
+        cp(v("lim"), v("thm"))
+        limits()
+        ts(v("Ident"), v("mm"), v("pcF"), OP.is_equal)
+        for nm, c in (("In1", -1.0), ("In2", -2.0), ("Ibig", BIG), ("Im256", -256.0), ("Im4k", -4096.0)):
+            ts(v(nm), v("Ident"), c, OP.mult)
+        fill(v("ones"), 1.0)
+        ts(v("IdF"), v("mm"), v("pcF"), OP.is_equal)
+
+    def consts2():
+        ts(v("blkF"), v("mg"), v("p4F"), OP.is_equal)
+        tt(v("f1", 0, 128), v("mq"), v("blkF"), OP.mult)
+        ts(v("f1", 128, 256), v("blkF"), -99.0, OP.mult, 99.0, OP.add)
+        tt(v("mq"), v("f1", 0, 128), v("f1", 128, 256), OP.add)
+        ts(v("e1"), v("pcF"), 0.0, OP.is_equal)
+        ts(v("e2"), v("pcF"), 1.0, OP.is_equal, 3840.0, OP.mult)
+        ts(v("ws"), v("pcF"), 2.0, OP.is_equal, -BIG, OP.mult)
+        tt(v("e2"), v("e2"), v("ws"), OP.add)
+        ts(v("CR"), v("cc"), v("e1"), OP.mult, v("e2"), OP.add)
+        for q in range(16):
+            ts(v("LQ1", q * 128, q * 128 + 128), v("mq"), float(q), OP.is_equal)
+        ts(v("LQk"), v("LQ1"), 4096.0, OP.mult)
+        ts(v("bcY"), v("bcI"), v("pmF"), OP.add)
+        ts(v("LQh"), v("LQ1"), -0.5, OP.mult)
+        cp(v("wF"), v("WI"))
+        ts(v("LW"), v("LQ1"), v("wF"), OP.mult)
+        ts(v("LM"), v("QC"), v("pmF"), OP.is_le, -16384.0, OP.mult)
+        ts(v("blk"), v("mg"), v("p4F"), OP.is_equal)
+        ts(v("blk8k"), v("blk"), 8192.0, OP.mult)
+        fill(v("onesF"), 1.0)
+        ts(v("G8T"), v("mm", 0, 8), v("p4F"), OP.is_equal)
+
+    ts(v("TR"), v("f2", 0, 16), v("pmF"), OP.add)
+
+    def limits():
+        ts(v("live"), v("nn"), 4.0, OP.is_ge)
+        wide("ngB", "nn", 1.08, -3.29)
+        wide("nlB", "nn", 1.0, -1.0)
+
+    PP = v("pb7", 0, 256)
+
+    def masks():
+        act(v("m1"), PP, AF.Identity, scale=-8192.0, bias=131074.0)
+        act(v("Pb"), PP)
+        tt(v("Vg"), v("ngB"), PP, OP.is_ge)
+        tt(v("VL"), v("nlB"), PP, OP.is_ge)
+        tt(v("PW"), v("m1"), v("V"), OP.add)
+
+    def dedupe(z, gap1, gap2):
+        tt(v("Hx"), bc(v(z)), v("DG"), OP.mult)
+        wide("zb", z)
+        mm(v("pb4", 0, 256), v("blkF"), v("Hx"), True, True)
+        gap1()
+        tt(v("pb0", 0, 256), v("pb4", 0, 256), v("LM"), OP.add)
+        cp(v("Ru"), v("pb4", 0, 256))
+        tt(v("EQ", 0, 256), v("zb"), v("pb0", 0, 256), OP.is_equal)
+        mm(v("pb5", 0, 256), v("blk8k"), v("EQ", 0, 256), True, False)
+        at = 256
+        for a in range(15):
+            w = 240 - 16 * a
+            ts(v("EQ", at, at + w), v("Ru", 256 - w, 256), v(z, a, a + 1), OP.is_equal)
+            mm(v("pb5", 256 - w, 256), v("blk8k"), v("EQ", at, at + w), False, a == 14)
+            at += w
+        gap2()
+        tt(v("f1"), v("pb5", 0, 256), v("DG"), OP.mult)
+        scan(v("f2"), v("RS"), v("f1"), OP.mult, OP.add)
+        tt(v("s5"), last("f2"), v("hp"), OP.add)
+        tt(v("s8"), v("s5"), v("TR"), OP.min)
+        ts(v("off16"), v("s8"), -2.0, OP.add)
+
+    def names(yes):
+        line(v("s6"), v(yes), -16384.0, 16384.0)
+        tt(v("hp"), v("s6"), v("zL"), OP.add)
+
+    def send(buf, dst_buf, dst_rank, lsem, asem):
+        dst = T.cores[dst_rank]
+        rid, pid, _se = topo.addr(dst)
+        n = len(topo.engines(core, dst))
+
+        def emit(rd, wr):
+            wait("G", need("G", rd, wr))
+            g.remote_dma(T[dst_buf][:], T[buf][:], T.sem[asem], T.sem[lsem], pid, rid, topo.mask(core, dst))
+            record("Gr", bump("G", lsem, n), rd, wr)
+        return add("G", emit, [v(buf)], [], 1.5, 3.0)
+
+    def arrive(buf, asem, src_rank, sent):
+        n = len(topo.engines(T.cores[src_rank], core))
+
+        def emit(rd, wr):
+            count[asem] = n
+            clock[(asem, n)] = {}
+            recs[buf] = [(0, 99999, (asem, n), "far", True)]
+        add("F", emit, [], [v(buf)], 0.0, 1.0, [sent])
+
+    def gv(c):
+        (cp if c == 0 else act)(v("GV%d" % c), ind(v("X", 0, W), v("LST", 64 * c, 64 * c + 64)))
+
+    gv(0)
+    consts1()
+    consts2()
+    for t in range(ST):
+        d = 1 + t % 3
+        to, frm = (rank + d) % 4, (rank - d) % 4
+        rL, rP, rY, rB = "rL%d" % t, "rP%d" % t, "rY%d" % t, "rB%d" % t
+        lastt = t == ST - 1
+
+        def gc(c):
+            act(v("GC%d" % c), ind(v("X", 0, W), v("LST", 512 + 64 * c, 512 + 64 * c + 64)))
+
+        def ss(c):
+            tt(v("SS%d" % c), ind(v("X", 0, W), v("LST", 256 + 64 * c, 256 + 64 * c + 64)), v("GV%d" % c), OP.add)
+
+        def dd(c):
+            for k in range(2):
+                b = "pb%d" % (2 * (c % 2) + k)
+                mm(v(b), v("Ident"), v("SS%d" % c, 512 * k, 512 * k + 512), True, False)
+                mm(v(b), v("In2"), v("GC%d" % c, 512 * k, 512 * k + 512), False, True)
+
+        def ab(c):
+            for k in range(2):
+                act(v("AB%d" % (c % 2), 512 * k, 512 * k + 512), v("pb%d" % (2 * (c % 2) + k)), AF.Abs)
+
+        def key(c):
+            o = v("pb%d" % (4 + c % 2), 0, 64)
+            mm(o, v("ones"), v("CR"), True, False)
+            mm(o, v("Im256"), v("Pb", 64 * c, 64 * c + 64), False, False)
+            mm(o, v("Ibig"), v("Vg", 64 * c, 64 * c + 64), False, False)
+            for q in range(16):
+                mm(o, v("LQk", 128 * q, 128 * q + 128), v("AB%d" % (c % 2), q, 1024, 16), False, q == 15)
+
+        def pick_a(c):
+            k = v("pb%d" % (4 + c % 2), 0, 64)
+            lo, hi = 64 * c, 64 * c + 64
+            a, b = 4 * c, 4 * c + 4
+            scan(v("SK", lo, hi), v("RS", 0, 64), k, OP.mult, OP.max)
+            ts(v("KA", a, b), last("SK", a, b), 63, OP.bitwise_and)
+            ts(v("o16", a, b), v("KA", a, b), 16.0, OP.mult, v("pmF"), OP.add)
+            cp(v("SYs", lo, hi), ind(v("GC%d" % c), v("o16", a, b)))
+            act(v("KS", lo, hi), k)
+            tt(v("GYs", lo, hi), ind(v("SS%d" % c), v("o16", a, b)), v("SYs", lo, hi), OP.subtract)
+            ts(v("KB", a, b), last("SK", a, b), 3840, OP.bitwise_and)
+            ts(v("kp2", a, b), v("KB", a, b), -1.0 / 256, OP.mult, 17.0, OP.add)
+            ts(v("Y", lo, hi), v("GYs", lo, hi), 0.0, OP.max, 63.0, OP.min)
+
+        def ee(c):
+            lo, hi = 64 * c, 64 * c + 64
+            tt(v("EE%d" % (c % 2)), ind(v("Y", lo, hi), v("bcY")), v("GV%d" % c), OP.max)
+            tt(v("B3", lo, hi), ind(v("kp2"), v("bcA", 4 * c, 4 * c + 4)), v("Pb", lo, hi), OP.is_le)
+
+        def ds(c):
+            lo, hi = 64 * c, 64 * c + 64
+            o = v("pb7", lo, hi)
+            mm(o, v("Im4k"), v("VL", lo, hi), True, False)
+            for q in range(16):
+                mm(o, v("LQh", 128 * q, 128 * q + 128), v("GV%d" % c, q, 1024, 16), False, False)
+            mm(o, v("Im4k"), v("B3", lo, hi), False, False)
+            for q in range(16):
+                mm(o, v("LQ1", 128 * q, 128 * q + 128), v("EE%d" % (c % 2), q, 1024, 16), False, q == 15)
+
+        par[0] = 0
+        sent = {}
+        sent["R"] = send("VNC", rL, to, "lR", "aR%d" % t)
+        masks()
+        sent["P"] = send("Pb", rP, to, "lP", "aP%d" % t)
+        for w in MEASURE.split():
+            {"ss": ss, "gc": gc, "gv": gv, "dd": dd, "ab": ab, "ky": key, "pk": pick_a, "ee": ee, "ds": ds}[w[:2]](int(w[2:]))
+        act(v("kb"), ind(v("SK"), v("bc15")))
+        sent["Y"] = send("Y", rY, to, "lY", "aY%d" % t)
+        for q in range(16):
+            mm(v("pb6", 16, 32), v("LQh", 128 * q, 128 * q + 128), v("Y", q, 256, 16), q == 0, q == 15)
+        for q in range(16):
+            mm(v("pb6", 0, 16), v("LW", 128 * q, 128 * q + 128), v("Y", q, 256, 16), q == 0, q == 15)
+        ts(v("Tl"), v("pb6", 16, 32), -1.0, OP.mult, v("lim"), OP.add)
+        wide("TB", "Tl")
+        OH, O15, KV, K2 = v("pb0", 256, 512), v("pb1", 0, 256), v("pb1", 256, 512), v("pb2", 0, 256)
+        t1, SN, SC, PS = v("pb2", 256, 512), v("pb3", 0, 256), v("pb6", 0, 256), v("pb0", 0, 256)
+        act(v("pb2", 256, 512), v("Pb"))
+        tt(OH, v("kb"), v("KS"), OP.is_equal)
+        tt(v("m2"), v("V"), OH, OP.mult)
+        tt(v("m3"), v("N"), OH, OP.mult)
+        scan(v("m4"), v("RS"), v("m2"), OP.mult, OP.add)
+        scan(v("m5"), v("RS"), v("m3"), OP.mult, OP.add)
+        ts(v("K37"), last("m4"), 37.0, OP.mult)
+        kq = v("SB", 16, 32)
+        line(kq, v("kp2"), -1.0, 17.0)
+        cp(v("UI"), v("pb6", 0, 16))
+        ts(v("UI"), v("UI"), 4095, OP.bitwise_and)
+        tt(v("HI"), v("UI"), v("UI"), OP.mult)
+        ts(v("HI"), v("HI"), 5, OP.arith_shift_right)
+        line(v("SB", 32, 48), last("m5"), 1.0, 2.0)
+        tt(v("HI"), v("HI"), v("K37"), OP.add)
+        ts(v("HI"), v("HI"), 4095, OP.bitwise_and)
+        ts(v("H2"), v("HI"), 2.0, OP.add)
+        act(v("NKB"), ind(v("m5"), v("bc15")))
+        act(v("VKB"), ind(v("m4"), v("bc15")))
+        ts(v("rest"), v("kp2"), 17.0, OP.is_equal)
+        F = v("pb0", 0, 256)
+        tt(F, v("TB"), v("pb7", 0, 256), OP.is_ge)
+        tt(v("m1"), F, v("PW"), OP.mult)
+        scan(v("SM"), v("RS"), v("m1"), OP.mult, OP.max)
+        ts(v("close"), last("SM"), 0.0, OP.is_gt)
+        ts(v("MX"), last("SM"), 13, OP.arith_shift_right)
+        ts(v("VM"), last("SM"), 8191, OP.bitwise_and)
+        tt(v("s1"), kq, v("MX"), OP.subtract)
+        tt(v("SB", 0, 16), v("s1"), v("close"), OP.mult)
+        sent["B"] = send("SB", rB, to, "lB", "aB%d" % t)
+        tt(v("grow"), v("live"), v("close"), OP.subtract)
+        tt(v("zL"), v("H2"), v("grow"), OP.mult)
+        names("grow")
+        wide("s6B", "grow", 16.0, -1.0)
+        tt(v("x"), v("zL"), v("VM"), OP.add)
+
+        def gap1():
+            wide("xB", "x", 1.0, -2.0)
+            tt(v("s3"), v("nn"), v("grow"), OP.add)
+            ts(v("s3"), v("s3"), 16.0, OP.min)
+            tt(O15, v("s6B"), v("pb2", 256, 512), OP.is_equal)
+            tt(v("nn"), v("s3"), v("SB", 0, 16), OP.subtract)
+            act(KV, O15, AF.Identity, scale=-1.0, bias=1.0)
+            act(v("KVs"), O15, AF.Identity, scale=-1.0, bias=1.0)
+            op("V", lambda e: e.tensor_reduce(v("cs1")[0], v("close")[0], AxisListType.X, OP.add), [v("close")], [v("cs1")])
+            tt(v("MXe"), v("MX"), v("grow"), OP.add)
+
+        def gap2():
+            mm(v("pb6", 0, 1), v("onesF"), v("cs1"), True, True)
+            tt(K2, v("KVs"), OH, OP.subtract)
+            tt(v("m7"), v("xB"), O15, OP.mult)
+            tt(t1, v("V"), KV, OP.mult)
+            tt(v("V"), t1, v("m7"), OP.add)
+
+        dedupe("zL", gap1, gap2)
+        cp(ind(v("X"), v("off16")), v("Y"))
+        if not lastt:
+            tt(v("m8"), v("xB"), OH, OP.mult)
+            tt(v("m9"), v("NKB"), O15, OP.mult)
+            mm(SN, v("IdF"), v("m8"), True, False)
+            mm(SN, v("IdF"), v("m9"), False, False)
+        tt(v("nC"), v("VKB"), O15, OP.mult)
+        cp(v("cI"), v("pb6", 0, 1))
+        ts(v("cI"), v("cI"), 31, OP.bitwise_and)
+        ts(v("lim"), v("cI"), 0.5, OP.mult, v("thm"), OP.add)
+        mm(SC, v("IdF"), v("m3"), True, False)
+        mm(SC, v("IdF"), v("nC"), False, False)
+        for m, b in (("R", rL), ("P", rP), ("Y", rY), ("B", rB)):
+            arrive(b, "a%s%d" % (m, t), frm, sent[m])
+        par[0] = 1
+        e_, k_, n_ = v(rB, 0, 16), v(rB, 16, 32), v(rB, 32, 48)
+        act(v("s4"), k_, AF.Sign)
+        tt(v("s1"), e_, v("nn"), OP.is_gt)
+        ts(v("s7"), v("nn"), 1.0, OP.is_ge)
+        tt(v("s9"), v("s7"), v("s4"), OP.mult)
+        tt(v("Z0"), v("V0"), v("s9"), OP.mult)
+        tt(v("Z1"), n_, v("Z0"), OP.subtract)
+        tt(v("take"), v("s1"), v("rest"), OP.mult)
+        tt(v("Z1"), v("Z1"), v("take"), OP.mult)
+        tt(v("zL"), v("Z0"), v("Z1"), OP.add)
+        tt(v("has"), v("s9"), v("take"), OP.max)
+        names("has")
+        tt(v("s2"), n_, v("V0"), OP.subtract)
+        tt(v("s3"), e_, v("nn"), OP.subtract)
+        wide("TKb", "take")
+        act(v("pb1", 0, 256), v("TKb"))
+        act(v("pb1", 256, 512), v("TKb"), AF.Identity, scale=-1.0, bias=1.0)
+        TP, NT = v("pb1", 0, 256), v("pb1", 256, 512)
+        tt(v("s2"), v("s2"), v("take"), OP.mult)
+        tt(v("s3"), v("s3"), v("take"), OP.mult)
+        tt(v("V0"), v("V0"), v("s2"), OP.add)
+        tt(v("nn"), v("nn"), v("s3"), OP.add)
+        ts(v("z16"), v("V0"), -2.0, OP.add)
+
+        def take(k, acc):
+            own = v("VNC", 256 * k, 256 * k + 256)
+            a, b = v("m%d" % (2 * k)), v("m%d" % (2 * k + 1))
+            tt(a, own, v("pb2", 0, 256), OP.mult)
+            tt(b, v(rL, 256 * k, 256 * k + 256), TP, OP.mult)
+            mm(acc, v("IdF"), a, False, False)
+            mm(acc, v("IdF"), b, False, True)
+            act(own, acc)
+            if not lastt:
+                cp(v("LST", 256 * k, 256 * k + 256), acc)
+
+        def gap3():
+            tt(t1, v("V"), NT, OP.mult)
+            tt(v("m1"), v(rL, 0, 256), TP, OP.mult)
+            tt(v("V"), t1, v("m1"), OP.add)
+            if not lastt:
+                cp(v("LST", 0, 256), v("V"))
+            tt(K2, K2, v("TKb"), OP.subtract)
+            tt(v("s2"), v("take"), k_, OP.mult)
+            line(v("s3"), v("take"), 16.0, 0.0)
+            tt(v("MXe"), v("MXe"), v("s2"), OP.add)
+            tt(v("kqe"), kq, v("s3"), OP.add)
+            wide("MXB", "MXe")
+            wide("kqB", "kqe")
+            line(v("kthB"), v("kqB"), -1.0, 15.0)
+            line(v("mthB"), v("MXB"), -1.0, 16.0)
+            limits()
+
+        def gap4():
+            tt(v("Pa"), v("Pb"), NT, OP.mult)
+            tt(v("Pr"), v(rP), TP, OP.mult)
+            tt(v("BL"), ind(v("X", 0, W), v("z16")), v(rY), OP.add)
+            ts(v("BL2"), v("BL"), 0.5, OP.mult, 159.75, OP.add)
+            ts(v("BL"), v("BL2"), -160.0, OP.add)
+            if not lastt:
+                take(1, SN)
+            take(2, SC)
+
+        dedupe("zL", gap3, gap4)
+        cp(ind(v("X"), v("off16")), v("BL"))
+        if lastt:
+            dma("Y", T.yx[:, 0:half], T.X[:, 0:half], [v("X", 0, half)], [])
+            dma("S", T.yx[:, half:W], T.X[:, half:W], [v("X", half, W)], [])
+        else:
+            gv(0)
+        mm(PS, v("Ident"), v("Pa"), True, False)
+        mm(PS, v("Ident"), v("Pr"), False, True)
+        ga, gb = v("pb2", 0, 256), v("pb2", 256, 512)
+        tt(ga, v("kthB"), PS, OP.is_lt)
+        tt(gb, v("mthB"), PS, OP.is_le)
+        tt(v("g1"), v("MXB"), ga, OP.mult)
+        tt(v("g2"), v("kqB"), gb, OP.mult)
+        mm(PP, v("Ident"), v("Pa"), True, False)
+        mm(PP, v("Ident"), v("Pr"), False, False)
+        mm(PP, v("Ident"), v("g1"), False, False)
+        mm(PP, v("In1"), v("g2"), False, True)
+
+    tt(v("Hx"), bc(v("nn")), v("DG"), OP.mult)
+    op("T", lambda e: e.matmul(T.pb4[0:8, 0:256], T.G8T[:], v("Hx")[0], True, True), [v("G8T"), v("Hx")], [v("pb4", 0, 256)])
+    ts(v("m7"), v("V"), 4096.0, OP.mult)
+    VC = v("pb2", 0, 256)
+    tt(VC, v("m7"), v("C"), OP.add)
+    tt(v("pb3", 0, 256), v("nlB"), PP, OP.is_ge)
+    line(v("m6"), v("pb3", 0, 256), -100.0, 100.0)
+    tt(v("Pa"), PP, v("m6"), OP.add)
+    op("V", lambda e: e.tensor_copy(T.LNF[0:8, :], T.pb4[0:8, 0:256]), [v("pb4", 0, 256)], [v("LNF")])
+    dma("Y", T.yn[:], T.LNF[0:8, :], [v("LNF")], [])
+    for p in range(16):
+        b, pr, sn = v(("g1", "g2", "Pr")[p % 3]), v("m%d" % (2 + p % 3)), ("m5", "m7", "m8")[p % 3]
+        ts(b, v("Pa"), float(p), OP.is_equal)
+        tt(pr, b, VC, OP.mult)
+        scan(v(sn), v("RS"), pr, OP.mult, OP.add)
+        act(v("SO", p, 256, 16), last(sn))
+    conv("SO", "VCB")
+    cp(v("iw"), v("VCB"))
+    ts(v("IV"), v("iw"), 12, OP.arith_shift_right)
+    ts(v("IC"), v("iw"), 4095, OP.bitwise_and)
+    cp(v("V"), v("IV"))
+    dma("Y", T.yv[:], v("V")[0], [v("V")], [])
+    cp(v("C"), v("IC"))
+    dma("S", T.yc[:], v("C")[0], [v("C")], [])
+    for i in order():
+        OPS[i][1](OPS[i][2], OPS[i][3])
+    for s in sorted(count):
+        if known["G"].get(s, 0) < count[s]:
+            g.wait_ge(T.sem[s], count[s])

@@ -3,14 +3,13 @@ from concourse.mybir import AluOpType, AxisListType, ActivationFunctionType
 OP = AluOpType
 AF = ActivationFunctionType
 W, L, S, ST = 4096, 256, 16, 5
-BIG = 8388608.0
+BIG, KZ, NONE = 4194304.0, 262144.0, 8191.0
 F32, BF, I32, U16 = "float32", "bfloat16", "int32", "uint16"
 
-MEASURE = ("gc0 ss0 dd0 gv1 ab0 ky0 ss1 gc1 dd1 pk0 ee0 gv2 ab1 ky1 ss2 gc2 dd2 pk1 ds0 ee1 "
-           "gv3 ab2 ky2 ss3 gc3 dd3 pk2 ds1 ee2 ab3 ky3 pk3 ds2 ee3 ds3")
-CYC, GATHER, SCATTER, WAKE, SLACK = 0.001, 1.5, 3.8, 0.18, 0.02
-BETA = 0.03
-SCRATCH = {"X": ("sbuf", [128, W + L], BF)}
+WHO_V, WHO_C = "SVSSSSSS", "VVVVVVVV"
+CYC, GATHER, SCATTER, WAKE, SLACK = 0.0009, 1.5, 3.8, 0.16, 0.02
+BETA = 0.01
+SCRATCH = {"X": ("sbuf", [128, 2 * W], BF)}
 ALIAS = {}
 
 
@@ -26,44 +25,45 @@ def _add(names, cols, d):
         SCRATCH[n] = ("sbuf", [128, cols], d)
 
 
-for _c in range(4):
-    _add("GV%d SS%d GC%d" % (_c, _c, _c), 1024, BF)
-_add("AB0 AB1 EE0 EE1", 1024, BF)
-_pack("VNC", "V N C", 256, F32)
-_add("VCB CIN2 CT1 CT2 DG", 256, F32)
-_pack("MF", "PW m1 m2 m3 m4 m5 m6 m7 m8 m9 KS LM RS MP CT3 QC Hx f1 f2 SO VCA kb s6B zb xB NKB VKB TKb kthB mthB MXB kqB ngB nlB KVs TB nC oC "
-      "m1' m2' m3' m4' m5' m6' m7' m8' m9' Hx' f1' f2' zb'", 256, F32)
+_add("GV0 GV1 DC0 DC1", 2064, BF)
+_add("AB0 AB1", 2048, BF)
+_add("EE0 EE1", 1792, BF)
+_add("EQ", 4096, BF)
+_add("VK", 288, F32)
+ALIAS["V"], ALIAS["cumk"], ALIAS["Vn"] = ("VK", 0, 256, F32), ("VK", 256, 16, F32), ("VK", 272, 16, F32)
+_add("Cp", 256, F32)
+_add("rRV rRC", 272, F32)
+_add("OHp posp negp", 272, BF)
+ALIAS["OH"], ALIAS["pos"], ALIAS["neg"] = ("OHp", 16, 256, BF), ("posp", 16, 256, BF), ("negp", 16, 256, BF)
+_pack("MF", "Cd C1 C1x PW m1 m2 m3 m4 m5 m6 m7 m8 fxV fxC eN tV tC Wz Ez RSf RSm DGf i32s SO f1 f2 QC", 256, F32)
+_pack("MB", "val cum nw sgp sgx sgB kpw sk stepm mN gw cw tw ntw RS DG El pa pb pc Yn BL BL2 BL3 CR CX C4 g1 g2 g3 cumP", 256, BF)
+_add("Y", 256, BF)
 _add("SK SM IV IC iw LNI", 256, I32)
-_add("Pb Vg VL B3 Y Yn SYs GYs BL BL2 Pa Pr g1 g2", 256, BF)
-_add("LST", 768, U16)
-_pack("RR", "Ru Ru'", 256, U16)
-_pack("EQQ", "EQ EQ'", 2176, BF)
-_pack("PLF", "nn V0 live kp2 H2 Z0 Z1 close grow rest MXe TR hp s1 s2 s3 s4 s5 s6 s7 s8 s9 zL take kqe mth kth x Tl "
-      "s1' s2' s3' s4' s5' s6' s7' s8' s9' hp' zL' has", 16, F32)
-_pack("PLI", "KA KB UI HI K37 MX VM", 16, I32)
-_pack("PLU", "o16 off16 z16 bcA bc15", 16, U16)
-_add("bcY", 64, U16)
-_pack("COF", "pcF pmF p4F btF thm lim cs1 e1 e2 wF ws", 1, F32)
-_pack("COI", "pcI pmI p4I btI cI", 1, I32)
+_add("LV LC Ru", 256, U16)
+_pack("PLF", "nn V0 live lv kp close grow rest hk kn Vk hh e s1 s2 s3 s4 s5 s6 s7 s8 s9 z z0 dz th2 take lose zA oA TR size n1 dn dv0", 16, F32)
+_pack("PLI", "KA KB UI HI K37 VM", 16, I32)
+_pack("PLU", "o16 o17 off16 z16 bcA", 16, U16)
+_pack("PLB", "OB zero", 16, BF)
+_pack("COF", "pcF pmF p4F thm lim cs1 e1 e2 e3 wF wq wp", 1, F32)
+_pack("COI", "pcI pmI p4I cI", 1, I32)
 _add("WI THI", 1, I32)
-_add("mq mg mm blkF onesF G8 IdF", 128, F32)
-_pack("IDS", "Ident In1 In2 Ibig Im256 Im4k ones blk blk8k", 128, BF)
-_add("LQ1 LQk LQh LW", 2048, BF)
-_add("CR", 64, BF)
-_add("cc", 64, F32)
+_pack("MQ", "mg mm onesF G8 IdF LIM PW2", 128, F32)
+_pack("IDS", "Ident In1 Ih Inh Ibig Ibigh I108 I094 IZb IZv I4k In4k ones Yw", 128, BF)
+_pack("N8", "blk8 BKk EEw GVw W8 BM32 BM8k BW8", 8, BF)
+_add("BW", 64, BF)
+_add("blk8F", 8, F32)
 _add("LNF THF", 256, F32)
-_add("G8T", 8, F32)
-_add("bcI", 64, I32)
 for _t in range(ST):
-    _add("rL%d" % _t, 768, F32)
-    _add("rP%d rY%d" % (_t, _t), 256, BF)
-    _add("rB%d" % _t, 48, F32)
-_add("SB", 48, F32)
+    _add("rK%d" % _t, 288, F32)
+    _add("rC%d" % _t, 256, F32)
+    _add("rY%d" % _t, 256, BF)
+    _add("rB%d" % _t, 16, I32)
+_add("SB", 16, I32)
 for _b in range(8):
     SCRATCH["pb%d" % _b] = ("psum", [128, 512], F32)
 
-SEMAPHORES = ["sV", "sS", "sT", "sG", "lR", "lP", "lY", "lB"]
-SEMAPHORES += ["a%s%d" % (m, t) for m in "RPYB" for t in range(ST)]
+SEMAPHORES = ["sV", "sS", "sT", "sG", "lK", "lC", "lY", "lB"]
+SEMAPHORES += ["a%s%d" % (m, t) for m in "KCYB" for t in range(ST)]
 SEMAPHORES += ["d%d" % k for k in range(24)]
 
 
@@ -78,11 +78,7 @@ def rank_program(g, core, T, topo):
     recs = {}
     ndma = [0]
 
-    par = [0]
-
     def v(name, lo=0, hi=None, step=1, p=None):
-        if par[0] and name + "'" in ALIAS:
-            name += "'"
         if name in ALIAS:
             name, at, width, _d = ALIAS[name]
             hi = at + (width if hi is None else hi)
@@ -158,7 +154,7 @@ def rank_program(g, core, T, topo):
             record(q, bump(q, sem, 1), rd, wr)
         return add(q, emit, reads, writes, cost)
 
-    def dma(q, out, in_, reads=(), writes=()):
+    def dma(q, out, in_, reads=(), writes=(), lat=2.2):
         sem = "d%d" % ndma[0]
         ndma[0] += 1
 
@@ -166,7 +162,7 @@ def rank_program(g, core, T, topo):
             wait(q, need(q, rd, wr))
             queues[q].dma_start(out, in_).then_inc(T.sem[sem], 16)
             record(q + "d", bump(q, sem, 16), rd, wr)
-        return add(q, emit, reads, writes, 0.1, 5.0 if writes and writes[0][1][0][0] == "X" else 2.2)
+        return add(q, emit, reads, writes, 0.1, lat)
 
     def order():
         seen, deps, succ = {}, [], [[] for _ in OPS]
@@ -189,7 +185,7 @@ def rank_program(g, core, T, topo):
             for acc, wr in [(a, 0) for a in o[2]] + [(a, 1) for a in o[3]]:
                 name, lo, hi = acc
                 old = seen.get(name, [])
-                if wr:
+                if wr and not name.startswith("pb"):
                     old = [r for r in old if not (lo <= r[0] and r[1] <= hi)]
                 seen[name] = old + [(lo, hi, i, q, wr)]
             dp.pop(i, None)
@@ -236,9 +232,9 @@ def rank_program(g, core, T, topo):
     def vcost(out, a, b=None):
         views = [x for x in (out, a, b) if x is not None]
         if out[3]:
-            return 0.06 + SCATTER * CYC * out[2]
+            return 0.05 + SCATTER * CYC * out[2]
         if any(x[3] for x in views):
-            return 0.06 + GATHER * CYC * out[2]
+            return 0.05 + GATHER * CYC * out[2]
         n = max(out[2], a[2])
         psum = any(x[1][0][0].startswith("pb") for x in views[1:])
         small = all(SCRATCH[x[1][0][0]][2] in (BF, U16) for x in views)
@@ -264,21 +260,26 @@ def rank_program(g, core, T, topo):
         op("V", lambda e: e.tensor_copy(out[0], a[0]), [a], [out], vcost(out, a))
 
     def act(out, a, f=AF.Copy, scale=1.0, bias=0.0):
-        c = (0.07 + GATHER * CYC * out[2]) if a[3] else 0.06 + CYC * max(64, out[2])
+        c = (0.07 + GATHER * CYC * out[2]) if a[3] else CYC * max(64, out[2])
         op("S", lambda e: e.activation(out[0], a[0], f, bias=bias, scale=scale), [a], [out], c)
 
     def mm(out, l, r, start, stop):
         c = max(64, r[2]) * CYC * (4 if SCRATCH[r[1][0][0]][2] == F32 else 1)
         op("T", lambda e: e.matmul(out[0], l[0], r[0], start, stop), [l, r], [out], c)
 
-    def scan(out, d0, d1, o0, o1):
-        op("V", lambda e: e.tensor_tensor_scan(out[0], d0[0], d1[0], 0.0, o0, o1), [d0, d1], [out], max(64, out[2]) * CYC)
+    def mms(out, terms):
+        for k, (l, r) in enumerate(terms):
+            mm(out, l, r, k == 0, k == len(terms) - 1)
 
-    def tr(out, a):
-        op("V", lambda e: e.transpose(out[0], a[0]), [a], [out], vcost(out, a))
+    def scan(out, d0, d1, o0, o1, init=0.0):
+        small = all(SCRATCH[x[1][0][0]][2] == BF for x in (out, d0, d1))
+        op("V", lambda e: e.tensor_tensor_scan(out[0], d0[0], d1[0], init, o0, o1), [d0, d1], [out], max(64, out[2] * (0.5 if small else 1)) * CYC)
+
+    def total(out, a):
+        op("V", lambda e: e.tensor_reduce(out[0], a[0], AxisListType.X, OP.add), [a], [out], max(64, a[2]) * CYC)
 
     def fill(out, c):
-        op("V", lambda e: e.memset(out[0], c), [], [out])
+        op("V", lambda e: e.memset(out[0], c), [], [out], max(64, out[2] * 0.5) * CYC)
 
     def iota(out, pat, base, cm):
         if SCRATCH[out[1][0][0]][2] == I32:
@@ -286,11 +287,8 @@ def rank_program(g, core, T, topo):
         else:
             op("G", lambda e: e.iota(out[0], pat, base, cm, allow_small_or_imprecise_dtypes=True), [], [out], 0.13 + 2 * CYC * out[2])
 
-    def bc(x):
-        return ind(x, v("bcA"))
-
-    def wide(dst, x, scale=1.0, bias=0.0):
-        act(v(dst), bc(v(x)), AF.Copy if (scale, bias) == (1.0, 0.0) else AF.Identity, scale, bias)
+    def bc(x, h=None):
+        return ind(v(x), v("bcA") if h is None else v("bcA", 8 * h, 8 * h + 8))
 
     def line(dst, x, scale, bias):
         act(dst, x, AF.Identity, scale, bias)
@@ -298,149 +296,133 @@ def rank_program(g, core, T, topo):
     def last(name, a0=0, a1=16):
         return v(name, a0 * 16 + 15, a1 * 16, 16)
 
+    def turn(dst, src):
+        for h in range(2):
+            mm(v(dst[0], dst[1] + 128 * h, dst[1] + 128 * h + 128), v(src, 128 * h, 128 * h + 128), v("IdF"), True, True)
+
+    def to_list(dst, src, mat, start, stop):
+        for h in range(2):
+            mm(v(dst, 8 * h, 8 * h + 8), v(src, 128 * h, 128 * h + 128), v(mat), start, stop and (start or h == 1))
+
     half = W // 2
     dma("Y", T.IV[:], T.vl[:], [], [v("IV")])
     dma("S", T.IC[:], T.cl[:], [], [v("IC")])
-    dma("Y", T.X[:, 0:half], T.xc[:, 0:half], [], [v("X", 0, half)])
-    dma("S", T.X[:, half:W], T.xc[:, half:W], [], [v("X", half, W)])
+    dma("Y", T.X[:, 0:half], T.xc[:, 0:half], [], [v("X", 0, half)], 5.0)
+    dma("S", T.X[:, half:W], T.xc[:, half:W], [], [v("X", half, W)], 5.0)
     dma("Y", T.LNI[0:8, :], T.ln[:], [], [v("LNI")])
     dma("S", T.WI[:], T.wt[:], [], [v("WI")])
     dma("Y", T.THI[0:8, :], T.th[:], [], [v("THI")])
 
     iota(v("pcI"), [[0, 1]], 0, 1)
-    iota(v("MP"), [[0, 8], [1, 2], [0, 16]], 0, 0)
+    iota(v("mm"), [[1, 128]], 0, 0)
     iota(v("iw", 0, 16), [[1, 16]], 0, 0)
-    iota(v("iw", 16, 32), [[16, 16]], 15, 0)
     iota(v("QC"), [[0, 16], [1, 16]], 0, 0)
     iota(v("mg"), [[1, 8], [0, 16]], 0, 0)
-    iota(v("mq"), [[0, 8], [1, 16]], 0, 0)
-    iota(v("mm"), [[1, 128]], 0, 0)
-    iota(v("cc"), [[1, 64]], 0, 0)
-    iota(v("bcI"), [[16, 4], [0, 16]], 0, 0)
-    iota(v("f2", 0, 16), [[16, 16]], W + 2, 0)
+    iota(v("TR"), [[16, 16]], W, 0)
+    iota(v("OB"), [[0, 2], [256, 8]], 0, 0)
+    iota(v("EQ"), [[0, 4096]], 0, 0)
+    iota(v("X", W, 2 * W), [[0, W]], 0, 0)
     ts(v("pmI"), v("pcI"), 15, OP.bitwise_and)
     ts(v("p4I"), v("pcI"), 4, OP.arith_shift_right)
-    ts(v("btI"), v("p4I"), 1, OP.bitwise_and)
-    for a, b in (("pcF", "pcI"), ("pmF", "pmI"), ("p4F", "p4I"), ("btF", "btI")):
+    for a, b in (("pcF", "pcI"), ("pmF", "pmI"), ("p4F", "p4I")):
         cp(v(a), v(b))
-    ts(v("MP"), v("MP"), v("btF"), OP.is_equal)
     cp(v("bcA"), v("iw", 0, 16))
-    cp(v("bc15"), v("iw", 16, 32))
+    cp(v("LV"), v("IV"))
+    cp(v("LC"), v("IC"))
+    ts(v("IdF"), v("mm"), v("pcF"), OP.is_equal)
+    for nm, c in (("Ident", 1.0), ("In1", -1.0), ("Ih", 0.5), ("Inh", -0.5), ("Ibig", BIG), ("Ibigh", BIG / 2), ("I108", 1.078125),
+                  ("I094", 0.9375), ("IZb", KZ * 1024), ("IZv", KZ * 2048), ("I4k", 4096.0), ("In4k", -4096.0)):
+        line(v(nm), v("IdF"), c, 0.0)
+    fill(v("ones"), 1.0)
+    fill(v("onesF"), 1.0)
+    fill(v("zero"), 0.0)
+    for nm in ("GV0", "GV1", "DC0", "DC1"):
+        fill(v(nm, 2048, 2064), 0.0)
+    for nm in ("OHp", "posp", "negp", "rRV", "rRC"):
+        fill(v(nm, 0, 16), 0.0)
+    fill(v("pb5"), 0.0)
+    fill(v("m3", 255, 256), 0.0)
+    ts(v("DGf"), v("QC"), v("pmF"), OP.is_equal)
+    act(v("DG"), v("DGf"))
+    ts(v("RSf"), v("QC"), 0.0, OP.is_gt)
+    act(v("RS"), v("RSf"))
+    line(v("RSm"), v("RSf"), 1048576.0, -1.0)
+    line(v("i32s"), v("QC"), -32.0, 512.0)
+    ts(v("TR"), v("TR"), v("pmF"), OP.add)
+    ts(v("e1"), v("pmF"), 16.0, OP.mult, 16.0, OP.add)
+    ts(v("OB"), v("OB"), v("e1"), OP.add)
+    ts(v("blk8F"), v("mm", 0, 8), v("p4F"), OP.is_equal)
+    for nm, c in (("blk8", 1.0), ("BKk", 2048.0), ("EEw", -4 * KZ), ("GVw", 2 * KZ), ("BM32", -1.0 / 32), ("BM8k", 8192.0), ("BW8", 2.0 ** 70)):
+        line(v(nm), v("blk8F"), c, 0.0)
+    ts(v("Yw"), v("mg"), v("p4F"), OP.is_equal, KZ, OP.mult)
+    cp(v("wF"), v("WI"))
+    ts(v("W8"), v("blk8F"), v("wF"), OP.mult)
+    ts(v("e1"), v("pcF"), 0.0, OP.is_equal)
+    ts(v("e2"), v("pcF"), 1.0, OP.is_equal, -1.5 * BIG, OP.mult)
+    ts(v("CR"), v("i32s"), v("e1"), OP.mult, v("e2"), OP.add)
+    ts(v("f1"), v("QC"), 15.0, OP.is_equal, -15.0, OP.add)
+    tt(v("f2"), v("f1"), v("QC"), OP.add)
+    ts(v("CX"), v("f2"), v("e1"), OP.mult)
+    ts(v("C4"), v("QC"), 0.0, OP.mult, v("e1"), OP.add)
+    ts(v("C4"), v("C4"), 4096.0, OP.mult)
+    fill(v("f1", 0, 128), 0.5)
+    fill(v("f1", 128, 256), 0.0)
+    scan(v("PW2"), v("f1", 0, 128), v("f1", 128, 256), OP.mult, OP.add, 2.0 ** 61)
+    tt(v("f2", 0, 128), v("PW2"), v("IdF"), OP.mult)
+    total(v("wp"), v("f2", 0, 128))
+    ts(v("wp"), v("wp"), 2.5, OP.mult)
+    tt(v("f2", 128, 144), v("PW2", 0, 16), v("DGf", 0, 16), OP.mult)
+    total(v("wq"), v("f2", 128, 144))
+    for a in range(8):
+        ts(v("BW", 8 * a, 8 * a + 8), v("blk8F"), v("wq"), OP.mult, 2.0 ** (-16 * a), OP.mult)
 
-    def conv(src, dst):
-        act(v("CIN2", 0, 240), v(src, 16, 256))
-        act(v("CIN2", 240, 256), v(src, 0, 16))
-        tr(v("CT1"), v(src))
-        tr(v("CT2"), v("CIN2"))
-        act(v("pb6", 16, 256), v("CT2", 0, 240))
-        act(v("pb6", 0, 16), v("CT2", 240, 256))
-        tt(v("pb5", 0, 256), v("CT1"), v("pb6", 0, 256), OP.subtract)
-        tt(v("m9"), v("pb5", 0, 256), v("MP"), OP.mult)
-        tt(v(dst), v("m9"), v("pb6", 0, 256), OP.add)
+    act(v("m1"), v("IV"))
+    act(v("m2"), v("IC"))
+    turn(("pb6", 0), "m1")
+    turn(("pb7", 0), "m2")
+    act(v("V"), v("pb6", 0, 256))
+    cp(v("LNF", p=8), v("LNI", p=8))
+    cp(v("THF", 0, 1, p=8), v("THI", p=8))
+    ts(v("G8", p=8), v("mg", p=8), v("pcF", p=8), OP.is_equal)
+    for h in range(2):
+        mm(v("pb2", 8 * h, 8 * h + 8), v("LNF", 128 * h, 128 * h + 128, p=8), v("IdF", 0, 8, p=8), True, True)
+    cp(v("nn"), v("pb2", 0, 16))
+    tt(v("m4"), bc("nn"), v("QC"), OP.is_le)
+    line(v("m5"), v("m4"), 4096.0, 0.0)
+    tt(v("Cd"), v("pb7", 0, 256), v("m5"), OP.add)
+    act(v("V0"), v("V", 0, 256, 16))
+    ts(v("thm", p=8), v("THF", 0, 1, p=8), KZ, OP.mult, KZ * (0.5 - 3072), OP.add)
+    ts(v("LIM", p=8), v("G8", p=8), v("thm", p=8), OP.mult)
 
-    ts(v("m1"), v("IV"), 4096.0, OP.mult)
-    tt(v("VCA"), v("m1"), v("IC"), OP.add)
-    conv("VCA", "VCB")
-    cp(v("iw"), v("VCB"))
-    ts(v("IV"), v("iw"), 12, OP.arith_shift_right)
-    cp(v("LST", 0, 256), v("IV"))
-    ts(v("IC"), v("iw"), 4095, OP.bitwise_and)
-    cp(v("LST", 256, 511), v("IV", 1, 256))
-    cp(v("LST", 511, 512), v("IV", 255, 256))
-    cp(v("LST", 512, 768), v("IC"))
+    def counts():
+        ts(v("val"), v("Cd"), 4096.0, OP.is_lt)
+        scan(v("cum"), v("RS"), v("val"), OP.mult, OP.add)
 
-    def consts1():
-        cp(v("V"), v("IV"))
-        cp(v("C"), v("IC"))
-        cp(v("N", 0, 255), v("V", 1, 256))
-        cp(v("N", 255, 256), v("V", 255, 256))
-        ts(v("V0"), v("V", 0, 256, 16), 2.0, OP.add)
-        ts(v("DG"), v("QC"), v("pmF"), OP.is_equal)
-        ts(v("RS"), v("QC"), 0.0, OP.is_gt)
-        op("V", lambda e: e.tensor_scalar(T.G8[0:8, :], T.mg[0:8, :], v("pcF", p=8)[0], None, OP.is_equal), [v("mg"), v("pcF")], [v("G8")])
-        op("V", lambda e: e.tensor_copy(T.LNF[0:8, :], T.LNI[0:8, :]), [v("LNI")], [v("LNF")])
-        op("V", lambda e: e.tensor_copy(T.THF[0:8, 0:1], T.THI[0:8, :]), [v("THI")], [v("THF")])
-        op("T", lambda e: e.matmul(T.pb0[:, 0:256], T.G8[0:8, :], T.LNF[0:8, :], True, True), [v("G8"), v("LNF")], [v("pb0", 0, 256)])
-        op("T", lambda e: e.matmul(T.pb1[:, 0:1], T.G8[0:8, :], T.THF[0:8, 0:1], True, True), [v("G8"), v("THF")], [v("pb1", 0, 1)])
-        cp(v("pb7", 0, 256), v("QC"))
-        tt(v("f1"), v("pb0", 0, 256), v("DG"), OP.mult)
-        scan(v("f2"), v("RS"), v("f1"), OP.mult, OP.add)
-        cp(v("nn"), last("f2"))
-        ts(v("thm"), v("pb1", 0, 1), 0.5, OP.mult, -8192.0, OP.add)
-        cp(v("lim"), v("thm"))
-        limits()
-        ts(v("Ident"), v("mm"), v("pcF"), OP.is_equal)
-        for nm, c in (("In1", -1.0), ("In2", -2.0), ("Ibig", BIG), ("Im256", -256.0), ("Im4k", -4096.0)):
-            ts(v(nm), v("Ident"), c, OP.mult)
-        fill(v("ones"), 1.0)
-        ts(v("IdF"), v("mm"), v("pcF"), OP.is_equal)
-
-    def consts2():
-        ts(v("blkF"), v("mg"), v("p4F"), OP.is_equal)
-        tt(v("f1", 0, 128), v("mq"), v("blkF"), OP.mult)
-        ts(v("f1", 128, 256), v("blkF"), -99.0, OP.mult, 99.0, OP.add)
-        tt(v("mq"), v("f1", 0, 128), v("f1", 128, 256), OP.add)
-        ts(v("e1"), v("pcF"), 0.0, OP.is_equal)
-        ts(v("e2"), v("pcF"), 1.0, OP.is_equal, 3840.0, OP.mult)
-        ts(v("ws"), v("pcF"), 2.0, OP.is_equal, -BIG, OP.mult)
-        tt(v("e2"), v("e2"), v("ws"), OP.add)
-        ts(v("CR"), v("cc"), v("e1"), OP.mult, v("e2"), OP.add)
-        for q in range(16):
-            ts(v("LQ1", q * 128, q * 128 + 128), v("mq"), float(q), OP.is_equal)
-        ts(v("LQk"), v("LQ1"), 4096.0, OP.mult)
-        ts(v("bcY"), v("bcI"), v("pmF"), OP.add)
-        ts(v("LQh"), v("LQ1"), -0.5, OP.mult)
-        cp(v("wF"), v("WI"))
-        ts(v("LW"), v("LQ1"), v("wF"), OP.mult)
-        ts(v("LM"), v("QC"), v("pmF"), OP.is_le, -16384.0, OP.mult)
-        ts(v("blk"), v("mg"), v("p4F"), OP.is_equal)
-        ts(v("blk8k"), v("blk"), 8192.0, OP.mult)
-        fill(v("onesF"), 1.0)
-        ts(v("G8T"), v("mm", 0, 8), v("p4F"), OP.is_equal)
-
-    ts(v("TR"), v("f2", 0, 16), v("pmF"), OP.add)
-
-    def limits():
-        ts(v("live"), v("nn"), 4.0, OP.is_ge)
-        wide("ngB", "nn", 1.08, -3.29)
-        wide("nlB", "nn", 1.0, -1.0)
-
-    PP = v("pb7", 0, 256)
-
-    def masks():
-        act(v("m1"), PP, AF.Identity, scale=-8192.0, bias=131074.0)
-        act(v("Pb"), PP)
-        tt(v("Vg"), v("ngB"), PP, OP.is_ge)
-        tt(v("VL"), v("nlB"), PP, OP.is_ge)
-        tt(v("PW"), v("m1"), v("V"), OP.add)
-
-    def dedupe(z, gap1, gap2):
-        tt(v("Hx"), bc(v(z)), v("DG"), OP.mult)
-        wide("zb", z)
-        mm(v("pb4", 0, 256), v("blkF"), v("Hx"), True, True)
+    def dedupe(gap1, gap2, values):
+        act(v("Wz"), bc("z"))
+        tt(v("Ez"), bc("z"), v("DGf"), OP.mult)
+        to_list("pb1", "Ez", "blk8F", True, True)
+        turn(("pb0", 0), "Wz")
+        act(v("zA"), v("pb1", 0, 16))
+        cp(v("Ru"), v("pb0", 0, 256))
+        mm(v("pb3", 0, 16), v("Ident"), v("zero"), True, False)
+        to_list("pb3", "Ez", "blk8F", False, False)
+        mm(v("pb2", 0, 16), v("Ident"), v("zero"), True, False)
         gap1()
-        tt(v("pb0", 0, 256), v("pb4", 0, 256), v("LM"), OP.add)
-        cp(v("Ru"), v("pb4", 0, 256))
-        tt(v("EQ", 0, 256), v("zb"), v("pb0", 0, 256), OP.is_equal)
-        mm(v("pb5", 0, 256), v("blk8k"), v("EQ", 0, 256), True, False)
-        at = 256
-        for a in range(15):
-            w = 240 - 16 * a
-            ts(v("EQ", at, at + w), v("Ru", 256 - w, 256), v(z, a, a + 1), OP.is_equal)
-            mm(v("pb5", 256 - w, 256), v("blk8k"), v("EQ", at, at + w), False, a == 14)
-            at += w
+        for a in range(16):
+            ts(v("EQ", 272 * a, 256 * a + 256), v("Ru", 16 * a, 256), v("zA", a, a + 1), OP.is_equal)
+            for h in range(a // 8, 2):
+                mm(v("pb2", 8 * h, 8 * h + 8), v("EQ", 256 * a + 128 * h, 256 * a + 128 * h + 128),
+                   v("BW", 8 * (a % 8), 8 * (a % 8) + 8) if h == a // 8 else v("BW8"), False, a == 15)
         gap2()
-        tt(v("f1"), v("pb5", 0, 256), v("DG"), OP.mult)
-        scan(v("f2"), v("RS"), v("f1"), OP.mult, OP.add)
-        tt(v("s5"), last("f2"), v("hp"), OP.add)
-        tt(v("s8"), v("s5"), v("TR"), OP.min)
-        ts(v("off16"), v("s8"), -2.0, OP.add)
+        ts(v("lose"), v("pb2", 0, 16), v("wp"), OP.is_ge)
+        tt(v("El"), bc("lose"), v("DG"), OP.mult)
+        to_list("pb3", "El", "BM8k", False, True)
+        tt(v("oA"), v("pb3", 0, 16), v("TR"), OP.min)
+        cp(v("off16"), v("oA"))
+        cp(ind(v("X", 0, W + L), v("off16")), v(values))
 
-    def names(yes):
-        line(v("s6"), v(yes), -16384.0, 16384.0)
-        tt(v("hp"), v("s6"), v("zL"), OP.add)
-
-    def send(buf, dst_buf, dst_rank, lsem, asem):
+    def send(buf, dst_buf, dst_rank, lsem, asem, cost=2.0):
         dst = T.cores[dst_rank]
         rid, pid, _se = topo.addr(dst)
         n = len(topo.engines(core, dst))
@@ -449,7 +431,7 @@ def rank_program(g, core, T, topo):
             wait("G", need("G", rd, wr))
             g.remote_dma(T[dst_buf][:], T[buf][:], T.sem[asem], T.sem[lsem], pid, rid, topo.mask(core, dst))
             record("Gr", bump("G", lsem, n), rd, wr)
-        return add("G", emit, [v(buf)], [], 1.5, 3.0)
+        return add("G", emit, [v(buf)], [], 1.0, cost)
 
     def arrive(buf, asem, src_rank, sent):
         n = len(topo.engines(T.cores[src_rank], core))
@@ -458,265 +440,268 @@ def rank_program(g, core, T, topo):
             count[asem] = n
             clock[(asem, n)] = {}
             recs[buf] = [(0, 99999, (asem, n), "far", True)]
-        add("F", emit, [], [v(buf)], 0.0, 1.0, [sent])
+        add("F", emit, [], [v(buf)], 0.0, 0.0, [sent])
 
-    def gv(c):
-        (cp if c == 0 else act)(v("GV%d" % c), ind(v("X", 0, W), v("LST", 64 * c, 64 * c + 64)))
-
-    gv(0)
-    consts1()
-    consts2()
+    Vp, dV, dC = v("pb4", 0, 256), v("pb5", 0, 256), v("pb5", 256, 512)
+    counts()
     for t in range(ST):
         d = 1 + t % 3
         to, frm = (rank + d) % 4, (rank - d) % 4
-        rL, rP, rY, rB = "rL%d" % t, "rP%d" % t, "rY%d" % t, "rB%d" % t
+        rK, rC, rY, rB = "rK%d" % t, "rC%d" % t, "rY%d" % t, "rB%d" % t
         lastt = t == ST - 1
-
-        def gc(c):
-            act(v("GC%d" % c), ind(v("X", 0, W), v("LST", 512 + 64 * c, 512 + 64 * c + 64)))
-
-        def ss(c):
-            tt(v("SS%d" % c), ind(v("X", 0, W), v("LST", 256 + 64 * c, 256 + 64 * c + 64)), v("GV%d" % c), OP.add)
-
-        def dd(c):
-            for k in range(2):
-                b = "pb%d" % (2 * (c % 2) + k)
-                mm(v(b), v("Ident"), v("SS%d" % c, 512 * k, 512 * k + 512), True, False)
-                mm(v(b), v("In2"), v("GC%d" % c, 512 * k, 512 * k + 512), False, True)
-
-        def ab(c):
-            for k in range(2):
-                act(v("AB%d" % (c % 2), 512 * k, 512 * k + 512), v("pb%d" % (2 * (c % 2) + k)), AF.Abs)
-
-        def key(c):
-            o = v("pb%d" % (4 + c % 2), 0, 64)
-            mm(o, v("ones"), v("CR"), True, False)
-            mm(o, v("Im256"), v("Pb", 64 * c, 64 * c + 64), False, False)
-            mm(o, v("Ibig"), v("Vg", 64 * c, 64 * c + 64), False, False)
-            for q in range(16):
-                mm(o, v("LQk", 128 * q, 128 * q + 128), v("AB%d" % (c % 2), q, 1024, 16), False, q == 15)
-
-        def pick_a(c):
-            k = v("pb%d" % (4 + c % 2), 0, 64)
-            lo, hi = 64 * c, 64 * c + 64
-            a, b = 4 * c, 4 * c + 4
-            scan(v("SK", lo, hi), v("RS", 0, 64), k, OP.mult, OP.max)
-            ts(v("KA", a, b), last("SK", a, b), 63, OP.bitwise_and)
-            ts(v("o16", a, b), v("KA", a, b), 16.0, OP.mult, v("pmF"), OP.add)
-            cp(v("SYs", lo, hi), ind(v("GC%d" % c), v("o16", a, b)))
-            act(v("KS", lo, hi), k)
-            tt(v("GYs", lo, hi), ind(v("SS%d" % c), v("o16", a, b)), v("SYs", lo, hi), OP.subtract)
-            ts(v("KB", a, b), last("SK", a, b), 3840, OP.bitwise_and)
-            ts(v("kp2", a, b), v("KB", a, b), -1.0 / 256, OP.mult, 17.0, OP.add)
-            ts(v("Y", lo, hi), v("GYs", lo, hi), 0.0, OP.max, 63.0, OP.min)
-
-        def ee(c):
-            lo, hi = 64 * c, 64 * c + 64
-            tt(v("EE%d" % (c % 2)), ind(v("Y", lo, hi), v("bcY")), v("GV%d" % c), OP.max)
-            tt(v("B3", lo, hi), ind(v("kp2"), v("bcA", 4 * c, 4 * c + 4)), v("Pb", lo, hi), OP.is_le)
-
-        def ds(c):
-            lo, hi = 64 * c, 64 * c + 64
-            o = v("pb7", lo, hi)
-            mm(o, v("Im4k"), v("VL", lo, hi), True, False)
-            for q in range(16):
-                mm(o, v("LQh", 128 * q, 128 * q + 128), v("GV%d" % c, q, 1024, 16), False, False)
-            mm(o, v("Im4k"), v("B3", lo, hi), False, False)
-            for q in range(16):
-                mm(o, v("LQ1", 128 * q, 128 * q + 128), v("EE%d" % (c % 2), q, 1024, 16), False, q == 15)
-
-        par[0] = 0
         sent = {}
-        sent["R"] = send("VNC", rL, to, "lR", "aR%d" % t)
-        masks()
-        sent["P"] = send("Pb", rP, to, "lP", "aP%d" % t)
-        for w in MEASURE.split():
-            {"ss": ss, "gc": gc, "gv": gv, "dd": dd, "ab": ab, "ky": key, "pk": pick_a, "ee": ee, "ds": ds}[w[:2]](int(w[2:]))
-        act(v("kb"), ind(v("SK"), v("bc15")))
-        sent["Y"] = send("Y", rY, to, "lY", "aY%d" % t)
-        for q in range(16):
-            mm(v("pb6", 16, 32), v("LQh", 128 * q, 128 * q + 128), v("Y", q, 256, 16), q == 0, q == 15)
-        for q in range(16):
-            mm(v("pb6", 0, 16), v("LW", 128 * q, 128 * q + 128), v("Y", q, 256, 16), q == 0, q == 15)
-        ts(v("Tl"), v("pb6", 16, 32), -1.0, OP.mult, v("lim"), OP.add)
-        wide("TB", "Tl")
-        OH, O15, KV, K2 = v("pb0", 256, 512), v("pb1", 0, 256), v("pb1", 256, 512), v("pb2", 0, 256)
-        t1, SN, SC, PS = v("pb2", 256, 512), v("pb3", 0, 256), v("pb6", 0, 256), v("pb0", 0, 256)
-        act(v("pb2", 256, 512), v("Pb"))
-        tt(OH, v("kb"), v("KS"), OP.is_equal)
-        tt(v("m2"), v("V"), OH, OP.mult)
-        tt(v("m3"), v("N"), OH, OP.mult)
-        scan(v("m4"), v("RS"), v("m2"), OP.mult, OP.add)
-        scan(v("m5"), v("RS"), v("m3"), OP.mult, OP.add)
+
+        def gv(c):
+            out, src = v("GV%d" % (c // 4), 512 * (c % 4), 512 * (c % 4) + 512), ind(v("X", 0, W), v("LV", 32 * c, 32 * c + 32))
+            if WHO_V[c] == "S":
+                line(out, src, 0.5, 0.0)
+            else:
+                ts(out, src, 0.5, OP.mult)
+
+        def gate(c):
+            h, lo = c // 4, 512 * (c % 4)
+            GV, DC = "GV%d" % h, "DC%d" % h
+            src = ind(v("X", 0, 2 * W if t else W), v("LC", 32 * c, 32 * c + 32))
+            terms = [(v("Ident"), v(DC, lo, lo + 511)), (v("In1"), v(GV, lo + 1, lo + 512))]
+            if WHO_C[c] == "S":
+                act(v(DC, lo, lo + 512), src)
+                terms.append((v("In1"), v(GV, lo, lo + 511)))
+            else:
+                tt(v(DC, lo, lo + 512), src, v(GV, lo, lo + 512), OP.subtract)
+            b = v("pb%d" % (c % 2), 0, 511)
+            mms(b, terms[::-1])
+            act(v("AB%d" % h, lo, lo + 511), b, AF.Abs)
+
+        def pick(h):
+            lo, hi, a, b = 128 * h, 128 * h + 128, 8 * h, 8 * h + 8
+            pb, GV, DC = "pb%d" % (2 + h), "GV%d" % h, "DC%d" % h
+            k = v(pb, 0, 128)
+            mm(k, v("ones"), v("CR", 0, 128), True, False)
+            mm(k, v("Ident"), v("cum", lo, hi), False, False)
+            mm(k, v("Ibig"), v("val", lo, hi), False, False)
+            mm(k, v("Ibigh"), v("sgp", lo, hi), False, False)
+            for s in range(14):
+                mm(v(pb, s, 128, 16), v("AB%d" % h, s, 2048, 16), v("BKk"), False, s == 13)
+            scan(v("SK", lo, hi), v("RSf", 0, 128), k, OP.mult, OP.max)
+            ts(v("KA", a, b), last("SK", a, b), 992, OP.bitwise_and)
+            tt(v("El", lo, hi), bc("KA", h), v("DG", lo, hi), OP.mult)
+            o = v(pb, 128, 136)
+            mms(o, [(v("Ident"), v("OB", a, b)), (v("El", lo, hi), v("BM32"))])
+            cp(v("o16", a, b), o)
+            ts(v("o17", a, b), o, 1.0, OP.add)
+            cp(v("pa", lo, hi), ind(v(DC), v("o16", a, b)))
+            act(v("pb", lo, hi), ind(v(GV), v("o16", a, b)))
+            cp(v("pc", lo, hi), ind(v(GV), v("o17", a, b)))
+            y = v(pb, 256, 384)
+            mm(y, v("Inh"), v("pa", lo, hi), True, False)
+            runs = [(0, 4)] if len(set(WHO_C[4 * h:4 * h + 4])) == 1 else [(c, c + 1) for c in range(4)]
+            for c0, c1 in runs:
+                mm(v(pb, 256 + 32 * c0, 256 + 32 * c1), v("Ih" if WHO_C[4 * h + c0] == "V" else "Ident"), v("pb", lo + 32 * c0, lo + 32 * c1), False, False)
+            mm(y, v("Ident"), v("pc", lo, hi), False, True)
+            yh = v("pb4", 256 + lo, 256 + hi)
+            ts(yh, y, 0.0, OP.max, 31.5, OP.min)
+            ts(v("Y", lo, hi), yh, 2.0, OP.mult)
+            ts(v("KB", a, b), last("SK", a, b), 31, OP.bitwise_and)
+            tt(v("kp", a, b), v("KB", a, b), v("lv", a, b), OP.add)
+            act(v("kpw", lo, hi), bc("kp", h))
+            p = v("pb7", lo, hi)
+            mms(p, [(v("Ident"), v("cum", lo, hi)), (v("In1"), v("kpw", lo, hi))])
+            act(v("sgB", lo, hi), p, AF.Sign, 1.0, -1.5)
+            mm(v("pb6", 256 + a, 256 + b), v("Y", lo, hi), v("W8"), True, True)
+            cp(v("UI", a, b), v("pb6", 256 + a, 256 + b))
+            tt(v("OH", lo, hi), bc("KA", h), v("i32s", lo, hi), OP.is_equal)
+            tt(v("m2", lo, hi), v("OH", lo, hi), v("pb4", lo, hi), OP.mult)
+            tt(v("m3", lo, hi - h), v("OH", lo, hi - h), v("pb4", lo + 1, hi + 1 - h), OP.mult)
+            scan(v("m4", lo, hi), v("RSf", lo, hi), v("m2", lo, hi), OP.mult, OP.add)
+            scan(v("m5", lo, hi), v("RSf", lo, hi), v("m3", lo, hi), OP.mult, OP.add)
+
+        def near(h):
+            lo, hi = 128 * h, 128 * h + 128
+            pb, GV, EE = "pb%d" % (2 + h), "GV%d" % h, "EE%d" % h
+            z = v(pb, 384, 512)
+            mm(z, v("onesF", p=8), v("LIM", p=8), True, False)
+            mm(z, v("IZv"), v("val", lo, hi), False, False)
+            for s in range(2, 16):
+                mm(v(pb, 384 + s, 512, 16), v(GV, s, 2048, 16), v("GVw"), False, False)
+            mm(z, v("Y", lo, hi), v("Yw"), False, False)
+            mm(z, v("IZb"), v("sgB", lo, hi), False, False)
+            for s in range(2, 16):
+                e = v(EE, 128 * s - 256, 128 * s - 128)
+                tt(e, v(GV, s, 2048, 16), v("pb4", 256 + lo, 256 + hi), OP.max)
+                mm(v(pb, 384 + s, 512, 16), e, v("EEw"), False, s == 15)
+            tt(v("m1", lo, hi), z, v("PW", lo, hi), OP.min)
+            scan(v("SM", lo, hi), v("RSm", lo, hi), v("m1", lo, hi), OP.min, OP.max)
+
+        gv(0)
+        gv(1)
+        act(v("nw"), bc("nn"))
+        act(Vp, v("V"))
+        mms(v("pb6", 0, 256), [(v("I108"), v("nw")), (v("In1"), v("cum"))])
+        act(v("sgp"), v("pb6", 0, 256), AF.Sign, 1.0, -2.28)
+        mms(v("pb7", 0, 256), [(v("I094"), v("nw")), (v("In1"), v("cum")), (v("ones"), v("CX"))])
+        act(v("sgx"), v("pb7", 0, 256), AF.Sign, 1.0, 0.97)
+        line(v("pb6", 0, 256), v("cum"), -4096.0, 69632.0)
+        tt(v("PW"), v("pb6", 0, 256), v("V"), OP.add)
+        ts(v("live"), v("nn"), 4.0, OP.is_ge)
+        line(v("lv"), v("live"), -100.0, 100.0)
+        line(v("rest"), v("live"), -1.0, 1.0)
+        tt(v("pb5", 0, 255), v("pb4", 1, 256), v("V", 0, 255), OP.subtract)
+        for c in range(8):
+            if c >= 2:
+                gv(c)
+            gate(c)
+            if c == 3:
+                pick(0)
+        near(0)
+        pick(1)
+        sent["Y"] = send("Y", rY, to, "lY", "aY%d" % t, 3.0)
+        act(v("Vn"), last("m5"))
+        act(v("Vk"), last("m4"))
+        cp(v("cumk"), v("KB"))
+        sent["K"] = send("VK", rK, to, "lK", "aK%d" % t, 4.0)
         ts(v("K37"), last("m4"), 37.0, OP.mult)
-        kq = v("SB", 16, 32)
-        line(kq, v("kp2"), -1.0, 17.0)
-        cp(v("UI"), v("pb6", 0, 16))
         ts(v("UI"), v("UI"), 4095, OP.bitwise_and)
         tt(v("HI"), v("UI"), v("UI"), OP.mult)
         ts(v("HI"), v("HI"), 5, OP.arith_shift_right)
-        line(v("SB", 32, 48), last("m5"), 1.0, 2.0)
         tt(v("HI"), v("HI"), v("K37"), OP.add)
         ts(v("HI"), v("HI"), 4095, OP.bitwise_and)
-        ts(v("H2"), v("HI"), 2.0, OP.add)
-        act(v("NKB"), ind(v("m5"), v("bc15")))
-        act(v("VKB"), ind(v("m4"), v("bc15")))
-        ts(v("rest"), v("kp2"), 17.0, OP.is_equal)
-        F = v("pb0", 0, 256)
-        tt(F, v("TB"), v("pb7", 0, 256), OP.is_ge)
-        tt(v("m1"), F, v("PW"), OP.mult)
-        scan(v("SM"), v("RS"), v("m1"), OP.mult, OP.max)
-        ts(v("close"), last("SM"), 0.0, OP.is_gt)
-        ts(v("MX"), last("SM"), 13, OP.arith_shift_right)
-        ts(v("VM"), last("SM"), 8191, OP.bitwise_and)
-        tt(v("s1"), kq, v("MX"), OP.subtract)
-        tt(v("SB", 0, 16), v("s1"), v("close"), OP.mult)
-        sent["B"] = send("SB", rB, to, "lB", "aB%d" % t)
+        ts(v("hh"), v("HI"), -NONE, OP.add)
+        tt(v("hk"), v("HI"), v("Vk"), OP.subtract)
+        tt(v("kn"), v("Vk"), v("Vn"), OP.subtract)
+        scan(v("sk"), v("RS"), v("OHp", 15, 271), OP.mult, OP.add)
+        line(v("pb7", 0, 256), v("OH"), -1.0, 1.0)
+        tt(dC, v("pb7", 0, 256), v("Cd"), OP.mult)
+        tt(v("C1"), dC, v("m3"), OP.add)
+        tt(v("pb5", 256, 511), v("C1", 1, 256), v("C1", 0, 255), OP.subtract)
+        mms(v("pb6", 0, 256), [(v("Inh"), v("sgx")), (v("Ident"), v("OH")), (v("Ident"), v("sk"))])
+        act(v("pos"), v("pb6", 0, 256), AF.Relu, 1.0, -0.5)
+        act(v("neg"), v("pb6", 0, 256), AF.Relu, -1.0, 0.5)
+        mms(v("pb7", 0, 256), [(v("Ident"), v("negp", 15, 271)), (v("In1"), v("neg")), (v("Ident"), v("posp", 15, 271)), (v("In1"), v("posp", 14, 270)),
+                               (v("Ident"), v("RS"))])
+        act(v("mN"), v("pb7", 0, 256), AF.Relu, 1.0, -1.0)
+        for dd, rR, fx, new in ((dV, "rRV", "fxV", "hk"), (dC, "rRC", "fxC", "kn")):
+            tt(v(rR, 16, 272), v("pos"), dd, OP.mult)
+            tt(dd, v("neg"), dd, OP.mult)
+            tt(dd, dd, v(rR, 15, 271), OP.subtract)
+            tt(v(fx), bc(new), v("mN"), OP.mult)
+            tt(dd, dd, v(fx), OP.add)
+        near(1)
+        ts(v("SB"), last("SM"), 12, OP.logical_shift_right)
+        sent["B"] = send("SB", rB, to, "lB", "aB%d" % t, 1.6)
+        ts(v("close"), last("SM"), 0.0, OP.is_ge)
         tt(v("grow"), v("live"), v("close"), OP.subtract)
-        tt(v("zL"), v("H2"), v("grow"), OP.mult)
-        names("grow")
-        wide("s6B", "grow", 16.0, -1.0)
-        tt(v("x"), v("zL"), v("VM"), OP.add)
+        tt(v("s1"), v("hh"), v("grow"), OP.mult)
+        ts(v("z"), v("s1"), NONE, OP.add)
+        for m, b in (("K", rK), ("Y", rY), ("B", rB)):
+            arrive(b, "a%s%d" % (m, t), frm, sent[m])
+        rck, rVn = v(rK, 256, 272), v(rK, 272, 288)
 
         def gap1():
-            wide("xB", "x", 1.0, -2.0)
-            tt(v("s3"), v("nn"), v("grow"), OP.add)
-            ts(v("s3"), v("s3"), 16.0, OP.min)
-            tt(O15, v("s6B"), v("pb2", 256, 512), OP.is_equal)
-            tt(v("nn"), v("s3"), v("SB", 0, 16), OP.subtract)
-            act(KV, O15, AF.Identity, scale=-1.0, bias=1.0)
-            act(v("KVs"), O15, AF.Identity, scale=-1.0, bias=1.0)
-            op("V", lambda e: e.tensor_reduce(v("cs1")[0], v("close")[0], AxisListType.X, OP.add), [v("close")], [v("cs1")])
-            tt(v("MXe"), v("MX"), v("grow"), OP.add)
+            ts(v("stepm"), v("SM"), 0.0, OP.is_ge)
+            act(v("gw"), bc("grow"))
+            line(v("cw"), bc("close"), 1.0, -1.0)
+            mms(v("pb6", 0, 256), [(v("ones"), v("C4")), (v("In4k"), v("sk")), (v("I4k"), v("stepm"))])
+            tt(v("Cp"), v("pb6", 0, 256), v("Cd"), OP.max)
+            sent["C"] = send("Cp", rC, to, "lC", "aC%d" % t, 4.0)
+            arrive(rC, "aC%d" % t, frm, sent["C"])
+            mms(v("pb7", 0, 256), [(v("I4k"), v("sk")), (v("In4k"), v("stepm")), (v("I4k"), v("cw"))])
+            tt(v("C1x"), v("pb7", 0, 256), v("C1"), OP.max)
+            ts(v("VM"), last("SM"), 4095, OP.bitwise_and)
+            tt(v("s2"), v("VM"), v("Vn"), OP.subtract)
+            tt(v("e"), v("s2"), v("close"), OP.mult)
+            tt(v("s3"), rck, v("nn"), OP.add)
+            line(v("s4"), v("s3"), -1.0, 16.0)
+            tt(v("th2"), v("s4"), v("rest"), OP.mult)
+            tt(v("s5"), rck, v("nn"), OP.min)
+            line(v("s6"), v("V0"), 1.0, -NONE)
+            ts(v("s5"), v("s5"), 1.0, OP.min)
+            tt(v("s7"), v("s6"), v("s5"), OP.mult)
+            line(v("z0"), v("s7"), 1.0, NONE)
+            tt(v("dz"), rVn, v("z0"), OP.subtract)
+            tt(v("dv0"), rVn, v("V0"), OP.subtract)
 
         def gap2():
-            mm(v("pb6", 0, 1), v("onesF"), v("cs1"), True, True)
-            tt(K2, v("KVs"), OH, OP.subtract)
-            tt(v("m7"), v("xB"), O15, OP.mult)
-            tt(t1, v("V"), KV, OP.mult)
-            tt(v("V"), t1, v("m7"), OP.add)
-
-        dedupe("zL", gap1, gap2)
-        cp(ind(v("X"), v("off16")), v("Y"))
-        if not lastt:
-            tt(v("m8"), v("xB"), OH, OP.mult)
-            tt(v("m9"), v("NKB"), O15, OP.mult)
-            mm(SN, v("IdF"), v("m8"), True, False)
-            mm(SN, v("IdF"), v("m9"), False, False)
-        tt(v("nC"), v("VKB"), O15, OP.mult)
-        cp(v("cI"), v("pb6", 0, 1))
-        ts(v("cI"), v("cI"), 31, OP.bitwise_and)
-        ts(v("lim"), v("cI"), 0.5, OP.mult, v("thm"), OP.add)
-        mm(SC, v("IdF"), v("m3"), True, False)
-        mm(SC, v("IdF"), v("nC"), False, False)
-        for m, b in (("R", rL), ("P", rP), ("Y", rY), ("B", rB)):
-            arrive(b, "a%s%d" % (m, t), frm, sent[m])
-        par[0] = 1
-        e_, k_, n_ = v(rB, 0, 16), v(rB, 16, 32), v(rB, 32, 48)
-        act(v("s4"), k_, AF.Sign)
-        tt(v("s1"), e_, v("nn"), OP.is_gt)
-        ts(v("s7"), v("nn"), 1.0, OP.is_ge)
-        tt(v("s9"), v("s7"), v("s4"), OP.mult)
-        tt(v("Z0"), v("V0"), v("s9"), OP.mult)
-        tt(v("Z1"), n_, v("Z0"), OP.subtract)
-        tt(v("take"), v("s1"), v("rest"), OP.mult)
-        tt(v("Z1"), v("Z1"), v("take"), OP.mult)
-        tt(v("zL"), v("Z0"), v("Z1"), OP.add)
-        tt(v("has"), v("s9"), v("take"), OP.max)
-        names("has")
-        tt(v("s2"), n_, v("V0"), OP.subtract)
-        tt(v("s3"), e_, v("nn"), OP.subtract)
-        wide("TKb", "take")
-        act(v("pb1", 0, 256), v("TKb"))
-        act(v("pb1", 256, 512), v("TKb"), AF.Identity, scale=-1.0, bias=1.0)
-        TP, NT = v("pb1", 0, 256), v("pb1", 256, 512)
-        tt(v("s2"), v("s2"), v("take"), OP.mult)
-        tt(v("s3"), v("s3"), v("take"), OP.mult)
-        tt(v("V0"), v("V0"), v("s2"), OP.add)
-        tt(v("nn"), v("nn"), v("s3"), OP.add)
-        ts(v("z16"), v("V0"), -2.0, OP.add)
-
-        def take(k, acc):
-            own = v("VNC", 256 * k, 256 * k + 256)
-            a, b = v("m%d" % (2 * k)), v("m%d" % (2 * k + 1))
-            tt(a, own, v("pb2", 0, 256), OP.mult)
-            tt(b, v(rL, 256 * k, 256 * k + 256), TP, OP.mult)
-            mm(acc, v("IdF"), a, False, False)
-            mm(acc, v("IdF"), b, False, True)
-            act(own, acc)
+            tt(Vp, v(rK, 0, 256), Vp, OP.subtract)
+            tt(dV, v("gw"), dV, OP.mult)
+            tt(dV, dV, v("V"), OP.add)
+            tt(v("eN"), bc("e"), v("OHp", 15, 271), OP.mult)
+            tt(dV, dV, v("eN"), OP.add)
+            tt(dC, v("gw"), dC, OP.mult)
+            tt(dC, dC, v("C1x"), OP.add)
+            tt(v("s8"), v("SB"), v("cumk"), OP.add)
+            ts(v("s8"), v("s8"), -16.0, OP.add)
+            tt(v("size"), v("s8"), v("close"), OP.mult)
+            tt(v("s9"), v("nn"), v("grow"), OP.add)
+            ts(v("s9"), v("s9"), 16.0, OP.min)
+            tt(v("n1"), v("s9"), v("size"), OP.add)
             if not lastt:
-                cp(v("LST", 256 * k, 256 * k + 256), acc)
+                total(v("cs1"), v("close"))
+                mm(v("pb6", 0, 1), v("onesF"), v("cs1"), True, True)
+                cp(v("cI"), v("pb6", 0, 1))
+                ts(v("cI"), v("cI"), 31, OP.bitwise_and)
+                ts(v("lim", p=8), v("cI", p=8), KZ, OP.mult, v("thm", p=8), OP.add)
+                ts(v("LIM", p=8), v("G8", p=8), v("lim", p=8), OP.mult)
+
+        dedupe(gap1, gap2, "Y")
+        tt(v("take"), v(rB), v("th2"), OP.is_lt)
+        tt(v("s1"), v("take"), v("dz"), OP.mult)
+        tt(v("z"), v("s1"), v("z0"), OP.add)
 
         def gap3():
-            tt(t1, v("V"), NT, OP.mult)
-            tt(v("m1"), v(rL, 0, 256), TP, OP.mult)
-            tt(v("V"), t1, v("m1"), OP.add)
+            cp(v("z16"), v("zA"))
+            act(v("tw"), bc("take"))
+            line(v("ntw"), v("tw"), -1.0, 1.0)
+            act(v("pb7", 0, 256), v("tw"))
+            tt(v("tV"), v("tw"), Vp, OP.mult)
+            tt(v("V"), dV, v("tV"), OP.add)
             if not lastt:
-                cp(v("LST", 0, 256), v("V"))
-            tt(K2, K2, v("TKb"), OP.subtract)
-            tt(v("s2"), v("take"), k_, OP.mult)
-            line(v("s3"), v("take"), 16.0, 0.0)
-            tt(v("MXe"), v("MXe"), v("s2"), OP.add)
-            tt(v("kqe"), kq, v("s3"), OP.add)
-            wide("MXB", "MXe")
-            wide("kqB", "kqe")
-            line(v("kthB"), v("kqB"), -1.0, 15.0)
-            line(v("mthB"), v("MXB"), -1.0, 16.0)
-            limits()
+                turn(("pb6", 0), "V")
+                cp(v("LV"), v("pb6", 0, 256))
+            tt(v("BL"), ind(v("X"), v("z16")), v(rY), OP.add)
+            line(v("BL2"), v("BL"), 0.5, 159.75)
+            line(v("BL3"), v("BL2"), 1.0, -160.0)
 
         def gap4():
-            tt(v("Pa"), v("Pb"), NT, OP.mult)
-            tt(v("Pr"), v(rP), TP, OP.mult)
-            tt(v("BL"), ind(v("X", 0, W), v("z16")), v(rY), OP.add)
-            ts(v("BL2"), v("BL"), 0.5, OP.mult, 159.75, OP.add)
-            ts(v("BL"), v("BL2"), -160.0, OP.add)
+            tt(dC, dC, v("ntw"), OP.mult)
+            tt(v("tC"), v("pb7", 0, 256), v(rC), OP.mult)
+            tt(v("Cd"), dC, v("tC"), OP.add)
             if not lastt:
-                take(1, SN)
-            take(2, SC)
+                turn(("pb7", 256), "Cd")
+                cp(v("LC"), v("pb7", 256, 512))
+            counts()
+            tt(v("s2"), v("s4"), v(rB), OP.subtract)
+            tt(v("dn"), v("s2"), v("take"), OP.mult)
+            tt(v("nn"), v("n1"), v("dn"), OP.add)
+            tt(v("s3"), v("dv0"), v("take"), OP.mult)
+            tt(v("V0"), v("V0"), v("s3"), OP.add)
 
-        dedupe("zL", gap3, gap4)
-        cp(ind(v("X"), v("off16")), v("BL"))
+        dedupe(gap3, gap4, "BL3")
         if lastt:
-            dma("Y", T.yx[:, 0:half], T.X[:, 0:half], [v("X", 0, half)], [])
-            dma("S", T.yx[:, half:W], T.X[:, half:W], [v("X", half, W)], [])
-        else:
-            gv(0)
-        mm(PS, v("Ident"), v("Pa"), True, False)
-        mm(PS, v("Ident"), v("Pr"), False, True)
-        ga, gb = v("pb2", 0, 256), v("pb2", 256, 512)
-        tt(ga, v("kthB"), PS, OP.is_lt)
-        tt(gb, v("mthB"), PS, OP.is_le)
-        tt(v("g1"), v("MXB"), ga, OP.mult)
-        tt(v("g2"), v("kqB"), gb, OP.mult)
-        mm(PP, v("Ident"), v("Pa"), True, False)
-        mm(PP, v("Ident"), v("Pr"), False, False)
-        mm(PP, v("Ident"), v("g1"), False, False)
-        mm(PP, v("In1"), v("g2"), False, True)
+            dma("Y", T.yx[:, 0:half], T.X[:, 0:half], [v("X", 0, half)], [], 5.0)
+            dma("S", T.yx[:, half:W], T.X[:, half:W], [v("X", half, W)], [], 5.0)
 
-    tt(v("Hx"), bc(v("nn")), v("DG"), OP.mult)
-    op("T", lambda e: e.matmul(T.pb4[0:8, 0:256], T.G8T[:], v("Hx")[0], True, True), [v("G8T"), v("Hx")], [v("pb4", 0, 256)])
-    ts(v("m7"), v("V"), 4096.0, OP.mult)
-    VC = v("pb2", 0, 256)
-    tt(VC, v("m7"), v("C"), OP.add)
-    tt(v("pb3", 0, 256), v("nlB"), PP, OP.is_ge)
-    line(v("m6"), v("pb3", 0, 256), -100.0, 100.0)
-    tt(v("Pa"), PP, v("m6"), OP.add)
-    op("V", lambda e: e.tensor_copy(T.LNF[0:8, :], T.pb4[0:8, 0:256]), [v("pb4", 0, 256)], [v("LNF")])
+    for h in range(2):
+        mm(v("pb1", 128 * h, 128 * h + 128, p=8), v("nn", 8 * h, 8 * h + 8), v("IdF"), True, True)
+    act(v("LNF", p=8), v("pb1", 0, 256, p=8))
     dma("Y", T.yn[:], T.LNF[0:8, :], [v("LNF")], [])
+    VC = v("pb4", 0, 256)
+    line(v("pb4", 256, 512), v("V"), 4096.0, 0.0)
+    tt(VC, v("pb4", 256, 512), v("Cd"), OP.add)
+    tt(v("cumP"), v("cum"), v("val"), OP.mult)
     for p in range(16):
-        b, pr, sn = v(("g1", "g2", "Pr")[p % 3]), v("m%d" % (2 + p % 3)), ("m5", "m7", "m8")[p % 3]
-        ts(b, v("Pa"), float(p), OP.is_equal)
+        b, pr, sn = v(("g1", "g2", "g3")[p % 3]), v("m%d" % (1 + p % 3)), ("m4", "m5", "m6")[p % 3]
+        ts(b, v("cumP"), float(p + 1), OP.is_equal)
         tt(pr, b, VC, OP.mult)
-        scan(v(sn), v("RS"), pr, OP.mult, OP.add)
+        scan(v(sn), v("RSf"), pr, OP.mult, OP.add)
         act(v("SO", p, 256, 16), last(sn))
-    conv("SO", "VCB")
-    cp(v("iw"), v("VCB"))
+    turn(("pb6", 0), "SO")
+    cp(v("iw"), v("pb6", 0, 256))
     ts(v("IV"), v("iw"), 12, OP.arith_shift_right)
     ts(v("IC"), v("iw"), 4095, OP.bitwise_and)
-    cp(v("V"), v("IV"))
-    dma("Y", T.yv[:], v("V")[0], [v("V")], [])
-    cp(v("C"), v("IC"))
-    dma("S", T.yc[:], v("C")[0], [v("C")], [])
+    cp(v("f1"), v("IV"))
+    dma("Y", T.yv[:], v("f1")[0], [v("f1")], [])
+    cp(v("f2"), v("IC"))
+    dma("S", T.yc[:], v("f2")[0], [v("f2")], [])
     for i in order():
         OPS[i][1](OPS[i][2], OPS[i][3])
     for s in sorted(count):

@@ -7,8 +7,14 @@ BIG, KZ, NONE = 4194304.0, 262144.0, 8191.0
 F32, BF, I32, U16 = "float32", "bfloat16", "int32", "uint16"
 
 WHO_V, WHO_C = "SVSSSSSS", "VVVVVVVV"
-CYC, GATHER, SCATTER, WAKE, SLACK = 0.0009, 1.5, 3.8, 0.16, 0.02
-BETA = 0.01
+WHO_Y = "SSSSSS"
+SEQ = 11
+NABS = (0, 0)
+SMASK = 6
+CYC, GATHER, SCATTER, WAKE, SLACK = 0.00086, 1.5, 3.8, 0.15, 0.02
+BETA, PASSES = 0.01, 8
+DBANK = "01301010"
+PLAN = {}
 SCRATCH = {"X": ("sbuf", [128, 2 * W], BF)}
 ALIAS = {}
 
@@ -35,22 +41,23 @@ _add("Cp", 256, F32)
 _add("rRV rRC", 272, F32)
 _add("OHp posp negp", 272, BF)
 ALIAS["OH"], ALIAS["pos"], ALIAS["neg"] = ("OHp", 16, 256, BF), ("posp", 16, 256, BF), ("negp", 16, 256, BF)
-_pack("MF", "Cd C1 C1x PW m1 m2 m3 m4 m5 m6 m7 m8 fxV fxC eN tV tC Wz Ez RSf RSm DGf i32s SO f1 f2 QC", 256, F32)
-_pack("MB", "val cum nw sgp sgx sgB kpw sk stepm mN gw cw tw ntw RS DG El pa pb pc Yn BL BL2 BL3 CR CX C4 g1 g2 g3 cumP", 256, BF)
+_pack("MF", "Cd C1 C1x PW m1 m2 m3 m4 m5 m6 m7 m8 fxV fxC xw kw tV tC Wz Ez RSf RSm DGf THR i32s SO f1 f2 QC", 256, F32)
+_pack("MB", "sv val cum nw sgp sgx stx sgB kpw sk sgm Ag gw cw tw ntw RS DG El pa pb pc BL BL2 BL3 CR CX g1 g2 g3 a1 a2 cumP cumI", 256, BF)
 _add("Y", 256, BF)
 _add("SK SM IV IC iw LNI", 256, I32)
 _add("LV LC Ru", 256, U16)
-_pack("PLF", "nn V0 live lv kp close grow rest hk kn Vk hh e s1 s2 s3 s4 s5 s6 s7 s8 s9 z z0 dz th2 take lose zA oA TR size n1 dn dv0", 16, F32)
+_pack("PLF", "nn V0 live lv kp close grow rest x kn Vk hF hh s1 s2 s3 s4 s5 s6 s7 s8 s9 z z0 dz th2 take zA oA TR dv0", 16, F32)
 _pack("PLI", "KA KB UI HI K37 VM", 16, I32)
-_pack("PLU", "o16 o17 off16 z16 bcA", 16, U16)
-_pack("PLB", "OB zero", 16, BF)
-_pack("COF", "pcF pmF p4F thm lim cs1 e1 e2 e3 wF wq wp", 1, F32)
-_pack("COI", "pcI pmI p4I cI", 1, I32)
+_pack("PLU", "o16 o17 off16 z16 bcA bc15", 16, U16)
+_pack("PLB", "OB BMh", 16, BF)
+_pack("COF", "pcF pmF p4F thm lim cs1 e1 e2 e3 e4 eK wF wq wp", 1, F32)
+_pack("COI", "pcI pmI p4I cI tI", 1, I32)
 _add("WI THI", 1, I32)
-_pack("MQ", "mg mm onesF G8 IdF LIM PW2", 128, F32)
-_pack("IDS", "Ident In1 Ih Inh Ibig Ibigh I108 I094 IZb IZv I4k In4k ones Yw", 128, BF)
-_pack("N8", "blk8 BKk EEw GVw W8 BM32 BM8k BW8", 8, BF)
-_add("BW", 64, BF)
+_pack("MQ", "mg mm onesF G8 IdF Id4k PW2", 128, F32)
+_pack("IDS", "Ident In1 Ih Inh Ibig Ibigh I108 I094 IZb IZv I4k In2k ones Yw0 Yw1 LIM blkw CQ zero", 128, BF)
+_pack("N8", "BKk EEw GVw ABw W8 BM32", 8, BF)
+_add("BW", 576, BF)
+_add("dS", 576, F32)
 _add("blk8F", 8, F32)
 _add("LNF THF", 256, F32)
 for _t in range(ST):
@@ -185,7 +192,7 @@ def rank_program(g, core, T, topo):
             for acc, wr in [(a, 0) for a in o[2]] + [(a, 1) for a in o[3]]:
                 name, lo, hi = acc
                 old = seen.get(name, [])
-                if wr and not name.startswith("pb"):
+                if wr:
                     old = [r for r in old if not (lo <= r[0] and r[1] <= hi)]
                 seen[name] = old + [(lo, hi, i, q, wr)]
             dp.pop(i, None)
@@ -193,41 +200,54 @@ def rank_program(g, core, T, topo):
             for j in dp:
                 succ[j].append(i)
         n = len(OPS)
-        prio = [0.0] * n
-        for i in range(n - 1, -1, -1):
-            prio[i] = OPS[i][4] + OPS[i][5] + max([prio[j] + (WAKE if deps[j][i] else -OPS[i][4]) for j in succ[i]] or [0.0])
-        left = [len(dp) for dp in deps]
-        start, fin = [0.0] * n, [0.0] * n
-        free, ready, out = {}, {}, []
+        cost = [o[4] for o in OPS]
+        fwd = [[(j, cost[j] + (OPS[j][5] + WAKE if k else 0.0)) for j, k in deps[i].items()] for i in range(n)]
+        bwd = [[(j, cost[j] + (OPS[i][5] + WAKE if deps[j][i] else 0.0)) for j in succ[i]] for i in range(n)]
 
-        def push(i):
-            r = 0.0
-            for j, k in deps[i].items():
-                r = max(r, fin[j] + WAKE if k else start[j])
-            ready.setdefault(OPS[i][0], []).append((r, BETA * i - prio[i], i))
-        for i in range(n):
-            if left[i] == 0:
-                push(i)
-        while len(out) < n:
-            best = None
-            for q, lst in ready.items():
-                if lst:
-                    t0 = max(free.get(q, 0.0), min(lst)[0])
-                    p, i, r = min((c[1], c[2], c) for c in lst if c[0] <= t0 + SLACK)
-                    st = max(t0, r[0])
-                    if best is None or st < best[0]:
-                        best = (st, q, i, r)
-            st, q, i, r = best
-            ready[q].remove(r)
-            start[i] = st
-            fin[i] = st + OPS[i][4] + OPS[i][5]
-            free[q] = st + OPS[i][4]
-            out.append(i)
-            for j in succ[i]:
-                left[j] -= 1
-                if left[j] == 0:
-                    push(j)
-        return out
+        def place(key, before, after, first):
+            left = [len(b) for b in before]
+            start, free, ready, out = [0.0] * n, {}, {}, []
+
+            def push(i):
+                ready.setdefault(OPS[i][0], []).append((max([first[i]] + [start[j] + w for j, w in before[i]]), key[i], i))
+            for i in range(n):
+                if left[i] == 0:
+                    push(i)
+            while len(out) < n:
+                best = None
+                for q, lst in ready.items():
+                    if lst:
+                        t0 = max(free.get(q, 0.0), min(lst)[0])
+                        r = min((c for c in lst if c[0] <= t0 + SLACK), key=lambda c: c[1:])
+                        st = max(t0, r[0])
+                        if best is None or st < best[0]:
+                            best = (st, q, r)
+                st, q, r = best
+                i = r[2]
+                ready[q].remove(r)
+                start[i] = st
+                free[q] = st + cost[i]
+                out.append(i)
+                for j, _w in after[i]:
+                    left[j] -= 1
+                    if left[j] == 0:
+                        push(j)
+            return start, out
+        none, lat = [0.0] * n, [o[5] for o in OPS]
+        tail = [0.0] * n
+        for i in range(n - 1, -1, -1):
+            tail[i] = max([lat[i]] + [tail[j] + w for j, w in bwd[i]])
+        key = [BETA * i - tail[i] - cost[i] for i in range(n)]
+        best = None
+        for _ in range(PASSES):
+            start, seq = place(key, fwd, bwd, none)
+            end = max(start[i] + cost[i] + lat[i] for i in range(n))
+            if best is None or end < best[0]:
+                best = (end, seq)
+            late, _seq = place([-start[i] - cost[i] for i in range(n)], bwd, fwd, lat)
+            key = [-late[i] - cost[i] for i in range(n)]
+        PLAN["end"] = best[0]
+        return best[1]
 
     def vcost(out, a, b=None):
         views = [x for x in (out, a, b) if x is not None]
@@ -259,9 +279,15 @@ def rank_program(g, core, T, topo):
     def cp(out, a):
         op("V", lambda e: e.tensor_copy(out[0], a[0]), [a], [out], vcost(out, a))
 
-    def act(out, a, f=AF.Copy, scale=1.0, bias=0.0):
+    def act(out, a, f=AF.Copy, scale=1.0, bias=0.0, total=None):
         c = (0.07 + GATHER * CYC * out[2]) if a[3] else CYC * max(64, out[2])
-        op("S", lambda e: e.activation(out[0], a[0], f, bias=bias, scale=scale), [a], [out], c)
+        rd = [a] + [x for x in (scale, bias) if isinstance(x, tuple)]
+        sc = scale[0] if isinstance(scale, tuple) else scale
+        bi = bias[0] if isinstance(bias, tuple) else bias
+        if total is None:
+            op("S", lambda e: e.activation(out[0], a[0], f, bias=bi, scale=sc), rd, [out], c)
+        else:
+            op("S", lambda e: e.activation(out[0], a[0], f, bias=bi, scale=sc, accum_out=total[0]), rd, [out, total], c + 0.02)
 
     def mm(out, l, r, start, stop):
         c = max(64, r[2]) * CYC * (4 if SCRATCH[r[1][0][0]][2] == F32 else 1)
@@ -318,8 +344,11 @@ def rank_program(g, core, T, topo):
     iota(v("iw", 0, 16), [[1, 16]], 0, 0)
     iota(v("QC"), [[0, 16], [1, 16]], 0, 0)
     iota(v("mg"), [[1, 8], [0, 16]], 0, 0)
-    iota(v("TR"), [[16, 16]], W, 0)
+    iota(v("iw", 16, 32), [[16, 16]], 15, 0)
+    iota(v("TR"), [[2048, 2], [0, 8]], W, 0)
     iota(v("OB"), [[0, 2], [256, 8]], 0, 0)
+    iota(v("s1"), [[256, 16]], 2 * W, 0)
+    iota(v("f2", 0, 64), [[1, 8], [0, 8]], 0, 0)
     iota(v("EQ"), [[0, 4096]], 0, 0)
     iota(v("X", W, 2 * W), [[0, W]], 0, 0)
     ts(v("pmI"), v("pcI"), 15, OP.bitwise_and)
@@ -327,11 +356,12 @@ def rank_program(g, core, T, topo):
     for a, b in (("pcF", "pcI"), ("pmF", "pmI"), ("p4F", "p4I")):
         cp(v(a), v(b))
     cp(v("bcA"), v("iw", 0, 16))
+    cp(v("bc15"), v("iw", 16, 32))
     cp(v("LV"), v("IV"))
     cp(v("LC"), v("IC"))
     ts(v("IdF"), v("mm"), v("pcF"), OP.is_equal)
     for nm, c in (("Ident", 1.0), ("In1", -1.0), ("Ih", 0.5), ("Inh", -0.5), ("Ibig", BIG), ("Ibigh", BIG / 2), ("I108", 1.078125),
-                  ("I094", 0.9375), ("IZb", KZ * 1024), ("IZv", KZ * 2048), ("I4k", 4096.0), ("In4k", -4096.0)):
+                  ("I094", 0.9375), ("IZb", KZ * 1024), ("IZv", KZ * 2048), ("I4k", 4096.0), ("In2k", -2048.0), ("Id4k", 4096.0)):
         line(v(nm), v("IdF"), c, 0.0)
     fill(v("ones"), 1.0)
     fill(v("onesF"), 1.0)
@@ -340,41 +370,52 @@ def rank_program(g, core, T, topo):
         fill(v(nm, 2048, 2064), 0.0)
     for nm in ("OHp", "posp", "negp", "rRV", "rRC"):
         fill(v(nm, 0, 16), 0.0)
-    fill(v("pb5"), 0.0)
-    fill(v("m3", 255, 256), 0.0)
+    for k in (255, 511):
+        fill(v("pb5", k, k + 1), 0.0)
     ts(v("DGf"), v("QC"), v("pmF"), OP.is_equal)
     act(v("DG"), v("DGf"))
     ts(v("RSf"), v("QC"), 0.0, OP.is_gt)
     act(v("RS"), v("RSf"))
     line(v("RSm"), v("RSf"), 1048576.0, -1.0)
     line(v("i32s"), v("QC"), -32.0, 512.0)
-    ts(v("TR"), v("TR"), v("pmF"), OP.add)
+    ts(v("e4"), v("p4F"), 256.0, OP.mult, v("pmF"), OP.add)
+    ts(v("TR"), v("TR"), v("e4"), OP.add)
     ts(v("e1"), v("pmF"), 16.0, OP.mult, 16.0, OP.add)
     ts(v("OB"), v("OB"), v("e1"), OP.add)
     ts(v("blk8F"), v("mm", 0, 8), v("p4F"), OP.is_equal)
-    for nm, c in (("blk8", 1.0), ("BKk", 2048.0), ("EEw", -4 * KZ), ("GVw", 2 * KZ), ("BM32", -1.0 / 32), ("BM8k", 8192.0), ("BW8", 2.0 ** 70)):
+    for nm, c in (("BKk", 2048.0), ("EEw", -4 * KZ), ("GVw", 2 * KZ), ("ABw", -2 * KZ), ("BM32", -1.0 / 32)):
         line(v(nm), v("blk8F"), c, 0.0)
-    ts(v("Yw"), v("mg"), v("p4F"), OP.is_equal, KZ, OP.mult)
+    for h in range(2):
+        tt(v("BMh", 8 * h, 8 * h + 8), v("s1", 8 * h, 8 * h + 8), v("blk8F"), OP.mult)
+    ts(v("blkw"), v("mg"), v("p4F"), OP.is_equal)
+    for h in range(2):
+        ts(v("m3", 128 * h, 128 * h + 128), v("QC", 0, 128), 2.0 + NABS[h], OP.is_ge, KZ, OP.mult)
+        tt(v("Yw%d" % h), v("m3", 128 * h, 128 * h + 128), v("blkw"), OP.mult)
+    fill(v("m3", 255, 256), 0.0)
     cp(v("wF"), v("WI"))
     ts(v("W8"), v("blk8F"), v("wF"), OP.mult)
     ts(v("e1"), v("pcF"), 0.0, OP.is_equal)
     ts(v("e2"), v("pcF"), 1.0, OP.is_equal, -1.5 * BIG, OP.mult)
     ts(v("CR"), v("i32s"), v("e1"), OP.mult, v("e2"), OP.add)
     ts(v("f1"), v("QC"), 15.0, OP.is_equal, -15.0, OP.add)
-    tt(v("f2"), v("f1"), v("QC"), OP.add)
-    ts(v("CX"), v("f2"), v("e1"), OP.mult)
-    ts(v("C4"), v("QC"), 0.0, OP.mult, v("e1"), OP.add)
-    ts(v("C4"), v("C4"), 4096.0, OP.mult)
+    tt(v("m7"), v("f1"), v("QC"), OP.add)
+    ts(v("CX"), v("m7"), v("e1"), OP.mult)
+    ts(v("e2"), v("pcF"), 1.0, OP.is_equal, -4096.0, OP.mult)
+    ts(v("CQ"), v("QC", 0, 128), v("e1"), OP.mult, v("e2"), OP.add)
     fill(v("f1", 0, 128), 0.5)
     fill(v("f1", 128, 256), 0.0)
     scan(v("PW2"), v("f1", 0, 128), v("f1", 128, 256), OP.mult, OP.add, 2.0 ** 61)
-    tt(v("f2", 0, 128), v("PW2"), v("IdF"), OP.mult)
-    total(v("wp"), v("f2", 0, 128))
-    ts(v("wp"), v("wp"), 2.5, OP.mult)
-    tt(v("f2", 128, 144), v("PW2", 0, 16), v("DGf", 0, 16), OP.mult)
-    total(v("wq"), v("f2", 128, 144))
+    tt(v("m8", 0, 128), v("PW2"), v("IdF"), OP.mult)
+    total(v("wp"), v("m8", 0, 128))
+    ts(v("m7"), v("DGf"), v("wp"), OP.mult, 2.5, OP.mult)
+    line(v("m6"), v("DGf"), -2.0 ** 90, 2.0 ** 90)
+    tt(v("THR"), v("m7"), v("m6"), OP.add)
+    tt(v("m8", 128, 144), v("PW2", 0, 16), v("DGf", 0, 16), OP.mult)
+    total(v("wq"), v("m8", 128, 144))
+    ts(v("f2", 64, 128), v("f2", 0, 64), v("p4F"), OP.is_equal)
     for a in range(8):
-        ts(v("BW", 8 * a, 8 * a + 8), v("blk8F"), v("wq"), OP.mult, 2.0 ** (-16 * a), OP.mult)
+        ts(v("BW", 64 * a, 64 * a + 64), v("f2", 64, 128), v("wq"), OP.mult, 2.0 ** (-16 * a), OP.mult)
+    line(v("BW", 512, 576), v("f2", 64, 128), 2.0 ** 70, 0.0)
 
     act(v("m1"), v("IV"))
     act(v("m2"), v("IC"))
@@ -391,36 +432,52 @@ def rank_program(g, core, T, topo):
     line(v("m5"), v("m4"), 4096.0, 0.0)
     tt(v("Cd"), v("pb7", 0, 256), v("m5"), OP.add)
     act(v("V0"), v("V", 0, 256, 16))
-    ts(v("thm", p=8), v("THF", 0, 1, p=8), KZ, OP.mult, KZ * (0.5 - 3072), OP.add)
-    ts(v("LIM", p=8), v("G8", p=8), v("thm", p=8), OP.mult)
+    mm(v("pb3", 0, 1), v("G8", p=8), v("THF", 0, 1, p=8), True, True)
+    cp(v("tI"), v("pb3", 0, 1))
+    ts(v("tI"), v("tI"), 31, OP.bitwise_and)
+    ts(v("e1"), v("pmF"), 0.0, OP.is_equal, KZ, OP.mult)
+    ts(v("eK"), v("pmF"), 1.0, OP.is_equal, KZ, OP.mult)
+    tt(v("e2"), v("pb3", 0, 1), v("tI"), OP.subtract)
+    ts(v("e2"), v("e2"), -3072.0, OP.add, v("e1"), OP.mult)
+    ts(v("e3"), v("tI"), 0.5, OP.add, v("eK"), OP.mult)
+    tt(v("thm"), v("e2"), v("e3"), OP.add)
+    ts(v("LIM"), v("blkw"), v("thm"), OP.mult)
 
     def counts():
-        ts(v("val"), v("Cd"), 4096.0, OP.is_lt)
+        act(v("sv"), v("Cd"), AF.Sign, -1.0, 4095.5)
+        act(v("val"), v("sv"), AF.Relu)
         scan(v("cum"), v("RS"), v("val"), OP.mult, OP.add)
+        act(v("nn"), last("cum"))
 
     def dedupe(gap1, gap2, values):
         act(v("Wz"), bc("z"))
         tt(v("Ez"), bc("z"), v("DGf"), OP.mult)
-        to_list("pb1", "Ez", "blk8F", True, True)
+        for h in range(2):
+            mm(v("pb1", 8 * h, 8 * h + 8), v("Ez", 128 * h, 128 * h + 128), v("blk8F"), True, True)
         turn(("pb0", 0), "Wz")
         act(v("zA"), v("pb1", 0, 16))
         cp(v("Ru"), v("pb0", 0, 256))
-        mm(v("pb3", 0, 16), v("Ident"), v("zero"), True, False)
-        to_list("pb3", "Ez", "blk8F", False, False)
-        mm(v("pb2", 0, 16), v("Ident"), v("zero"), True, False)
+        mm(v("pb3", 0, 16), v("CQ"), v("ones", 0, 16), True, False)
+        mm(v("pb2", 0, 128), v("Ident"), v("zero"), True, False)
         gap1()
+        for a in range(SEQ, 16):
+            act(v("dS", 16 * (a - SEQ) * (33 - a - SEQ) // 2, 16 * (a + 1 - SEQ) * (32 - a - SEQ) // 2), v("pb0", 16 * a, 256), AF.Abs, -1.0, v("zA", a, a + 1))
+        for a in range(SEQ, 16):
+            act(v("EQ", 272 * a, 256 * a + 256), v("dS", 16 * (a - SEQ) * (33 - a - SEQ) // 2, 16 * (a + 1 - SEQ) * (32 - a - SEQ) // 2), AF.Relu, -1.0, 1.0)
         for a in range(16):
-            ts(v("EQ", 272 * a, 256 * a + 256), v("Ru", 16 * a, 256), v("zA", a, a + 1), OP.is_equal)
+            if a < SEQ:
+                ts(v("EQ", 272 * a, 256 * a + 256), v("Ru", 16 * a, 256), v("zA", a, a + 1), OP.is_equal)
             for h in range(a // 8, 2):
-                mm(v("pb2", 8 * h, 8 * h + 8), v("EQ", 256 * a + 128 * h, 256 * a + 128 * h + 128),
-                   v("BW", 8 * (a % 8), 8 * (a % 8) + 8) if h == a // 8 else v("BW8"), False, a == 15)
+                k = a % 8 if h == a // 8 else 8
+                mm(v("pb2", 64 * h, 64 * h + 64), v("EQ", 256 * a + 128 * h, 256 * a + 128 * h + 128), v("BW", 64 * k, 64 * k + 64), False, a == 15)
         gap2()
-        ts(v("lose"), v("pb2", 0, 16), v("wp"), OP.is_ge)
-        tt(v("El"), bc("lose"), v("DG"), OP.mult)
-        to_list("pb3", "El", "BM8k", False, True)
-        tt(v("oA"), v("pb3", 0, 16), v("TR"), OP.min)
+        for k in range(2):
+            tt(v("El", k, 256, 2), v("pb2", 0, 128), v("THR", k, 256, 2), OP.is_ge)
+        for h in range(2):
+            mm(v("pb3", 8 * h, 8 * h + 8), v("El", 128 * h, 128 * h + 128), v("BMh", 8 * h, 8 * h + 8), False, h == 1)
+        tt(v("oA"), v("pb3", 0, 16), v("zA"), OP.max)
         cp(v("off16"), v("oA"))
-        cp(ind(v("X", 0, W + L), v("off16")), v(values))
+        cp(ind(v("X"), v("off16")), v(values))
 
     def send(buf, dst_buf, dst_rank, lsem, asem, cost=2.0):
         dst = T.cores[dst_rank]
@@ -468,7 +525,7 @@ def rank_program(g, core, T, topo):
                 terms.append((v("In1"), v(GV, lo, lo + 511)))
             else:
                 tt(v(DC, lo, lo + 512), src, v(GV, lo, lo + 512), OP.subtract)
-            b = v("pb%d" % (c % 2), 0, 511)
+            b = v("pb" + DBANK[c], 0, 511)
             mms(b, terms[::-1])
             act(v("AB%d" % h, lo, lo + 511), b, AF.Abs)
 
@@ -489,9 +546,8 @@ def rank_program(g, core, T, topo):
             mms(o, [(v("Ident"), v("OB", a, b)), (v("El", lo, hi), v("BM32"))])
             cp(v("o16", a, b), o)
             ts(v("o17", a, b), o, 1.0, OP.add)
-            cp(v("pa", lo, hi), ind(v(DC), v("o16", a, b)))
-            act(v("pb", lo, hi), ind(v(GV), v("o16", a, b)))
-            cp(v("pc", lo, hi), ind(v(GV), v("o17", a, b)))
+            for who, dst, src, lst in zip(WHO_Y[3 * h:], ("pa", "pb", "pc"), (DC, GV, GV), ("o16", "o16", "o17")):
+                (cp if who == "V" else act)(v(dst, lo, hi), ind(v(src), v(lst, a, b)))
             y = v(pb, 256, 384)
             mm(y, v("Inh"), v("pa", lo, hi), True, False)
             runs = [(0, 4)] if len(set(WHO_C[4 * h:4 * h + 4])) == 1 else [(c, c + 1) for c in range(4)]
@@ -519,27 +575,35 @@ def rank_program(g, core, T, topo):
             lo, hi = 128 * h, 128 * h + 128
             pb, GV, EE = "pb%d" % (2 + h), "GV%d" % h, "EE%d" % h
             z = v(pb, 384, 512)
-            mm(z, v("onesF", p=8), v("LIM", p=8), True, False)
+            mm(z, v("ones"), v("LIM"), True, False)
             mm(z, v("IZv"), v("val", lo, hi), False, False)
-            for s in range(2, 16):
+            first = 2 + NABS[h]
+            for s in range(first, 16):
                 mm(v(pb, 384 + s, 512, 16), v(GV, s, 2048, 16), v("GVw"), False, False)
-            mm(z, v("Y", lo, hi), v("Yw"), False, False)
+            mm(z, v("Y", lo, hi), v("Yw%d" % h), False, False)
             mm(z, v("IZb"), v("sgB", lo, hi), False, False)
-            for s in range(2, 16):
-                e = v(EE, 128 * s - 256, 128 * s - 128)
-                tt(e, v(GV, s, 2048, 16), v("pb4", 256 + lo, 256 + hi), OP.max)
-                mm(v(pb, 384 + s, 512, 16), e, v("EEw"), False, s == 15)
+            for s0 in range(2, first, 4):
+                b, s1 = "pb%d" % (s0 // 4 % 2), min(s0 + 4, first)
+                for s in range(s0, s1):
+                    mms(v(b, 128 * (s - s0), 128 * (s - s0) + 128), [(v("Ident"), v(GV, s, 2048, 16)), (v("Inh"), v("Y", lo, hi))])
+                act(v(EE, 128 * s0 - 256, 128 * s1 - 256), v(b, 0, 128 * (s1 - s0)), AF.Abs)
+            for s in range(first, 16):
+                tt(v(EE, 128 * s - 256, 128 * s - 128), v(GV, s, 2048, 16), v("pb4", 256 + lo, 256 + hi), OP.max)
+            slots = list(range(first, 15)) + list(range(2, first)) + [15]
+            for s in slots:
+                mm(v(pb, 384 + s, 512, 16), v(EE, 128 * s - 256, 128 * s - 128), v("ABw" if s < first else "EEw"), False, s == 15)
             tt(v("m1", lo, hi), z, v("PW", lo, hi), OP.min)
             scan(v("SM", lo, hi), v("RSm", lo, hi), v("m1", lo, hi), OP.min, OP.max)
 
         gv(0)
         gv(1)
-        act(v("nw"), bc("nn"))
+        act(v("nw"), ind(v("cum"), v("bc15")))
         act(Vp, v("V"))
         mms(v("pb6", 0, 256), [(v("I108"), v("nw")), (v("In1"), v("cum"))])
         act(v("sgp"), v("pb6", 0, 256), AF.Sign, 1.0, -2.28)
         mms(v("pb7", 0, 256), [(v("I094"), v("nw")), (v("In1"), v("cum")), (v("ones"), v("CX"))])
         act(v("sgx"), v("pb7", 0, 256), AF.Sign, 1.0, 0.97)
+        act(v("stx"), v("sgx"), AF.Relu)
         line(v("pb6", 0, 256), v("cum"), -4096.0, 69632.0)
         tt(v("PW"), v("pb6", 0, 256), v("V"), OP.add)
         ts(v("live"), v("nn"), 4.0, OP.is_ge)
@@ -565,82 +629,78 @@ def rank_program(g, core, T, topo):
         ts(v("HI"), v("HI"), 5, OP.arith_shift_right)
         tt(v("HI"), v("HI"), v("K37"), OP.add)
         ts(v("HI"), v("HI"), 4095, OP.bitwise_and)
-        ts(v("hh"), v("HI"), -NONE, OP.add)
-        tt(v("hk"), v("HI"), v("Vk"), OP.subtract)
+        tt(v("hh"), v("HI"), v("TR"), OP.subtract)
         tt(v("kn"), v("Vk"), v("Vn"), OP.subtract)
+        act(v("kw"), bc("kn"))
         scan(v("sk"), v("RS"), v("OHp", 15, 271), OP.mult, OP.add)
-        line(v("pb7", 0, 256), v("OH"), -1.0, 1.0)
-        tt(dC, v("pb7", 0, 256), v("Cd"), OP.mult)
-        tt(v("C1"), dC, v("m3"), OP.add)
-        tt(v("pb5", 256, 511), v("C1", 1, 256), v("C1", 0, 255), OP.subtract)
-        mms(v("pb6", 0, 256), [(v("Inh"), v("sgx")), (v("Ident"), v("OH")), (v("Ident"), v("sk"))])
-        act(v("pos"), v("pb6", 0, 256), AF.Relu, 1.0, -0.5)
-        act(v("neg"), v("pb6", 0, 256), AF.Relu, -1.0, 0.5)
-        mms(v("pb7", 0, 256), [(v("Ident"), v("negp", 15, 271)), (v("In1"), v("neg")), (v("Ident"), v("posp", 15, 271)), (v("In1"), v("posp", 14, 270)),
-                               (v("Ident"), v("RS"))])
-        act(v("mN"), v("pb7", 0, 256), AF.Relu, 1.0, -1.0)
-        for dd, rR, fx, new in ((dV, "rRV", "fxV", "hk"), (dC, "rRC", "fxC", "kn")):
-            tt(v(rR, 16, 272), v("pos"), dd, OP.mult)
-            tt(dd, v("neg"), dd, OP.mult)
-            tt(dd, dd, v(rR, 15, 271), OP.subtract)
-            tt(v(fx), bc(new), v("mN"), OP.mult)
-            tt(dd, dd, v(fx), OP.add)
+        C1p = v("pb6", 0, 256)
+        line(v("pb6", 256, 512), v("OH"), -1.0, 1.0)
+        tt(C1p, v("pb6", 256, 512), v("Cd"), OP.mult)
+        tt(C1p, C1p, v("m3"), OP.add)
+        act(v("C1"), C1p)
+        tt(v("pb5", 256, 511), v("pb6", 1, 256), v("C1", 0, 255), OP.subtract)
+        mms(v("pb7", 256, 512), [(v("In1"), v("stx")), (v("Ident"), v("sk"))])
         near(1)
         ts(v("SB"), last("SM"), 12, OP.logical_shift_right)
         sent["B"] = send("SB", rB, to, "lB", "aB%d" % t, 1.6)
         ts(v("close"), last("SM"), 0.0, OP.is_ge)
         tt(v("grow"), v("live"), v("close"), OP.subtract)
         tt(v("s1"), v("hh"), v("grow"), OP.mult)
-        ts(v("z"), v("s1"), NONE, OP.add)
+        tt(v("z"), v("s1"), v("TR"), OP.add)
         for m, b in (("K", rK), ("Y", rY), ("B", rB)):
             arrive(b, "a%s%d" % (m, t), frm, sent[m])
         rck, rVn = v(rK, 256, 272), v(rK, 272, 288)
 
         def gap1():
-            ts(v("stepm"), v("SM"), 0.0, OP.is_ge)
             act(v("gw"), bc("grow"))
+            act(v("sgm"), v("SM"), AF.Sign, 1.0, 0.5)
             line(v("cw"), bc("close"), 1.0, -1.0)
-            mms(v("pb6", 0, 256), [(v("ones"), v("C4")), (v("In4k"), v("sk")), (v("I4k"), v("stepm"))])
-            tt(v("Cp"), v("pb6", 0, 256), v("Cd"), OP.max)
+            tt(v("Ag"), v("pb7", 256, 512), v("gw"), OP.mult)
+            mms(v("pb6", 0, 256), [(v("I4k"), v("sk")), (v("In2k"), v("sgm")), (v("I4k"), v("cw"))])
+            mms(v("pb7", 0, 256), [(v("Ident"), v("OH")), (v("Ident"), v("Ag"))])
+            act(v("pos"), v("pb7", 0, 256), AF.Relu)
+            act(v("neg"), v("pb7", 0, 256), AF.Relu, -1.0)
+            line(v("pb6", 256, 512), v("pb6", 0, 256), -1.0, 6144.0)
+            line(v("a1"), v("pb6", 0, 256), 1.0, -2048.0)
+            tt(v("Cp"), v("pb6", 256, 512), v("Cd"), OP.max)
             sent["C"] = send("Cp", rC, to, "lC", "aC%d" % t, 4.0)
             arrive(rC, "aC%d" % t, frm, sent["C"])
-            mms(v("pb7", 0, 256), [(v("I4k"), v("sk")), (v("In4k"), v("stepm")), (v("I4k"), v("cw"))])
-            tt(v("C1x"), v("pb7", 0, 256), v("C1"), OP.max)
+            mms(v("pb7", 0, 256), [(v("Ident"), v("negp", 15, 271)), (v("In1"), v("neg")), (v("Ident"), v("posp", 15, 271)), (v("In1"), v("posp", 14, 270))])
+            act(v("pb7", 256, 512), v("pb7", 0, 256), AF.Relu)
             ts(v("VM"), last("SM"), 4095, OP.bitwise_and)
-            tt(v("s2"), v("VM"), v("Vn"), OP.subtract)
-            tt(v("e"), v("s2"), v("close"), OP.mult)
+            tt(v("s2"), v("HI"), v("VM"), OP.subtract)
+            tt(v("s8"), v("VM"), v("Vk"), OP.subtract)
+            tt(v("s9"), v("s2"), v("grow"), OP.mult)
+            tt(v("x"), v("s8"), v("s9"), OP.add)
+            act(v("xw"), bc("x"))
             tt(v("s3"), rck, v("nn"), OP.add)
             line(v("s4"), v("s3"), -1.0, 16.0)
             tt(v("th2"), v("s4"), v("rest"), OP.mult)
             tt(v("s5"), rck, v("nn"), OP.min)
-            line(v("s6"), v("V0"), 1.0, -NONE)
-            ts(v("s5"), v("s5"), 1.0, OP.min)
-            tt(v("s7"), v("s6"), v("s5"), OP.mult)
-            line(v("z0"), v("s7"), 1.0, NONE)
+            tt(v("s6"), v("V0"), v("TR"), OP.subtract)
+            act(v("hF"), v("s5"), AF.Sign)
+            tt(v("s7"), v("s6"), v("hF"), OP.mult)
+            tt(v("z0"), v("s7"), v("TR"), OP.add)
             tt(v("dz"), rVn, v("z0"), OP.subtract)
             tt(v("dv0"), rVn, v("V0"), OP.subtract)
 
         def gap2():
             tt(Vp, v(rK, 0, 256), Vp, OP.subtract)
-            tt(dV, v("gw"), dV, OP.mult)
-            tt(dV, dV, v("V"), OP.add)
-            tt(v("eN"), bc("e"), v("OHp", 15, 271), OP.mult)
-            tt(dV, dV, v("eN"), OP.add)
-            tt(dC, v("gw"), dC, OP.mult)
-            tt(dC, dC, v("C1x"), OP.add)
-            tt(v("s8"), v("SB"), v("cumk"), OP.add)
-            ts(v("s8"), v("s8"), -16.0, OP.add)
-            tt(v("size"), v("s8"), v("close"), OP.mult)
-            tt(v("s9"), v("nn"), v("grow"), OP.add)
-            ts(v("s9"), v("s9"), 16.0, OP.min)
-            tt(v("n1"), v("s9"), v("size"), OP.add)
+            for dd, rR, fx, new, old in ((dV, "rRV", "fxV", "xw", "V"), (dC, "rRC", "fxC", "kw", "C1")):
+                tt(v(rR, 16, 272), v("pos"), dd, OP.mult)
+                tt(dd, v("neg"), dd, OP.mult)
+                tt(dd, dd, v(old), OP.add)
+                tt(dd, dd, v(rR, 15, 271), OP.subtract)
+                tt(v(fx), v("pb7", 256, 512), v(new), OP.mult)
+                tt(dd, dd, v(fx), OP.add)
+            tt(dC, dC, v("a1"), OP.max)
             if not lastt:
-                total(v("cs1"), v("close"))
+                act(v("s4"), v("close"), AF.Identity, total=v("cs1"))
                 mm(v("pb6", 0, 1), v("onesF"), v("cs1"), True, True)
                 cp(v("cI"), v("pb6", 0, 1))
                 ts(v("cI"), v("cI"), 31, OP.bitwise_and)
-                ts(v("lim", p=8), v("cI", p=8), KZ, OP.mult, v("thm", p=8), OP.add)
-                ts(v("LIM", p=8), v("G8", p=8), v("lim", p=8), OP.mult)
+                line(v("lim"), v("cI"), v("eK"), v("thm"))
+                line(v("LIM"), v("blkw"), v("lim"), 0.0)
 
         dedupe(gap1, gap2, "Y")
         tt(v("take"), v(rB), v("th2"), OP.is_lt)
@@ -669,11 +729,9 @@ def rank_program(g, core, T, topo):
                 turn(("pb7", 256), "Cd")
                 cp(v("LC"), v("pb7", 256, 512))
             counts()
-            tt(v("s2"), v("s4"), v(rB), OP.subtract)
-            tt(v("dn"), v("s2"), v("take"), OP.mult)
-            tt(v("nn"), v("n1"), v("dn"), OP.add)
-            tt(v("s3"), v("dv0"), v("take"), OP.mult)
-            tt(v("V0"), v("V0"), v("s3"), OP.add)
+            if not lastt:
+                tt(v("s3"), v("dv0"), v("take"), OP.mult)
+                tt(v("V0"), v("V0"), v("s3"), OP.add)
 
         dedupe(gap3, gap4, "BL3")
         if lastt:
@@ -685,15 +743,23 @@ def rank_program(g, core, T, topo):
     act(v("LNF", p=8), v("pb1", 0, 256, p=8))
     dma("Y", T.yn[:], T.LNF[0:8, :], [v("LNF")], [])
     VC = v("pb4", 0, 256)
-    line(v("pb4", 256, 512), v("V"), 4096.0, 0.0)
-    tt(VC, v("pb4", 256, 512), v("Cd"), OP.add)
-    tt(v("cumP"), v("cum"), v("val"), OP.mult)
+    for h in range(2):
+        lo, hi = 128 * h, 128 * h + 128
+        mms(v("pb4", lo, hi), [(v("V", lo, hi), v("Id4k")), (v("Cd", lo, hi), v("IdF"))])
+        mms(v("pb6", lo, hi), [(v("cum", lo, hi), v("Ident")), (v("val", lo, hi), v("Ibigh"))])
+    line(v("cumI"), v("pb6", 0, 256), 1.0, -BIG / 2)
     for p in range(16):
-        b, pr, sn = v(("g1", "g2", "g3")[p % 3]), v("m%d" % (1 + p % 3)), ("m4", "m5", "m6")[p % 3]
-        ts(b, v("cumP"), float(p + 1), OP.is_equal)
-        tt(pr, b, VC, OP.mult)
-        scan(v(sn), v("RSf"), pr, OP.mult, OP.add)
-        act(v("SO", p, 256, 16), last(sn))
+        b, pr = v(("g1", "g2", "g3")[p % 3]), "m%d" % (1 + p % 6)
+        if p % 2 and p < 2 * SMASK:
+            b = v(("pa", "pb", "pc")[p // 2 % 3])
+            act(v("a2"), v("cumI"), AF.Abs, 1.0, -1.0 - p)
+            act(b, v("a2"), AF.Relu, -1.0, 1.0)
+        else:
+            ts(b, v("cumI"), float(p + 1), OP.is_equal)
+        tt(v(pr), b, VC, OP.mult)
+        for h in range(2):
+            mm(v("pb7", 128 * h + p, 128 * h + 128, 16), v(pr, 128 * h, 128 * h + 128), v("blk8F"), True, True)
+    act(v("SO"), v("pb7", 0, 256))
     turn(("pb6", 0), "SO")
     cp(v("iw"), v("pb6", 0, 256))
     ts(v("IV"), v("iw"), 12, OP.arith_shift_right)
@@ -702,7 +768,9 @@ def rank_program(g, core, T, topo):
     dma("Y", T.yv[:], v("f1")[0], [v("f1")], [])
     cp(v("f2"), v("IC"))
     dma("S", T.yc[:], v("f2")[0], [v("f2")], [])
-    for i in order():
+    if "order" not in PLAN:
+        PLAN["order"] = order()
+    for i in PLAN["order"]:
         OPS[i][1](OPS[i][2], OPS[i][3])
     for s in sorted(count):
         if known["G"].get(s, 0) < count[s]:

@@ -3,19 +3,27 @@ from concourse.mybir import AluOpType, AxisListType, ActivationFunctionType
 OP = AluOpType
 AF = ActivationFunctionType
 W, L, S, ST = 4096, 256, 16, 5
-BIG, KZ, NONE = 4194304.0, 262144.0, 8191.0
-F32, BF, I32, U16 = "float32", "bfloat16", "int32", "uint16"
+BIG, KZ, MID = 4194304.0, 262144.0, 2048.0
+F32, BF, I32, U16, F16 = "float32", "bfloat16", "int32", "uint16", "float16"
 
-WHO_V, WHO_C = "SVSSSSSS", "VVVVVVVV"
-WHO_Y = "SSSSSS"
-SEQ = 11
-NABS = (0, 0)
-SMASK = 6
-CYC, GATHER, SCATTER, WAKE, SLACK = 0.00086, 1.5, 3.8, 0.15, 0.02
-BETA, PASSES = 0.01, 8
-DBANK = "01301010"
+RUNS = ((("S", 16), ("V", 16), ("S", 32), ("S", 32), ("S", 32)), (("S", 32), ("V", 32), ("S", 32), ("S", 16), ("S", 16)))
+DWIDE = 256
+WZ = "SS"
+WHO_Y = "VVVVSV"
+WHO_B, WHO_T = "V", "S"
+NRUN = 7
+NABS = (14, 0)
+SMASK = 0
+CYC, GATHER, SCATTER, WAKE, SLACK = 0.00083, 1.4, 3.4, 0.19, 0.02
+TFIX, HALF = 0.006, 1
+RULES = [(b, l, u) for b in (0.0, 0.01, 0.03) for l, u in ((0.3, 0.3), (0.5, 0.5), (0.5, 1.5))]
+PASSES = 6
+FAR = 3.0
+ZBANK = "10"
+WHO_O = "T"
 PLAN = {}
-SCRATCH = {"X": ("sbuf", [128, 2 * W], BF)}
+XW = W + 2 * L
+SCRATCH = {"X": ("sbuf", [128, XW], BF)}
 ALIAS = {}
 
 
@@ -35,42 +43,41 @@ _add("GV0 GV1 DC0 DC1", 2064, BF)
 _add("AB0 AB1", 2048, BF)
 _add("EE0 EE1", 1792, BF)
 _add("EQ", 4096, BF)
-_add("VK", 288, F32)
-ALIAS["V"], ALIAS["cumk"], ALIAS["Vn"] = ("VK", 0, 256, F32), ("VK", 256, 16, F32), ("VK", 272, 16, F32)
-_add("Cp", 256, F32)
-_add("rRV rRC", 272, F32)
-_add("OHp posp negp", 272, BF)
-ALIAS["OH"], ALIAS["pos"], ALIAS["neg"] = ("OHp", 16, 256, BF), ("posp", 16, 256, BF), ("negp", 16, 256, BF)
-_pack("MF", "Cd C1 C1x PW m1 m2 m3 m4 m5 m6 m7 m8 fxV fxC xw kw tV tC Wz Ez RSf RSm DGf THR i32s SO f1 f2 QC", 256, F32)
-_pack("MB", "sv val cum nw sgp sgx stx sgB kpw sk sgm Ag gw cw tw ntw RS DG El pa pb pc BL BL2 BL3 CR CX g1 g2 g3 a1 a2 cumP cumI", 256, BF)
-_add("Y", 256, BF)
+_add("VK", 272, F16)
+ALIAS["V"], ALIAS["live"] = ("VK", 0, 256, F16), ("VK", 256, 16, F16)
+_pack("YC", "Y Cp", 256, F16)
+_pack("MH", "Cd Wz Ez i1 i2 m3 upV upC dnV dnC fxV fxC kpV kpC inV inC", 256, F16)
+_pack("MI", "IdH Id4k", 128, F16)
+_add("blk8H", 8, F16)
+_add("OHp posp mPp", 272, BF)
+ALIAS["OH"], ALIAS["pos"], ALIAS["mP"] = ("OHp", 16, 256, BF), ("posp", 16, 256, BF), ("mPp", 16, 256, BF)
+_pack("MF", "PW m0 m1 m2 m4 m5 m6 m7 m8 xw kw RSf RSm RSk DGf THR i32s SO f1 f2 QC", 256, F32)
+_pack("MB", "val cum nw sgp sgx stx sgB kpw sk sgm Ag gw tw keep neg RS DG El pa pb pc BL CR CX CV C4 g1 g2 g3 a1 a2 a3 cumI", 256, BF)
 _add("SK SM IV IC iw LNI", 256, I32)
 _add("LV LC Ru", 256, U16)
-_pack("PLF", "nn V0 live lv kp close grow rest x kn Vk hF hh s1 s2 s3 s4 s5 s6 s7 s8 s9 z z0 dz th2 take zA oA TR dv0", 16, F32)
-_pack("PLI", "KA KB UI HI K37 VM", 16, I32)
-_pack("PLU", "o16 o17 off16 z16 bcA bc15", 16, U16)
-_pack("PLB", "OB BMh", 16, BF)
+_pack("PLF", "nn ng V0 lv nc grow x kn K37 hh s1 s2 s3 s4 s5 s6 s7 z z0 dz th2 take zA zU oA TR TRu Vk", 16, F32)
+_pack("PLI", "KA KB UI HI VM", 16, I32)
+_pack("PLU", "o160 o161 off16 z16 bcA bc15", 16, U16)
+_pack("PLB", "OB O1 BM32 BMh", 16, BF)
 _pack("COF", "pcF pmF p4F thm lim cs1 e1 e2 e3 e4 eK wF wq wp", 1, F32)
 _pack("COI", "pcI pmI p4I cI tI", 1, I32)
 _add("WI THI", 1, I32)
-_pack("MQ", "mg mm onesF G8 IdF Id4k PW2", 128, F32)
-_pack("IDS", "Ident In1 Ih Inh Ibig Ibigh I108 I094 IZb IZv I4k In2k ones Yw0 Yw1 LIM blkw CQ zero", 128, BF)
-_pack("N8", "BKk EEw GVw ABw W8 BM32", 8, BF)
+_pack("MQ", "mg mm onesF G8 IdF PW2", 128, F32)
+_pack("IDS", "Ident In1 In2 Ih Inh Ibig Ibigh I094 IZb IZv I4k In2k In4k I2k ones Yw0 Yw1 LIM blkw CQ zero", 128, BF)
+_pack("N8", "BKk EEw GVw ABw W8", 8, BF)
 _add("BW", 576, BF)
-_add("dS", 576, F32)
 _add("blk8F", 8, F32)
 _add("LNF THF", 256, F32)
 for _t in range(ST):
-    _add("rK%d" % _t, 288, F32)
-    _add("rC%d" % _t, 256, F32)
-    _add("rY%d" % _t, 256, BF)
-    _add("rB%d" % _t, 16, I32)
-_add("SB", 16, I32)
+    _add("rK%d" % _t, 272, F16)
+    _pack("rP%d" % _t, "rY%d rC%d" % (_t, _t), 256, F16)
+    _add("rB%d" % _t, 32, I32)
+_add("SB", 32, I32)
 for _b in range(8):
     SCRATCH["pb%d" % _b] = ("psum", [128, 512], F32)
 
-SEMAPHORES = ["sV", "sS", "sT", "sG", "lK", "lC", "lY", "lB"]
-SEMAPHORES += ["a%s%d" % (m, t) for m in "KCYB" for t in range(ST)]
+SEMAPHORES = ["sV", "sS", "sT", "sG", "lK", "lC", "lB"]
+SEMAPHORES += ["a%s%d" % (m, t) for m in "KCB" for t in range(ST)]
 SEMAPHORES += ["d%d" % k for k in range(24)]
 
 
@@ -150,7 +157,7 @@ def rank_program(g, core, T, topo):
     OPS = []
 
     def add(q, emit, reads, writes, cost, lat=0.0, after=()):
-        OPS.append([q, emit, [a for x in reads for a in x[1]], [a for x in writes for a in x[1]], cost, lat, list(after)])
+        OPS.append([q, emit, [a for x in reads for a in x[1]], [a for x in writes for a in x[1]], cost, lat, list(after), []])
         return len(OPS) - 1
 
     def op(q, fn, reads, writes, cost=0.06):
@@ -175,6 +182,8 @@ def rank_program(g, core, T, topo):
         seen, deps, succ = {}, [], [[] for _ in OPS]
         for i, o in enumerate(OPS):
             q, dp = o[0], {}
+            for j in o[7]:
+                dp[j] = 0
             for j in o[6]:
                 dp[j] = 1
             for acc, wr in [(a, 0) for a in o[2]] + [(a, 1) for a in o[3]]:
@@ -204,7 +213,7 @@ def rank_program(g, core, T, topo):
         fwd = [[(j, cost[j] + (OPS[j][5] + WAKE if k else 0.0)) for j, k in deps[i].items()] for i in range(n)]
         bwd = [[(j, cost[j] + (OPS[i][5] + WAKE if deps[j][i] else 0.0)) for j in succ[i]] for i in range(n)]
 
-        def place(key, before, after, first):
+        def place(key, before, after, first, look, urge):
             left = [len(b) for b in before]
             start, free, ready, out = [0.0] * n, {}, {}, []
 
@@ -219,6 +228,9 @@ def rank_program(g, core, T, topo):
                     if lst:
                         t0 = max(free.get(q, 0.0), min(lst)[0])
                         r = min((c for c in lst if c[0] <= t0 + SLACK), key=lambda c: c[1:])
+                        soon = [c for c in lst if c[0] <= t0 + look * cost[r[2]] and c[1] < r[1] - urge]
+                        if soon:
+                            r = min(soon, key=lambda c: c[1:])
                         st = max(t0, r[0])
                         if best is None or st < best[0]:
                             best = (st, q, r)
@@ -237,15 +249,17 @@ def rank_program(g, core, T, topo):
         tail = [0.0] * n
         for i in range(n - 1, -1, -1):
             tail[i] = max([lat[i]] + [tail[j] + w for j, w in bwd[i]])
-        key = [BETA * i - tail[i] - cost[i] for i in range(n)]
         best = None
-        for _ in range(PASSES):
-            start, seq = place(key, fwd, bwd, none)
-            end = max(start[i] + cost[i] + lat[i] for i in range(n))
-            if best is None or end < best[0]:
-                best = (end, seq)
-            late, _seq = place([-start[i] - cost[i] for i in range(n)], bwd, fwd, lat)
-            key = [-late[i] - cost[i] for i in range(n)]
+        for beta, look, urge in RULES:
+            key = [beta * i - tail[i] - cost[i] for i in range(n)]
+            for _ in range(PASSES):
+                start, seq = place(key, fwd, bwd, none, look, urge)
+                end = max(start[i] + cost[i] + lat[i] for i in range(n))
+                if best is None or end < best[0]:
+                    best = (end, seq)
+                    PLAN["rule"] = (beta, look, urge)
+                late, _seq = place([-start[i] - cost[i] for i in range(n)], bwd, fwd, lat, look, urge)
+                key = [-late[i] - cost[i] for i in range(n)]
         PLAN["end"] = best[0]
         return best[1]
 
@@ -257,7 +271,7 @@ def rank_program(g, core, T, topo):
             return 0.05 + GATHER * CYC * out[2]
         n = max(out[2], a[2])
         psum = any(x[1][0][0].startswith("pb") for x in views[1:])
-        small = all(SCRATCH[x[1][0][0]][2] in (BF, U16) for x in views)
+        small = all(SCRATCH[x[1][0][0]][2] in (BF, U16, F16) for x in views)
         if b is not None:
             n *= 1 if psum else 2
         elif small:
@@ -280,7 +294,7 @@ def rank_program(g, core, T, topo):
         op("V", lambda e: e.tensor_copy(out[0], a[0]), [a], [out], vcost(out, a))
 
     def act(out, a, f=AF.Copy, scale=1.0, bias=0.0, total=None):
-        c = (0.07 + GATHER * CYC * out[2]) if a[3] else CYC * max(64, out[2])
+        c = (0.07 + GATHER * CYC * out[2]) if a[3] else 0.12 + CYC * max(64, out[2])
         rd = [a] + [x for x in (scale, bias) if isinstance(x, tuple)]
         sc = scale[0] if isinstance(scale, tuple) else scale
         bi = bias[0] if isinstance(bias, tuple) else bias
@@ -290,7 +304,7 @@ def rank_program(g, core, T, topo):
             op("S", lambda e: e.activation(out[0], a[0], f, bias=bi, scale=sc, accum_out=total[0]), rd, [out, total], c + 0.02)
 
     def mm(out, l, r, start, stop):
-        c = max(64, r[2]) * CYC * (4 if SCRATCH[r[1][0][0]][2] == F32 else 1)
+        c = TFIX + max(64, r[2]) * CYC * {F32: 4, F16: HALF}.get(SCRATCH[r[1][0][0]][2], 1)
         op("T", lambda e: e.matmul(out[0], l[0], r[0], start, stop), [l, r], [out], c)
 
     def mms(out, terms):
@@ -322,13 +336,9 @@ def rank_program(g, core, T, topo):
     def last(name, a0=0, a1=16):
         return v(name, a0 * 16 + 15, a1 * 16, 16)
 
-    def turn(dst, src):
+    def turn(dst, src, ident="IdH"):
         for h in range(2):
-            mm(v(dst[0], dst[1] + 128 * h, dst[1] + 128 * h + 128), v(src, 128 * h, 128 * h + 128), v("IdF"), True, True)
-
-    def to_list(dst, src, mat, start, stop):
-        for h in range(2):
-            mm(v(dst, 8 * h, 8 * h + 8), v(src, 128 * h, 128 * h + 128), v(mat), start, stop and (start or h == 1))
+            mm(v(dst[0], dst[1] + 128 * h, dst[1] + 128 * h + 128), v(src, 128 * h, 128 * h + 128), v(ident), True, True)
 
     half = W // 2
     dma("Y", T.IV[:], T.vl[:], [], [v("IV")])
@@ -345,12 +355,12 @@ def rank_program(g, core, T, topo):
     iota(v("QC"), [[0, 16], [1, 16]], 0, 0)
     iota(v("mg"), [[1, 8], [0, 16]], 0, 0)
     iota(v("iw", 16, 32), [[16, 16]], 15, 0)
-    iota(v("TR"), [[2048, 2], [0, 8]], W, 0)
+    iota(v("TR"), [[256, 2], [0, 8]], W // 2, 2)
     iota(v("OB"), [[0, 2], [256, 8]], 0, 0)
-    iota(v("s1"), [[256, 16]], 2 * W, 0)
+    iota(v("s1"), [[32, 16]], W + 2048, 0)
     iota(v("f2", 0, 64), [[1, 8], [0, 8]], 0, 0)
+    iota(v("X", W, XW), [[0, 2 * L]], 0, 0)
     iota(v("EQ"), [[0, 4096]], 0, 0)
-    iota(v("X", W, 2 * W), [[0, W]], 0, 0)
     ts(v("pmI"), v("pcI"), 15, OP.bitwise_and)
     ts(v("p4I"), v("pcI"), 4, OP.arith_shift_right)
     for a, b in (("pcF", "pcI"), ("pmF", "pmI"), ("p4F", "p4I")):
@@ -360,48 +370,58 @@ def rank_program(g, core, T, topo):
     cp(v("LV"), v("IV"))
     cp(v("LC"), v("IC"))
     ts(v("IdF"), v("mm"), v("pcF"), OP.is_equal)
-    for nm, c in (("Ident", 1.0), ("In1", -1.0), ("Ih", 0.5), ("Inh", -0.5), ("Ibig", BIG), ("Ibigh", BIG / 2), ("I108", 1.078125),
-                  ("I094", 0.9375), ("IZb", KZ * 1024), ("IZv", KZ * 2048), ("I4k", 4096.0), ("In2k", -2048.0), ("Id4k", 4096.0)):
+    for nm, c in (("Ident", 1.0), ("In1", -1.0), ("In2", -2.0), ("Ih", 0.5), ("Inh", -0.5), ("Ibig", BIG), ("Ibigh", BIG / 2),
+                  ("I094", 0.9375), ("IZb", KZ * 1024), ("IZv", KZ * 2048), ("I4k", 4096.0), ("In2k", -2048.0), ("In4k", -4096.0), ("I2k", 2048.0)):
         line(v(nm), v("IdF"), c, 0.0)
+    cp(v("IdH"), v("IdF"))
+    ts(v("Id4k"), v("IdF"), 4096.0, OP.mult)
     fill(v("ones"), 1.0)
     fill(v("onesF"), 1.0)
     fill(v("zero"), 0.0)
     for nm in ("GV0", "GV1", "DC0", "DC1"):
         fill(v(nm, 2048, 2064), 0.0)
-    for nm in ("OHp", "posp", "negp", "rRV", "rRC"):
+    for nm in ("OHp", "posp", "mPp"):
         fill(v(nm, 0, 16), 0.0)
-    for k in (255, 511):
-        fill(v("pb5", k, k + 1), 0.0)
+    for nm, k in (("upV", 0), ("upC", 0), ("dnV", 127), ("dnC", 127)):
+        ts(v(nm, k, 256, 128), v("QC", 0, 2), 0.0, OP.mult)
+    ts(v("m3", 255, 256), v("QC", 0, 1), 0.0, OP.mult)
     ts(v("DGf"), v("QC"), v("pmF"), OP.is_equal)
     act(v("DG"), v("DGf"))
     ts(v("RSf"), v("QC"), 0.0, OP.is_gt)
     act(v("RS"), v("RSf"))
-    line(v("RSm"), v("RSf"), 1048576.0, -1.0)
+    line(v("RSm"), v("RSf"), 1048576.0, -4097.0)
+    line(v("RSk"), v("RSf"), BIG, 31.0)
     line(v("i32s"), v("QC"), -32.0, 512.0)
-    ts(v("e4"), v("p4F"), 256.0, OP.mult, v("pmF"), OP.add)
-    ts(v("TR"), v("TR"), v("e4"), OP.add)
     ts(v("e1"), v("pmF"), 16.0, OP.mult, 16.0, OP.add)
     ts(v("OB"), v("OB"), v("e1"), OP.add)
     ts(v("blk8F"), v("mm", 0, 8), v("p4F"), OP.is_equal)
-    for nm, c in (("BKk", 2048.0), ("EEw", -4 * KZ), ("GVw", 2 * KZ), ("ABw", -2 * KZ), ("BM32", -1.0 / 32)):
+    cp(v("blk8H"), v("blk8F"))
+    for nm, c in (("BKk", 2048.0), ("EEw", -4 * KZ), ("GVw", 2 * KZ), ("ABw", -2 * KZ)):
         line(v(nm), v("blk8F"), c, 0.0)
     for h in range(2):
+        line(v("BM32", 8 * h, 8 * h + 8), v("blk8F"), -1.0 / 32, 0.0)
+        fill(v("O1", 8 * h, 8 * h + 8), float(h))
         tt(v("BMh", 8 * h, 8 * h + 8), v("s1", 8 * h, 8 * h + 8), v("blk8F"), OP.mult)
     ts(v("blkw"), v("mg"), v("p4F"), OP.is_equal)
     for h in range(2):
-        ts(v("m3", 128 * h, 128 * h + 128), v("QC", 0, 128), 2.0 + NABS[h], OP.is_ge, KZ, OP.mult)
-        tt(v("Yw%d" % h), v("m3", 128 * h, 128 * h + 128), v("blkw"), OP.mult)
-    fill(v("m3", 255, 256), 0.0)
+        ts(v("m2", 128 * h, 128 * h + 128), v("QC", 0, 128), 2.0 + NABS[h], OP.is_ge, KZ, OP.mult)
+        tt(v("Yw%d" % h), v("m2", 128 * h, 128 * h + 128), v("blkw"), OP.mult)
     cp(v("wF"), v("WI"))
     ts(v("W8"), v("blk8F"), v("wF"), OP.mult)
     ts(v("e1"), v("pcF"), 0.0, OP.is_equal)
-    ts(v("e2"), v("pcF"), 1.0, OP.is_equal, -1.5 * BIG, OP.mult)
+    ts(v("e2"), v("pcF"), 1.0, OP.is_equal, -2 * BIG, OP.mult)
     ts(v("CR"), v("i32s"), v("e1"), OP.mult, v("e2"), OP.add)
     ts(v("f1"), v("QC"), 15.0, OP.is_equal, -15.0, OP.add)
     tt(v("m7"), v("f1"), v("QC"), OP.add)
     ts(v("CX"), v("m7"), v("e1"), OP.mult)
-    ts(v("e2"), v("pcF"), 1.0, OP.is_equal, -4096.0, OP.mult)
-    ts(v("CQ"), v("QC", 0, 128), v("e1"), OP.mult, v("e2"), OP.add)
+    ts(v("e4"), v("e1"), 4096.0, OP.mult)
+    ts(v("C4"), v("RS"), 0.0, OP.mult, v("e4"), OP.add)
+    ts(v("e2"), v("pcF"), 1.0, OP.is_equal, -MID, OP.mult)
+    ts(v("e3"), v("e1"), 2.0, OP.mult)
+    ts(v("CQ"), v("QC", 0, 128), v("e3"), OP.mult, v("e2"), OP.add)
+    ts(v("e2"), v("e2"), -4096.0, OP.mult)
+    ts(v("e3"), v("e1"), 2048.0, OP.mult, v("e2"), OP.add)
+    ts(v("CV", 0, 128), v("QC", 0, 128), 0.0, OP.mult, v("e3"), OP.add)
     fill(v("f1", 0, 128), 0.5)
     fill(v("f1", 128, 256), 0.0)
     scan(v("PW2"), v("f1", 0, 128), v("f1", 128, 256), OP.mult, OP.add, 2.0 ** 61)
@@ -417,11 +437,11 @@ def rank_program(g, core, T, topo):
         ts(v("BW", 64 * a, 64 * a + 64), v("f2", 64, 128), v("wq"), OP.mult, 2.0 ** (-16 * a), OP.mult)
     line(v("BW", 512, 576), v("f2", 64, 128), 2.0 ** 70, 0.0)
 
-    act(v("m1"), v("IV"))
-    act(v("m2"), v("IC"))
-    turn(("pb6", 0), "m1")
-    turn(("pb7", 0), "m2")
-    act(v("V"), v("pb6", 0, 256))
+    ts(v("i1"), v("IV"), -MID, OP.add)
+    ts(v("i2"), v("IC"), -MID, OP.add)
+    turn(("pb4", 0), "i1")
+    turn(("pb7", 0), "i2")
+    cp(v("V"), v("pb4", 0, 256))
     cp(v("LNF", p=8), v("LNI", p=8))
     cp(v("THF", 0, 1, p=8), v("THI", p=8))
     ts(v("G8", p=8), v("mg", p=8), v("pcF", p=8), OP.is_equal)
@@ -429,9 +449,11 @@ def rank_program(g, core, T, topo):
         mm(v("pb2", 8 * h, 8 * h + 8), v("LNF", 128 * h, 128 * h + 128, p=8), v("IdF", 0, 8, p=8), True, True)
     cp(v("nn"), v("pb2", 0, 16))
     tt(v("m4"), bc("nn"), v("QC"), OP.is_le)
-    line(v("m5"), v("m4"), 4096.0, 0.0)
-    tt(v("Cd"), v("pb7", 0, 256), v("m5"), OP.add)
-    act(v("V0"), v("V", 0, 256, 16))
+    line(v("m5"), v("m4"), 4096.0, -MID)
+    tt(v("Cd"), v("pb7", 0, 256), v("m5"), OP.max)
+    tt(v("s2"), v("V", 0, 256, 16), v("TR"), OP.subtract)
+    ts(v("s3"), v("nn"), 1.0, OP.min)
+    tt(v("V0"), v("s2"), v("s3"), OP.mult)
     mm(v("pb3", 0, 1), v("G8", p=8), v("THF", 0, 1, p=8), True, True)
     cp(v("tI"), v("pb3", 0, 1))
     ts(v("tI"), v("tI"), 31, OP.bitwise_and)
@@ -443,30 +465,24 @@ def rank_program(g, core, T, topo):
     tt(v("thm"), v("e2"), v("e3"), OP.add)
     ts(v("LIM"), v("blkw"), v("thm"), OP.mult)
 
-    def counts():
-        act(v("sv"), v("Cd"), AF.Sign, -1.0, 4095.5)
-        act(v("val"), v("sv"), AF.Relu)
-        scan(v("cum"), v("RS"), v("val"), OP.mult, OP.add)
-        act(v("nn"), last("cum"))
+    def counts(h):
+        lo, hi = 128 * h, 128 * h + 128
+        ts(v("val", lo, hi), v("Cd", lo, hi), MID, OP.is_lt)
+        scan(v("cum", lo, hi), v("RS", lo, hi), v("val", lo, hi), OP.mult, OP.add)
 
     def dedupe(gap1, gap2, values):
-        act(v("Wz"), bc("z"))
+        (act if WZ[values != "Y"] == "S" else cp)(v("Wz"), bc("z"))
         tt(v("Ez"), bc("z"), v("DGf"), OP.mult)
         for h in range(2):
-            mm(v("pb1", 8 * h, 8 * h + 8), v("Ez", 128 * h, 128 * h + 128), v("blk8F"), True, True)
+            mm(v("pb1", 8 * h, 8 * h + 8), v("Ez", 128 * h, 128 * h + 128), v("blk8H"), True, True)
         turn(("pb0", 0), "Wz")
-        act(v("zA"), v("pb1", 0, 16))
-        cp(v("Ru"), v("pb0", 0, 256))
+        ts(v("zU"), v("pb1", 0, 16), MID, OP.add)
+        ts(v("Ru"), v("pb0", 0, 256), MID, OP.add)
         mm(v("pb3", 0, 16), v("CQ"), v("ones", 0, 16), True, False)
         mm(v("pb2", 0, 128), v("Ident"), v("zero"), True, False)
         gap1()
-        for a in range(SEQ, 16):
-            act(v("dS", 16 * (a - SEQ) * (33 - a - SEQ) // 2, 16 * (a + 1 - SEQ) * (32 - a - SEQ) // 2), v("pb0", 16 * a, 256), AF.Abs, -1.0, v("zA", a, a + 1))
-        for a in range(SEQ, 16):
-            act(v("EQ", 272 * a, 256 * a + 256), v("dS", 16 * (a - SEQ) * (33 - a - SEQ) // 2, 16 * (a + 1 - SEQ) * (32 - a - SEQ) // 2), AF.Relu, -1.0, 1.0)
         for a in range(16):
-            if a < SEQ:
-                ts(v("EQ", 272 * a, 256 * a + 256), v("Ru", 16 * a, 256), v("zA", a, a + 1), OP.is_equal)
+            ts(v("EQ", 272 * a, 256 * a + 256), v("Ru", 16 * a, 256), v("zU", a, a + 1), OP.is_equal)
             for h in range(a // 8, 2):
                 k = a % 8 if h == a // 8 else 8
                 mm(v("pb2", 64 * h, 64 * h + 64), v("EQ", 256 * a + 128 * h, 256 * a + 128 * h + 128), v("BW", 64 * k, 64 * k + 64), False, a == 15)
@@ -475,7 +491,7 @@ def rank_program(g, core, T, topo):
             tt(v("El", k, 256, 2), v("pb2", 0, 128), v("THR", k, 256, 2), OP.is_ge)
         for h in range(2):
             mm(v("pb3", 8 * h, 8 * h + 8), v("El", 128 * h, 128 * h + 128), v("BMh", 8 * h, 8 * h + 8), False, h == 1)
-        tt(v("oA"), v("pb3", 0, 16), v("zA"), OP.max)
+        tt(v("oA"), v("pb3", 0, 16), v("zU"), OP.max)
         cp(v("off16"), v("oA"))
         cp(ind(v("X"), v("off16")), v(values))
 
@@ -499,8 +515,8 @@ def rank_program(g, core, T, topo):
             recs[buf] = [(0, 99999, (asem, n), "far", True)]
         add("F", emit, [], [v(buf)], 0.0, 0.0, [sent])
 
-    Vp, dV, dC = v("pb4", 0, 256), v("pb5", 0, 256), v("pb5", 256, 512)
-    counts()
+    counts(0)
+    counts(1)
     for t in range(ST):
         d = 1 + t % 3
         to, frm = (rank + d) % 4, (rank - d) % 4
@@ -508,63 +524,71 @@ def rank_program(g, core, T, topo):
         lastt = t == ST - 1
         sent = {}
 
-        def gv(c):
-            out, src = v("GV%d" % (c // 4), 512 * (c % 4), 512 * (c % 4) + 512), ind(v("X", 0, W), v("LV", 32 * c, 32 * c + 32))
-            if WHO_V[c] == "S":
-                line(out, src, 0.5, 0.0)
-            else:
-                ts(out, src, 0.5, OP.mult)
+        def bends(h):
+            GV, DC, at = "GV%d" % h, "DC%d" % h, 0
+            for c, (who, n) in enumerate(RUNS[h]):
+                lo, hi, lst = 16 * at, 16 * (at + n), (128 * h + at, 128 * h + at + n)
+                src = ind(v("X", 0, W), v("LV", *lst))
+                if who == "S":
+                    line(v(GV, lo, hi), src, 0.5, 0.0)
+                else:
+                    ts(v(GV, lo, hi), src, 0.5, OP.mult)
+                tt(v(DC, lo, hi), ind(v("X", 0, XW if t else W), v("LC", *lst)), v(GV, lo, hi), OP.subtract)
+                pb = "pb%d" % ((c + h * len(RUNS[0])) % 2)
+                for a in range(0, hi - lo, DWIDE):
+                    b = min(a + DWIDE, hi - lo - 1)
+                    mms(v(pb, a, b), [(v("In1"), v(GV, lo + a + 1, lo + b + 1)), (v("Ident"), v(DC, lo + a, lo + b))])
+                act(v("AB%d" % h, lo, hi - 1), v(pb, 0, hi - lo - 1), AF.Abs)
+                at += n
 
-        def gate(c):
-            h, lo = c // 4, 512 * (c % 4)
-            GV, DC = "GV%d" % h, "DC%d" % h
-            src = ind(v("X", 0, 2 * W if t else W), v("LC", 32 * c, 32 * c + 32))
-            terms = [(v("Ident"), v(DC, lo, lo + 511)), (v("In1"), v(GV, lo + 1, lo + 512))]
-            if WHO_C[c] == "S":
-                act(v(DC, lo, lo + 512), src)
-                terms.append((v("In1"), v(GV, lo, lo + 511)))
-            else:
-                tt(v(DC, lo, lo + 512), src, v(GV, lo, lo + 512), OP.subtract)
-            b = v("pb" + DBANK[c], 0, 511)
-            mms(b, terms[::-1])
-            act(v("AB%d" % h, lo, lo + 511), b, AF.Abs)
+        def key(h):
+            lo, hi = 128 * h, 128 * h + 128
+            pb = "pb%d" % (2 + h)
+            k = v(pb, 0, 128)
+            mm(k, v("ones"), v("CR", 0, 128), True, False)
+            mm(k, v("Ident"), v("cum", lo, hi), False, False)
+            mm(k, v("Ibig"), v("val", lo, hi), False, False)
+            mm(k, v("Ibig"), v("sgp", lo, hi), False, False)
+            for s in range(14):
+                mm(v(pb, s, 128, 16), v("AB%d" % h, s, 2048, 16), v("BKk"), False, s == 13)
+
+        def gates(h):
+            lo, hi = 128 * h, 128 * h + 128
+            a, b = 8 * h, 8 * h + 8
+            ts(v("ng", a, b), last("cum", a, b), 1.08, OP.mult, -2.29, OP.add)
+            tt(v("sgp", lo, hi), bc("ng", h), v("cum", lo, hi), OP.is_ge)
+
+        def spare(_c):
+            act(v("nw"), ind(v("cum"), v("bc15")))
+            mms(v("pb7", 256, 512), [(v("I094"), v("nw")), (v("In1"), v("cum")), (v("ones"), v("CX"))])
+            act(v("sgx"), v("pb7", 256, 512), AF.Sign, 1.0, 0.97)
+            act(v("stx"), v("sgx"), AF.Relu)
 
         def pick(h):
             lo, hi, a, b = 128 * h, 128 * h + 128, 8 * h, 8 * h + 8
             pb, GV, DC = "pb%d" % (2 + h), "GV%d" % h, "DC%d" % h
             k = v(pb, 0, 128)
-            mm(k, v("ones"), v("CR", 0, 128), True, False)
-            mm(k, v("Ident"), v("cum", lo, hi), False, False)
-            mm(k, v("Ibig"), v("val", lo, hi), False, False)
-            mm(k, v("Ibigh"), v("sgp", lo, hi), False, False)
-            for s in range(14):
-                mm(v(pb, s, 128, 16), v("AB%d" % h, s, 2048, 16), v("BKk"), False, s == 13)
-            scan(v("SK", lo, hi), v("RSf", 0, 128), k, OP.mult, OP.max)
+            scan(v("SK", lo, hi), v("RSk", 0, 128), k, OP.min, OP.max, 31.0)
             ts(v("KA", a, b), last("SK", a, b), 992, OP.bitwise_and)
             tt(v("El", lo, hi), bc("KA", h), v("DG", lo, hi), OP.mult)
-            o = v(pb, 128, 136)
-            mms(o, [(v("Ident"), v("OB", a, b)), (v("El", lo, hi), v("BM32"))])
-            cp(v("o16", a, b), o)
-            ts(v("o17", a, b), o, 1.0, OP.add)
-            for who, dst, src, lst in zip(WHO_Y[3 * h:], ("pa", "pb", "pc"), (DC, GV, GV), ("o16", "o16", "o17")):
-                (cp if who == "V" else act)(v(dst, lo, hi), ind(v(src), v(lst, a, b)))
+            o, lst = v(pb, 128, 144), "o16%d" % h
+            mms(o, [(v("Ident"), v("OB")), (v("Ident"), v("O1")), (v("El", lo, hi), v("BM32"))])
+            cp(v(lst), o)
+            for who, dst, src, at in zip(WHO_Y[3 * h:], ("pa", "pb", "pc"), (DC, GV, GV), (0, 0, 8)):
+                (cp if who == "V" else act)(v(dst, lo, hi), ind(v(src), v(lst, at, at + 8)))
             y = v(pb, 256, 384)
-            mm(y, v("Inh"), v("pa", lo, hi), True, False)
-            runs = [(0, 4)] if len(set(WHO_C[4 * h:4 * h + 4])) == 1 else [(c, c + 1) for c in range(4)]
-            for c0, c1 in runs:
-                mm(v(pb, 256 + 32 * c0, 256 + 32 * c1), v("Ih" if WHO_C[4 * h + c0] == "V" else "Ident"), v("pb", lo + 32 * c0, lo + 32 * c1), False, False)
-            mm(y, v("Ident"), v("pc", lo, hi), False, True)
+            mms(y, [(v("Inh"), v("pa", lo, hi)), (v("Ih"), v("pb", lo, hi)), (v("Ident"), v("pc", lo, hi))])
             yh = v("pb4", 256 + lo, 256 + hi)
             ts(yh, y, 0.0, OP.max, 31.5, OP.min)
             ts(v("Y", lo, hi), yh, 2.0, OP.mult)
             ts(v("KB", a, b), last("SK", a, b), 31, OP.bitwise_and)
-            tt(v("kp", a, b), v("KB", a, b), v("lv", a, b), OP.add)
-            act(v("kpw", lo, hi), bc("kp", h))
+            act(v("kpw", lo, hi), bc("KB", h))
             p = v("pb7", lo, hi)
             mms(p, [(v("Ident"), v("cum", lo, hi)), (v("In1"), v("kpw", lo, hi))])
             act(v("sgB", lo, hi), p, AF.Sign, 1.0, -1.5)
+            line(p, p, -4096.0, 69632.0 + MID)
+            tt(v("PW", lo, hi), p, v("V", lo, hi), OP.add)
             mm(v("pb6", 256 + a, 256 + b), v("Y", lo, hi), v("W8"), True, True)
-            cp(v("UI", a, b), v("pb6", 256 + a, 256 + b))
             tt(v("OH", lo, hi), bc("KA", h), v("i32s", lo, hi), OP.is_equal)
             tt(v("m2", lo, hi), v("OH", lo, hi), v("pb4", lo, hi), OP.mult)
             tt(v("m3", lo, hi - h), v("OH", lo, hi - h), v("pb4", lo + 1, hi + 1 - h), OP.mult)
@@ -573,7 +597,7 @@ def rank_program(g, core, T, topo):
 
         def near(h):
             lo, hi = 128 * h, 128 * h + 128
-            pb, GV, EE = "pb%d" % (2 + h), "GV%d" % h, "EE%d" % h
+            pb, GV, EE = "pb" + ZBANK[h], "GV%d" % h, "EE%d" % h
             z = v(pb, 384, 512)
             mm(z, v("ones"), v("LIM"), True, False)
             mm(z, v("IZv"), v("val", lo, hi), False, False)
@@ -582,120 +606,117 @@ def rank_program(g, core, T, topo):
                 mm(v(pb, 384 + s, 512, 16), v(GV, s, 2048, 16), v("GVw"), False, False)
             mm(z, v("Y", lo, hi), v("Yw%d" % h), False, False)
             mm(z, v("IZb"), v("sgB", lo, hi), False, False)
-            for s0 in range(2, first, 4):
-                b, s1 = "pb%d" % (s0 // 4 % 2), min(s0 + 4, first)
-                for s in range(s0, s1):
-                    mms(v(b, 128 * (s - s0), 128 * (s - s0) + 128), [(v("Ident"), v(GV, s, 2048, 16)), (v("Inh"), v("Y", lo, hi))])
-                act(v(EE, 128 * s0 - 256, 128 * s1 - 256), v(b, 0, 128 * (s1 - s0)), AF.Abs)
-            for s in range(first, 16):
-                tt(v(EE, 128 * s - 256, 128 * s - 128), v(GV, s, 2048, 16), v("pb4", 256 + lo, 256 + hi), OP.max)
-            slots = list(range(first, 15)) + list(range(2, first)) + [15]
-            for s in slots:
+            for s in range(2 + h * NABS[1], 16):
+                tt(v(EE, 128 * s - 256, 128 * s - 128), v(GV, s, 2048, 16), v("pb4", 256 + lo, 256 + hi), OP.subtract if s < first else OP.max)
+            if h == 0:
+                for s0 in range(2, first, NRUN):
+                    e = v(EE, 128 * s0 - 256, 128 * min(s0 + NRUN, first) - 256)
+                    act(e, e, AF.Abs)
+            elif first > 2:
+                for s in range(2, first):
+                    mms(v("pb2", 128 * s - 256, 128 * s - 128), [(v("Ident"), v(GV, s, 2048, 16)), (v("Inh"), v("Y", lo, hi))])
+                act(v(EE, 0, 128 * first - 256), v("pb2", 0, 128 * first - 256), AF.Abs)
+            for s in (range(2, 16) if h == 0 else list(range(first, 15)) + list(range(2, first)) + [15]):
                 mm(v(pb, 384 + s, 512, 16), v(EE, 128 * s - 256, 128 * s - 128), v("ABw" if s < first else "EEw"), False, s == 15)
             tt(v("m1", lo, hi), z, v("PW", lo, hi), OP.min)
-            scan(v("SM", lo, hi), v("RSm", lo, hi), v("m1", lo, hi), OP.min, OP.max)
+            scan(v("SM", lo, hi), v("RSm", lo, hi), v("m1", lo, hi), OP.min, OP.max, -4097.0)
 
-        gv(0)
-        gv(1)
-        act(v("nw"), ind(v("cum"), v("bc15")))
-        act(Vp, v("V"))
-        mms(v("pb6", 0, 256), [(v("I108"), v("nw")), (v("In1"), v("cum"))])
-        act(v("sgp"), v("pb6", 0, 256), AF.Sign, 1.0, -2.28)
-        mms(v("pb7", 0, 256), [(v("I094"), v("nw")), (v("In1"), v("cum")), (v("ones"), v("CX"))])
-        act(v("sgx"), v("pb7", 0, 256), AF.Sign, 1.0, 0.97)
-        act(v("stx"), v("sgx"), AF.Relu)
-        line(v("pb6", 0, 256), v("cum"), -4096.0, 69632.0)
-        tt(v("PW"), v("pb6", 0, 256), v("V"), OP.add)
-        ts(v("live"), v("nn"), 4.0, OP.is_ge)
-        line(v("lv"), v("live"), -100.0, 100.0)
-        line(v("rest"), v("live"), -1.0, 1.0)
-        tt(v("pb5", 0, 255), v("pb4", 1, 256), v("V", 0, 255), OP.subtract)
-        for c in range(8):
-            if c >= 2:
-                gv(c)
-            gate(c)
-            if c == 3:
-                pick(0)
-        near(0)
-        pick(1)
-        sent["Y"] = send("Y", rY, to, "lY", "aY%d" % t, 3.0)
-        act(v("Vn"), last("m5"))
-        act(v("Vk"), last("m4"))
-        cp(v("cumk"), v("KB"))
-        sent["K"] = send("VK", rK, to, "lK", "aK%d" % t, 4.0)
-        ts(v("K37"), last("m4"), 37.0, OP.mult)
+        ts(v("live"), last("cum"), 4.0, OP.is_ge)
+        sent["K"] = send("VK", rK, to, "lK", "aK%d" % t, 5.0)
+        ts(v("lv"), v("live"), -100.0, OP.mult, 16.0, OP.add)
+        tt(v("th2"), v("lv"), last("cum"), OP.subtract)
+        ts(v("s6"), v("live"), -8192.0, OP.mult)
+        tt(v("s1"), v("s6"), v("TR"), OP.add)
+        for part, h in ((bends, 0), (gates, 0), (key, 0), (pick, 0), (bends, 1), (gates, 1), (spare, 0), (near, 0), (key, 1), (pick, 1)):
+            part(h)
+        cp(v("SB", 16, 32), last("m5"))
+        ts(v("K37"), last("m4"), 37.0, OP.mult, 37.0 * MID, OP.add)
+        cp(v("UI"), v("pb6", 256, 272))
         ts(v("UI"), v("UI"), 4095, OP.bitwise_and)
         tt(v("HI"), v("UI"), v("UI"), OP.mult)
         ts(v("HI"), v("HI"), 5, OP.arith_shift_right)
         tt(v("HI"), v("HI"), v("K37"), OP.add)
         ts(v("HI"), v("HI"), 4095, OP.bitwise_and)
-        tt(v("hh"), v("HI"), v("TR"), OP.subtract)
-        tt(v("kn"), v("Vk"), v("Vn"), OP.subtract)
-        act(v("kw"), bc("kn"))
+        ts(v("x"), v("HI"), -MID, OP.add)
+        tt(v("hh"), v("x"), v("s1"), OP.max)
+        act(v("kw"), ind(v("m4"), v("bc15")))
         scan(v("sk"), v("RS"), v("OHp", 15, 271), OP.mult, OP.add)
-        C1p = v("pb6", 0, 256)
-        line(v("pb6", 256, 512), v("OH"), -1.0, 1.0)
-        tt(C1p, v("pb6", 256, 512), v("Cd"), OP.mult)
-        tt(C1p, C1p, v("m3"), OP.add)
-        act(v("C1"), C1p)
-        tt(v("pb5", 256, 511), v("pb6", 1, 256), v("C1", 0, 255), OP.subtract)
+        line(v("pb6", 0, 256), v("OH"), -1.0, 1.0)
+        tt(v("i1"), v("pb6", 0, 256), v("Cd"), OP.mult)
+        mms(v("pb5", 0, 256), [(v("IdH"), v("m3")), (v("IdH"), v("i1"))])
         mms(v("pb7", 256, 512), [(v("In1"), v("stx")), (v("Ident"), v("sk"))])
         near(1)
-        ts(v("SB"), last("SM"), 12, OP.logical_shift_right)
-        sent["B"] = send("SB", rB, to, "lB", "aB%d" % t, 1.6)
-        ts(v("close"), last("SM"), 0.0, OP.is_ge)
-        tt(v("grow"), v("live"), v("close"), OP.subtract)
-        tt(v("s1"), v("hh"), v("grow"), OP.mult)
-        tt(v("z"), v("s1"), v("TR"), OP.add)
-        for m, b in (("K", rK), ("Y", rY), ("B", rB)):
+        ts(v("SB", 0, 16), last("SM"), 12, OP.logical_shift_right)
+        sent["B"] = send("SB", rB, to, "lB", "aB%d" % t, FAR)
+        tt(v("kn"), last("SM"), v("TR"), OP.min)
+        tt(v("z"), v("kn"), v("hh"), OP.max)
+        ts(v("nc"), last("SM"), 0.0, OP.is_lt)
+        tt(v("grow"), v("live"), v("nc"), OP.mult)
+        for m, b in (("K", rK), ("B", rB)):
             arrive(b, "a%s%d" % (m, t), frm, sent[m])
-        rck, rVn = v(rK, 256, 272), v(rK, 272, 288)
+        rVn = v(rB, 16, 32)
 
         def gap1():
             act(v("gw"), bc("grow"))
             act(v("sgm"), v("SM"), AF.Sign, 1.0, 0.5)
-            line(v("cw"), bc("close"), 1.0, -1.0)
+            if WHO_O == "T":
+                mms(v("pb6", 256, 512), [(v("ones"), v("C4")), (v("In4k"), v("sk")), (v("I2k"), v("sgm"))])
+                tt(v("Cp"), v("pb6", 256, 512), v("Cd"), OP.max)
             tt(v("Ag"), v("pb7", 256, 512), v("gw"), OP.mult)
-            mms(v("pb6", 0, 256), [(v("I4k"), v("sk")), (v("In2k"), v("sgm")), (v("I4k"), v("cw"))])
-            mms(v("pb7", 0, 256), [(v("Ident"), v("OH")), (v("Ident"), v("Ag"))])
-            act(v("pos"), v("pb7", 0, 256), AF.Relu)
-            act(v("neg"), v("pb7", 0, 256), AF.Relu, -1.0)
-            line(v("pb6", 256, 512), v("pb6", 0, 256), -1.0, 6144.0)
-            line(v("a1"), v("pb6", 0, 256), 1.0, -2048.0)
-            tt(v("Cp"), v("pb6", 256, 512), v("Cd"), OP.max)
-            sent["C"] = send("Cp", rC, to, "lC", "aC%d" % t, 4.0)
-            arrive(rC, "aC%d" % t, frm, sent["C"])
-            mms(v("pb7", 0, 256), [(v("Ident"), v("negp", 15, 271)), (v("In1"), v("neg")), (v("Ident"), v("posp", 15, 271)), (v("In1"), v("posp", 14, 270))])
-            act(v("pb7", 256, 512), v("pb7", 0, 256), AF.Relu)
+            mms(v("pb6", 0, 256), [(v("I4k"), v("sk")), (v("In2k"), v("sgm")), (v("In4k"), v("gw"))])
+            mms(v("pb7", 0, 256), [(v("In2"), v("OH")), (v("In1"), v("Ag"))])
+            act(v("pos"), v("pb7", 0, 256), AF.Relu, -1.0, -1.0)
+            act(v("neg"), v("pb7", 0, 256), AF.Relu)
+            if WHO_O == "S":
+                line(v("pb6", 256, 512), v("pb6", 0, 256), -1.0, 4096.0)
+            line(v("a1"), v("pb6", 0, 256), 1.0, -4096.0)
+            if WHO_O == "S":
+                tt(v("Cp"), v("pb6", 256, 512), v("Cd"), OP.max)
+            sent["C"] = send("YC", "rP%d" % t, to, "lC", "aC%d" % t, FAR + 1.5)
+            OPS[-1][7].append(sent["B"])
+            arrive("rP%d" % t, "aC%d" % t, frm, sent["C"])
+            mms(v("pb7", 256, 512), [(v("Ident"), v("OH")), (v("Ident"), v("posp", 15, 271)), (v("In1"), v("pos"))])
             ts(v("VM"), last("SM"), 4095, OP.bitwise_and)
-            tt(v("s2"), v("HI"), v("VM"), OP.subtract)
-            tt(v("s8"), v("VM"), v("Vk"), OP.subtract)
-            tt(v("s9"), v("s2"), v("grow"), OP.mult)
-            tt(v("x"), v("s8"), v("s9"), OP.add)
-            act(v("xw"), bc("x"))
-            tt(v("s3"), rck, v("nn"), OP.add)
-            line(v("s4"), v("s3"), -1.0, 16.0)
-            tt(v("th2"), v("s4"), v("rest"), OP.mult)
-            tt(v("s5"), rck, v("nn"), OP.min)
-            tt(v("s6"), v("V0"), v("TR"), OP.subtract)
-            act(v("hF"), v("s5"), AF.Sign)
-            tt(v("s7"), v("s6"), v("hF"), OP.mult)
+            ts(v("s5"), v("VM"), -MID, OP.add)
+            tt(v("s2"), v("s5"), v("z"), OP.min)
+            act(v("xw"), bc("s2"))
+            ts(v("mP"), v("Ag"), 0.0, OP.max)
+            tt(v("s7"), v("V0"), v(rK, 256, 272), OP.mult)
             tt(v("z0"), v("s7"), v("TR"), OP.add)
             tt(v("dz"), rVn, v("z0"), OP.subtract)
-            tt(v("dv0"), rVn, v("V0"), OP.subtract)
+
+        def moved(h):
+            lo, hi = 128 * h, 128 * h + 128
+            for b, x in (("pb4", "V"), ("pb5", "C")):
+                tt(v("up" + x, lo + 1, hi), v("mP", lo, hi - 1), v(b, lo, hi - 1), OP.mult)
+                tt(v("dn" + x, lo, hi - 1), v("neg", lo, hi - 1), v(b, lo + 1, hi), OP.mult)
+
+        def taken(h):
+            lo, hi = 128 * h, 128 * h + 128
+            b = "pb6"
+            for old, x, came in (("pb4", "V", rK), ("pb5", "C", rC)):
+                tt(v("kp" + x, lo, hi), v("keep", lo, hi), v(old, lo, hi), OP.mult)
+                tt(v("in" + x, lo, hi), v("pb7", lo, hi), v(came, lo, hi), OP.mult)
+            parts = ("up", "dn", "fx", "kp", "in")
+            mms(v("pb4", lo, hi), [(v("IdH"), v(p + "V", lo, hi)) for p in parts])
+            act(v("V", lo, hi), v("pb4", lo, hi))
+            if not lastt:
+                mm(v(b, 0, 128), v("V", lo, hi), v("IdH"), True, True)
+                ts(v("LV", lo, hi), v(b, 0, 128), MID, OP.add)
+            mms(v("pb5", 256 + lo, 256 + hi), [(v("IdH"), v(p + "C", lo, hi)) for p in parts])
+            tt(v("Cd", lo, hi), v("pb5", 256 + lo, 256 + hi), v("a1", lo, hi), OP.max)
+            if not lastt:
+                mm(v(b, 128, 256), v("Cd", lo, hi), v("IdH"), True, True)
+                ts(v("LC", lo, hi), v(b, 128, 256), MID, OP.add)
+            counts(h)
 
         def gap2():
-            tt(Vp, v(rK, 0, 256), Vp, OP.subtract)
-            for dd, rR, fx, new, old in ((dV, "rRV", "fxV", "xw", "V"), (dC, "rRC", "fxC", "kw", "C1")):
-                tt(v(rR, 16, 272), v("pos"), dd, OP.mult)
-                tt(dd, v("neg"), dd, OP.mult)
-                tt(dd, dd, v(old), OP.add)
-                tt(dd, dd, v(rR, 15, 271), OP.subtract)
-                tt(v(fx), v("pb7", 256, 512), v(new), OP.mult)
-                tt(dd, dd, v(fx), OP.add)
-            tt(dC, dC, v("a1"), OP.max)
+            tt(v("fxV"), v("pb7", 256, 512), v("xw"), OP.mult)
+            tt(v("fxC"), v("pb7", 256, 512), v("kw"), OP.mult)
+            moved(0)
+            moved(1)
             if not lastt:
-                act(v("s4"), v("close"), AF.Identity, total=v("cs1"))
+                act(v("s4"), v("nc"), AF.Identity, -1.0, 1.0, total=v("cs1"))
                 mm(v("pb6", 0, 1), v("onesF"), v("cs1"), True, True)
                 cp(v("cI"), v("pb6", 0, 1))
                 ts(v("cI"), v("cI"), 31, OP.bitwise_and)
@@ -703,70 +724,71 @@ def rank_program(g, core, T, topo):
                 line(v("LIM"), v("blkw"), v("lim"), 0.0)
 
         dedupe(gap1, gap2, "Y")
-        tt(v("take"), v(rB), v("th2"), OP.is_lt)
-        tt(v("s1"), v("take"), v("dz"), OP.mult)
-        tt(v("z"), v("s1"), v("z0"), OP.add)
+        tt(v("take"), v(rB, 0, 16), v("th2"), OP.is_lt)
+        tt(v("s3"), v("take"), v("dz"), OP.mult)
+        tt(v("z"), v("s3"), v("z0"), OP.add)
 
         def gap3():
-            cp(v("z16"), v("zA"))
+            cp(v("z16"), v("zU"))
             act(v("tw"), bc("take"))
-            line(v("ntw"), v("tw"), -1.0, 1.0)
-            act(v("pb7", 0, 256), v("tw"))
-            tt(v("tV"), v("tw"), Vp, OP.mult)
-            tt(v("V"), dV, v("tV"), OP.add)
-            if not lastt:
-                turn(("pb6", 0), "V")
-                cp(v("LV"), v("pb6", 0, 256))
-            tt(v("BL"), ind(v("X"), v("z16")), v(rY), OP.add)
-            line(v("BL2"), v("BL"), 0.5, 159.75)
-            line(v("BL3"), v("BL2"), 1.0, -160.0)
+            if WHO_T == "S":
+                act(v("pb7", 0, 256), v("tw"))
+            else:
+                mm(v("pb7", 0, 256), v("Ident"), v("tw"), True, True)
+            mms(v("pb6", 256, 512), [(v("In2"), v("posp", 15, 271)), (v("In2"), v("mPp", 15, 271)), (v("Ident"), v("Ag")), (v("In2"), v("tw"))])
+            act(v("keep"), v("pb6", 256, 512), AF.Relu, 1.0, 1.0)
+            if WHO_B == "S":
+                act(v("BL"), ind(v("X"), v("z16")))
+                mms(v("pb1", 256, 512), [(v("Ident"), v(rY)), (v("Ident"), v("BL"))])
+                ts(v("iw"), v("pb1", 256, 512), 0.5, OP.mult, -0.25, OP.add)
+            else:
+                tt(v("BL"), ind(v("X"), v("z16")), v(rY), OP.add)
+                ts(v("iw"), v("BL"), 0.5, OP.mult, -0.25, OP.add)
 
         def gap4():
-            tt(dC, dC, v("ntw"), OP.mult)
-            tt(v("tC"), v("pb7", 0, 256), v(rC), OP.mult)
-            tt(v("Cd"), dC, v("tC"), OP.add)
+            taken(0)
+            taken(1)
             if not lastt:
-                turn(("pb7", 256), "Cd")
-                cp(v("LC"), v("pb7", 256, 512))
-            counts()
-            if not lastt:
-                tt(v("s3"), v("dv0"), v("take"), OP.mult)
                 tt(v("V0"), v("V0"), v("s3"), OP.add)
 
-        dedupe(gap3, gap4, "BL3")
+        dedupe(gap3, gap4, "iw")
         if lastt:
             dma("Y", T.yx[:, 0:half], T.X[:, 0:half], [v("X", 0, half)], [], 5.0)
             dma("S", T.yx[:, half:W], T.X[:, half:W], [v("X", half, W)], [], 5.0)
 
     for h in range(2):
-        mm(v("pb1", 128 * h, 128 * h + 128, p=8), v("nn", 8 * h, 8 * h + 8), v("IdF"), True, True)
+        mm(v("pb1", 128 * h, 128 * h + 128, p=8), last("cum", 8 * h, 8 * h + 8), v("Ident"), True, True)
     act(v("LNF", p=8), v("pb1", 0, 256, p=8))
     dma("Y", T.yn[:], T.LNF[0:8, :], [v("LNF")], [])
     VC = v("pb4", 0, 256)
     for h in range(2):
         lo, hi = 128 * h, 128 * h + 128
-        mms(v("pb4", lo, hi), [(v("V", lo, hi), v("Id4k")), (v("Cd", lo, hi), v("IdF"))])
+        mms(v("pb4", lo, hi), [(v("V", lo, hi), v("Id4k")), (v("Cd", lo, hi), v("IdH")), (v("ones"), v("CV", 0, 128))])
         mms(v("pb6", lo, hi), [(v("cum", lo, hi), v("Ident")), (v("val", lo, hi), v("Ibigh"))])
     line(v("cumI"), v("pb6", 0, 256), 1.0, -BIG / 2)
     for p in range(16):
-        b, pr = v(("g1", "g2", "g3")[p % 3]), "m%d" % (1 + p % 6)
-        if p % 2 and p < 2 * SMASK:
-            b = v(("pa", "pb", "pc")[p // 2 % 3])
-            act(v("a2"), v("cumI"), AF.Abs, 1.0, -1.0 - p)
-            act(b, v("a2"), AF.Relu, -1.0, 1.0)
+        b, pr = v(("g1", "g2", "g3")[p % 3]), "m" + "012456"[p % 6]
+        if p >= 16 - SMASK:
+            b, a = v(("pa", "pb", "pc", "keep", "neg", "tw")[p % 6]), v(("a2", "a3")[p % 2])
+            act(a, v("cumI"), AF.Abs, 1.0, -1.0 - p)
+            act(b, a, AF.Relu, -1.0, 1.0)
         else:
             ts(b, v("cumI"), float(p + 1), OP.is_equal)
         tt(v(pr), b, VC, OP.mult)
         for h in range(2):
             mm(v("pb7", 128 * h + p, 128 * h + 128, 16), v(pr, 128 * h, 128 * h + 128), v("blk8F"), True, True)
-    act(v("SO"), v("pb7", 0, 256))
-    turn(("pb6", 0), "SO")
-    cp(v("iw"), v("pb6", 0, 256))
-    ts(v("IV"), v("iw"), 12, OP.arith_shift_right)
-    ts(v("IC"), v("iw"), 4095, OP.bitwise_and)
-    cp(v("f1"), v("IV"))
+    for h in range(2):
+        lo, hi = 128 * h, 128 * h + 128
+        cp(v("SO", lo, hi), v("pb7", lo, hi))
+    for h in range(2):
+        lo, hi = 128 * h, 128 * h + 128
+        mm(v("pb%d" % (2 + h), 0, 128), v("SO", lo, hi), v("IdF"), True, True)
+        cp(v("SK", lo, hi), v("pb%d" % (2 + h), 0, 128))
+        ts(v("IV", lo, hi), v("SK", lo, hi), 12, OP.arith_shift_right)
+        ts(v("IC", lo, hi), v("SK", lo, hi), 4095, OP.bitwise_and)
+        cp(v("f1", lo, hi), v("IV", lo, hi))
+        cp(v("f2", lo, hi), v("IC", lo, hi))
     dma("Y", T.yv[:], v("f1")[0], [v("f1")], [])
-    cp(v("f2"), v("IC"))
     dma("S", T.yc[:], v("f2")[0], [v("f2")], [])
     if "order" not in PLAN:
         PLAN["order"] = order()

@@ -1,3 +1,5 @@
+import numpy as np
+from concourse.bass import DstId, RemoteDMATransfer
 from concourse.mybir import AluOpType, AxisListType, ActivationFunctionType
 
 OP = AluOpType
@@ -6,32 +8,44 @@ W, L, S, ST = 4096, 256, 16, 5
 BIG, KZ, MID = 4194304.0, 262144.0, 2048.0
 F32, BF, I32, U16, F16 = "float32", "bfloat16", "int32", "uint16", "float16"
 
-RUNS = ((("S", 16), ("V", 16), ("S", 32), ("S", 32), ("S", 32)), (("S", 32), ("V", 32), ("S", 32), ("S", 16), ("S", 16)))
-DWIDE = 256
-WZ = "SS"
-WHO_Y = "VVVVSV"
-WHO_B, WHO_T = "V", "S"
+RUNS = ((("S", "V", 16), ("V", "T", 16), ("S", "T", 32), ("S", "T", 32), ("S", "T", 32)), (("S", "T", 32), ("V", "T", 32), ("S", "T", 32), ("S", "T", 16), ("S", "T", 16)))
+KEYS = (((0, 128),), ((0, 128),))
+DIFF = "01"
+AS = 14
+DRUN = 64
+NDMA = [sum(n for _w, how, n in r if how == "D") for r in RUNS]
+GDMA, ADMA, BDMA = 1.0, 2.0, 0.002
+PARTS = "b0 g0 k0 p0 b1 g1 n0 k1 p1"
+YGATHER = ((("S", 0, 3),), (("S", 0, 3),))
+SPLIT = 1
+MAXES = 0
+NT = 0
+WHO = {"kc": "S", "SB": "V", "ng": "V", "cI": "V", "Ru10": "S", "Ru11": "S", "Ru20": "S", "Ru21": "S", "blend": "V", "sq": "V", "tw": "T", "V": "S", "Cd": "V", "Kp": "V", "H": "V", "Cp": "V", "round": "V", "zRu1": "V", "zRu2": "S", "x": "V", "s5": "V", "LV0": "V", "LV1": "V", "LC0": "V", "LC1": "V", "UI": "V", "z16": "V"}
+YS = 1
+NABS = (10, 0)
 NRUN = 7
-NABS = (14, 0)
-SMASK = 0
+BANK = {"z": "10", "PW": "77", "u": "6", "Z": "6", "F": "7", "pm": "6", "keep": "6", "tw": "7", "list": "66", "c": "6", "bl": "1", "Ru": "10", "P1": "77", "P2": "66", "ET": "6"}
 CYC, GATHER, SCATTER, WAKE, SLACK = 0.00083, 1.4, 3.4, 0.19, 0.02
-TFIX, HALF = 0.006, 1
-RULES = [(b, l, u) for b in (0.0, 0.01, 0.03) for l, u in ((0.3, 0.3), (0.5, 0.5), (0.5, 1.5))]
-PASSES = 6
+TFIX = 0.006
+RULES = [(0.0, 0.3, 0.3), (0.03, 0.5, 0.5)]
+PASSES = 4
+LONG = 2
+SHAKES = 400
+SHAKE = 0.3
+SHARE = 0.2
 FAR = 3.0
-ZBANK = "10"
-WHO_O = "T"
 PLAN = {}
 XW = W + 2 * L
+GW = 2064
 SCRATCH = {"X": ("sbuf", [128, XW], BF)}
 ALIAS = {}
 
 
-def _pack(buf, names, cols, d):
+def _pack(buf, names, cols, d, pad=0):
     names = names.split()
     for k, n in enumerate(names):
-        ALIAS[n] = (buf, k * cols, cols, d)
-    SCRATCH[buf] = ("sbuf", [128, len(names) * cols], d)
+        ALIAS[n] = (buf, k * (cols + pad) + pad, cols, d)
+    SCRATCH[buf] = ("sbuf", [128, len(names) * (cols + pad)], d)
 
 
 def _add(names, cols, d):
@@ -39,46 +53,53 @@ def _add(names, cols, d):
         SCRATCH[n] = ("sbuf", [128, cols], d)
 
 
-_add("GV0 GV1 DC0 DC1", 2064, BF)
-_add("AB0 AB1", 2048, BF)
+for _h in "01":
+    SCRATCH["GD" + _h] = ("sbuf", [128, 2 * GW], BF)
+    ALIAS["GV" + _h], ALIAS["DC" + _h] = ("GD" + _h, 0, GW, BF), ("GD" + _h, GW, GW, BF)
+_add("AB0 AB1", 128 * AS, BF)
 _add("EE0 EE1", 1792, BF)
 _add("EQ", 4096, BF)
 _add("VK", 272, F16)
-ALIAS["V"], ALIAS["live"] = ("VK", 0, 256, F16), ("VK", 256, 16, F16)
-_pack("YC", "Y Cp", 256, F16)
-_pack("MH", "Cd Wz Ez i1 i2 m3 upV upC dnV dnC fxV fxC kpV kpC inV inC", 256, F16)
-_pack("MI", "IdH Id4k", 128, F16)
-_add("blk8H", 8, F16)
-_add("OHp posp mPp", 272, BF)
-ALIAS["OH"], ALIAS["pos"], ALIAS["mP"] = ("OHp", 16, 256, BF), ("posp", 16, 256, BF), ("mPp", 16, 256, BF)
-_pack("MF", "PW m0 m1 m2 m4 m5 m6 m7 m8 xw kw RSf RSm RSk DGf THR i32s SO f1 f2 QC", 256, F32)
-_pack("MB", "val cum nw sgp sgx stx sgB kpw sk sgm Ag gw tw keep neg RS DG El pa pb pc BL CR CX CV C4 g1 g2 g3 a1 a2 a3 cumI", 256, BF)
-_add("SK SM IV IC iw LNI", 256, I32)
-_add("LV LC Ru", 256, U16)
-_pack("PLF", "nn ng V0 lv nc grow x kn K37 hh s1 s2 s3 s4 s5 s6 s7 z z0 dz th2 take zA zU oA TR TRu Vk", 16, F32)
-_pack("PLI", "KA KB UI HI VM", 16, I32)
-_pack("PLU", "o160 o161 off16 z16 bcA bc15", 16, U16)
-_pack("PLB", "OB O1 BM32 BMh", 16, BF)
-_pack("COF", "pcF pmF p4F thm lim cs1 e1 e2 e3 e4 eK wF wq wp", 1, F32)
-_pack("COI", "pcI pmI p4I cI tI", 1, I32)
-_add("WI THI", 1, I32)
-_pack("MQ", "mg mm onesF G8 IdF PW2", 128, F32)
-_pack("IDS", "Ident In1 In2 Ih Inh Ibig Ibigh I094 IZb IZv I4k In2k In4k I2k ones Yw0 Yw1 LIM blkw CQ zero", 128, BF)
-_pack("N8", "BKk EEw GVw ABw W8", 8, BF)
-_add("BW", 576, BF)
-_add("blk8F", 8, F32)
-_add("LNF THF", 256, F32)
+ALIAS["V"], ALIAS["s1"] = ("VK", 0, 256, F16), ("VK", 256, 16, F16)
+_pack("YC", "Y Cd" if WHO["Cp"] == "S" else "Y Cp", 256, F16)
+_pack("YN", "low NF" if WHO["Cp"] == "S" else "low Cd", 256, F16)
 for _t in range(ST):
     _add("rK%d" % _t, 272, F16)
-    _pack("rP%d" % _t, "rY%d rC%d" % (_t, _t), 256, F16)
+    _pack("rC%d" % _t, "rY%d rP%d" % (_t, _t), 256, F16)
     _add("rB%d" % _t, 32, I32)
 _add("SB", 32, I32)
+_pack("MH", "Wz Ez Ru i1 m3 upV upC dnV dnC fxV fxC kpV kpC inV inC tV tC", 256, F16)
+_pack("MI", "IdH InH Uh0 Uh1 Uh2 Uh3 Uh4 Uh8 Uh12", 128, F16)
+_add("blk8H", 8, F16)
+_pack("MP", "OH ee mP Fu", 256, BF, 16)
+_pack("MF", "PW m1 m2 m4 m5 xw kw SO n0 n1 n2 n3 n4 n5 RSf RSm RSk RSn DGf THR i32s QC f1 f2 LNF", 256, F32)
+_pack("MQ", "mg mm onesF IdF PW2 G8", 128, F32)
+_pack("MB", "val cum av sgp sk dd sgm gw tw keep Dn FF Zs El cumI RS NR DG g1 g2 g3 BL C4", 256, BF)
+_add("pabc0 pabc1", 384, BF)
+_add("SK SM IV IC iw LNI", 256, I32)
+_add("LV LC", 256, U16)
+_pack("PLF", "nn ng V0 x kn kc Kp sq hh s2 s3 s4 s5 s6 s7 th2 TR TRm oA zz t1 t3", 16, F32)
+_pack("PL2", "zs dz take", 32, F32)
+_add("grow", 24, F32)
+_pack("PLI", "KA UI HI VM", 16, I32)
+_pack("PLU", "off16 z16 bcA bcG bcZ", 16, U16)
+_pack("OL", "olist0 olist1", 24, U16)
+_add("OB", 24, F16)
+_pack("PLB", "BM32 BMh", 24, BF)
+_pack("COF", "pcF pmF p4F thm lim cs1 e1 e2 e3 e4 eK eO eH eL eM wF wq wp", 1, F32)
+_pack("COI", "pcI pmI p4I cI tI", 1, I32)
+_add("WI THI", 1, I32)
+_pack("IDS", "Ident In1 In2 I2 I4 Ig Ih Inh Ibig IZv In4k In4 I64 I2k I8k In8k ones Yw0 Yw1 LIM blkw blkl CQ CR zero Ub0 Ub1 Ub2 Ub3", 128, BF)
+_pack("N8", "BKk EEw GVw ABw W8", 8, BF)
+_add("BW", 576, BF)
+_add("blk8F THF", 8, F32)
 for _b in range(8):
-    SCRATCH["pb%d" % _b] = ("psum", [128, 512], F32)
+    SCRATCH["pb%d" % _b] = ("psum", [128, 32, 16] if str(_b) in DIFF and AS == 14 else [128, 512], F32)
+SCRATCH["DV"] = ("sbuf", [128, 32, 16], BF)
 
 SEMAPHORES = ["sV", "sS", "sT", "sG", "lK", "lC", "lB"]
 SEMAPHORES += ["a%s%d" % (m, t) for m in "KCB" for t in range(ST)]
-SEMAPHORES += ["d%d" % k for k in range(24)]
+SEMAPHORES += ["d%d" % k for k in range(24)] + ["e%d%d" % (h, k) for h in range(2) for k in range(4)]
 
 
 def rank_program(g, core, T, topo):
@@ -97,10 +118,20 @@ def rank_program(g, core, T, topo):
             name, at, width, _d = ALIAS[name]
             hi = at + (width if hi is None else hi)
             lo += at
-        hi = SCRATCH[name][1][1] if hi is None else hi
         t = T[name]
+        if len(SCRATCH[name][1]) == 3:
+            hi = SCRATCH[name][1][1] * 16 if hi is None else hi
+            a, b, s = lo // 16, (hi + 15) // 16, lo % 16
+            p1 = p or 128
+            if step < 0:
+                return (t[:, a:b, s:s + 14], [(name, lo, hi)], (b - a) * 14, False)
+            if hi - lo < 16:
+                return (t[0:p1, a, s:s + hi - lo], [(name, lo, hi)], hi - lo, False)
+            return (t[0:p1, a:b, :] if step == 1 else t[0:p1, a:b, s], [(name, lo, hi)], (hi - lo + step - 1) // step, False)
+        hi = SCRATCH[name][1][1] if hi is None else hi
         sl = slice(lo, hi, step) if step != 1 else slice(lo, hi)
-        return (t[:, sl] if p is None else t[0:p, sl], [(name, lo, hi)], (hi - lo + step - 1) // step, False)
+        p0, p1 = p if isinstance(p, tuple) else (0, p or 128)
+        return (t[p0:p1, sl], [(name, lo, hi)], (hi - lo + step - 1) // step, False)
 
     def ind(win, off):
         return (win[0].indirect(off[0]), win[1] + off[1], off[2] * 16, True)
@@ -157,7 +188,7 @@ def rank_program(g, core, T, topo):
     OPS = []
 
     def add(q, emit, reads, writes, cost, lat=0.0, after=()):
-        OPS.append([q, emit, [a for x in reads for a in x[1]], [a for x in writes for a in x[1]], cost, lat, list(after), []])
+        OPS.append([q, emit, [a for x in reads for a in x[1]], [a for x in writes for a in x[1]], cost, lat, list(after), [], None])
         return len(OPS) - 1
 
     def op(q, fn, reads, writes, cost=0.06):
@@ -178,6 +209,13 @@ def rank_program(g, core, T, topo):
             record(q + "d", bump(q, sem, 16), rd, wr)
         return add(q, emit, reads, writes, 0.1, lat)
 
+    def addto(out, a, sem):
+        def emit(rd, wr):
+            wait("G", need("G", rd, wr))
+            g.dma_start(out[0], a[0], accum_op=OP.add).then_inc(T.sem[sem], 16)
+            record("Gd", bump("G", sem, 16), rd, wr)
+        return add("G", emit, [a, out], [out], GDMA, ADMA + out[2] * BDMA)
+
     def order():
         seen, deps, succ = {}, [], [[] for _ in OPS]
         for i, o in enumerate(OPS):
@@ -188,16 +226,9 @@ def rank_program(g, core, T, topo):
                 dp[j] = 1
             for acc, wr in [(a, 0) for a in o[2]] + [(a, 1) for a in o[3]]:
                 name, lo, hi = acc
-                bank = name.startswith("pb")
-                if bank and seen.get(name) and seen[name][0][3] != q:
-                    seen[name, "before"] = seen.pop(name)
-                for r in seen.get((name, "before"), []):
-                    dp[r[2]] = 1
                 for (l2, h2, j, q2, w2) in seen.get(name, []):
-                    if bank and q == "T":
-                        dp[j] = max(dp.get(j, 0), 0)
-                    elif lo < h2 and l2 < hi and (wr or w2):
-                        dp[j] = 1
+                    if lo < h2 and l2 < hi and (wr or w2):
+                        dp[j] = max(dp.get(j, 0), 0 if q == q2 == "T" else 1)
             for acc, wr in [(a, 0) for a in o[2]] + [(a, 1) for a in o[3]]:
                 name, lo, hi = acc
                 old = seen.get(name, [])
@@ -206,9 +237,40 @@ def rank_program(g, core, T, topo):
                 seen[name] = old + [(lo, hi, i, q, wr)]
             dp.pop(i, None)
             deps.append(dp)
-            for j in dp:
-                succ[j].append(i)
         n = len(OPS)
+        sums, opened = [], {}
+        for i, o in enumerate(OPS):
+            if o[8]:
+                b = o[3][0][0]
+                if o[8][0]:
+                    opened[b] = [b, i]
+                    sums.append(opened[b])
+                else:
+                    deps[i].setdefault(opened[b][1], 0)
+                    opened[b].append(i)
+                if o[8][1]:
+                    for j in opened[b][1:-1]:
+                        deps[i].setdefault(j, 0)
+        while True:
+            above = []
+            for i in range(n):
+                m = 0
+                for j in deps[i]:
+                    m |= above[j] | (1 << j)
+                above.append(m)
+            new, lastof = 0, {}
+            for s in sums:
+                for e in lastof.get(s[0], [])[-12:]:
+                    if not above[s[1]] >> e[-1] & 1 and (above[s[-1]] >> e[1] & 1 or len(s) > LONG or len(e) > LONG):
+                        deps[s[1]][e[-1]] = 0
+                        new += 1
+                lastof.setdefault(s[0], []).append(s)
+            if not new:
+                break
+        for i in range(n):
+            for j in deps[i]:
+                succ[j].append(i)
+        banks = [sorted({a[0] for a in o[2] + o[3] if a[0].startswith("pb")}) for o in OPS]
         cost = [o[4] for o in OPS]
         fwd = [[(j, cost[j] + (OPS[j][5] + WAKE if k else 0.0)) for j, k in deps[i].items()] for i in range(n)]
         bwd = [[(j, cost[j] + (OPS[i][5] + WAKE if deps[j][i] else 0.0)) for j in succ[i]] for i in range(n)]
@@ -216,29 +278,46 @@ def rank_program(g, core, T, topo):
         def place(key, before, after, first, look, urge):
             left = [len(b) for b in before]
             start, free, ready, out = [0.0] * n, {}, {}, []
+            held, busy = {}, set()
+            a, z = (0, 1) if before is fwd else (1, 0)
 
             def push(i):
                 ready.setdefault(OPS[i][0], []).append((max([first[i]] + [start[j] + w for j, w in before[i]]), key[i], i))
+
+            def now(c, q):
+                t0 = c[0]
+                for b in banks[c[2]]:
+                    if b in held and held[b][0] != q and held[b][1] > t0:
+                        t0 = held[b][1]
+                return (t0, c[1], c[2], c)
             for i in range(n):
                 if left[i] == 0:
                     push(i)
             while len(out) < n:
                 best = None
                 for q, lst in ready.items():
+                    lst = [now(c, q) for c in lst if not (q == "T" and OPS[c[2]][8][a] and banks[c[2]][0] in busy)]
                     if lst:
                         t0 = max(free.get(q, 0.0), min(lst)[0])
-                        r = min((c for c in lst if c[0] <= t0 + SLACK), key=lambda c: c[1:])
+                        r = min((c for c in lst if c[0] <= t0 + SLACK), key=lambda c: c[1:3])
                         soon = [c for c in lst if c[0] <= t0 + look * cost[r[2]] and c[1] < r[1] - urge]
                         if soon:
-                            r = min(soon, key=lambda c: c[1:])
+                            r = min(soon, key=lambda c: c[1:3])
                         st = max(t0, r[0])
                         if best is None or st < best[0]:
                             best = (st, q, r)
                 st, q, r = best
                 i = r[2]
-                ready[q].remove(r)
+                ready[q].remove(r[3])
                 start[i] = st
                 free[q] = st + cost[i]
+                for b in banks[i]:
+                    held[b] = (q, free[q] + WAKE)
+                if q == "T":
+                    if OPS[i][8][a]:
+                        busy.add(banks[i][0])
+                    if OPS[i][8][z]:
+                        busy.discard(banks[i][0])
                 out.append(i)
                 for j, _w in after[i]:
                     left[j] -= 1
@@ -249,6 +328,8 @@ def rank_program(g, core, T, topo):
         tail = [0.0] * n
         for i in range(n - 1, -1, -1):
             tail[i] = max([lat[i]] + [tail[j] + w for j, w in bwd[i]])
+        PLAN["chain"] = max(tail[i] + cost[i] for i in range(n))
+        PLAN["debug"] = (OPS, tail, cost, bwd, fwd)
         best = None
         for beta, look, urge in RULES:
             key = [beta * i - tail[i] - cost[i] for i in range(n)]
@@ -256,10 +337,26 @@ def rank_program(g, core, T, topo):
                 start, seq = place(key, fwd, bwd, none, look, urge)
                 end = max(start[i] + cost[i] + lat[i] for i in range(n))
                 if best is None or end < best[0]:
-                    best = (end, seq)
+                    best = (end, seq, start)
                     PLAN["rule"] = (beta, look, urge)
                 late, _seq = place([-start[i] - cost[i] for i in range(n)], bwd, fwd, lat, look, urge)
                 key = [-late[i] - cost[i] for i in range(n)]
+        rng = np.random.default_rng(1)
+        look, urge = PLAN["rule"][1:]
+        PLAN["tools"] = (place, fwd, bwd, none, lat, best)
+        kinds = {}
+        kind = [kinds.setdefault((o[0], str(o[3]), str([a for a in o[2] if a[0][0] != "r"])), len(kinds)) for o in OPS]
+        for k in range(SHAKES):
+            noise = rng.normal(0.0, SHAKE, len(kinds)) * (rng.random(len(kinds)) < SHARE)
+            if k % 2:
+                late, _seq = place([-best[2][i] - cost[i] + float(noise[kind[i]]) for i in range(n)], bwd, fwd, lat, look, urge)
+                key = [-late[i] - cost[i] for i in range(n)]
+            else:
+                key = [best[2][i] + float(noise[kind[i]]) for i in range(n)]
+            start, seq = place(key, fwd, bwd, none, look, urge)
+            end = max(start[i] + cost[i] + lat[i] for i in range(n))
+            if end < best[0]:
+                best = (end, seq, start)
         PLAN["end"] = best[0]
         return best[1]
 
@@ -303,9 +400,20 @@ def rank_program(g, core, T, topo):
         else:
             op("S", lambda e: e.activation(out[0], a[0], f, bias=bi, scale=sc, accum_out=total[0]), rd, [out, total], c + 0.02)
 
-    def mm(out, l, r, start, stop):
-        c = TFIX + max(64, r[2]) * CYC * {F32: 4, F16: HALF}.get(SCRATCH[r[1][0][0]][2], 1)
-        op("T", lambda e: e.matmul(out[0], l[0], r[0], start, stop), [l, r], [out], c)
+    def line(dst, x, scale, bias):
+        act(dst, x, AF.Identity, scale, bias)
+
+    def move(who, out, a, scale=None, bias=None):
+        if scale is None:
+            (cp if WHO[who] == "V" else act)(out, a)
+        elif WHO[who] == "V":
+            ts(out, a, scale, OP.mult, bias, OP.add)
+        else:
+            line(out, a, scale, bias)
+
+    def mm(out, l, r, start=True, stop=True):
+        c = TFIX + max(min(64, l[2]), r[2]) * CYC * (4 if SCRATCH[r[1][0][0]][2] == F32 else 1)
+        OPS[op("T", lambda e: e.matmul(out[0], l[0], r[0], start, stop), [l, r], [out], c)][8] = (start, stop)
 
     def mms(out, terms):
         for k, (l, r) in enumerate(terms):
@@ -327,18 +435,21 @@ def rank_program(g, core, T, topo):
         else:
             op("G", lambda e: e.iota(out[0], pat, base, cm, allow_small_or_imprecise_dtypes=True), [], [out], 0.13 + 2 * CYC * out[2])
 
-    def bc(x, h=None):
-        return ind(v(x), v("bcA") if h is None else v("bcA", 8 * h, 8 * h + 8))
+    def select(out, a, cmp, other, k):
+        op("G", lambda e: e.affine_select(out[0], a[0], [[1, out[2]]], cmp, other, k, -1), [a], [out], 0.17 + 2 * CYC * out[2])
 
-    def line(dst, x, scale, bias):
-        act(dst, x, AF.Identity, scale, bias)
+    def bc(x, h=None):
+        return ind(v(x), v("bcA")) if h is None else ind(v(x, 8 * h, 8 * h + 8), v("bcA", 0, 8))
 
     def last(name, a0=0, a1=16):
         return v(name, a0 * 16 + 15, a1 * 16, 16)
 
-    def turn(dst, src, ident="IdH"):
+    def turn(dst, src):
         for h in range(2):
-            mm(v(dst[0], dst[1] + 128 * h, dst[1] + 128 * h + 128), v(src, 128 * h, 128 * h + 128), v(ident), True, True)
+            mm(v(dst[0], dst[1] + 128 * h, dst[1] + 128 * h + 128), v(src, 128 * h, 128 * h + 128), v("IdH"))
+
+    def bank(name, lo, hi, h=0):
+        return v("pb" + BANK[name][h], lo, hi)
 
     half = W // 2
     dma("Y", T.IV[:], T.vl[:], [], [v("IV")])
@@ -351,443 +462,506 @@ def rank_program(g, core, T, topo):
 
     iota(v("pcI"), [[0, 1]], 0, 1)
     iota(v("mm"), [[1, 128]], 0, 0)
-    iota(v("iw", 0, 16), [[1, 16]], 0, 0)
     iota(v("QC"), [[0, 16], [1, 16]], 0, 0)
     iota(v("mg"), [[1, 8], [0, 16]], 0, 0)
-    iota(v("iw", 16, 32), [[16, 16]], 15, 0)
     iota(v("TR"), [[256, 2], [0, 8]], W // 2, 2)
-    iota(v("OB"), [[0, 2], [256, 8]], 0, 0)
-    iota(v("s1"), [[32, 16]], W + 2048, 0)
+    iota(v("OB", 0, 8), [[256, 8]], GW + 16, 0)
+    iota(v("OB", 8, 24), [[1, 2], [256, 8]], 16, 0)
+    iota(v("t1"), [[32, 16]], W + 2048, 0)
     iota(v("f2", 0, 64), [[1, 8], [0, 8]], 0, 0)
     iota(v("X", W, XW), [[0, 2 * L]], 0, 0)
     iota(v("EQ"), [[0, 4096]], 0, 0)
     ts(v("pmI"), v("pcI"), 15, OP.bitwise_and)
     ts(v("p4I"), v("pcI"), 4, OP.arith_shift_right)
-    for a, b in (("pcF", "pcI"), ("pmF", "pmI"), ("p4F", "p4I")):
-        cp(v(a), v(b))
-    cp(v("bcA"), v("iw", 0, 16))
-    cp(v("bc15"), v("iw", 16, 32))
+    cp(v("COF", 0, 3), v("COI", 0, 3))
     cp(v("LV"), v("IV"))
     cp(v("LC"), v("IC"))
+    ts(v("TRm"), v("TR"), -8192.0, OP.add)
+    cp(v("bcA"), v("mm", 0, 16))
+    ts(v("e1"), v("pmF"), 15.0, OP.is_equal, 16.0, OP.mult)
+    ts(v("t3"), v("mm", 0, 16), v("e1"), OP.max)
+    cp(v("bcG"), v("t3"))
+    ts(v("bcZ"), v("mm", 0, 16), 2.0, OP.mult, 1.0, OP.add)
+    fill(v("PL2"), 0.0)
     ts(v("IdF"), v("mm"), v("pcF"), OP.is_equal)
-    for nm, c in (("Ident", 1.0), ("In1", -1.0), ("In2", -2.0), ("Ih", 0.5), ("Inh", -0.5), ("Ibig", BIG), ("Ibigh", BIG / 2),
-                  ("I094", 0.9375), ("IZb", KZ * 1024), ("IZv", KZ * 2048), ("I4k", 4096.0), ("In2k", -2048.0), ("In4k", -4096.0), ("I2k", 2048.0)):
+    for nm, c in (("Ident", 1.0), ("Ih", 0.5), ("Ibig", BIG), ("IZv", KZ * 2048), ("In4k", -4096.0)) + (("I8k", 8192.0), ("In8k", -8192.0)) * MAXES:
         line(v(nm), v("IdF"), c, 0.0)
     cp(v("IdH"), v("IdF"))
-    ts(v("Id4k"), v("IdF"), 4096.0, OP.mult)
     fill(v("ones"), 1.0)
     fill(v("onesF"), 1.0)
     fill(v("zero"), 0.0)
+    fill(v("MP"), 0.0)
+    fill(v("g2"), -192.0)
+    fill(v("grow", 16, 24), 0.5)
+    ts(v("low"), v("QC"), 0.0, OP.mult)
     for nm in ("GV0", "GV1", "DC0", "DC1"):
-        fill(v(nm, 2048, 2064), 0.0)
-    for nm in ("OHp", "posp", "mPp"):
-        fill(v(nm, 0, 16), 0.0)
-    for nm, k in (("upV", 0), ("upC", 0), ("dnV", 127), ("dnC", 127)):
+        fill(v(nm, 2048, GW), 0.0)
+    for nm, k in (("upV", 0), ("upC", 0), ("dnV", 127), ("dnC", 127), ("m3", 127)):
         ts(v(nm, k, 256, 128), v("QC", 0, 2), 0.0, OP.mult)
-    ts(v("m3", 255, 256), v("QC", 0, 1), 0.0, OP.mult)
     ts(v("DGf"), v("QC"), v("pmF"), OP.is_equal)
     act(v("DG"), v("DGf"))
     ts(v("RSf"), v("QC"), 0.0, OP.is_gt)
     act(v("RS"), v("RSf"))
-    line(v("RSm"), v("RSf"), 1048576.0, -4097.0)
-    line(v("RSk"), v("RSf"), BIG, 31.0)
-    line(v("i32s"), v("QC"), -32.0, 512.0)
-    ts(v("e1"), v("pmF"), 16.0, OP.mult, 16.0, OP.add)
-    ts(v("OB"), v("OB"), v("e1"), OP.add)
+    line(v("NR"), v("RSf"), -1.0, 1.0)
+    line(v("RSm", 0, 128), v("RSf", 0, 128), 1048576.0, -4097.0)
+    line(v("RSk", 0, 128), v("RSf", 0, 128), BIG, 31.0)
+    line(v("RSn", 0, 128), v("RSf", 0, 128), 1048576.0, -16384.0)
+    line(v("i32s", 0, 128), v("QC", 0, 128), -32.0, 512.0)
+    ts(v("eO"), v("pmF"), 16.0, OP.mult)
     ts(v("blk8F"), v("mm", 0, 8), v("p4F"), OP.is_equal)
     cp(v("blk8H"), v("blk8F"))
-    for nm, c in (("BKk", 2048.0), ("EEw", -4 * KZ), ("GVw", 2 * KZ), ("ABw", -2 * KZ)):
+    for nm, c in (("BKk", 2048.0), ("EEw", 4 * KZ), ("GVw", -2 * KZ), ("ABw", -2 * KZ)):
         line(v(nm), v("blk8F"), c, 0.0)
+    for k in range(3):
+        ts(v("BM32", 8 * k, 8 * k + 8), v("blk8F"), -1.0 / 32, OP.mult)
     for h in range(2):
-        line(v("BM32", 8 * h, 8 * h + 8), v("blk8F"), -1.0 / 32, 0.0)
-        fill(v("O1", 8 * h, 8 * h + 8), float(h))
-        tt(v("BMh", 8 * h, 8 * h + 8), v("s1", 8 * h, 8 * h + 8), v("blk8F"), OP.mult)
+        tt(v("BMh", 8 * h, 8 * h + 8), v("t1", 8 * h, 8 * h + 8), v("blk8F"), OP.mult)
     ts(v("blkw"), v("mg"), v("p4F"), OP.is_equal)
     for h in range(2):
-        ts(v("m2", 128 * h, 128 * h + 128), v("QC", 0, 128), 2.0 + NABS[h], OP.is_ge, KZ, OP.mult)
-        tt(v("Yw%d" % h), v("m2", 128 * h, 128 * h + 128), v("blkw"), OP.mult)
+        ts(v("n0", 128 * h, 128 * h + 128), v("QC", 0, 128), 2.0 + NABS[h], OP.is_ge, KZ, OP.mult)
+        tt(v("Yw%d" % h), v("n0", 128 * h, 128 * h + 128), v("blkw"), OP.mult)
+    ts(v("e2"), v("pmF"), 2.0, OP.not_equal)
+    ts(v("n1", 0, 128), v("QC", 0, 128), 2.0, OP.is_lt, v("e2"), OP.max)
+    tt(v("blkl"), v("n1", 0, 128), v("blkw"), OP.mult)
     cp(v("wF"), v("WI"))
     ts(v("W8"), v("blk8F"), v("wF"), OP.mult)
     ts(v("e1"), v("pcF"), 0.0, OP.is_equal)
     ts(v("e2"), v("pcF"), 1.0, OP.is_equal, -2 * BIG, OP.mult)
-    ts(v("CR"), v("i32s"), v("e1"), OP.mult, v("e2"), OP.add)
-    ts(v("f1"), v("QC"), 15.0, OP.is_equal, -15.0, OP.add)
-    tt(v("m7"), v("f1"), v("QC"), OP.add)
-    ts(v("CX"), v("m7"), v("e1"), OP.mult)
-    ts(v("e4"), v("e1"), 4096.0, OP.mult)
-    ts(v("C4"), v("RS"), 0.0, OP.mult, v("e4"), OP.add)
-    ts(v("e2"), v("pcF"), 1.0, OP.is_equal, -MID, OP.mult)
+    ts(v("CR"), v("i32s", 0, 128), v("e1"), OP.mult, v("e2"), OP.add)
+    ts(v("e2"), v("pcF"), 1.0, OP.is_equal, -2 * MID, OP.mult)
     ts(v("e3"), v("e1"), 2.0, OP.mult)
     ts(v("CQ"), v("QC", 0, 128), v("e3"), OP.mult, v("e2"), OP.add)
-    ts(v("e2"), v("e2"), -4096.0, OP.mult)
-    ts(v("e3"), v("e1"), 2048.0, OP.mult, v("e2"), OP.add)
-    ts(v("CV", 0, 128), v("QC", 0, 128), 0.0, OP.mult, v("e3"), OP.add)
+    ts(v("eH"), v("pmF"), 0.25, OP.mult, 191.875, OP.add)
+    ts(v("eL"), v("pmF"), 768.0 + 1 - 64, OP.add)
+    ts(v("e4"), v("e1"), 4096.0, OP.mult)
+    ts(v("C4"), v("QC"), 0.0, OP.mult, v("e4"), OP.add)
+    for k in (0, 1, 2, 3, 4, 8, 12):
+        select(v("Uh%d" % k), v("low", 0, 128), OP.not_equal, 1.0, k)
+        if k < 4:
+            select(v("Ub%d" % k), v("blkw"), OP.is_ge, 0.0, k)
+            select(v("Ub%d" % k), v("Ub%d" % k), OP.not_equal, -63.0, k)
+    for nm, c in (("In4", -4.0), ("I64", 64.0), ("I2k", MID), ("I4", 4.0), ("Ig", 16.5), ("I2", 2.0), ("In2", -2.0), ("In1", -1.0), ("Inh", -0.5)):
+        select(v(nm), v("zero"), OP.not_equal, c, 0)
+    select(v("InH"), v("low", 0, 128), OP.not_equal, -1.0, 0)
+    ts(v("eM"), v("pmF"), 1.0 - 64, OP.add)
     fill(v("f1", 0, 128), 0.5)
     fill(v("f1", 128, 256), 0.0)
     scan(v("PW2"), v("f1", 0, 128), v("f1", 128, 256), OP.mult, OP.add, 2.0 ** 61)
-    tt(v("m8", 0, 128), v("PW2"), v("IdF"), OP.mult)
-    total(v("wp"), v("m8", 0, 128))
-    ts(v("m7"), v("DGf"), v("wp"), OP.mult, 2.5, OP.mult)
-    line(v("m6"), v("DGf"), -2.0 ** 90, 2.0 ** 90)
-    tt(v("THR"), v("m7"), v("m6"), OP.add)
-    tt(v("m8", 128, 144), v("PW2", 0, 16), v("DGf", 0, 16), OP.mult)
-    total(v("wq"), v("m8", 128, 144))
+    tt(v("n4", 0, 128), v("PW2"), v("IdF"), OP.mult)
+    total(v("wp"), v("n4", 0, 128))
+    ts(v("n5"), v("DGf"), v("wp"), OP.mult, 2.5, OP.mult)
+    line(v("n3"), v("DGf"), -2.0 ** 90, 2.0 ** 90)
+    tt(v("THR"), v("n5"), v("n3"), OP.add)
+    tt(v("n4", 128, 144), v("PW2", 0, 16), v("DGf", 0, 16), OP.mult)
+    total(v("wq"), v("n4", 128, 144))
     ts(v("f2", 64, 128), v("f2", 0, 64), v("p4F"), OP.is_equal)
     for a in range(8):
         ts(v("BW", 64 * a, 64 * a + 64), v("f2", 64, 128), v("wq"), OP.mult, 2.0 ** (-16 * a), OP.mult)
     line(v("BW", 512, 576), v("f2", 64, 128), 2.0 ** 70, 0.0)
-
-    ts(v("i1"), v("IV"), -MID, OP.add)
-    ts(v("i2"), v("IC"), -MID, OP.add)
-    turn(("pb4", 0), "i1")
-    turn(("pb7", 0), "i2")
-    cp(v("V"), v("pb4", 0, 256))
-    cp(v("LNF", p=8), v("LNI", p=8))
-    cp(v("THF", 0, 1, p=8), v("THI", p=8))
-    ts(v("G8", p=8), v("mg", p=8), v("pcF", p=8), OP.is_equal)
-    for h in range(2):
-        mm(v("pb2", 8 * h, 8 * h + 8), v("LNF", 128 * h, 128 * h + 128, p=8), v("IdF", 0, 8, p=8), True, True)
-    cp(v("nn"), v("pb2", 0, 16))
-    tt(v("m4"), bc("nn"), v("QC"), OP.is_le)
-    line(v("m5"), v("m4"), 4096.0, -MID)
-    tt(v("Cd"), v("pb7", 0, 256), v("m5"), OP.max)
-    tt(v("s2"), v("V", 0, 256, 16), v("TR"), OP.subtract)
-    ts(v("s3"), v("nn"), 1.0, OP.min)
-    tt(v("V0"), v("s2"), v("s3"), OP.mult)
-    mm(v("pb3", 0, 1), v("G8", p=8), v("THF", 0, 1, p=8), True, True)
-    cp(v("tI"), v("pb3", 0, 1))
-    ts(v("tI"), v("tI"), 31, OP.bitwise_and)
-    ts(v("e1"), v("pmF"), 0.0, OP.is_equal, KZ, OP.mult)
-    ts(v("eK"), v("pmF"), 1.0, OP.is_equal, KZ, OP.mult)
-    tt(v("e2"), v("pb3", 0, 1), v("tI"), OP.subtract)
-    ts(v("e2"), v("e2"), -3072.0, OP.add, v("e1"), OP.mult)
-    ts(v("e3"), v("tI"), 0.5, OP.add, v("eK"), OP.mult)
-    tt(v("thm"), v("e2"), v("e3"), OP.add)
-    ts(v("LIM"), v("blkw"), v("thm"), OP.mult)
 
     def counts(h):
         lo, hi = 128 * h, 128 * h + 128
         ts(v("val", lo, hi), v("Cd", lo, hi), MID, OP.is_lt)
         scan(v("cum", lo, hi), v("RS", lo, hi), v("val", lo, hi), OP.mult, OP.add)
 
-    def dedupe(gap1, gap2, values):
-        (act if WZ[values != "Y"] == "S" else cp)(v("Wz"), bc("z"))
-        tt(v("Ez"), bc("z"), v("DGf"), OP.mult)
+    ts(v("tV"), v("IV"), -MID, OP.add)
+    ts(v("tC"), v("IC"), -MID, OP.add)
+    turn(("pb4", 0), "tV")
+    turn(("pb7", 0), "tC")
+    cp(v("V"), v("pb4", 0, 256))
+    cp(v("LNF", p=8), v("LNI", p=8))
+    cp(v("THF", 0, 1, p=8), v("THI", p=8))
+    ts(v("G8", p=8), v("mg", p=8), v("pcF", p=8), OP.is_equal)
+    for h in range(2):
+        mm(v("pb2", 8 * h, 8 * h + 8), v("LNF", 128 * h, 128 * h + 128, p=8), v("IdF", 0, 8, p=8))
+    cp(v("nn"), v("pb2", 0, 16))
+    tt(v("m4"), bc("nn"), v("QC"), OP.is_le)
+    line(v("m5"), v("m4"), 4096.0, -MID)
+    tt(v("Cd"), v("pb7", 0, 256), v("m5"), OP.max)
+    mm(v("pb5", 256, 512), v("IdH"), v("Cd"))
+    ts(v("s3"), v("nn"), 1.0, OP.min, -8192.0, OP.mult)
+    tt(v("s2"), v("s3"), v("TR"), OP.add)
+    tt(v("V0"), v("V", 0, 256, 16), v("s2"), OP.max)
+    mm(v("pb3", 0, 1), v("G8", p=8), v("THF", 0, 1, p=8))
+    cp(v("tI"), v("pb3", 0, 1))
+    ts(v("tI"), v("tI"), 31, OP.bitwise_and)
+    ts(v("e1"), v("pmF"), 0.0, OP.is_equal, KZ, OP.mult)
+    ts(v("eK"), v("pmF"), 1.0, OP.is_equal, KZ, OP.mult)
+    ts(v("e4"), v("pmF"), 2.0, OP.is_equal, -4096 * KZ, OP.mult)
+    tt(v("e2"), v("pb3", 0, 1), v("tI"), OP.subtract)
+    ts(v("e2"), v("e2"), -4096.0, OP.add, v("e1"), OP.mult)
+    ts(v("e3"), v("tI"), 0.5, OP.add, v("eK"), OP.mult)
+    ts(v("thm"), v("e2"), v("e3"), OP.add, v("e4"), OP.add)
+    ts(v("LIM"), v("blkl"), v("thm"), OP.mult)
+
+    def dedupe(gap1, gap2, values, who):
+        tt(v("Ez"), ind(v("zs"), v("bcZ")), v("DG"), OP.mult)
         for h in range(2):
-            mm(v("pb1", 8 * h, 8 * h + 8), v("Ez", 128 * h, 128 * h + 128), v("blk8H"), True, True)
-        turn(("pb0", 0), "Wz")
-        ts(v("zU"), v("pb1", 0, 16), MID, OP.add)
-        ts(v("Ru"), v("pb0", 0, 256), MID, OP.add)
+            mm(v("pb1", 8 * h, 8 * h + 8), v("Ez", 128 * h, 128 * h + 128), v("blk8H"))
+        move("z" + who, v("zz"), v("pb1", 0, 16))
+        if SPLIT:
+            for h in (1, 0):
+                lo, hi = 128 * h, 128 * h + 128
+                act(v("Wz", lo, hi), ind(v("zs"), v("bcZ", 8 * h, 8 * h + 8)))
+                mm(bank("Ru", lo, hi, h), v("Wz", lo, hi), v("IdH"))
+                move(who + str(h), v("Ru", lo, hi), bank("Ru", lo, hi, h))
+        else:
+            act(v("Wz"), ind(v("zs"), v("bcZ")))
+            turn(("pb0", 0), "Wz")
+            move(who + "0", v("Ru"), v("pb0", 0, 256))
         mm(v("pb3", 0, 16), v("CQ"), v("ones", 0, 16), True, False)
-        mm(v("pb2", 0, 128), v("Ident"), v("zero"), True, False)
         gap1()
-        for a in range(16):
-            ts(v("EQ", 272 * a, 256 * a + 256), v("Ru", 16 * a, 256), v("zU", a, a + 1), OP.is_equal)
+        for a in list(range(8, 16)) + list(range(8)):
+            ts(v("EQ", 272 * a, 256 * a + 256), v("Ru", 16 * a, 256), v("zz", a, a + 1), OP.is_equal)
             for h in range(a // 8, 2):
                 k = a % 8 if h == a // 8 else 8
-                mm(v("pb2", 64 * h, 64 * h + 64), v("EQ", 256 * a + 128 * h, 256 * a + 128 * h + 128), v("BW", 64 * k, 64 * k + 64), False, a == 15)
+                mm(v("pb2", 64 * h, 64 * h + 64), v("EQ", 256 * a + 128 * h, 256 * a + 128 * h + 128), v("BW", 64 * k, 64 * k + 64), a == 8, a + h == 8 and a == 7)
         gap2()
         for k in range(2):
-            tt(v("El", k, 256, 2), v("pb2", 0, 128), v("THR", k, 256, 2), OP.is_ge)
+            out = v("El", k, 256, 2)
+            tt((out[0], v("El", 128 * k, 128 * k + 128)[1]) + out[2:], v("pb2", 0, 128), v("THR", k, 256, 2), OP.is_ge)
         for h in range(2):
-            mm(v("pb3", 8 * h, 8 * h + 8), v("El", 128 * h, 128 * h + 128), v("BMh", 8 * h, 8 * h + 8), False, h == 1)
-        tt(v("oA"), v("pb3", 0, 16), v("zU"), OP.max)
-        cp(v("off16"), v("oA"))
-        cp(ind(v("X"), v("off16")), v(values))
+            el = v("El", 128 * h, 128 * h + 128)
+            mm(v("pb3", 8 * h, 8 * h + 8), (el[0], v("El")[1]) + el[2:], v("BMh", 8 * h, 8 * h + 8), False, h == 1)
+        tt(v("oA"), v("pb3", 0, 16), v("zz"), OP.max)
+        ts(v("off16"), v("oA"), MID, OP.add)
+        if len(values) == 1:
+            cp(ind(v("X"), v("off16")), v(values[0]))
+        else:
+            tt(ind(v("X"), v("off16")), v(values[0]), v(values[1]), OP.add)
 
-    def send(buf, dst_buf, dst_rank, lsem, asem, cost=2.0):
-        dst = T.cores[dst_rank]
+    def message(m, bufs, t, cost, after=()):
+        d = 1 + t % 3
+        dst, src = T.cores[(rank + d) % 4], T.cores[(rank - d) % 4]
         rid, pid, _se = topo.addr(dst)
-        n = len(topo.engines(core, dst))
+        land, asem, lsem = "r%s%d" % (m, t), "a%s%d" % (m, t), "l" + m
 
         def emit(rd, wr):
             wait("G", need("G", rd, wr))
-            g.remote_dma(T[dst_buf][:], T[buf][:], T.sem[asem], T.sem[lsem], pid, rid, topo.mask(core, dst))
-            record("Gr", bump("G", lsem, n), rd, wr)
-        return add("G", emit, [v(buf)], [], 1.0, cost)
+            if len(bufs) == 1:
+                g.remote_dma(T[land][:], T[bufs[0]][:], T.sem[asem], T.sem[lsem], pid, rid, topo.mask(core, dst))
+            else:
+                g.remote_dma_fused([RemoteDMATransfer(dst_ids=[DstId(rid=rid, pnc=pid)], dma_engine_mask=topo.mask(core, dst), remote_sem=T.sem[asem],
+                                                      srcs=[T[x][:] for x in bufs], dsts=[T[land][:]], alu_op=2)], local_sem=T.sem[lsem])
+            record("Gr", bump("G", lsem, len(topo.engines(core, dst))), rd, wr)
+        sent = add("G", emit, [v(x) for x in bufs], [], 1.0, cost)
+        OPS[sent][7] += after
 
-    def arrive(buf, asem, src_rank, sent):
-        n = len(topo.engines(T.cores[src_rank], core))
-
-        def emit(rd, wr):
+        def came(rd, wr):
+            n = len(topo.engines(src, core))
             count[asem] = n
             clock[(asem, n)] = {}
-            recs[buf] = [(0, 99999, (asem, n), "far", True)]
-        add("F", emit, [], [v(buf)], 0.0, 0.0, [sent])
+            recs[land] = [(0, 99999, (asem, n), "far", True)]
+        add("F", came, [], [v(land)], 0.0, 0.0, [sent])
+        return sent
 
     counts(0)
     counts(1)
     for t in range(ST):
-        d = 1 + t % 3
-        to, frm = (rank + d) % 4, (rank - d) % 4
-        rK, rC, rY, rB = "rK%d" % t, "rC%d" % t, "rY%d" % t, "rB%d" % t
+        rK, rY, rP, rB = "rK%d" % t, "rY%d" % t, "rP%d" % t, "rB%d" % t
         lastt = t == ST - 1
-        sent = {}
+        turns = [0]
 
         def bends(h):
             GV, DC, at = "GV%d" % h, "DC%d" % h, 0
-            for c, (who, n) in enumerate(RUNS[h]):
+            for who, how, n in RUNS[h]:
                 lo, hi, lst = 16 * at, 16 * (at + n), (128 * h + at, 128 * h + at + n)
                 src = ind(v("X", 0, W), v("LV", *lst))
                 if who == "S":
-                    line(v(GV, lo, hi), src, 0.5, 0.0)
+                    line(v(GV, lo, hi), src, -0.5, 0.0)
                 else:
-                    ts(v(GV, lo, hi), src, 0.5, OP.mult)
-                tt(v(DC, lo, hi), ind(v("X", 0, XW if t else W), v("LC", *lst)), v(GV, lo, hi), OP.subtract)
-                pb = "pb%d" % ((c + h * len(RUNS[0])) % 2)
-                for a in range(0, hi - lo, DWIDE):
-                    b = min(a + DWIDE, hi - lo - 1)
-                    mms(v(pb, a, b), [(v("In1"), v(GV, lo + a + 1, lo + b + 1)), (v("Ident"), v(DC, lo + a, lo + b))])
-                act(v("AB%d" % h, lo, hi - 1), v(pb, 0, hi - lo - 1), AF.Abs)
+                    ts(v(GV, lo, hi), src, -0.5, OP.mult)
                 at += n
+            at = 0
+            for who, how, n in RUNS[h]:
+                lo, hi, lst = 16 * at, 16 * (at + n), (128 * h + at, 128 * h + at + n)
+                tt(v(DC, lo, hi), ind(v("X", 0, XW if t else W), v("LC", *lst)), v(GV, lo, hi), OP.add)
+                ab = v("AB%d" % h, 14 * at, 14 * (at + n))
+                if AS == 16:
+                    ab = v("AB%d" % h, lo, hi - 1)
+                    if how == "V":
+                        tt(ab, v(DC, lo, hi - 1), v(GV, lo + 1, hi), OP.add)
+                        act(ab, ab, AF.Abs)
+                    elif how == "D":
+                        if at + n == NDMA[h] or (at + n) % DRUN == 0:
+                            lo = 16 * ((at + n - 1) // DRUN * DRUN)
+                            addto(v(DC, lo, hi - 1), v(GV, lo + 1, hi), "e%d%d" % (h, lo // 16 // DRUN))
+                            act(v("AB%d" % h, lo, hi - 1), v(DC, lo, hi - 1), AF.Abs)
+                    else:
+                        pb = v("pb" + DIFF[turns[0] % len(DIFF)], 0, hi - lo - 1)
+                        turns[0] += 1
+                        mms(pb, [(v("Ident"), v(GV, lo + 1, hi)), (v("Ident"), v(DC, lo, hi - 1))])
+                        act(ab, pb, AF.Abs)
+                elif how == "V":
+                    tt(v("DV", 0, hi - lo), v(DC, lo, hi), v(GV, lo + 1, hi + 1), OP.add)
+                    act(ab, v("DV", 0, hi - lo, -1), AF.Abs)
+                else:
+                    pb = "pb" + DIFF[turns[0] % len(DIFF)]
+                    turns[0] += 1
+                    mms(v(pb, 0, hi - lo), [(v("Ident"), v(GV, lo + 1, hi + 1)), (v("Ident"), v(DC, lo, hi))])
+                    act(ab, v(pb, 0, hi - lo, -1), AF.Abs)
+                at += n
+
+        def gates(h):
+            lo, hi, a, b = 128 * h, 128 * h + 128, 8 * h, 8 * h + 8
+            move("ng", v("ng", a, b), last("cum", a, b), 1.08, -2.29)
+            tt(v("sgp", lo, hi), bc("ng", h), v("cum", lo, hi), OP.is_ge)
 
         def key(h):
             lo, hi = 128 * h, 128 * h + 128
             pb = "pb%d" % (2 + h)
             k = v(pb, 0, 128)
-            mm(k, v("ones"), v("CR", 0, 128), True, False)
-            mm(k, v("Ident"), v("cum", lo, hi), False, False)
+            mm(k, v("ones"), v("CR"), True, False)
             mm(k, v("Ibig"), v("val", lo, hi), False, False)
             mm(k, v("Ibig"), v("sgp", lo, hi), False, False)
-            for s in range(14):
-                mm(v(pb, s, 128, 16), v("AB%d" % h, s, 2048, 16), v("BKk"), False, s == 13)
-
-        def gates(h):
-            lo, hi = 128 * h, 128 * h + 128
-            a, b = 8 * h, 8 * h + 8
-            ts(v("ng", a, b), last("cum", a, b), 1.08, OP.mult, -2.29, OP.add)
-            tt(v("sgp", lo, hi), bc("ng", h), v("cum", lo, hi), OP.is_ge)
-
-        def spare(_c):
-            act(v("nw"), ind(v("cum"), v("bc15")))
-            mms(v("pb7", 256, 512), [(v("I094"), v("nw")), (v("In1"), v("cum")), (v("ones"), v("CX"))])
-            act(v("sgx"), v("pb7", 256, 512), AF.Sign, 1.0, 0.97)
-            act(v("stx"), v("sgx"), AF.Relu)
+            for p0, p1 in KEYS[h]:
+                for s in range(14):
+                    mm(v(pb, s, 128, 16, (p0, p1)), v("AB%d" % h, AS * p0 + s, AS * p1, AS), v("BKk"), False, s == 13 and p1 == 128)
 
         def pick(h):
             lo, hi, a, b = 128 * h, 128 * h + 128, 8 * h, 8 * h + 8
-            pb, GV, DC = "pb%d" % (2 + h), "GV%d" % h, "DC%d" % h
-            k = v(pb, 0, 128)
-            scan(v("SK", lo, hi), v("RSk", 0, 128), k, OP.min, OP.max, 31.0)
+            pb, lst, abc = "pb%d" % (2 + h), "olist%d" % h, "pabc%d" % h
+            scan(v("SK", lo, hi), v("RSk", 0, 128), v(pb, 0, 128), OP.min, OP.max, 31.0)
             ts(v("KA", a, b), last("SK", a, b), 992, OP.bitwise_and)
             tt(v("El", lo, hi), bc("KA", h), v("DG", lo, hi), OP.mult)
-            o, lst = v(pb, 128, 144), "o16%d" % h
-            mms(o, [(v("Ident"), v("OB")), (v("Ident"), v("O1")), (v("El", lo, hi), v("BM32"))])
-            cp(v(lst), o)
-            for who, dst, src, at in zip(WHO_Y[3 * h:], ("pa", "pb", "pc"), (DC, GV, GV), (0, 0, 8)):
-                (cp if who == "V" else act)(v(dst, lo, hi), ind(v(src), v(lst, at, at + 8)))
+            o = v(pb, 128, 152)
+            mms(o, [(v("IdH"), v("OB")), (v("El", lo, hi), v("BM32"))])
+            ts(v(lst), o, v("eO"), OP.add)
+            for who, c0, c1 in YGATHER[h]:
+                (cp if who == "V" else act)(v(abc, 128 * c0, 128 * c1), ind(v("GD%d" % h), v(lst, 8 * c0, 8 * c1)))
             y = v(pb, 256, 384)
-            mms(y, [(v("Inh"), v("pa", lo, hi)), (v("Ih"), v("pb", lo, hi)), (v("Ident"), v("pc", lo, hi))])
+            mm(y, v("Ih"), v(abc, 0, 128), True, False)
+            nd = NDMA[h]
+            if nd:
+                mm(v(pb, 256, 256 + nd), v("Ih"), v(abc, 256, 256 + nd), False, False)
+            if nd < 128:
+                mm(v(pb, 256 + nd, 384), v("Ident"), v(abc, 256 + nd, 384), False, False)
+            mm(y, v("Ih"), v(abc, 128, 256), False, True)
             yh = v("pb4", 256 + lo, 256 + hi)
-            ts(yh, y, 0.0, OP.max, 31.5, OP.min)
-            ts(v("Y", lo, hi), yh, 2.0, OP.mult)
-            ts(v("KB", a, b), last("SK", a, b), 31, OP.bitwise_and)
-            act(v("kpw", lo, hi), bc("KB", h))
-            p = v("pb7", lo, hi)
-            mms(p, [(v("Ident"), v("cum", lo, hi)), (v("In1"), v("kpw", lo, hi))])
-            act(v("sgB", lo, hi), p, AF.Sign, 1.0, -1.5)
-            line(p, p, -4096.0, 69632.0 + MID)
-            tt(v("PW", lo, hi), p, v("V", lo, hi), OP.add)
-            mm(v("pb6", 256 + a, 256 + b), v("Y", lo, hi), v("W8"), True, True)
-            tt(v("OH", lo, hi), bc("KA", h), v("i32s", lo, hi), OP.is_equal)
-            tt(v("m2", lo, hi), v("OH", lo, hi), v("pb4", lo, hi), OP.mult)
-            tt(v("m3", lo, hi - h), v("OH", lo, hi - h), v("pb4", lo + 1, hi + 1 - h), OP.mult)
-            scan(v("m4", lo, hi), v("RSf", lo, hi), v("m2", lo, hi), OP.mult, OP.add)
-            scan(v("m5", lo, hi), v("RSf", lo, hi), v("m3", lo, hi), OP.mult, OP.add)
+            ts(yh, y, 0.0, OP.min, -31.5, OP.max)
+            ts(v("Y", lo, hi), yh, -2.0, OP.mult)
+            mm(bank("u", 256 + a, 256 + b), v("Y", lo, hi), v("W8"))
+            tt(v("OH", lo, hi), bc("KA", h), v("i32s", 0, 128), OP.is_equal)
+            scan(v("sk", lo, hi), v("RS", lo, hi), v("OH", lo - 1, hi - 1), OP.mult, OP.add)
+            scan(v("dd", lo, hi), v("val", lo, hi), v("sk", lo, hi), OP.add, OP.mult)
+            scan(v("ee", lo, hi), v("val", lo, hi), v("sk", lo, hi), OP.max, OP.min)
+            p = bank("PW", lo, hi, h)
+            mms(p, [(v("IdH"), v("V", lo, hi)), (v("In4k"), v("dd", lo, hi))])
+            line(v("PW", lo, hi), p, 1.0, 69632.0 + MID)
+            if MAXES:
+                p1, p2 = bank("P1", 256 + lo, 256 + hi, h), bank("P2", lo, hi, h)
+                mms(p1, [(v("IdH"), v("V", lo, hi)), (v("I8k"), v("OH", lo, hi))])
+                scan(v("m4", lo, hi), v("RSm", 0, 128), p1, OP.min, OP.max, -4097.0)
+                mms(p2, [(v("IdH"), v("VK", lo + 1, hi + 1)), (v("I8k"), v("OH", lo, hi))])
+                line(v("m3", lo, hi), p2, 1.0, -8192.0)
+                scan(v("m5", lo, hi), v("RSn", 0, 128), v("m3", lo, hi), OP.min, OP.max, -16384.0)
+            else:
+                tt(v("m2", lo, hi), v("OH", lo, hi), v("pb4", lo, hi), OP.mult)
+                tt(v("m3", lo, hi - 1), v("OH", lo, hi - 1), v("pb4", lo + 1, hi), OP.mult)
+                scan(v("m4", lo, hi), v("RSf", lo, hi), v("m2", lo, hi), OP.mult, OP.add)
+                scan(v("m5", lo, hi), v("RSf", lo, hi), v("m3", lo, hi), OP.mult, OP.add)
 
         def near(h):
             lo, hi = 128 * h, 128 * h + 128
-            pb, GV, EE = "pb" + ZBANK[h], "GV%d" % h, "EE%d" % h
+            pb, GV, EE = "pb" + BANK["z"][h], "GV%d" % h, "EE%d" % h
             z = v(pb, 384, 512)
             mm(z, v("ones"), v("LIM"), True, False)
             mm(z, v("IZv"), v("val", lo, hi), False, False)
             first = 2 + NABS[h]
             for s in range(first, 16):
                 mm(v(pb, 384 + s, 512, 16), v(GV, s, 2048, 16), v("GVw"), False, False)
-            mm(z, v("Y", lo, hi), v("Yw%d" % h), False, False)
-            mm(z, v("IZb"), v("sgB", lo, hi), False, False)
-            for s in range(2 + h * NABS[1], 16):
-                tt(v(EE, 128 * s - 256, 128 * s - 128), v(GV, s, 2048, 16), v("pb4", 256 + lo, 256 + hi), OP.subtract if s < first else OP.max)
-            if h == 0:
-                for s0 in range(2, first, NRUN):
-                    e = v(EE, 128 * s0 - 256, 128 * min(s0 + NRUN, first) - 256)
-                    act(e, e, AF.Abs)
-            elif first > 2:
-                for s in range(2, first):
-                    mms(v("pb2", 128 * s - 256, 128 * s - 128), [(v("Ident"), v(GV, s, 2048, 16)), (v("Inh"), v("Y", lo, hi))])
-                act(v(EE, 0, 128 * first - 256), v("pb2", 0, 128 * first - 256), AF.Abs)
-            for s in (range(2, 16) if h == 0 else list(range(first, 15)) + list(range(2, first)) + [15]):
+            if first < 16:
+                mm(z, v("Y", lo, hi), v("Yw%d" % h), False, False)
+            mm(z, v("IZv"), v("ee", lo - 1, hi - 1), False, False)
+            nt = 2 + (NT if h == 0 else 0)
+            for s0 in range(2, nt, 4):
+                s1 = min(s0 + 4, nt)
+                for s in range(s0, s1):
+                    mms(bank("ET", 128 * (s - s0), 128 * (s - s0 + 1), (s0 // 4) % len(BANK["ET"])), [(v("Ident"), v(GV, s, 2048, 16)), (v("Ih"), v("Y", lo, hi))])
+                act(v(EE, 128 * s0 - 256, 128 * s1 - 256), bank("ET", 0, 128 * (s1 - s0), (s0 // 4) % len(BANK["ET"])), AF.Abs)
+            for s in range(nt, 16):
+                tt(v(EE, 128 * s - 256, 128 * s - 128), v(GV, s, 2048, 16), v("pb4", 256 + lo, 256 + hi), OP.subtract if s < first else OP.min)
+            for s0 in range(nt, first, NRUN):
+                e = v(EE, 128 * s0 - 256, 128 * min(s0 + NRUN, first) - 256)
+                act(e, e, AF.Abs)
+            for s in range(2, 16):
                 mm(v(pb, 384 + s, 512, 16), v(EE, 128 * s - 256, 128 * s - 128), v("ABw" if s < first else "EEw"), False, s == 15)
             tt(v("m1", lo, hi), z, v("PW", lo, hi), OP.min)
-            scan(v("SM", lo, hi), v("RSm", lo, hi), v("m1", lo, hi), OP.min, OP.max, -4097.0)
+            scan(v("SM", lo, hi), v("RSm", 0, 128), v("m1", lo, hi), OP.min, OP.max, -4097.0)
 
-        ts(v("live"), last("cum"), 4.0, OP.is_ge)
-        sent["K"] = send("VK", rK, to, "lK", "aK%d" % t, 5.0)
-        ts(v("lv"), v("live"), -100.0, OP.mult, 16.0, OP.add)
-        tt(v("th2"), v("lv"), last("cum"), OP.subtract)
-        ts(v("s6"), v("live"), -8192.0, OP.mult)
-        tt(v("s1"), v("s6"), v("TR"), OP.add)
-        for part, h in ((bends, 0), (gates, 0), (key, 0), (pick, 0), (bends, 1), (gates, 1), (spare, 0), (near, 0), (key, 1), (pick, 1)):
-            part(h)
-        cp(v("SB", 16, 32), last("m5"))
-        ts(v("K37"), last("m4"), 37.0, OP.mult, 37.0 * MID, OP.add)
-        cp(v("UI"), v("pb6", 256, 272))
+        ts(v("s6"), last("cum"), 4.0, OP.is_lt, -8192.0, OP.mult)
+        tt(v("s1"), v("TRm"), v("s6"), OP.subtract)
+        message("K", ["VK"], t, 5.0)
+        ts(v("s7"), last("cum"), 4.0, OP.is_lt, 16.0, OP.mult)
+        tt(v("th2"), v("s7"), last("cum"), OP.subtract)
+        scan(v("av"), v("NR"), v("val"), OP.max, OP.min)
+        for part in PARTS.split():
+            {"b": bends, "g": gates, "k": key, "p": pick, "n": near}[part[0]](int(part[1]))
+        move("SB", v("SB", 16, 32), last("m5"))
+        move("Kp", v("Kp"), last("m4"), 1184.0, -1184.0 * (MID + 8192 * MAXES))
+        move("UI", v("UI"), bank("u", 256, 272))
         ts(v("UI"), v("UI"), 4095, OP.bitwise_and)
-        tt(v("HI"), v("UI"), v("UI"), OP.mult)
-        ts(v("HI"), v("HI"), 5, OP.arith_shift_right)
-        tt(v("HI"), v("HI"), v("K37"), OP.add)
-        ts(v("HI"), v("HI"), 4095, OP.bitwise_and)
-        ts(v("x"), v("HI"), -MID, OP.add)
+        if WHO["sq"] == "V":
+            tt(v("sq"), v("UI"), v("UI"), OP.mult)
+        else:
+            act(v("sq"), v("UI"), AF.Square)
+        tt(v("HI"), v("sq"), v("Kp"), OP.add)
+        ts(v("HI"), v("HI"), 5, OP.arith_shift_right, 4095, OP.bitwise_and)
+        move("x", v("x"), v("HI"), 1.0, -MID)
         tt(v("hh"), v("x"), v("s1"), OP.max)
-        act(v("kw"), ind(v("m4"), v("bc15")))
-        scan(v("sk"), v("RS"), v("OHp", 15, 271), OP.mult, OP.add)
-        line(v("pb6", 0, 256), v("OH"), -1.0, 1.0)
-        tt(v("i1"), v("pb6", 0, 256), v("Cd"), OP.mult)
-        mms(v("pb5", 0, 256), [(v("IdH"), v("m3")), (v("IdH"), v("i1"))])
-        mms(v("pb7", 256, 512), [(v("In1"), v("stx")), (v("Ident"), v("sk"))])
-        near(1)
+        if MAXES:
+            mms(v("pb5", 0, 256), [(v("IdH"), v("Cd")), (v("In8k"), v("OH"))])
+            tt(v("pb5", 0, 256), v("pb5", 0, 256), v("m3"), OP.max)
+        else:
+            tt(v("i1"), v("OH"), v("pb5", 256, 512), OP.mult)
+            mms(v("pb5", 0, 256), [(v("IdH"), v("Cd")), (v("IdH"), v("m3")), (v("InH"), v("i1"))])
+        near(1 - int(PARTS[PARTS.index("n") + 1]))
         ts(v("SB", 0, 16), last("SM"), 12, OP.logical_shift_right)
-        sent["B"] = send("SB", rB, to, "lB", "aB%d" % t, FAR)
+        short = message("B", ["SB"], t, FAR)
         tt(v("kn"), last("SM"), v("TR"), OP.min)
-        tt(v("z"), v("kn"), v("hh"), OP.max)
-        ts(v("nc"), last("SM"), 0.0, OP.is_lt)
-        tt(v("grow"), v("live"), v("nc"), OP.mult)
-        for m, b in (("K", rK), ("B", rB)):
-            arrive(b, "a%s%d" % (m, t), frm, sent[m])
-        rVn = v(rB, 16, 32)
+        tt(v("zs", 1, 32, 2), v("kn"), v("hh"), OP.max)
+        tt(v("grow", 0, 16), last("SM"), v("s6"), OP.is_lt)
+        F = bank("F", 256, 512)
 
         def gap1():
-            act(v("gw"), bc("grow"))
+            act(v("gw"), ind(v("grow"), v("bcG")))
             act(v("sgm"), v("SM"), AF.Sign, 1.0, 0.5)
-            if WHO_O == "T":
-                mms(v("pb6", 256, 512), [(v("ones"), v("C4")), (v("In4k"), v("sk")), (v("I2k"), v("sgm"))])
-                tt(v("Cp"), v("pb6", 256, 512), v("Cd"), OP.max)
-            tt(v("Ag"), v("pb7", 256, 512), v("gw"), OP.mult)
-            mms(v("pb6", 0, 256), [(v("I4k"), v("sk")), (v("In2k"), v("sgm")), (v("In4k"), v("gw"))])
-            mms(v("pb7", 0, 256), [(v("In2"), v("OH")), (v("In1"), v("Ag"))])
-            act(v("pos"), v("pb7", 0, 256), AF.Relu, -1.0, -1.0)
-            act(v("neg"), v("pb7", 0, 256), AF.Relu)
-            if WHO_O == "S":
-                line(v("pb6", 256, 512), v("pb6", 0, 256), -1.0, 4096.0)
-            line(v("a1"), v("pb6", 0, 256), 1.0, -4096.0)
-            if WHO_O == "S":
-                tt(v("Cp"), v("pb6", 256, 512), v("Cd"), OP.max)
-            sent["C"] = send("YC", "rP%d" % t, to, "lC", "aC%d" % t, FAR + 1.5)
-            OPS[-1][7].append(sent["B"])
-            arrive("rP%d" % t, "aC%d" % t, frm, sent["C"])
-            mms(v("pb7", 256, 512), [(v("Ident"), v("OH")), (v("Ident"), v("posp", 15, 271)), (v("In1"), v("pos"))])
+            c = 1.0
+            pm = bank("pm", 256, 512)
+            if WHO["Cp"] == "S":
+                mms(pm, [(v("Ident"), v("sk")), (v("Inh"), v("sgm"))])
+                line(v("NF"), pm, -4096.0, MID + MID * c)
+                message("C", ["YC", "YN"], t, FAR + 3.5, [short])
+            else:
+                mms(pm, [(v("ones"), v("C4")), (v("In4k"), v("sk")), (v("I2k"), v("sgm"))])
+                tt(v("Cp"), pm, v("Cd"), OP.max)
+                message("C", ["YC"], t, FAR + 1.5, [short])
+            Z = bank("Z", 0, 256)
+            mms(Z, [(v("In1"), v("av")), (v("In2"), v("sk")), (v("I4"), v("OH")), (v("I2"), v("sgm")), (v("Ig"), v("gw"))])
+            act(v("Zs"), Z, AF.Abs, 1.0, 2.0 * c - 9.125)
+            ts(v("FF"), v("Zs"), 11.0, OP.is_ge)
+            ts(v("Fu"), v("Zs"), 10.375, OP.is_equal)
+            mms(F, [(v("Ident"), v("FF")), (v("Ident"), v("Fu", -1, 255))])
+            ts(v("mP"), v("Zs"), 4.375, OP.is_equal)
+            ts(v("Dn"), v("Zs"), 7.375, OP.is_equal)
             ts(v("VM"), last("SM"), 4095, OP.bitwise_and)
-            ts(v("s5"), v("VM"), -MID, OP.add)
-            tt(v("s2"), v("s5"), v("z"), OP.min)
+            move("s5", v("s5"), v("VM"), 1.0, -MID)
+            tt(v("s2"), v("s5"), v("zs", 1, 32, 2), OP.min)
             act(v("xw"), bc("s2"))
-            ts(v("mP"), v("Ag"), 0.0, OP.max)
-            tt(v("s7"), v("V0"), v(rK, 256, 272), OP.mult)
-            tt(v("z0"), v("s7"), v("TR"), OP.add)
-            tt(v("dz"), rVn, v("z0"), OP.subtract)
-
-        def moved(h):
-            lo, hi = 128 * h, 128 * h + 128
-            for b, x in (("pb4", "V"), ("pb5", "C")):
-                tt(v("up" + x, lo + 1, hi), v("mP", lo, hi - 1), v(b, lo, hi - 1), OP.mult)
-                tt(v("dn" + x, lo, hi - 1), v("neg", lo, hi - 1), v(b, lo + 1, hi), OP.mult)
-
-        def taken(h):
-            lo, hi = 128 * h, 128 * h + 128
-            b = "pb6"
-            for old, x, came in (("pb4", "V", rK), ("pb5", "C", rC)):
-                tt(v("kp" + x, lo, hi), v("keep", lo, hi), v(old, lo, hi), OP.mult)
-                tt(v("in" + x, lo, hi), v("pb7", lo, hi), v(came, lo, hi), OP.mult)
-            parts = ("up", "dn", "fx", "kp", "in")
-            mms(v("pb4", lo, hi), [(v("IdH"), v(p + "V", lo, hi)) for p in parts])
-            act(v("V", lo, hi), v("pb4", lo, hi))
-            if not lastt:
-                mm(v(b, 0, 128), v("V", lo, hi), v("IdH"), True, True)
-                ts(v("LV", lo, hi), v(b, 0, 128), MID, OP.add)
-            mms(v("pb5", 256 + lo, 256 + hi), [(v("IdH"), v(p + "C", lo, hi)) for p in parts])
-            tt(v("Cd", lo, hi), v("pb5", 256 + lo, 256 + hi), v("a1", lo, hi), OP.max)
-            if not lastt:
-                mm(v(b, 128, 256), v("Cd", lo, hi), v("IdH"), True, True)
-                ts(v("LC", lo, hi), v(b, 128, 256), MID, OP.add)
-            counts(h)
+            if MAXES:
+                move("kc", v("kc"), v("kn"), 1.0, 8192.0)
+                tt(v("kc"), last("m4"), v("kc"), OP.max)
+                line(v("kw"), bc("kc"), 1.0, -8192.0)
+            else:
+                tt(v("kc"), last("m4"), v("kn"), OP.max)
+                act(v("kw"), bc("kc"))
+            tt(v("dz", 1, 32, 2), v("V0"), v(rK, 256, 272), OP.max)
+            tt(v("dz", 0, 32, 2), v(rB, 16, 32), v("dz", 1, 32, 2), OP.subtract)
 
         def gap2():
-            tt(v("fxV"), v("pb7", 256, 512), v("xw"), OP.mult)
-            tt(v("fxC"), v("pb7", 256, 512), v("kw"), OP.mult)
-            moved(0)
-            moved(1)
+            tt(v("fxV"), F, v("xw"), OP.mult)
+            tt(v("fxC"), F, v("kw"), OP.mult)
+            for h in range(2):
+                lo, hi = 128 * h, 128 * h + 128
+                for b, x in (("pb4", "V"), ("pb5", "C")):
+                    tt(v("up" + x, lo + 1, hi), v("mP", lo, hi - 1), v(b, lo, hi - 1), OP.mult)
+                    tt(v("dn" + x, lo, hi - 1), v("Dn", lo, hi - 1), v(b, lo + 1, hi), OP.mult)
             if not lastt:
-                act(v("s4"), v("nc"), AF.Identity, -1.0, 1.0, total=v("cs1"))
-                mm(v("pb6", 0, 1), v("onesF"), v("cs1"), True, True)
-                cp(v("cI"), v("pb6", 0, 1))
+                act(v("s4"), last("SM"), AF.Sign, 1.0, 0.5, total=v("cs1"))
+                mm(bank("c", 0, 1), v("onesF"), v("cs1"))
+                move("cI", v("cI"), bank("c", 0, 1), 0.5, 1024.0)
                 ts(v("cI"), v("cI"), 31, OP.bitwise_and)
                 line(v("lim"), v("cI"), v("eK"), v("thm"))
-                line(v("LIM"), v("blkw"), v("lim"), 0.0)
+                line(v("LIM"), v("blkl"), v("lim"), 0.0)
 
-        dedupe(gap1, gap2, "Y")
-        tt(v("take"), v(rB, 0, 16), v("th2"), OP.is_lt)
-        tt(v("s3"), v("take"), v("dz"), OP.mult)
-        tt(v("z"), v("s3"), v("z0"), OP.add)
+        dedupe(gap1, gap2, ("Y",) if YS == 1 else ("Yb", "Yb"), "Ru1")
+        tt(v("take", 1, 32, 2), v(rB, 0, 16), v("th2"), OP.is_lt)
+        scan(v("zs"), v("take"), v("dz"), OP.mult, OP.add)
+        if not lastt:
+            tt(v("s3"), v("zs", 1, 32, 2), v("dz", 1, 32, 2), OP.subtract)
+            tt(v("V0"), v("V0"), v("s3"), OP.add)
+        tw = bank("tw", 0, 256)
 
         def gap3():
-            cp(v("z16"), v("zU"))
-            act(v("tw"), bc("take"))
-            if WHO_T == "S":
-                act(v("pb7", 0, 256), v("tw"))
+            move("z16", v("z16"), v("zz"), 1.0, MID)
+            act(v("tw"), ind(v("take"), v("bcZ")))
+            if WHO["tw"] == "S":
+                act(tw, v("tw"))
             else:
-                mm(v("pb7", 0, 256), v("Ident"), v("tw"), True, True)
-            mms(v("pb6", 256, 512), [(v("In2"), v("posp", 15, 271)), (v("In2"), v("mPp", 15, 271)), (v("Ident"), v("Ag")), (v("In2"), v("tw"))])
-            act(v("keep"), v("pb6", 256, 512), AF.Relu, 1.0, 1.0)
-            if WHO_B == "S":
+                mm(tw, v("Ident"), v("tw"))
+            keep = bank("keep", 256, 512)
+            mms(keep, [(v("In1"), v(x, -k, 256 - k)) for x, k in (("FF", 0), ("Fu", 1), ("mP", 1), ("Dn", 0), ("tw", 0))])
+            line(v("keep"), keep, 1.0, 1.0)
+            if WHO["blend"] == "S":
                 act(v("BL"), ind(v("X"), v("z16")))
-                mms(v("pb1", 256, 512), [(v("Ident"), v(rY)), (v("Ident"), v("BL"))])
-                ts(v("iw"), v("pb1", 256, 512), 0.5, OP.mult, -0.25, OP.add)
+                mms(bank("bl", 256, 512), [(v("IdH" if YS == 1 else "I2H"), v(rY)), (v("Ident"), v("BL"))])
+                if WHO["round"] == "V":
+                    ts(v("iw"), bank("bl", 256, 512), 0.5, OP.mult, -0.25, OP.add)
+                else:
+                    line(v("g1"), bank("bl", 256, 512), 0.5, 191.75)
             else:
                 tt(v("BL"), ind(v("X"), v("z16")), v(rY), OP.add)
                 ts(v("iw"), v("BL"), 0.5, OP.mult, -0.25, OP.add)
 
+        def taken(h):
+            lo, hi = 128 * h, 128 * h + 128
+            for old, x, came in (("pb4", "V", rK), ("pb5", "C", rP)):
+                tt(v("kp" + x, lo, hi), v("keep", lo, hi), v(old, lo, hi), OP.mult)
+                tt(v("in" + x, lo, hi), bank("tw", lo, hi), v(came, lo, hi), OP.mult)
+            for k, (x, name, new) in enumerate((("V", "V", v("pb4", lo, hi)), ("C", "Cd", v("pb5", 256 + lo, 256 + hi)))):
+                mms(new, [(v("IdH"), v(p + x, lo, hi)) for p in ("up", "dn", "fx", "kp", "in")])
+                move(name, v(name, lo, hi), new)
+                if not lastt:
+                    b = bank("list", 128 * k, 128 * k + 128, k)
+                    mm(b, v(name, lo, hi), v("IdH"))
+                    move("L%s%d" % (x, h), v("L" + x, lo, hi), b, 1.0, MID)
+            counts(h)
+
         def gap4():
             taken(0)
             taken(1)
-            if not lastt:
-                tt(v("V0"), v("V0"), v("s3"), OP.add)
 
-        dedupe(gap3, gap4, "iw")
+        dedupe(gap3, gap4, ("g1", "g2") if WHO["blend"] + WHO["round"] == "SS" else ("iw",), "Ru2")
         if lastt:
             dma("Y", T.yx[:, 0:half], T.X[:, 0:half], [v("X", 0, half)], [], 5.0)
             dma("S", T.yx[:, half:W], T.X[:, half:W], [v("X", half, W)], [], 5.0)
 
     for h in range(2):
-        mm(v("pb1", 128 * h, 128 * h + 128, p=8), last("cum", 8 * h, 8 * h + 8), v("Ident"), True, True)
+        mm(v("pb1", 128 * h, 128 * h + 128, p=8), last("cum", 8 * h, 8 * h + 8), v("Ident"))
     act(v("LNF", p=8), v("pb1", 0, 256, p=8))
-    dma("Y", T.yn[:], T.LNF[0:8, :], [v("LNF")], [])
-    VC = v("pb4", 0, 256)
-    for h in range(2):
-        lo, hi = 128 * h, 128 * h + 128
-        mms(v("pb4", lo, hi), [(v("V", lo, hi), v("Id4k")), (v("Cd", lo, hi), v("IdH")), (v("ones"), v("CV", 0, 128))])
-        mms(v("pb6", lo, hi), [(v("cum", lo, hi), v("Ident")), (v("val", lo, hi), v("Ibigh"))])
-    line(v("cumI"), v("pb6", 0, 256), 1.0, -BIG / 2)
-    for p in range(16):
-        b, pr = v(("g1", "g2", "g3")[p % 3]), "m" + "012456"[p % 6]
-        if p >= 16 - SMASK:
-            b, a = v(("pa", "pb", "pc", "keep", "neg", "tw")[p % 6]), v(("a2", "a3")[p % 2])
-            act(a, v("cumI"), AF.Abs, 1.0, -1.0 - p)
-            act(b, a, AF.Relu, -1.0, 1.0)
-        else:
-            ts(b, v("cumI"), float(p + 1), OP.is_equal)
-        tt(v(pr), b, VC, OP.mult)
-        for h in range(2):
-            mm(v("pb7", 128 * h + p, 128 * h + 128, 16), v(pr, 128 * h, 128 * h + 128), v("blk8F"), True, True)
-    for h in range(2):
-        lo, hi = 128 * h, 128 * h + 128
-        cp(v("SO", lo, hi), v("pb7", lo, hi))
-    for h in range(2):
-        lo, hi = 128 * h, 128 * h + 128
-        mm(v("pb%d" % (2 + h), 0, 128), v("SO", lo, hi), v("IdF"), True, True)
-        cp(v("SK", lo, hi), v("pb%d" % (2 + h), 0, 128))
-        ts(v("IV", lo, hi), v("SK", lo, hi), 12, OP.arith_shift_right)
-        ts(v("IC", lo, hi), v("SK", lo, hi), 4095, OP.bitwise_and)
-        cp(v("f1", lo, hi), v("IV", lo, hi))
-        cp(v("f2", lo, hi), v("IC", lo, hi))
+    dma("Y", T.yn[:], v("LNF", p=8)[0], [v("LNF")], [])
+    halves = [(128 * h, 128 * h + 128) for h in range(2)]
+    for lo, hi in halves:
+        mm(v("pb6", lo, hi), v("cum", lo, hi), v("In1"))
+    line(v("g1"), v("pb6", 0, 256), 0.25, v("eH"))
+    for lo, hi in halves:
+        mm(v("pb6", 256 + lo, 256 + hi), v("cum", lo, hi), v("In1"), lo == 0, False)
+        mm(v("pb6", 256 + lo, 256 + hi), v("val", lo, hi), v("I64"), False, False)
+    mm(v("pb6", 256, 512), v("In4"), v("g1"), False, True)
+    line(v("g2"), v("pb6", 256, 512), 1.0, v("eL"))
+    turn(("pb7", 0), "V")
+    turn(("pb7", 256), "Cd")
+    cp(v("nn"), last("cum"))
+    tt(v("gw"), bc("nn"), v("QC"), OP.is_gt)
+    masks = ("sgm", "keep", "Dn", "FF")
+    for b in range(4):
+        ts(v(masks[b]), v("g2"), float(b), OP.is_equal)
+        mm(v("pb1", 0, 256), v("Ub%d" % b), v(masks[b]), b == 0, b == 3)
+        for old, part, new in ((("pb7", 0, 256), ("upV", "dnV", "fxV", "kpV"), "pb4"), (("pb7", 256, 512), ("upC", "dnC", "fxC", "kpC"), "pb5")):
+            tt(v(part[b]), v(masks[b]), v(*old), OP.mult)
+            mm(v(new, 0, 256), v("Uh%d" % b), v(part[b]), b == 0, b == 3)
+    line(v("g3"), v("pb1", 0, 256), -1.0, v("eM"))
+    for new in ("pb7", "pb6"):
+        for lo, hi in halves:
+            mm(v(new, lo, hi), v("gw", lo, hi), v("I2k"), lo == 0, False)
+    masks = ("El", "Zs", "av", "sk")
+    for a in range(4):
+        ts(v(masks[a]), v("g3"), 4.0 * a, OP.is_equal)
+        for old, part, new in (("pb4", ("inV", "i1", "Wz", "tV"), "pb7"), ("pb5", ("inC", "m3", "Ez", "tC"), "pb6")):
+            tt(v(part[a]), v(masks[a]), v(old, 0, 256), OP.mult)
+            mm(v(new, 0, 256), v("Uh%d" % (4 * a)), v(part[a]), False, a == 3)
+    act(v("f1"), v("pb7", 0, 256))
+    cp(v("f2"), v("pb6", 0, 256))
     dma("Y", T.yv[:], v("f1")[0], [v("f1")], [])
     dma("S", T.yc[:], v("f2")[0], [v("f2")], [])
     if "order" not in PLAN:

@@ -5,35 +5,43 @@ from concourse.mybir import AluOpType, AxisListType, ActivationFunctionType
 OP = AluOpType
 AF = ActivationFunctionType
 W, L, S, ST = 4096, 256, 16, 5
-BIG, KZ, MID = 4194304.0, 262144.0, 2048.0
+BIG, KZ, MID, ZU = 4194304.0, 262144.0, 2048.0, 3072.0
 F32, BF, I32, U16, F16 = "float32", "bfloat16", "int32", "uint16", "float16"
 
-RUNS = ((("S", "V", 16), ("V", "T", 16), ("S", "T", 32), ("S", "T", 32), ("S", "T", 32)), (("S", "T", 32), ("V", "T", 32), ("S", "T", 32), ("S", "T", 16), ("S", "T", 16)))
-KEYS = (((0, 128),), ((0, 128),))
-DIFF = "01"
+RUNS = ((("S", "V", 16), ("V", "T", 16), ("S", "T", 32), ("S", "T", 32), ("S", "T", 32)), (("S", "T", 32), ("S", "T", 32), ("S", "T", 32), ("S", "V", 16), ("S", "T", 16)))
+KEYS = (((0, 128),), ((0, 96), (96, 128)))
+DIFF = "017"
 AS = 14
 DRUN = 64
 NDMA = [sum(n for _w, how, n in r if how == "D") for r in RUNS]
 GDMA, ADMA, BDMA = 1.0, 2.0, 0.002
-PARTS = "b0 g0 k0 p0 b1 g1 n0 k1 p1"
+PARTS = "b0 b1 g0 g1 k0 p0 k1 n0 p1"
 YGATHER = ((("S", 0, 3),), (("S", 0, 3),))
 SPLIT = 1
-MAXES = 0
+MAXES = 1
 NT = 0
-WHO = {"kc": "S", "SB": "V", "ng": "V", "cI": "V", "Ru10": "S", "Ru11": "S", "Ru20": "S", "Ru21": "S", "blend": "V", "sq": "V", "tw": "T", "V": "S", "Cd": "V", "Kp": "V", "H": "V", "Cp": "V", "round": "V", "zRu1": "V", "zRu2": "S", "x": "V", "s5": "V", "LV0": "V", "LV1": "V", "LC0": "V", "LC1": "V", "UI": "V", "z16": "V"}
+KEEPF = 0
+TW = 256 * KEEPF
+WHO = {"half": "V", "kc": "S", "SB": "V", "ng": "V", "cI": "S", "Ru10": "S", "Ru11": "S", "Ru20": "S", "Ru21": "S", "blend": "V", "sq": "S", "tw": "T", "V": "S", "Cd": "V", "Kp": "S", "H": "V", "Cp": "V", "round": "V", "zRu1": "V", "zRu2": "S", "x": "S", "s5": "S", "LV0": "V", "LV1": "V", "LC0": "V", "LC1": "V", "UI": "S", "z16": "S"}
 YS = 1
-NABS = (10, 0)
+NABS = (14, 0)
 NRUN = 7
-BANK = {"z": "10", "PW": "77", "u": "6", "Z": "6", "F": "7", "pm": "6", "keep": "6", "tw": "7", "list": "66", "c": "6", "bl": "1", "Ru": "10", "P1": "77", "P2": "66", "ET": "6"}
+BANK = {"z": "10", "PW": "77", "u": "6", "Z": "6", "F": "7", "pm": "6", "keep": "6", "tw": "7", "list": "66", "c": "6", "bl": "1", "Ru": "10", "zU": "3", "P1": "23", "P2": "23", "ET": "6"}
 CYC, GATHER, SCATTER, WAKE, SLACK = 0.00083, 1.4, 3.4, 0.19, 0.02
 TFIX = 0.006
 RULES = [(0.0, 0.3, 0.3), (0.03, 0.5, 0.5)]
 PASSES = 4
 LONG = 2
-SHAKES = 400
+SEED = 1
+SWAPS = 4000
+HEAT = 0.03
+SHAKES = 300
 SHAKE = 0.3
 SHARE = 0.2
-FAR = 3.0
+ISSUE = 0.8
+LOAD = 4.2
+SMALL = 1.8
+FAR = 2.2
 PLAN = {}
 XW = W + 2 * L
 GW = 2064
@@ -68,11 +76,11 @@ for _t in range(ST):
     _pack("rC%d" % _t, "rY%d rP%d" % (_t, _t), 256, F16)
     _add("rB%d" % _t, 32, I32)
 _add("SB", 32, I32)
-_pack("MH", "Wz Ez Ru i1 m3 upV upC dnV dnC fxV fxC kpV kpC inV inC tV tC", 256, F16)
+_pack("MH", "Wz Ez Ru i1 m3 upV upC dnV dnC fxV fxC kpV kpC inV inC tV tC" + " m2 m4 m5" * (1 - MAXES), 256, F16)
 _pack("MI", "IdH InH Uh0 Uh1 Uh2 Uh3 Uh4 Uh8 Uh12", 128, F16)
 _add("blk8H", 8, F16)
 _pack("MP", "OH ee mP Fu", 256, BF, 16)
-_pack("MF", "PW m1 m2 m4 m5 xw kw SO n0 n1 n2 n3 n4 n5 RSf RSm RSk RSn DGf THR i32s QC f1 f2 LNF", 256, F32)
+_pack("MF", "m2 m4 m5 " * MAXES + "PW m1 xw kw n0 n1 n2 n3 n4 n5 RSf RSm RSk RSn DGf THR i32s QC f1 f2 LNF", 256, F32)
 _pack("MQ", "mg mm onesF IdF PW2 G8", 128, F32)
 _pack("MB", "val cum av sgp sk dd sgm gw tw keep Dn FF Zs El cumI RS NR DG g1 g2 g3 BL C4", 256, BF)
 _add("pabc0 pabc1", 384, BF)
@@ -89,7 +97,7 @@ _pack("PLB", "BM32 BMh", 24, BF)
 _pack("COF", "pcF pmF p4F thm lim cs1 e1 e2 e3 e4 eK eO eH eL eM wF wq wp", 1, F32)
 _pack("COI", "pcI pmI p4I cI tI", 1, I32)
 _add("WI THI", 1, I32)
-_pack("IDS", "Ident In1 In2 I2 I4 Ig Ih Inh Ibig IZv In4k In4 I64 I2k I8k In8k ones Yw0 Yw1 LIM blkw blkl CQ CR zero Ub0 Ub1 Ub2 Ub3", 128, BF)
+_pack("IDS", "Ident In1 Za Zk Zo Zg Ih Ibig IZv In4k In4 I64 I2k I8k In8k ones Yw0 Yw1 LIM blkw blkl CQ CR zero Ub0 Ub1 Ub2 Ub3", 128, BF)
 _pack("N8", "BKk EEw GVw ABw W8", 8, BF)
 _add("BW", 576, BF)
 _add("blk8F THF", 8, F32)
@@ -199,7 +207,7 @@ def rank_program(g, core, T, topo):
             record(q, bump(q, sem, 1), rd, wr)
         return add(q, emit, reads, writes, cost)
 
-    def dma(q, out, in_, reads=(), writes=(), lat=2.2):
+    def dma(q, out, in_, reads=(), writes=(), lat=SMALL):
         sem = "d%d" % ndma[0]
         ndma[0] += 1
 
@@ -341,7 +349,7 @@ def rank_program(g, core, T, topo):
                     PLAN["rule"] = (beta, look, urge)
                 late, _seq = place([-start[i] - cost[i] for i in range(n)], bwd, fwd, lat, look, urge)
                 key = [-late[i] - cost[i] for i in range(n)]
-        rng = np.random.default_rng(1)
+        rng = np.random.default_rng(SEED)
         look, urge = PLAN["rule"][1:]
         PLAN["tools"] = (place, fwd, bwd, none, lat, best)
         kinds = {}
@@ -357,8 +365,74 @@ def rank_program(g, core, T, topo):
             end = max(start[i] + cost[i] + lat[i] for i in range(n))
             if end < best[0]:
                 best = (end, seq, start)
-        PLAN["end"] = best[0]
-        return best[1]
+        qs = [o[0] for o in OPS]
+        opens = [o[8] and any(o[8]) and (o[8][0], o[8][1], banks[i][0]) for i, o in enumerate(OPS)]
+
+        def replay(seq):
+            start, why, free, held, busy, end, at = [0.0] * n, [-1] * n, {}, {}, set(), 0.0, -1
+            for i in seq:
+                q = qs[i]
+                st, y = free.get(q, (0.0, -1))
+                for j, w in fwd[i]:
+                    if start[j] + w > st:
+                        st, y = start[j] + w, j
+                for b in banks[i]:
+                    h = held.get(b)
+                    if h and h[0] != q and h[1] > st:
+                        st, y = h[1], h[2]
+                if opens[i]:
+                    a, z, b = opens[i]
+                    if a and b in busy:
+                        return None
+                    if a and not z:
+                        busy.add(b)
+                    elif z:
+                        busy.discard(b)
+                start[i], why[i] = st, y
+                st += cost[i]
+                free[q] = (st, i)
+                for b in banks[i]:
+                    held[b] = (q, st + WAKE, i)
+                if st + lat[i] > end:
+                    end, at = st + lat[i], i
+            return end, why, at
+        seq = list(best[1])
+        end, why, at = replay(seq)
+        top = (end, seq)
+        for k in range(SWAPS):
+            if k % 8 == 0 or changed:
+                pos = {i: s for s, i in enumerate(seq)}
+                path, i = [], at
+                while why[i] >= 0:
+                    if why[i] not in deps[i]:
+                        path.append((why[i], i))
+                    i = why[i]
+            changed = False
+            j, i = path[int(rng.integers(len(path)))]
+            a, b = pos[j], pos[i]
+            if rng.random() < 0.5:
+                take, rest = {i}, []
+                for x in reversed(seq[a:b]):
+                    if any(x in deps[y] for y in take):
+                        take.add(x)
+                if j in take:
+                    continue
+            else:
+                drop = {j}
+                for x in seq[a + 1:b + 1]:
+                    if any(y in deps[x] for y in drop):
+                        drop.add(x)
+                if i in drop:
+                    continue
+                take = set(seq[a:b + 1]) - drop
+            new = seq[:a] + [x for x in seq[a:b + 1] if x in take] + [x for x in seq[a:b + 1] if x not in take] + seq[b + 1:]
+            r = replay(new)
+            if r and r[0] <= end + HEAT * (1 - k / SWAPS) * rng.random():
+                seq, (end, why, at), changed = new, r, True
+                if end < top[0]:
+                    top = (end, seq)
+        PLAN["end"] = top[0]
+        return top[1]
 
     def vcost(out, a, b=None):
         views = [x for x in (out, a, b) if x is not None]
@@ -411,16 +485,16 @@ def rank_program(g, core, T, topo):
         else:
             line(out, a, scale, bias)
 
-    def mm(out, l, r, start=True, stop=True):
+    def mm(out, l, r, start=True, stop=True, pause=False):
         c = TFIX + max(min(64, l[2]), r[2]) * CYC * (4 if SCRATCH[r[1][0][0]][2] == F32 else 1)
-        OPS[op("T", lambda e: e.matmul(out[0], l[0], r[0], start, stop), [l, r], [out], c)][8] = (start, stop)
+        OPS[op("T", lambda e: e.matmul(out[0], l[0], r[0], start, stop or pause), [l, r], [out], c)][8] = (start, stop)
 
     def mms(out, terms):
         for k, (l, r) in enumerate(terms):
             mm(out, l, r, k == 0, k == len(terms) - 1)
 
     def scan(out, d0, d1, o0, o1, init=0.0):
-        small = all(SCRATCH[x[1][0][0]][2] == BF for x in (out, d0, d1))
+        small = all(SCRATCH[x[1][0][0]][2] in (BF, F16) for x in (out, d0, d1))
         op("V", lambda e: e.tensor_tensor_scan(out[0], d0[0], d1[0], init, o0, o1), [d0, d1], [out], max(64, out[2] * (0.5 if small else 1)) * CYC)
 
     def total(out, a):
@@ -454,8 +528,8 @@ def rank_program(g, core, T, topo):
     half = W // 2
     dma("Y", T.IV[:], T.vl[:], [], [v("IV")])
     dma("S", T.IC[:], T.cl[:], [], [v("IC")])
-    dma("Y", T.X[:, 0:half], T.xc[:, 0:half], [], [v("X", 0, half)], 5.0)
-    dma("S", T.X[:, half:W], T.xc[:, half:W], [], [v("X", half, W)], 5.0)
+    dma("Y", T.X[:, 0:half], T.xc[:, 0:half], [], [v("X", 0, half)], LOAD)
+    dma("S", T.X[:, half:W], T.xc[:, half:W], [], [v("X", half, W)], LOAD)
     dma("Y", T.LNI[0:8, :], T.ln[:], [], [v("LNI")])
     dma("S", T.WI[:], T.wt[:], [], [v("WI")])
     dma("Y", T.THI[0:8, :], T.th[:], [], [v("THI")])
@@ -533,14 +607,12 @@ def rank_program(g, core, T, topo):
     ts(v("CQ"), v("QC", 0, 128), v("e3"), OP.mult, v("e2"), OP.add)
     ts(v("eH"), v("pmF"), 0.25, OP.mult, 191.875, OP.add)
     ts(v("eL"), v("pmF"), 768.0 + 1 - 64, OP.add)
-    ts(v("e4"), v("e1"), 4096.0, OP.mult)
-    ts(v("C4"), v("QC"), 0.0, OP.mult, v("e4"), OP.add)
     for k in (0, 1, 2, 3, 4, 8, 12):
         select(v("Uh%d" % k), v("low", 0, 128), OP.not_equal, 1.0, k)
         if k < 4:
             select(v("Ub%d" % k), v("blkw"), OP.is_ge, 0.0, k)
             select(v("Ub%d" % k), v("Ub%d" % k), OP.not_equal, -63.0, k)
-    for nm, c in (("In4", -4.0), ("I64", 64.0), ("I2k", MID), ("I4", 4.0), ("Ig", 16.5), ("I2", 2.0), ("In2", -2.0), ("In1", -1.0), ("Inh", -0.5)):
+    for nm, c in (("In4", -4.0), ("I64", 64.0), ("I2k", MID), ("Za", -ZU / 4), ("Zk", -2 * ZU), ("Zo", ZU), ("Zg", 16 * ZU), ("In1", -1.0)):
         select(v(nm), v("zero"), OP.not_equal, c, 0)
     select(v("InH"), v("low", 0, 128), OP.not_equal, -1.0, 0)
     ts(v("eM"), v("pmF"), 1.0 - 64, OP.add)
@@ -578,7 +650,8 @@ def rank_program(g, core, T, topo):
     tt(v("m4"), bc("nn"), v("QC"), OP.is_le)
     line(v("m5"), v("m4"), 4096.0, -MID)
     tt(v("Cd"), v("pb7", 0, 256), v("m5"), OP.max)
-    mm(v("pb5", 256, 512), v("IdH"), v("Cd"))
+    if not MAXES:
+        mm(v("pb5", 256, 512), v("IdH"), v("Cd"))
     ts(v("s3"), v("nn"), 1.0, OP.min, -8192.0, OP.mult)
     tt(v("s2"), v("s3"), v("TR"), OP.add)
     tt(v("V0"), v("V", 0, 256, 16), v("s2"), OP.max)
@@ -597,8 +670,8 @@ def rank_program(g, core, T, topo):
     def dedupe(gap1, gap2, values, who):
         tt(v("Ez"), ind(v("zs"), v("bcZ")), v("DG"), OP.mult)
         for h in range(2):
-            mm(v("pb1", 8 * h, 8 * h + 8), v("Ez", 128 * h, 128 * h + 128), v("blk8H"))
-        move("z" + who, v("zz"), v("pb1", 0, 16))
+            mm(bank("zU", 496 + 8 * h, 504 + 8 * h), v("Ez", 128 * h, 128 * h + 128), v("blk8H"))
+        move("z" + who, v("zz"), bank("zU", 496, 512))
         if SPLIT:
             for h in (1, 0):
                 lo, hi = 128 * h, 128 * h + 128
@@ -609,7 +682,6 @@ def rank_program(g, core, T, topo):
             act(v("Wz"), ind(v("zs"), v("bcZ")))
             turn(("pb0", 0), "Wz")
             move(who + "0", v("Ru"), v("pb0", 0, 256))
-        mm(v("pb3", 0, 16), v("CQ"), v("ones", 0, 16), True, False)
         gap1()
         for a in list(range(8, 16)) + list(range(8)):
             ts(v("EQ", 272 * a, 256 * a + 256), v("Ru", 16 * a, 256), v("zz", a, a + 1), OP.is_equal)
@@ -620,6 +692,7 @@ def rank_program(g, core, T, topo):
         for k in range(2):
             out = v("El", k, 256, 2)
             tt((out[0], v("El", 128 * k, 128 * k + 128)[1]) + out[2:], v("pb2", 0, 128), v("THR", k, 256, 2), OP.is_ge)
+        mm(v("pb3", 0, 16), v("CQ"), v("ones", 0, 16), True, False)
         for h in range(2):
             el = v("El", 128 * h, 128 * h + 128)
             mm(v("pb3", 8 * h, 8 * h + 8), (el[0], v("El")[1]) + el[2:], v("BMh", 8 * h, 8 * h + 8), False, h == 1)
@@ -644,7 +717,7 @@ def rank_program(g, core, T, topo):
                 g.remote_dma_fused([RemoteDMATransfer(dst_ids=[DstId(rid=rid, pnc=pid)], dma_engine_mask=topo.mask(core, dst), remote_sem=T.sem[asem],
                                                       srcs=[T[x][:] for x in bufs], dsts=[T[land][:]], alu_op=2)], local_sem=T.sem[lsem])
             record("Gr", bump("G", lsem, len(topo.engines(core, dst))), rd, wr)
-        sent = add("G", emit, [v(x) for x in bufs], [], 1.0, cost)
+        sent = add("G", emit, [v(x) for x in bufs], [], ISSUE, cost)
         OPS[sent][7] += after
 
         def came(rd, wr):
@@ -713,10 +786,14 @@ def rank_program(g, core, T, topo):
             k = v(pb, 0, 128)
             mm(k, v("ones"), v("CR"), True, False)
             mm(k, v("Ibig"), v("val", lo, hi), False, False)
-            mm(k, v("Ibig"), v("sgp", lo, hi), False, False)
+            whole = len(KEYS[h]) == 1
+            if whole:
+                mm(k, v("Ibig"), v("sgp", lo, hi), False, False)
             for p0, p1 in KEYS[h]:
                 for s in range(14):
-                    mm(v(pb, s, 128, 16, (p0, p1)), v("AB%d" % h, AS * p0 + s, AS * p1, AS), v("BKk"), False, s == 13 and p1 == 128)
+                    mm(v(pb, s, 128, 16, (p0, p1)), v("AB%d" % h, AS * p0 + s, AS * p1, AS), v("BKk"), False, s == 13 and whole)
+            if not whole:
+                mm(k, v("Ibig"), v("sgp", lo, hi), False, True)
 
         def pick(h):
             lo, hi, a, b = 128 * h, 128 * h + 128, 8 * h, 8 * h + 8
@@ -758,8 +835,8 @@ def rank_program(g, core, T, topo):
             else:
                 tt(v("m2", lo, hi), v("OH", lo, hi), v("pb4", lo, hi), OP.mult)
                 tt(v("m3", lo, hi - 1), v("OH", lo, hi - 1), v("pb4", lo + 1, hi), OP.mult)
-                scan(v("m4", lo, hi), v("RSf", lo, hi), v("m2", lo, hi), OP.mult, OP.add)
-                scan(v("m5", lo, hi), v("RSf", lo, hi), v("m3", lo, hi), OP.mult, OP.add)
+                scan(v("m4", lo, hi), v("RS", lo, hi), v("m2", lo, hi), OP.mult, OP.add)
+                scan(v("m5", lo, hi), v("RS", lo, hi), v("m3", lo, hi), OP.mult, OP.add)
 
         def near(h):
             lo, hi = 128 * h, 128 * h + 128
@@ -791,7 +868,7 @@ def rank_program(g, core, T, topo):
 
         ts(v("s6"), last("cum"), 4.0, OP.is_lt, -8192.0, OP.mult)
         tt(v("s1"), v("TRm"), v("s6"), OP.subtract)
-        message("K", ["VK"], t, 5.0)
+        message("K", ["VK"], t, FAR + 2.0)
         ts(v("s7"), last("cum"), 4.0, OP.is_lt, 16.0, OP.mult)
         tt(v("th2"), v("s7"), last("cum"), OP.subtract)
         scan(v("av"), v("NR"), v("val"), OP.max, OP.min)
@@ -824,26 +901,19 @@ def rank_program(g, core, T, topo):
         F = bank("F", 256, 512)
 
         def gap1():
-            act(v("gw"), ind(v("grow"), v("bcG")))
+            line(v("gw"), ind(v("grow"), v("bcG")), 1.0, 0.125)
             act(v("sgm"), v("SM"), AF.Sign, 1.0, 0.5)
-            c = 1.0
-            pm = bank("pm", 256, 512)
-            if WHO["Cp"] == "S":
-                mms(pm, [(v("Ident"), v("sk")), (v("Inh"), v("sgm"))])
-                line(v("NF"), pm, -4096.0, MID + MID * c)
-                message("C", ["YC", "YN"], t, FAR + 3.5, [short])
-            else:
-                mms(pm, [(v("ones"), v("C4")), (v("In4k"), v("sk")), (v("I2k"), v("sgm"))])
-                tt(v("Cp"), pm, v("Cd"), OP.max)
-                message("C", ["YC"], t, FAR + 1.5, [short])
             Z = bank("Z", 0, 256)
-            mms(Z, [(v("In1"), v("av")), (v("In2"), v("sk")), (v("I4"), v("OH")), (v("I2"), v("sgm")), (v("Ig"), v("gw"))])
-            act(v("Zs"), Z, AF.Abs, 1.0, 2.0 * c - 9.125)
-            ts(v("FF"), v("Zs"), 11.0, OP.is_ge)
-            ts(v("Fu"), v("Zs"), 10.375, OP.is_equal)
-            mms(F, [(v("Ident"), v("FF")), (v("Ident"), v("Fu", -1, 255))])
-            ts(v("mP"), v("Zs"), 4.375, OP.is_equal)
-            ts(v("Dn"), v("Zs"), 7.375, OP.is_equal)
+            mms(Z, [(v("Za"), v("av")), (v("Zk"), v("sk")), (v("Zo"), v("OH")), (v("Zo"), v("sgm")), (v("Zg"), v("gw"))])
+            tt(v("Cp"), Z, v("Cd"), OP.max)
+            message("C", ["YC"], t, FAR + 1.5, [short])
+            act(v("Zs"), Z, AF.Abs, 1.0 / ZU, -8.625)
+            ts(v("FF"), v("Zs"), 9.25, OP.is_ge)
+            ts(v("Fu"), v("Zs"), 9.125, OP.is_equal)
+            mm(F, v("Ident"), v("FF"), True, False)
+            mm(F, v("Ident"), v("Fu", -1, 255), False, not KEEPF, True)
+            ts(v("mP"), v("Zs"), 6.125, OP.is_equal)
+            ts(v("Dn"), v("Zs"), 8.375, OP.is_equal)
             ts(v("VM"), last("SM"), 4095, OP.bitwise_and)
             move("s5", v("s5"), v("VM"), 1.0, -MID)
             tt(v("s2"), v("s5"), v("zs", 1, 32, 2), OP.min)
@@ -880,7 +950,7 @@ def rank_program(g, core, T, topo):
         if not lastt:
             tt(v("s3"), v("zs", 1, 32, 2), v("dz", 1, 32, 2), OP.subtract)
             tt(v("V0"), v("V0"), v("s3"), OP.add)
-        tw = bank("tw", 0, 256)
+        tw = bank("tw", TW, TW + 256)
 
         def gap3():
             move("z16", v("z16"), v("zz"), 1.0, MID)
@@ -889,9 +959,14 @@ def rank_program(g, core, T, topo):
                 act(tw, v("tw"))
             else:
                 mm(tw, v("Ident"), v("tw"))
-            keep = bank("keep", 256, 512)
-            mms(keep, [(v("In1"), v(x, -k, 256 - k)) for x, k in (("FF", 0), ("Fu", 1), ("mP", 1), ("Dn", 0), ("tw", 0))])
-            line(v("keep"), keep, 1.0, 1.0)
+            if KEEPF:
+                for x, k in (("mP", 1), ("Dn", 0), ("tw", 0)):
+                    mm(F, v("Ident"), v(x, -k, 256 - k), False, x == "tw")
+                line(v("keep"), F, -1.0, 1.0)
+            else:
+                keep = bank("keep", 256, 512)
+                mms(keep, [(v("In1"), v(x, -k, 256 - k)) for x, k in (("FF", 0), ("Fu", 1), ("mP", 1), ("Dn", 0), ("tw", 0))])
+                line(v("keep"), keep, 1.0, 1.0)
             if WHO["blend"] == "S":
                 act(v("BL"), ind(v("X"), v("z16")))
                 mms(bank("bl", 256, 512), [(v("IdH" if YS == 1 else "I2H"), v(rY)), (v("Ident"), v("BL"))])
@@ -901,30 +976,30 @@ def rank_program(g, core, T, topo):
                     line(v("g1"), bank("bl", 256, 512), 0.5, 191.75)
             else:
                 tt(v("BL"), ind(v("X"), v("z16")), v(rY), OP.add)
-                ts(v("iw"), v("BL"), 0.5, OP.mult, -0.25, OP.add)
+                move("half", v("g1"), v("BL"), 0.5, 191.75)
 
         def taken(h):
             lo, hi = 128 * h, 128 * h + 128
             for old, x, came in (("pb4", "V", rK), ("pb5", "C", rP)):
                 tt(v("kp" + x, lo, hi), v("keep", lo, hi), v(old, lo, hi), OP.mult)
-                tt(v("in" + x, lo, hi), bank("tw", lo, hi), v(came, lo, hi), OP.mult)
+                tt(v("in" + x, lo, hi), bank("tw", TW + lo, TW + hi), v(came, lo, hi), OP.mult)
             for k, (x, name, new) in enumerate((("V", "V", v("pb4", lo, hi)), ("C", "Cd", v("pb5", 256 + lo, 256 + hi)))):
                 mms(new, [(v("IdH"), v(p + x, lo, hi)) for p in ("up", "dn", "fx", "kp", "in")])
                 move(name, v(name, lo, hi), new)
                 if not lastt:
                     b = bank("list", 128 * k, 128 * k + 128, k)
                     mm(b, v(name, lo, hi), v("IdH"))
-                    move("L%s%d" % (x, h), v("L" + x, lo, hi), b, 1.0, MID)
+                    ts(v("L" + x, lo, hi), b, MID, OP.add, float(W), OP.min)
             counts(h)
 
         def gap4():
             taken(0)
             taken(1)
 
-        dedupe(gap3, gap4, ("g1", "g2") if WHO["blend"] + WHO["round"] == "SS" else ("iw",), "Ru2")
+        dedupe(gap3, gap4, ("iw",) if WHO["blend"] + WHO["round"] == "SV" else ("g1", "g2"), "Ru2")
         if lastt:
-            dma("Y", T.yx[:, 0:half], T.X[:, 0:half], [v("X", 0, half)], [], 5.0)
-            dma("S", T.yx[:, half:W], T.X[:, half:W], [v("X", half, W)], [], 5.0)
+            dma("Y", T.yx[:, 0:half], T.X[:, 0:half], [v("X", 0, half)], [], LOAD)
+            dma("S", T.yx[:, half:W], T.X[:, half:W], [v("X", half, W)], [], LOAD)
 
     for h in range(2):
         mm(v("pb1", 128 * h, 128 * h + 128, p=8), last("cum", 8 * h, 8 * h + 8), v("Ident"))

@@ -1,5 +1,4 @@
 import numpy as np
-from concourse.bass import DstId, RemoteDMATransfer
 from concourse.mybir import AluOpType, AxisListType, ActivationFunctionType
 
 OP = AluOpType
@@ -8,43 +7,45 @@ W, L, S, ST = 4096, 256, 16, 5
 BIG, KZ, MID, ZU = 4194304.0, 262144.0, 2048.0, 3072.0
 F32, BF, I32, U16, F16 = "float32", "bfloat16", "int32", "uint16", "float16"
 
-RUNS = ((("S", "V", 16), ("V", "T", 16), ("S", "T", 32), ("S", "T", 32), ("S", "T", 32)), (("S", "T", 32), ("S", "T", 32), ("S", "T", 32), ("S", "V", 16), ("S", "T", 16)))
-KEYS = (((0, 128),), ((0, 96), (96, 128)))
-DIFF = "017"
-AS = 14
-DRUN = 64
-NDMA = [sum(n for _w, how, n in r if how == "D") for r in RUNS]
-GDMA, ADMA, BDMA = 1.0, 2.0, 0.002
-PARTS = "b0 b1 g0 g1 k0 p0 k1 n0 p1"
+RUNS = "SVM32 SVM64 SVM32|VVM16 SVM48 SVM64"
+SLOTS = ("A4 R5 R5", "T4 T4 A6")
+DIFF = "07"
+PARTS = "b1 b0 g1 k1 p1 h1 g0 k0 n1 p0 y2 c1 h0 d1 z1 f1 n0 w1 c0 t1 d0 e1 z0 m2 s1 r1 w0 f0 t0 q0 e0 l2 s0 r0 x1 x0"
+APART = ("Ru1", "Ru2")
 YGATHER = ((("S", 0, 3),), (("S", 0, 3),))
-SPLIT = 1
-MAXES = 1
-NT = 0
-KEEPF = 0
-TW = 256 * KEEPF
-WHO = {"half": "V", "kc": "S", "SB": "V", "ng": "V", "cI": "S", "Ru10": "S", "Ru11": "S", "Ru20": "S", "Ru21": "S", "blend": "V", "sq": "S", "tw": "T", "V": "S", "Cd": "V", "Kp": "S", "H": "V", "Cp": "V", "round": "V", "zRu1": "V", "zRu2": "S", "x": "S", "s5": "S", "LV0": "V", "LV1": "V", "LC0": "V", "LC1": "V", "UI": "S", "z16": "S"}
-YS = 1
-NABS = (14, 0)
-NRUN = 7
-BANK = {"z": "10", "PW": "77", "u": "6", "Z": "6", "F": "7", "pm": "6", "keep": "6", "tw": "7", "list": "66", "c": "6", "bl": "1", "Ru": "10", "zU": "3", "P1": "23", "P2": "23", "ET": "6"}
-CYC, GATHER, SCATTER, WAKE, SLACK = 0.00083, 1.4, 3.4, 0.19, 0.02
+WHO = {"Y": "SS", "SB": "VV", "sgm": "SS", "off1": "SS", "off2": "SS", "cI": "SS", "Ru1": "SS", "Ru2": "SS", "blend": "SS", "sq": "SS", "V": "SS", "Cd": "SS", "Kp": "SS", "zz1": "SS", "zz2": "SS", "x": "SS", "s5": "SS", "LV": "SS", "UI": "SS", "z16": "SS", "PW": "SS", "keep": "SS", "xw": "VS", "gw": "VS", "tw": "VS", "Fc": "SS"}
+QUICK = (1, 1)
+NABS = (0, 7)
+NRUN = (4, 4)
+BANK = {"key": "23", "z": "16", "PW": "23", "u": "23", "Z": "16", "F": "54", "keep": "16", "tw": "54", "list": "16", "c": "77", "old": "54", "Cx": "54", "Cn": "54", "Ru1": "23", "Ru2": "07", "zU1": "23", "zU2": "07", "sum1": "23", "sum2": "07", "off1": "23", "off2": "07"}
+SPOT = {"key": (0, 0), "o": (128, 0), "y": (256, 0), "z": (384, 0), "PW": (384, 0), "u": (160, 8), "Z": (0, 0), "F": (256, 0), "keep": (128, 0), "tw": (384, 0), "list": (256, 0), "c": (0, 0), "old": (0, 0), "Cx": (128, 0), "Cn": (256, 0), "Ru1": (0, 0), "Ru2": (128, 0), "zU1": (448, 8), "zU2": (464, 8), "sum1": (256, 0), "sum2": (320, 0), "off1": (480, 8), "off2": (496, 8)}
+CYC, GATHER, SCATTER = 0.00083, 1.56, 3.8
+WAKE = 0.215
 TFIX = 0.006
-RULES = [(0.0, 0.3, 0.3), (0.03, 0.5, 0.5)]
-PASSES = 4
-LONG = 2
-SEED = 1
-SWAPS = 4000
-HEAT = 0.03
-SHAKES = 300
-SHAKE = 0.3
-SHARE = 0.2
-ISSUE = 0.8
+VFIX = 0.0
+ISSUE = 0.9
 LOAD = 4.2
 SMALL = 1.8
-FAR = 2.2
+FAR = 2.5
+LATER = 0.8
+LONG = 2
+SEED = 1
+TURNS = 3500
+WARM = 0.3
+SLOW = (0.04, 0.5, 0.8, 0.4)
+SHAKE = 0.3
+SHIFT = 1.0
 PLAN = {}
 XW = W + 2 * L
 GW = 2064
+KEYS = []
+for _r in RUNS.split("|"):
+    KEYS.append([])
+    for _k in _r.split("/"):
+        _p = KEYS[-1][-1][1] if KEYS[-1] else 0
+        KEYS[-1].append((_p, _p + sum(int(x[3:]) for x in _k.split()), _k.split()[0][2]))
+RUNS = [[(x[:2], x[2], int(x[3:])) for x in r.split() if x != "/"] for r in RUNS.split("|")]
+SLOTS = [[(x[0], int(x[1:])) for x in r.split()] for r in SLOTS]
 SCRATCH = {"X": ("sbuf", [128, XW], BF)}
 ALIAS = {}
 
@@ -64,50 +65,267 @@ def _add(names, cols, d):
 for _h in "01":
     SCRATCH["GD" + _h] = ("sbuf", [128, 2 * GW], BF)
     ALIAS["GV" + _h], ALIAS["DC" + _h] = ("GD" + _h, 0, GW, BF), ("GD" + _h, GW, GW, BF)
-_add("AB0 AB1", 128 * AS, BF)
+_add("AB0 AB1 CG0 CG1", 2048, BF)
+_add("DV0 DV1", 2048, F16)
 _add("EE0 EE1", 1792, BF)
-_add("EQ", 4096, BF)
-_add("VK", 272, F16)
-ALIAS["V"], ALIAS["s1"] = ("VK", 0, 256, F16), ("VK", 256, 16, F16)
-_pack("YC", "Y Cd" if WHO["Cp"] == "S" else "Y Cp", 256, F16)
-_pack("YN", "low NF" if WHO["Cp"] == "S" else "low Cd", 256, F16)
+_add("EQ", 2048, BF)
+_pack("VY", "VK YV", 272, F16)
+ALIAS["V"], ALIAS["s1"] = ("VY", 0, 256, F16), ("VY", 256, 16, F16)
+ALIAS["Yn"], ALIAS["Vn"] = ("VY", 272, 256, F16), ("VY", 528, 16, F16)
+_pack("YN", "Cp Cd Y BL", 256, F16)
 for _t in range(ST):
-    _add("rK%d" % _t, 272, F16)
-    _pack("rC%d" % _t, "rY%d rP%d" % (_t, _t), 256, F16)
-    _add("rB%d" % _t, 32, I32)
-_add("SB", 32, I32)
-_pack("MH", "Wz Ez Ru i1 m3 upV upC dnV dnC fxV fxC kpV kpC inV inC tV tC" + " m2 m4 m5" * (1 - MAXES), 256, F16)
-_pack("MI", "IdH InH Uh0 Uh1 Uh2 Uh3 Uh4 Uh8 Uh12", 128, F16)
+    _add("rK%d" % _t, 544, F16)
+    ALIAS["rY%d" % _t] = ("rK%d" % _t, 272, 272, F16)
+    _add("rC%d" % _t, 256, F16)
+    _add("rB%d" % _t, 16, I32)
+_add("SB", 16, I32)
+_pack("MH", "Wz1 Ez1 Ru1 Wz2 Ez2 Ru2 xw kw i1 m2 m3 m4 m5 upV upC dnV dnC fxV fxC kpV kpC inV inC tV tC", 256, F16)
+_pack("MI", "IdH InH CQ Uh0 Uh1 Uh2 Uh3 Uh4 Uh8 Uh12", 128, F16)
 _add("blk8H", 8, F16)
-_pack("MP", "OH ee mP Fu", 256, BF, 16)
-_pack("MF", "m2 m4 m5 " * MAXES + "PW m1 xw kw n0 n1 n2 n3 n4 n5 RSf RSm RSk RSn DGf THR i32s QC f1 f2 LNF", 256, F32)
-_pack("MQ", "mg mm onesF IdF PW2 G8", 128, F32)
-_pack("MB", "val cum av sgp sk dd sgm gw tw keep Dn FF Zs El cumI RS NR DG g1 g2 g3 BL C4", 256, BF)
+_pack("MP", "ee0 ee1 mP0 mP1 Fu0 Fu1", 128, BF, 16)
+if "z2" in PARTS:
+    for _n in ("mP", "Fu"):
+        _at = ALIAS[_n + "0"][1]
+        ALIAS[_n + "1"], ALIAS[_n + "2"] = ("MP", _at + 128, 128, BF), ("MP", _at, 256, BF)
+_pack("MZ", "zs1 sx", 256, F16)
+_add("zs2", 768, F16)
+_add("take", 768, BF)
+_pack("MF", "PW m1 QC f1 f2 LNF", 256, F32)
+_pack("MQ", "mm onesF PW2 G8 n3 n4 RSm RSk THR", 128, F32)
+_pack("MB", "val cum av sgp sk dd sgm gw tw keep Dn FF Fc Zs El Em1 Em2 rc Dk g1 g2 g3 grow OH RS RS2 CZ", 256, BF)
 _add("pabc0 pabc1", 384, BF)
-_add("SK SM IV IC iw LNI", 256, I32)
+_add("SK SM KA IV IC LNI", 256, I32)
 _add("LV LC", 256, U16)
-_pack("PLF", "nn ng V0 x kn kc Kp sq hh s2 s3 s4 s5 s6 s7 th2 TR TRm oA zz t1 t3", 16, F32)
-_pack("PL2", "zs dz take", 32, F32)
-_add("grow", 24, F32)
-_pack("PLI", "KA UI HI VM", 16, I32)
-_pack("PLU", "off16 z16 bcA bcG bcZ", 16, U16)
+_pack("PLF", "nn V0 x kn Kp sq hh s2 s3 s4 s5 s6 s7 s8 th2 TR TRm oA1 oA2 zz1 zz2 t1", 16, F32)
+_add("dz", 48, F32)
+_pack("PLI", "UI HI VM", 16, I32)
+_pack("PLU", "off1 off2 z16 bcA bcG bcT bcK", 16, U16)
 _pack("OL", "olist0 olist1", 24, U16)
 _add("OB", 24, F16)
 _pack("PLB", "BM32 BMh", 24, BF)
-_pack("COF", "pcF pmF p4F thm lim cs1 e1 e2 e3 e4 eK eO eH eL eM wF wq wp", 1, F32)
+_pack("COF", "pcF pmF p4F thm lim cs1 e1 e2 e3 e4 e5 eK eO eQ eH eL eM wF wq wp", 1, F32)
 _pack("COI", "pcI pmI p4I cI tI", 1, I32)
 _add("WI THI", 1, I32)
-_pack("IDS", "Ident In1 Za Zk Zo Zg Ih Ibig IZv In4k In4 I64 I2k I8k In8k ones Yw0 Yw1 LIM blkw blkl CQ CR zero Ub0 Ub1 Ub2 Ub3", 128, BF)
-_pack("N8", "BKk EEw GVw ABw W8", 8, BF)
-_add("BW", 576, BF)
-_add("blk8F THF", 8, F32)
+_pack("IDS", "Ident In1 Za Zk Zo Zg Ih Ibig IZv In4k In4 I64 I2k I8k ones Yw0 Yw1 LIM blkw blkl CR zero two NR DG Ub0 Ub1 Ub2 Ub3", 128, BF)
+_pack("N8", "BKk BK2 BKn EEw GVw W8", 8, BF)
+_add("BW", 64, BF)
+_add("blk8F THF IdF", 8, F32)
+LOOPWISE = any(k[2] == "T" for r in KEYS for k in r)
 for _b in range(8):
-    SCRATCH["pb%d" % _b] = ("psum", [128, 32, 16] if str(_b) in DIFF and AS == 14 else [128, 512], F32)
-SCRATCH["DV"] = ("sbuf", [128, 32, 16], BF)
+    SCRATCH["pb%d" % _b] = ("psum", [128, 32, 16] if str(_b) in DIFF and LOOPWISE else [128, 512], F32)
 
-SEMAPHORES = ["sV", "sS", "sT", "sG", "lK", "lC", "lB"]
-SEMAPHORES += ["a%s%d" % (m, t) for m in "KCB" for t in range(ST)]
-SEMAPHORES += ["d%d" % k for k in range(24)] + ["e%d%d" % (h, k) for h in range(2) for k in range(4)]
+MAIL = ("K0", "Y0", "B0", "B1", "C0", "C1")
+SEMAPHORES = ["sV", "sS", "sT", "sG"] + ["l" + m for m in MAIL] + ["a%s%d" % (m, t) for m in MAIL for t in range(ST)]
+SEMAPHORES += ["d%d" % k for k in range(12)]
+
+
+def order(OPS):
+    n = len(OPS)
+    seen, deps = {}, []
+    for i, o in enumerate(OPS):
+        q, dp = o[0], {}
+        for j in o[7]:
+            dp[j] = 0
+        for j in o[6]:
+            dp[j] = 1
+        for acc, wr in [(a, 0) for a in o[2]] + [(a, 1) for a in o[3]]:
+            name, lo, hi = acc
+            for (l2, h2, j, q2, w2) in seen.get(name, []):
+                if lo < h2 and l2 < hi and (wr or w2):
+                    dp[j] = max(dp.get(j, 0), 0 if q == q2 == "T" else 1)
+        for acc, wr in [(a, 0) for a in o[2]] + [(a, 1) for a in o[3]]:
+            name, lo, hi = acc
+            old = seen.get(name, [])
+            if wr:
+                old = [r for r in old if not (lo <= r[0] and r[1] <= hi)]
+            seen[name] = old + [(lo, hi, i, q, wr)]
+        dp.pop(i, None)
+        deps.append(dp)
+    sums, opened = [], {}
+    for i, o in enumerate(OPS):
+        if o[8]:
+            b = o[3][0][0]
+            if o[8][0]:
+                opened[b] = [b, i]
+                sums.append(opened[b])
+            else:
+                deps[i].setdefault(opened[b][1], 0)
+                opened[b].append(i)
+            if o[8][1]:
+                for j in opened[b][1:-1]:
+                    deps[i].setdefault(j, 0)
+    lastof = {}
+    for s in sums:
+        for e in reversed(lastof.setdefault(s[0], [])):
+            if len(s) > LONG or len(e) > LONG:
+                deps[s[1]].setdefault(e[-1], 0)
+            if len(e) > LONG:
+                break
+        lastof[s[0]].append(s)
+    above = []
+    for i in range(n):
+        m = 0
+        for j in sorted(deps[i], reverse=True):
+            if m >> j & 1 and any(deps[i][k] >= deps[i][j] and above[k] >> j & 1 and OPS[j][5] == 0 for k in deps[i]):
+                del deps[i][j]
+            m |= above[j] | (1 << j)
+        above.append(m)
+    qs, cost, lat = [o[0] for o in OPS], [o[4] for o in OPS], [o[5] for o in OPS]
+    banks = [sorted({a[0] for a in o[2] + o[3] if a[0].startswith("pb")}) for o in OPS]
+    fwd = [[(j, cost[j] + (lat[j] + WAKE if k else 0.0)) for j, k in deps[i].items()] for i in range(n)]
+    bwd = [[] for _ in OPS]
+    for i in range(n):
+        for j, w in fwd[i]:
+            bwd[j].append((i, w - cost[j] + cost[i]))
+
+    def fit(key, before, first, line):
+        for i in line:
+            x = key[i]
+            for j, _w in before[i]:
+                if key[j] >= x:
+                    x = key[j] + 1e-7
+            key[i] = x
+        line = np.argsort(key, kind="stable").tolist()
+        start, busy = [0.0] * n, {q: ([], []) for q in "VSTGYF"}
+        held = {"pb%d" % b: ([], [], []) for b in range(8)}
+        for i in line:
+            q, c, t = qs[i], cost[i], first[i]
+            for j, w in before[i]:
+                if start[j] + w > t:
+                    t = start[j] + w
+            s, e = busy[q]
+            k = len(e)
+            while k and e[k - 1] > t + 1e-9:
+                k -= 1
+            while True:
+                while k < len(s) and s[k] < t + c - 1e-9:
+                    if e[k] > t:
+                        t = e[k]
+                    k += 1
+                moved = False
+                for b in banks[i]:
+                    be, bs, bq = held[b]
+                    m = len(be)
+                    while m and be[m - 1] > t - WAKE + 1e-9:
+                        m -= 1
+                        if bq[m] != q and bs[m] < t + c + WAKE - 1e-9:
+                            t, moved = be[m] + WAKE, True
+                            break
+                if not moved:
+                    break
+            start[i] = t
+            if k and e[k - 1] >= t - 1e-9:
+                if k < len(s) and s[k] <= t + c + 1e-9:
+                    e[k - 1] = e[k]
+                    del s[k], e[k]
+                else:
+                    e[k - 1] = t + c
+            elif k < len(s) and s[k] <= t + c + 1e-9:
+                s[k] = t
+            else:
+                s.insert(k, t)
+                e.insert(k, t + c)
+            for b in banks[i]:
+                be, bs, bq = held[b]
+                m = len(be)
+                while m and be[m - 1] > t + c:
+                    m -= 1
+                be.insert(m, t + c)
+                bs.insert(m, t)
+                bq.insert(m, q)
+        return np.array(start), line
+    none, up, down = [0.0] * n, range(n), range(n - 1, -1, -1)
+    took, whole = np.array(cost), np.array(cost) + np.array(lat)
+
+    def forth(key):
+        start, line = fit(key.tolist(), fwd, none, up)
+        return float((start + whole).max()), start, line
+
+    def again(start):
+        return forth(-fit((-start - took).tolist(), bwd, lat, down)[0] - took)
+
+    def blocked(start):
+        st, ends, out = start.tolist(), {}, []
+        for i in range(n):
+            ends[(qs[i], round(st[i] + cost[i], 5))] = i
+            for b in banks[i]:
+                ends[(b, round(st[i] + cost[i] + WAKE, 5))] = i
+        i = int((start + whole).argmax())
+        while st[i] > 1e-6:
+            j = [j for j, w in fwd[i] if abs(st[j] + w - st[i]) < 1e-6]
+            if not j:
+                j = [ends[c] for c in [(x, round(st[i], 5)) for x in [qs[i]] + banks[i]] if ends.get(c, i) != i]
+                if not j:
+                    break
+                out.append((j[0], i))
+            i = j[0]
+        return out
+    tail = [0.0] * n
+    for i in down:
+        tail[i] = max([lat[i]] + [tail[j] + w for j, w in bwd[i]])
+    PLAN["chain"] = max(tail[i] + cost[i] for i in range(n))
+    PLAN["debug"] = (OPS, tail, cost, bwd, fwd)
+    kinds, parts = {}, {}
+    kind = np.array([kinds.setdefault((o[0], str(o[3]), str([a for a in o[2] if a[0][0] != "r"])), len(kinds)) for o in OPS])
+    part = np.array([parts.setdefault(o[9] + o[0], len(parts)) for o in OPS])
+    slow = [cost[i] + SLOW[1] * (lat[i] > 0 and qs[i] == "G") for i in range(n)]
+    late = [[(j, slow[j] + ((lat[j] + WAKE + SLOW[0] + SLOW[2] * (qs[j] == "G" and lat[j] > 0)) if k else 0.0)) for j, k in deps[i].items()] for i in range(n)]
+
+    def both(plan):
+        place = np.empty(n)
+        place[plan[2]] = np.arange(n)
+        start, free, held = [0.0] * n, dict.fromkeys("VSTGYF", 0.0), {}
+        for i in np.lexsort((place, np.round(plan[1], 6))).tolist():
+            q = qs[i]
+            t = free[q]
+            for j, w in late[i]:
+                if start[j] + w > t:
+                    t = start[j] + w
+            for b in banks[i]:
+                if b in held and held[b][0] != q and held[b][1] > t:
+                    t = held[b][1]
+            start[i] = t
+            free[q] = t = t + slow[i]
+            for b in banks[i]:
+                held[b] = (q, t + WAKE + SLOW[0])
+        return (1 - SLOW[3]) * plan[0] + SLOW[3] * float((np.array(start) + whole).max())
+    rng = np.random.default_rng(SEED)
+    best = now = again(forth(-np.array(tail) - took)[1])
+    least = mark = both(now)
+    pairs = None
+    for k in range(TURNS):
+        how, s = rng.random(), now[1]
+        if how < 0.5:
+            pairs = pairs or blocked(s)
+            noise = np.zeros(len(kinds))
+            for _ in range(1 + int(rng.integers(3))):
+                j, i = pairs[int(rng.integers(len(pairs)))]
+                if rng.random() < 0.5:
+                    noise[kind[j]] = s[i] - s[j] + 0.01 + rng.random() * 0.5
+                else:
+                    goal, todo = s[j] - 0.01, [i]
+                    while todo:
+                        x = todo.pop()
+                        if s[x] + noise[kind[x]] > goal:
+                            noise[kind[x]] = goal - s[x]
+                            todo += deps[x]
+            new = forth(s + noise[kind])
+            if now[0] - 1e-6 < new[0] < now[0] + 1.5:
+                new = min(new, again(new[1]), key=lambda r: r[0])
+        elif how < 0.75:
+            new = again(s - (rng.normal(0.0, SHIFT, len(parts)) * (rng.random(len(parts)) < 0.1))[part])
+        else:
+            new = again(s - (rng.normal(0.0, SHAKE, len(kinds)) * (rng.random(len(kinds)) < 0.2))[kind])
+        room = WARM * (1 - k / TURNS) * rng.random()
+        if new[0] < now[0] + room + 0.5:
+            x = both(new)
+            if x < mark + room:
+                now, pairs, mark = new, None, x
+                if x < least:
+                    best, least = now, x
+    PLAN["end"], PLAN["start"] = best[0], best[1].tolist()
+    place = {i: k for k, i in enumerate(best[2])}
+    return sorted(range(n), key=lambda i: (round(PLAN["start"][i], 6), place[i]))
 
 
 def rank_program(g, core, T, topo):
@@ -120,6 +338,7 @@ def rank_program(g, core, T, topo):
     clock = {}
     recs = {}
     ndma = [0]
+    part = ["", -1]
 
     def v(name, lo=0, hi=None, step=1, p=None):
         if name in ALIAS:
@@ -140,6 +359,11 @@ def rank_program(g, core, T, topo):
         sl = slice(lo, hi, step) if step != 1 else slice(lo, hi)
         p0, p1 = p if isinstance(p, tuple) else (0, p or 128)
         return (t[p0:p1, sl], [(name, lo, hi)], (hi - lo + step - 1) // step, False)
+
+    def back(name, lo, hi, step=1):
+        x = v(name, lo, hi, step)
+        name, lo, hi = x[1][0]
+        return (T[name][:, hi - 1:(lo - 1 if lo else None):-step],) + x[1:]
 
     def ind(win, off):
         return (win[0].indirect(off[0]), win[1] + off[1], off[2] * 16, True)
@@ -196,7 +420,7 @@ def rank_program(g, core, T, topo):
     OPS = []
 
     def add(q, emit, reads, writes, cost, lat=0.0, after=()):
-        OPS.append([q, emit, [a for x in reads for a in x[1]], [a for x in writes for a in x[1]], cost, lat, list(after), [], None])
+        OPS.append([q, emit, [a for x in reads for a in x[1]], [a for x in writes for a in x[1]], cost, lat, list(after), [], None, part[0], part[1]])
         return len(OPS) - 1
 
     def op(q, fn, reads, writes, cost=0.06):
@@ -205,7 +429,7 @@ def rank_program(g, core, T, topo):
             sem = "s" + q
             fn(queues[q]).then_inc(T.sem[sem], 1)
             record(q, bump(q, sem, 1), rd, wr)
-        return add(q, emit, reads, writes, cost)
+        return add(q, emit, reads, writes, cost + VFIX * (q == "V"))
 
     def dma(q, out, in_, reads=(), writes=(), lat=SMALL):
         sem = "d%d" % ndma[0]
@@ -216,223 +440,6 @@ def rank_program(g, core, T, topo):
             queues[q].dma_start(out, in_).then_inc(T.sem[sem], 16)
             record(q + "d", bump(q, sem, 16), rd, wr)
         return add(q, emit, reads, writes, 0.1, lat)
-
-    def addto(out, a, sem):
-        def emit(rd, wr):
-            wait("G", need("G", rd, wr))
-            g.dma_start(out[0], a[0], accum_op=OP.add).then_inc(T.sem[sem], 16)
-            record("Gd", bump("G", sem, 16), rd, wr)
-        return add("G", emit, [a, out], [out], GDMA, ADMA + out[2] * BDMA)
-
-    def order():
-        seen, deps, succ = {}, [], [[] for _ in OPS]
-        for i, o in enumerate(OPS):
-            q, dp = o[0], {}
-            for j in o[7]:
-                dp[j] = 0
-            for j in o[6]:
-                dp[j] = 1
-            for acc, wr in [(a, 0) for a in o[2]] + [(a, 1) for a in o[3]]:
-                name, lo, hi = acc
-                for (l2, h2, j, q2, w2) in seen.get(name, []):
-                    if lo < h2 and l2 < hi and (wr or w2):
-                        dp[j] = max(dp.get(j, 0), 0 if q == q2 == "T" else 1)
-            for acc, wr in [(a, 0) for a in o[2]] + [(a, 1) for a in o[3]]:
-                name, lo, hi = acc
-                old = seen.get(name, [])
-                if wr:
-                    old = [r for r in old if not (lo <= r[0] and r[1] <= hi)]
-                seen[name] = old + [(lo, hi, i, q, wr)]
-            dp.pop(i, None)
-            deps.append(dp)
-        n = len(OPS)
-        sums, opened = [], {}
-        for i, o in enumerate(OPS):
-            if o[8]:
-                b = o[3][0][0]
-                if o[8][0]:
-                    opened[b] = [b, i]
-                    sums.append(opened[b])
-                else:
-                    deps[i].setdefault(opened[b][1], 0)
-                    opened[b].append(i)
-                if o[8][1]:
-                    for j in opened[b][1:-1]:
-                        deps[i].setdefault(j, 0)
-        while True:
-            above = []
-            for i in range(n):
-                m = 0
-                for j in deps[i]:
-                    m |= above[j] | (1 << j)
-                above.append(m)
-            new, lastof = 0, {}
-            for s in sums:
-                for e in lastof.get(s[0], [])[-12:]:
-                    if not above[s[1]] >> e[-1] & 1 and (above[s[-1]] >> e[1] & 1 or len(s) > LONG or len(e) > LONG):
-                        deps[s[1]][e[-1]] = 0
-                        new += 1
-                lastof.setdefault(s[0], []).append(s)
-            if not new:
-                break
-        for i in range(n):
-            for j in deps[i]:
-                succ[j].append(i)
-        banks = [sorted({a[0] for a in o[2] + o[3] if a[0].startswith("pb")}) for o in OPS]
-        cost = [o[4] for o in OPS]
-        fwd = [[(j, cost[j] + (OPS[j][5] + WAKE if k else 0.0)) for j, k in deps[i].items()] for i in range(n)]
-        bwd = [[(j, cost[j] + (OPS[i][5] + WAKE if deps[j][i] else 0.0)) for j in succ[i]] for i in range(n)]
-
-        def place(key, before, after, first, look, urge):
-            left = [len(b) for b in before]
-            start, free, ready, out = [0.0] * n, {}, {}, []
-            held, busy = {}, set()
-            a, z = (0, 1) if before is fwd else (1, 0)
-
-            def push(i):
-                ready.setdefault(OPS[i][0], []).append((max([first[i]] + [start[j] + w for j, w in before[i]]), key[i], i))
-
-            def now(c, q):
-                t0 = c[0]
-                for b in banks[c[2]]:
-                    if b in held and held[b][0] != q and held[b][1] > t0:
-                        t0 = held[b][1]
-                return (t0, c[1], c[2], c)
-            for i in range(n):
-                if left[i] == 0:
-                    push(i)
-            while len(out) < n:
-                best = None
-                for q, lst in ready.items():
-                    lst = [now(c, q) for c in lst if not (q == "T" and OPS[c[2]][8][a] and banks[c[2]][0] in busy)]
-                    if lst:
-                        t0 = max(free.get(q, 0.0), min(lst)[0])
-                        r = min((c for c in lst if c[0] <= t0 + SLACK), key=lambda c: c[1:3])
-                        soon = [c for c in lst if c[0] <= t0 + look * cost[r[2]] and c[1] < r[1] - urge]
-                        if soon:
-                            r = min(soon, key=lambda c: c[1:3])
-                        st = max(t0, r[0])
-                        if best is None or st < best[0]:
-                            best = (st, q, r)
-                st, q, r = best
-                i = r[2]
-                ready[q].remove(r[3])
-                start[i] = st
-                free[q] = st + cost[i]
-                for b in banks[i]:
-                    held[b] = (q, free[q] + WAKE)
-                if q == "T":
-                    if OPS[i][8][a]:
-                        busy.add(banks[i][0])
-                    if OPS[i][8][z]:
-                        busy.discard(banks[i][0])
-                out.append(i)
-                for j, _w in after[i]:
-                    left[j] -= 1
-                    if left[j] == 0:
-                        push(j)
-            return start, out
-        none, lat = [0.0] * n, [o[5] for o in OPS]
-        tail = [0.0] * n
-        for i in range(n - 1, -1, -1):
-            tail[i] = max([lat[i]] + [tail[j] + w for j, w in bwd[i]])
-        PLAN["chain"] = max(tail[i] + cost[i] for i in range(n))
-        PLAN["debug"] = (OPS, tail, cost, bwd, fwd)
-        best = None
-        for beta, look, urge in RULES:
-            key = [beta * i - tail[i] - cost[i] for i in range(n)]
-            for _ in range(PASSES):
-                start, seq = place(key, fwd, bwd, none, look, urge)
-                end = max(start[i] + cost[i] + lat[i] for i in range(n))
-                if best is None or end < best[0]:
-                    best = (end, seq, start)
-                    PLAN["rule"] = (beta, look, urge)
-                late, _seq = place([-start[i] - cost[i] for i in range(n)], bwd, fwd, lat, look, urge)
-                key = [-late[i] - cost[i] for i in range(n)]
-        rng = np.random.default_rng(SEED)
-        look, urge = PLAN["rule"][1:]
-        PLAN["tools"] = (place, fwd, bwd, none, lat, best)
-        kinds = {}
-        kind = [kinds.setdefault((o[0], str(o[3]), str([a for a in o[2] if a[0][0] != "r"])), len(kinds)) for o in OPS]
-        for k in range(SHAKES):
-            noise = rng.normal(0.0, SHAKE, len(kinds)) * (rng.random(len(kinds)) < SHARE)
-            if k % 2:
-                late, _seq = place([-best[2][i] - cost[i] + float(noise[kind[i]]) for i in range(n)], bwd, fwd, lat, look, urge)
-                key = [-late[i] - cost[i] for i in range(n)]
-            else:
-                key = [best[2][i] + float(noise[kind[i]]) for i in range(n)]
-            start, seq = place(key, fwd, bwd, none, look, urge)
-            end = max(start[i] + cost[i] + lat[i] for i in range(n))
-            if end < best[0]:
-                best = (end, seq, start)
-        qs = [o[0] for o in OPS]
-        opens = [o[8] and any(o[8]) and (o[8][0], o[8][1], banks[i][0]) for i, o in enumerate(OPS)]
-
-        def replay(seq):
-            start, why, free, held, busy, end, at = [0.0] * n, [-1] * n, {}, {}, set(), 0.0, -1
-            for i in seq:
-                q = qs[i]
-                st, y = free.get(q, (0.0, -1))
-                for j, w in fwd[i]:
-                    if start[j] + w > st:
-                        st, y = start[j] + w, j
-                for b in banks[i]:
-                    h = held.get(b)
-                    if h and h[0] != q and h[1] > st:
-                        st, y = h[1], h[2]
-                if opens[i]:
-                    a, z, b = opens[i]
-                    if a and b in busy:
-                        return None
-                    if a and not z:
-                        busy.add(b)
-                    elif z:
-                        busy.discard(b)
-                start[i], why[i] = st, y
-                st += cost[i]
-                free[q] = (st, i)
-                for b in banks[i]:
-                    held[b] = (q, st + WAKE, i)
-                if st + lat[i] > end:
-                    end, at = st + lat[i], i
-            return end, why, at
-        seq = list(best[1])
-        end, why, at = replay(seq)
-        top = (end, seq)
-        for k in range(SWAPS):
-            if k % 8 == 0 or changed:
-                pos = {i: s for s, i in enumerate(seq)}
-                path, i = [], at
-                while why[i] >= 0:
-                    if why[i] not in deps[i]:
-                        path.append((why[i], i))
-                    i = why[i]
-            changed = False
-            j, i = path[int(rng.integers(len(path)))]
-            a, b = pos[j], pos[i]
-            if rng.random() < 0.5:
-                take, rest = {i}, []
-                for x in reversed(seq[a:b]):
-                    if any(x in deps[y] for y in take):
-                        take.add(x)
-                if j in take:
-                    continue
-            else:
-                drop = {j}
-                for x in seq[a + 1:b + 1]:
-                    if any(y in deps[x] for y in drop):
-                        drop.add(x)
-                if i in drop:
-                    continue
-                take = set(seq[a:b + 1]) - drop
-            new = seq[:a] + [x for x in seq[a:b + 1] if x in take] + [x for x in seq[a:b + 1] if x not in take] + seq[b + 1:]
-            r = replay(new)
-            if r and r[0] <= end + HEAT * (1 - k / SWAPS) * rng.random():
-                seq, (end, why, at), changed = new, r, True
-                if end < top[0]:
-                    top = (end, seq)
-        PLAN["end"] = top[0]
-        return top[1]
 
     def vcost(out, a, b=None):
         views = [x for x in (out, a, b) if x is not None]
@@ -477,17 +484,17 @@ def rank_program(g, core, T, topo):
     def line(dst, x, scale, bias):
         act(dst, x, AF.Identity, scale, bias)
 
-    def move(who, out, a, scale=None, bias=None):
+    def move(who, h, out, a, scale=None, bias=None):
         if scale is None:
-            (cp if WHO[who] == "V" else act)(out, a)
-        elif WHO[who] == "V":
+            (cp if WHO[who][h % 2] == "V" else act)(out, a)
+        elif WHO[who][h % 2] == "V":
             ts(out, a, scale, OP.mult, bias, OP.add)
         else:
             line(out, a, scale, bias)
 
-    def mm(out, l, r, start=True, stop=True, pause=False):
+    def mm(out, l, r, start=True, stop=True):
         c = TFIX + max(min(64, l[2]), r[2]) * CYC * (4 if SCRATCH[r[1][0][0]][2] == F32 else 1)
-        OPS[op("T", lambda e: e.matmul(out[0], l[0], r[0], start, stop or pause), [l, r], [out], c)][8] = (start, stop)
+        OPS[op("T", lambda e: e.matmul(out[0], l[0], r[0], start, stop), [l, r], [out], c)][8] = (start, stop)
 
     def mms(out, terms):
         for k, (l, r) in enumerate(terms):
@@ -496,6 +503,13 @@ def rank_program(g, core, T, topo):
     def scan(out, d0, d1, o0, o1, init=0.0):
         small = all(SCRATCH[x[1][0][0]][2] in (BF, F16) for x in (out, d0, d1))
         op("V", lambda e: e.tensor_tensor_scan(out[0], d0[0], d1[0], init, o0, o1), [d0, d1], [out], max(64, out[2] * (0.5 if small else 1)) * CYC)
+
+    def alone(out, a, ones):
+        scan(out, a, ones, OP.add, OP.mult)
+
+    def hold(out, x, h, step=1, keep="RS"):
+        lo, hi = span(h)[:2]
+        scan(back(out, lo, hi), v(keep, 0, hi - lo), back(x, lo * step, hi * step, step), OP.mult, OP.add)
 
     def total(out, a):
         op("V", lambda e: e.tensor_reduce(out[0], a[0], AxisListType.X, OP.add), [a], [out], max(64, a[2]) * CYC)
@@ -509,21 +523,40 @@ def rank_program(g, core, T, topo):
         else:
             op("G", lambda e: e.iota(out[0], pat, base, cm, allow_small_or_imprecise_dtypes=True), [], [out], 0.13 + 2 * CYC * out[2])
 
+    def mask(out, a, pat, cmp, other, base, cm):
+        op("G", lambda e: e.affine_select(out[0], a[0], pat, cmp, other, base, cm), [a], [out], 0.17 + 2 * CYC * out[2])
+
     def select(out, a, cmp, other, k):
-        op("G", lambda e: e.affine_select(out[0], a[0], [[1, out[2]]], cmp, other, k, -1), [a], [out], 0.17 + 2 * CYC * out[2])
+        mask(out, a, [[1, out[2]]], cmp, other, k, -1)
 
     def bc(x, h=None):
-        return ind(v(x), v("bcA")) if h is None else ind(v(x, 8 * h, 8 * h + 8), v("bcA", 0, 8))
+        return ind(v(x), v("bcA")) if h in (None, 2) else ind(v(x, 8 * h, 8 * h + 8), v("bcA", 0, 8))
 
     def last(name, a0=0, a1=16):
         return v(name, a0 * 16 + 15, a1 * 16, 16)
+
+    def third(x, h, step=48):
+        return v(x, 3 * span(h)[0] + step - 1, 3 * span(h)[1], step)
+
+    def pad(name, h):
+        return name + str(h)
 
     def turn(dst, src):
         for h in range(2):
             mm(v(dst[0], dst[1] + 128 * h, dst[1] + 128 * h + 128), v(src, 128 * h, 128 * h + 128), v("IdH"))
 
-    def bank(name, lo, hi, h=0):
-        return v("pb" + BANK[name][h], lo, hi)
+    def bank(name, h, lo=0, hi=128, step=1, p=None):
+        at, width = SPOT[name]
+        if h == 2:
+            assert BANK[name][0] == BANK[name][1] and width
+            h, hi = 0, hi + width
+        return v("pb" + BANK[{"o": "key", "y": "key"}.get(name, name)][h], at + h * width + lo, at + h * width + hi, step, p)
+
+    def span(h):
+        return (0, 256, 0, 16) if h == 2 else (128 * h, 128 * h + 128, 8 * h, 8 * h + 8)
+
+    def each(h):
+        return (1, 0) if h == 2 else (h,)
 
     half = W // 2
     dma("Y", T.IV[:], T.vl[:], [], [v("IV")])
@@ -537,121 +570,115 @@ def rank_program(g, core, T, topo):
     iota(v("pcI"), [[0, 1]], 0, 1)
     iota(v("mm"), [[1, 128]], 0, 0)
     iota(v("QC"), [[0, 16], [1, 16]], 0, 0)
-    iota(v("mg"), [[1, 8], [0, 16]], 0, 0)
+    slots = [[0, 8], [1, 16]]
+    for nm, c in (("ones", 1), ("zero", 0), ("onesF", 1), ("two", 2), ("g2", -192), ("dz", 0), ("KA", -32)):
+        iota(v(nm), [[0, v(nm)[2]]], c, 0)
+    for x in (v("EQ"), v("take"), v("grow"), v("X", W, XW)):
+        fill(x, 0.0)
+    cp(v("MZ"), v("take", 0, 512))
+    cp(v("zs2"), v("take"))
     iota(v("TR"), [[256, 2], [0, 8]], W // 2, 2)
-    iota(v("OB", 0, 8), [[256, 8]], GW + 16, 0)
-    iota(v("OB", 8, 24), [[1, 2], [256, 8]], 16, 0)
+    iota(v("TRm"), [[256, 2], [0, 8]], W // 2 - 8192, 2)
+    iota(v("OB", 0, 8), [[256, 8]], GW, 0)
+    iota(v("OB", 8, 24), [[1, 2], [256, 8]], 0, 0)
     iota(v("t1"), [[32, 16]], W + 2048, 0)
     iota(v("f2", 0, 64), [[1, 8], [0, 8]], 0, 0)
-    iota(v("X", W, XW), [[0, 2 * L]], 0, 0)
-    iota(v("EQ"), [[0, 4096]], 0, 0)
+    iota(v("f2", 64, 88), [[0, 3], [1, 8]], 0, 0)
+    for nm in ("GV0", "GV1", "DC0", "DC1"):
+        iota(v(nm, 2048, GW), [[0, GW - 2048]], 0, 0)
+    iota(v("MP", 15, 6 * 144, 144), [[0, 6]], 0, 0)
+    iota(v("upV", 0, 512, 128), [[0, 4]], 0, 0)
+    iota(v("dnV", 127, 512, 128), [[0, 4]], 0, 0)
+    iota(v("CR"), [[0, 8], [-32, 16]], 512, 0)
+    iota(last("CR", 0, 8), [[0, 8]], int(BIG), 0)
+    iota(v("CZ"), [[0, 256]], int(2 * ZU), 0)
+    iota(last("CZ"), [[0, 16]], int(10 * ZU), 0)
+    iota(v("CQ"), [[0, 8], [2, 16]], -W // 2, 0)
+    for lo in (0, 128):
+        mask(v("RS", lo, lo + 128), v("ones"), slots, OP.is_gt, 0.0, 0, 0)
+        mask(v("RS2", lo, lo + 128), v("ones"), slots, OP.is_ge, 0.0, -2, 0)
+    mask(v("NR"), v("zero"), slots, OP.is_gt, 1.0, 0, 0)
+    mask(v("G8", p=8), v("onesF", p=8), [[-1, 8], [0, 16]], OP.is_equal, 0.0, 0, 1)
+    mask(v("blkw"), v("ones"), [[-16, 8], [0, 16]], OP.is_ge, 0.0, 0, 1)
+    mask(v("blkw"), v("blkw"), [[16, 8], [0, 16]], OP.is_ge, 0.0, 15, -1)
+    mask(v("blkl"), v("blkw"), [[256, 8], [-1, 16]], OP.is_ge, 0.0, 241, -16)
+    for h in range(2):
+        if NABS[h] < 14:
+            line(v("Yw%d" % h), v("blkw"), -KZ, 0.0)
+            mask(v("Yw%d" % h), v("Yw%d" % h), slots, OP.is_ge, 0.0, -2 - NABS[h], 0)
     ts(v("pmI"), v("pcI"), 15, OP.bitwise_and)
     ts(v("p4I"), v("pcI"), 4, OP.arith_shift_right)
     cp(v("COF", 0, 3), v("COI", 0, 3))
     cp(v("LV"), v("IV"))
     cp(v("LC"), v("IC"))
-    ts(v("TRm"), v("TR"), -8192.0, OP.add)
     cp(v("bcA"), v("mm", 0, 16))
-    ts(v("e1"), v("pmF"), 15.0, OP.is_equal, 16.0, OP.mult)
-    ts(v("t3"), v("mm", 0, 16), v("e1"), OP.max)
-    cp(v("bcG"), v("t3"))
-    ts(v("bcZ"), v("mm", 0, 16), 2.0, OP.mult, 1.0, OP.add)
-    fill(v("PL2"), 0.0)
-    ts(v("IdF"), v("mm"), v("pcF"), OP.is_equal)
-    for nm, c in (("Ident", 1.0), ("Ih", 0.5), ("Ibig", BIG), ("IZv", KZ * 2048), ("In4k", -4096.0)) + (("I8k", 8192.0), ("In8k", -8192.0)) * MAXES:
-        line(v(nm), v("IdF"), c, 0.0)
-    cp(v("IdH"), v("IdF"))
-    fill(v("ones"), 1.0)
-    fill(v("onesF"), 1.0)
-    fill(v("zero"), 0.0)
-    fill(v("MP"), 0.0)
-    fill(v("g2"), -192.0)
-    fill(v("grow", 16, 24), 0.5)
-    ts(v("low"), v("QC"), 0.0, OP.mult)
-    for nm in ("GV0", "GV1", "DC0", "DC1"):
-        fill(v(nm, 2048, GW), 0.0)
-    for nm, k in (("upV", 0), ("upC", 0), ("dnV", 127), ("dnC", 127), ("m3", 127)):
-        ts(v(nm, k, 256, 128), v("QC", 0, 2), 0.0, OP.mult)
-    ts(v("DGf"), v("QC"), v("pmF"), OP.is_equal)
-    act(v("DG"), v("DGf"))
-    ts(v("RSf"), v("QC"), 0.0, OP.is_gt)
-    act(v("RS"), v("RSf"))
-    line(v("NR"), v("RSf"), -1.0, 1.0)
-    line(v("RSm", 0, 128), v("RSf", 0, 128), 1048576.0, -4097.0)
-    line(v("RSk", 0, 128), v("RSf", 0, 128), BIG, 31.0)
-    line(v("RSn", 0, 128), v("RSf", 0, 128), 1048576.0, -16384.0)
-    line(v("i32s", 0, 128), v("QC", 0, 128), -32.0, 512.0)
-    ts(v("eO"), v("pmF"), 16.0, OP.mult)
+    if "S" in WHO["tw"]:
+        ts(v("bcT"), v("mm", 0, 16), 48.0, OP.mult, 47.0, OP.add)
+    if "S" in WHO["gw"]:
+        ts(v("e5"), v("pmF"), 15.0, OP.is_equal, 14.0, OP.add)
+        ts(v("bcG"), v("mm", 0, 16), 16.0, OP.mult, v("e5"), OP.add)
+    ts(v("IdH"), v("mm"), v("pcF"), OP.is_equal)
+    ts(v("IdF"), v("mm", 0, 8), v("pcF"), OP.is_equal)
+    for nm, c in (("Ident", 1.0), ("Ih", 0.5)):
+        line(v(nm), v("IdH"), c, 0.0)
+    ts(v("DG"), v("QC", 0, 128), v("pmF"), OP.is_equal)
+    line(v("RSm"), v("RS", 0, 128), 1048576.0, -4097.0)
+    line(v("RSk"), v("RS", 0, 128), BIG, 31.0)
+    ts(v("eO"), v("pmF"), 17.0, OP.mult, 1.0, OP.add)
+    if any(QUICK):
+        ts(v("eQ"), v("pmF"), 16.0, OP.mult, 16.0, OP.add)
+        ts(v("bcK"), v("mm", 0, 16), 16.0, OP.mult, 15.0, OP.add)
     ts(v("blk8F"), v("mm", 0, 8), v("p4F"), OP.is_equal)
     cp(v("blk8H"), v("blk8F"))
-    for nm, c in (("BKk", 2048.0), ("EEw", 4 * KZ), ("GVw", -2 * KZ), ("ABw", -2 * KZ)):
+    for nm, c in (("BKk", 2048.0), ("BK2", 4096.0), ("BKn", -2048.0), ("EEw", -4 * KZ), ("GVw", -2 * KZ)):
         line(v(nm), v("blk8F"), c, 0.0)
-    for k in range(3):
-        ts(v("BM32", 8 * k, 8 * k + 8), v("blk8F"), -1.0 / 32, OP.mult)
+    ts(v("BM32"), v("f2", 64, 88), v("p4F"), OP.is_equal, -1.0 / 32, OP.mult)
     for h in range(2):
         tt(v("BMh", 8 * h, 8 * h + 8), v("t1", 8 * h, 8 * h + 8), v("blk8F"), OP.mult)
-    ts(v("blkw"), v("mg"), v("p4F"), OP.is_equal)
-    for h in range(2):
-        ts(v("n0", 128 * h, 128 * h + 128), v("QC", 0, 128), 2.0 + NABS[h], OP.is_ge, KZ, OP.mult)
-        tt(v("Yw%d" % h), v("n0", 128 * h, 128 * h + 128), v("blkw"), OP.mult)
-    ts(v("e2"), v("pmF"), 2.0, OP.not_equal)
-    ts(v("n1", 0, 128), v("QC", 0, 128), 2.0, OP.is_lt, v("e2"), OP.max)
-    tt(v("blkl"), v("n1", 0, 128), v("blkw"), OP.mult)
     cp(v("wF"), v("WI"))
     ts(v("W8"), v("blk8F"), v("wF"), OP.mult)
-    ts(v("e1"), v("pcF"), 0.0, OP.is_equal)
-    ts(v("e2"), v("pcF"), 1.0, OP.is_equal, -2 * BIG, OP.mult)
-    ts(v("CR"), v("i32s", 0, 128), v("e1"), OP.mult, v("e2"), OP.add)
-    ts(v("e2"), v("pcF"), 1.0, OP.is_equal, -2 * MID, OP.mult)
-    ts(v("e3"), v("e1"), 2.0, OP.mult)
-    ts(v("CQ"), v("QC", 0, 128), v("e3"), OP.mult, v("e2"), OP.add)
-    ts(v("eH"), v("pmF"), 0.25, OP.mult, 191.875, OP.add)
-    ts(v("eL"), v("pmF"), 768.0 + 1 - 64, OP.add)
+    line(v("eH"), v("pmF"), 0.25, 191.875)
+    line(v("eL"), v("pmF"), 1.0, 768.0 + 1 - 64)
+    line(v("eM"), v("pmF"), 1.0, 1.0 - 64)
+    for nm, c in (("Ibig", BIG), ("IZv", KZ * 2048), ("In4k", -4096.0), ("Za", -ZU / 4), ("Zk", -2 * ZU), ("Zo", ZU), ("Zg", 16 * ZU), ("In1", -1.0),
+                  ("InH", -1.0), ("I8k", 8192.0), ("In4", -4.0), ("I64", 64.0), ("I2k", MID)):
+        select(v(nm), v("zero"), OP.not_equal, c, 0)
     for k in (0, 1, 2, 3, 4, 8, 12):
-        select(v("Uh%d" % k), v("low", 0, 128), OP.not_equal, 1.0, k)
-        if k < 4:
+        select(v("Uh%d" % k), v("zero"), OP.not_equal, 1.0, k)
+        if k >= 4:
+            select(v("Uh%d" % k), v("Uh%d" % k), OP.not_equal, -1.0, 0)
+        else:
             select(v("Ub%d" % k), v("blkw"), OP.is_ge, 0.0, k)
             select(v("Ub%d" % k), v("Ub%d" % k), OP.not_equal, -63.0, k)
-    for nm, c in (("In4", -4.0), ("I64", 64.0), ("I2k", MID), ("Za", -ZU / 4), ("Zk", -2 * ZU), ("Zo", ZU), ("Zg", 16 * ZU), ("In1", -1.0)):
-        select(v(nm), v("zero"), OP.not_equal, c, 0)
-    select(v("InH"), v("low", 0, 128), OP.not_equal, -1.0, 0)
-    ts(v("eM"), v("pmF"), 1.0 - 64, OP.add)
-    fill(v("f1", 0, 128), 0.5)
-    fill(v("f1", 128, 256), 0.0)
-    scan(v("PW2"), v("f1", 0, 128), v("f1", 128, 256), OP.mult, OP.add, 2.0 ** 61)
-    tt(v("n4", 0, 128), v("PW2"), v("IdF"), OP.mult)
-    total(v("wp"), v("n4", 0, 128))
-    ts(v("n5"), v("DGf"), v("wp"), OP.mult, 2.5, OP.mult)
-    line(v("n3"), v("DGf"), -2.0 ** 90, 2.0 ** 90)
-    tt(v("THR"), v("n5"), v("n3"), OP.add)
-    tt(v("n4", 128, 144), v("PW2", 0, 16), v("DGf", 0, 16), OP.mult)
-    total(v("wq"), v("n4", 128, 144))
-    ts(v("f2", 64, 128), v("f2", 0, 64), v("p4F"), OP.is_equal)
-    for a in range(8):
-        ts(v("BW", 64 * a, 64 * a + 64), v("f2", 64, 128), v("wq"), OP.mult, 2.0 ** (-16 * a), OP.mult)
-    line(v("BW", 512, 576), v("f2", 64, 128), 2.0 ** 70, 0.0)
+    scan(back("PW2", 0, 128), v("two"), v("zero"), OP.mult, OP.add, 2.0 ** -68)
+    tt(v("n4", 0, 16), v("PW2", 0, 16), v("DG", 0, 16), OP.mult)
+    total(v("wq"), v("n4", 0, 16))
+    tt(v("n4", 16, 24), v("PW2", 0, 128, 16), v("blk8F"), OP.mult)
+    total(v("wp"), v("n4", 16, 24))
+    ts(v("wp"), v("wp"), v("wq"), OP.mult, 2.5 * 2.0 ** -60, OP.mult)
+    line(v("n3"), v("DG"), -2.0 ** 90, 2.0 ** 90)
+    ts(v("THR"), v("n3"), v("wp"), OP.max)
+    ts(v("BW"), v("f2", 0, 64), v("p4F"), OP.is_equal, v("wq"), OP.mult)
 
     def counts(h):
         lo, hi = 128 * h, 128 * h + 128
         ts(v("val", lo, hi), v("Cd", lo, hi), MID, OP.is_lt)
-        scan(v("cum", lo, hi), v("RS", lo, hi), v("val", lo, hi), OP.mult, OP.add)
+        scan(v("cum", lo, hi), v("RS", 0, 128), v("val", lo, hi), OP.mult, OP.add)
 
-    ts(v("tV"), v("IV"), -MID, OP.add)
-    ts(v("tC"), v("IC"), -MID, OP.add)
-    turn(("pb4", 0), "tV")
+    line(v("tV"), v("IV"), 1.0, -MID)
+    line(v("tC"), v("IC"), 1.0, -MID)
     turn(("pb7", 0), "tC")
-    cp(v("V"), v("pb4", 0, 256))
-    cp(v("LNF", p=8), v("LNI", p=8))
-    cp(v("THF", 0, 1, p=8), v("THI", p=8))
-    ts(v("G8", p=8), v("mg", p=8), v("pcF", p=8), OP.is_equal)
     for h in range(2):
-        mm(v("pb2", 8 * h, 8 * h + 8), v("LNF", 128 * h, 128 * h + 128, p=8), v("IdF", 0, 8, p=8))
+        mm(bank("old", h), v("tV", 128 * h, 128 * h + 128), v("IdH"))
+        act(v("V", 128 * h, 128 * h + 128), bank("old", h))
+    act(v("LNF", p=8), v("LNI", p=8))
+    cp(v("THF", 0, 1, p=8), v("THI", p=8))
+    for h in range(2):
+        mm(v("pb2", 8 * h, 8 * h + 8), v("LNF", 128 * h, 128 * h + 128, p=8), v("IdF", p=8))
     cp(v("nn"), v("pb2", 0, 16))
     tt(v("m4"), bc("nn"), v("QC"), OP.is_le)
     line(v("m5"), v("m4"), 4096.0, -MID)
     tt(v("Cd"), v("pb7", 0, 256), v("m5"), OP.max)
-    if not MAXES:
-        mm(v("pb5", 256, 512), v("IdH"), v("Cd"))
     ts(v("s3"), v("nn"), 1.0, OP.min, -8192.0, OP.mult)
     tt(v("s2"), v("s3"), v("TR"), OP.add)
     tt(v("V0"), v("V", 0, 256, 16), v("s2"), OP.max)
@@ -660,347 +687,359 @@ def rank_program(g, core, T, topo):
     ts(v("tI"), v("tI"), 31, OP.bitwise_and)
     ts(v("e1"), v("pmF"), 0.0, OP.is_equal, KZ, OP.mult)
     ts(v("eK"), v("pmF"), 1.0, OP.is_equal, KZ, OP.mult)
-    ts(v("e4"), v("pmF"), 2.0, OP.is_equal, -4096 * KZ, OP.mult)
+    ts(v("e4"), v("pmF"), 15.0, OP.is_equal, -4096 * KZ, OP.mult)
     tt(v("e2"), v("pb3", 0, 1), v("tI"), OP.subtract)
     ts(v("e2"), v("e2"), -4096.0, OP.add, v("e1"), OP.mult)
     ts(v("e3"), v("tI"), 0.5, OP.add, v("eK"), OP.mult)
     ts(v("thm"), v("e2"), v("e3"), OP.add, v("e4"), OP.add)
     ts(v("LIM"), v("blkl"), v("thm"), OP.mult)
 
-    def dedupe(gap1, gap2, values, who):
-        tt(v("Ez"), ind(v("zs"), v("bcZ")), v("DG"), OP.mult)
-        for h in range(2):
-            mm(bank("zU", 496 + 8 * h, 504 + 8 * h), v("Ez", 128 * h, 128 * h + 128), v("blk8H"))
-        move("z" + who, v("zz"), bank("zU", 496, 512))
-        if SPLIT:
-            for h in (1, 0):
-                lo, hi = 128 * h, 128 * h + 128
-                act(v("Wz", lo, hi), ind(v("zs"), v("bcZ", 8 * h, 8 * h + 8)))
-                mm(bank("Ru", lo, hi, h), v("Wz", lo, hi), v("IdH"))
-                move(who + str(h), v("Ru", lo, hi), bank("Ru", lo, hi, h))
-        else:
-            act(v("Wz"), ind(v("zs"), v("bcZ")))
-            turn(("pb0", 0), "Wz")
-            move(who + "0", v("Ru"), v("pb0", 0, 256))
-        gap1()
-        for a in list(range(8, 16)) + list(range(8)):
-            ts(v("EQ", 272 * a, 256 * a + 256), v("Ru", 16 * a, 256), v("zz", a, a + 1), OP.is_equal)
-            for h in range(a // 8, 2):
-                k = a % 8 if h == a // 8 else 8
-                mm(v("pb2", 64 * h, 64 * h + 64), v("EQ", 256 * a + 128 * h, 256 * a + 128 * h + 128), v("BW", 64 * k, 64 * k + 64), a == 8, a + h == 8 and a == 7)
-        gap2()
-        for k in range(2):
-            out = v("El", k, 256, 2)
-            tt((out[0], v("El", 128 * k, 128 * k + 128)[1]) + out[2:], v("pb2", 0, 128), v("THR", k, 256, 2), OP.is_ge)
-        mm(v("pb3", 0, 16), v("CQ"), v("ones", 0, 16), True, False)
-        for h in range(2):
-            el = v("El", 128 * h, 128 * h + 128)
-            mm(v("pb3", 8 * h, 8 * h + 8), (el[0], v("El")[1]) + el[2:], v("BMh", 8 * h, 8 * h + 8), False, h == 1)
-        tt(v("oA"), v("pb3", 0, 16), v("zz"), OP.max)
-        ts(v("off16"), v("oA"), MID, OP.add)
-        if len(values) == 1:
-            cp(ind(v("X"), v("off16")), v(values[0]))
-        else:
-            tt(ind(v("X"), v("off16")), v(values[0]), v(values[1]), OP.add)
+    def dedupe(n, h):
+        zz, Ru, Em = "zz" + n, "Ru" + n, "Em" + n
+        for x in each(h):
+            lo, hi, a, b = span(x)
+            hold("Wz" + n, "zs" + n, x, 1 if n == "1" else 3)
+            alone(v("Ez" + n, lo, hi), v("Wz" + n, lo, hi), v("DG"))
+            mm(bank("zU" + n, x, 0, 8), v("Ez" + n, lo, hi), v("blk8H"))
+            mm(bank(Ru, x), v("Wz" + n, lo, hi), v("IdH"))
+        for x in each(h) if Ru in APART else (h,):
+            move(Ru, x, v(Ru, *span(x)[:2]), bank(Ru, x))
+        move(zz, h, v(zz, *span(h)[2:]), bank("zU" + n, h, 0, 8))
+        for x in each(h):
+            lo, hi, a, b = span(x)
+            for k in range(8):
+                at = 128 * (a + k)
+                ts(v("EQ", at + 16 * k, at + 128), v(Ru, lo + 16 * k, hi), v(zz, a + k, a + k + 1), OP.is_equal, 2.0 ** (-16 * k), OP.mult)
+                mm(bank("sum" + n, x, 0, 64), v("EQ", at, at + 128), v("BW"), k == 0, k == 7)
+            for k in range(2):
+                out = v(Em, lo + k, hi, 2)
+                tt((out[0], v(Em, lo + 64 * k, lo + 64 * k + 64)[1]) + out[2:], bank("sum" + n, x, 0, 64), v("THR", k, 128, 2), OP.is_ge)
+            mms(bank("off" + n, x, 0, 8), [(v("CQ", p=1), v("ones", 0, 8, p=1)), (v(Em, lo, hi), v("BMh", a, b))])
+        for x in each(h) if "off" + n in APART else (h,):
+            a, b = span(x)[2:]
+            move("off" + n, x, v("oA" + n, a, b), v(zz, a, b), 1.0, MID)
+            tt(v("off" + n, a, b), bank("off" + n, x, 0, 8), v("oA" + n, a, b), OP.max)
 
-    def message(m, bufs, t, cost, after=()):
+    def message(m, h, out, land, t, cost, after=()):
         d = 1 + t % 3
         dst, src = T.cores[(rank + d) % 4], T.cores[(rank - d) % 4]
         rid, pid, _se = topo.addr(dst)
-        land, asem, lsem = "r%s%d" % (m, t), "a%s%d" % (m, t), "l" + m
+        asem, lsem = "a%s%d%d" % (m, h % 2, t), "l%s%d" % (m, h % 2)
 
         def emit(rd, wr):
             wait("G", need("G", rd, wr))
-            if len(bufs) == 1:
-                g.remote_dma(T[land][:], T[bufs[0]][:], T.sem[asem], T.sem[lsem], pid, rid, topo.mask(core, dst))
-            else:
-                g.remote_dma_fused([RemoteDMATransfer(dst_ids=[DstId(rid=rid, pnc=pid)], dma_engine_mask=topo.mask(core, dst), remote_sem=T.sem[asem],
-                                                      srcs=[T[x][:] for x in bufs], dsts=[T[land][:]], alu_op=2)], local_sem=T.sem[lsem])
+            g.remote_dma(land[0], out[0], T.sem[asem], T.sem[lsem], pid, rid, topo.mask(core, dst))
             record("Gr", bump("G", lsem, len(topo.engines(core, dst))), rd, wr)
-        sent = add("G", emit, [v(x) for x in bufs], [], ISSUE, cost)
+        sent = add("G", emit, [out], [], ISSUE, cost)
         OPS[sent][7] += after
 
         def came(rd, wr):
             n = len(topo.engines(src, core))
             count[asem] = n
             clock[(asem, n)] = {}
-            recs[land] = [(0, 99999, (asem, n), "far", True)]
-        add("F", came, [], [v(land)], 0.0, 0.0, [sent])
+            recs.setdefault(wr[0][0], []).append(wr[0][1:] + ((asem, n), "far", True))
+        add("F", came, [], [land], 0.0, 0.0, [sent])
         return sent
 
     counts(0)
     counts(1)
     for t in range(ST):
-        rK, rY, rP, rB = "rK%d" % t, "rY%d" % t, "rP%d" % t, "rB%d" % t
+        rK, rC, rB, rY = "rK%d" % t, "rC%d" % t, "rB%d" % t, "rY%d" % t
         lastt = t == ST - 1
-        turns = [0]
+        turns, short, part[1] = [0], {}, t
+
+        def diff(n):
+            turns[0] += 1
+            return "pb" + DIFF[(turns[0] - 1) % len(DIFF)], 0, n
 
         def bends(h):
-            GV, DC, at = "GV%d" % h, "DC%d" % h, 0
+            GV, DC, DV, AB, at = "GV%d" % h, "DC%d" % h, "DV%d" % h, "AB%d" % h, 0
             for who, how, n in RUNS[h]:
                 lo, hi, lst = 16 * at, 16 * (at + n), (128 * h + at, 128 * h + at + n)
                 src = ind(v("X", 0, W), v("LV", *lst))
-                if who == "S":
-                    line(v(GV, lo, hi), src, -0.5, 0.0)
+                if who[0] == "S":
+                    line(v(GV, lo, hi), src, -0.5, -96.0)
                 else:
-                    ts(v(GV, lo, hi), src, -0.5, OP.mult)
+                    ts(v(GV, lo, hi), src, -0.5, OP.mult, -96.0, OP.add)
                 at += n
             at = 0
             for who, how, n in RUNS[h]:
                 lo, hi, lst = 16 * at, 16 * (at + n), (128 * h + at, 128 * h + at + n)
-                tt(v(DC, lo, hi), ind(v("X", 0, XW if t else W), v("LC", *lst)), v(GV, lo, hi), OP.add)
-                ab = v("AB%d" % h, 14 * at, 14 * (at + n))
-                if AS == 16:
-                    ab = v("AB%d" % h, lo, hi - 1)
-                    if how == "V":
-                        tt(ab, v(DC, lo, hi - 1), v(GV, lo + 1, hi), OP.add)
-                        act(ab, ab, AF.Abs)
-                    elif how == "D":
-                        if at + n == NDMA[h] or (at + n) % DRUN == 0:
-                            lo = 16 * ((at + n - 1) // DRUN * DRUN)
-                            addto(v(DC, lo, hi - 1), v(GV, lo + 1, hi), "e%d%d" % (h, lo // 16 // DRUN))
-                            act(v("AB%d" % h, lo, hi - 1), v(DC, lo, hi - 1), AF.Abs)
-                    else:
-                        pb = v("pb" + DIFF[turns[0] % len(DIFF)], 0, hi - lo - 1)
-                        turns[0] += 1
-                        mms(pb, [(v("Ident"), v(GV, lo + 1, hi)), (v("Ident"), v(DC, lo, hi - 1))])
-                        act(ab, pb, AF.Abs)
-                elif how == "V":
-                    tt(v("DV", 0, hi - lo), v(DC, lo, hi), v(GV, lo + 1, hi + 1), OP.add)
-                    act(ab, v("DV", 0, hi - lo, -1), AF.Abs)
+                src = ind(v("X", 0, XW if t else W), v("LC", *lst))
+                if who[1] == "S":
+                    act(v("CG%d" % h, lo, hi), src)
+                    scan(v(DC, lo, hi), v("CG%d" % h, lo, hi), v(GV, lo, hi), OP.max, OP.add)
                 else:
-                    pb = "pb" + DIFF[turns[0] % len(DIFF)]
-                    turns[0] += 1
-                    mms(v(pb, 0, hi - lo), [(v("Ident"), v(GV, lo + 1, hi + 1)), (v("Ident"), v(DC, lo, hi))])
-                    act(ab, v(pb, 0, hi - lo, -1), AF.Abs)
+                    tt(v(DC, lo, hi), src, v(GV, lo, hi), OP.add)
+                if how == "T":
+                    pb = diff(hi - lo)
+                    mms(v(*pb), [(v("Ident"), v(GV, lo + 1, hi + 1)), (v("Ident"), v(DC, lo, hi))])
+                    ab = 2 * max(k[0] for k in KEYS[h] if k[0] <= at) + 14 * at
+                    act(v(AB, ab, ab + 14 * n), v(*pb, -1), AF.Abs, 1.0, 192.0)
+                elif how != "M":
+                    scan(v(DV, lo, hi - 2), v(GV, lo + 1, hi - 1), v(DC, lo, hi - 2), OP.max, OP.add, -256.0)
+                    size(how, v(AB, lo, hi - 2), v(DV, lo, hi - 2))
                 at += n
+            if how == "M":
+                at = 0
+                for how, n in SLOTS[h]:
+                    out = v(AB, 128 * at, 128 * (at + n))
+                    pb = diff(128 * n) if how == "T" else None
+                    for s in range(at, at + n):
+                        a, b = v(GV, s + 1, 2048, 16), v(DC, s, 2048, 16)
+                        if pb:
+                            for k, x in enumerate((a, b)):
+                                mm(v(pb[0], 128 * (s - at), 128 * (s - at + 1)), v("Ident"), x, s == at and k == 0, s == at + n - 1 and k == 1)
+                        else:
+                            scan(v(DV, 128 * s, 128 * s + 128), a, b, OP.max, OP.add, -256.0)
+                    size(how, out, v(*pb) if pb else v(DV, 128 * at, 128 * (at + n)))
+                    at += n
+
+        def size(how, out, a):
+            if how == "R":
+                ts(out, a, -192.0, OP.max, 96.0, OP.add)
+            else:
+                act(out, a, AF.Abs, 1.0, 192.0)
 
         def gates(h):
             lo, hi, a, b = 128 * h, 128 * h + 128, 8 * h, 8 * h + 8
-            move("ng", v("ng", a, b), last("cum", a, b), 1.08, -2.29)
-            tt(v("sgp", lo, hi), bc("ng", h), v("cum", lo, hi), OP.is_ge)
+            hold("rc", "val", h)
+            ts(v("sgp", lo, hi), v("rc", lo, hi), 3.0, OP.is_ge, -2.0, OP.add)
+            ts(last("sgp", a, b), last("cum", a, b), 4.0, OP.is_ge, -3.0, OP.mult)
 
         def key(h):
             lo, hi = 128 * h, 128 * h + 128
-            pb = "pb%d" % (2 + h)
-            k = v(pb, 0, 128)
-            mm(k, v("ones"), v("CR"), True, False)
+            k = bank("key", h)
+            mm(k, v("ones", p=1), v("CR", p=1), True, False)
             mm(k, v("Ibig"), v("val", lo, hi), False, False)
             whole = len(KEYS[h]) == 1
             if whole:
                 mm(k, v("Ibig"), v("sgp", lo, hi), False, False)
-            for p0, p1 in KEYS[h]:
+            terms = []
+            for p0, p1, how in KEYS[h]:
                 for s in range(14):
-                    mm(v(pb, s, 128, 16, (p0, p1)), v("AB%d" % h, AS * p0 + s, AS * p1, AS), v("BKk"), False, s == 13 and whole)
+                    out, kind = bank("key", h, s, 128, 16, (p0, p1)), how
+                    if how == "T":
+                        at = (16 * p0 + s, 16 * p0 + 14 * (p1 - p0), 14)
+                    elif how == "M":
+                        at, kind = (128 * s, 128 * s + 128), "".join(c * n for c, n in SLOTS[h])[s]
+                    else:
+                        at = (16 * p0 + s, 16 * p1 - 15 + s, 16)
+                    if kind == "R":
+                        mm(out, v("DV%d" % h, *at), v("BKn"), False, False)
+                    terms.append((out, v("AB%d" % h, *at), v("BK2" if kind == "R" else "BKk")))
+            for o, l, r in terms:
+                mm(o, l, r, False, whole and o is terms[-1][0])
             if not whole:
                 mm(k, v("Ibig"), v("sgp", lo, hi), False, True)
 
         def pick(h):
             lo, hi, a, b = 128 * h, 128 * h + 128, 8 * h, 8 * h + 8
-            pb, lst, abc = "pb%d" % (2 + h), "olist%d" % h, "pabc%d" % h
-            scan(v("SK", lo, hi), v("RSk", 0, 128), v(pb, 0, 128), OP.min, OP.max, 31.0)
-            ts(v("KA", a, b), last("SK", a, b), 992, OP.bitwise_and)
-            tt(v("El", lo, hi), bc("KA", h), v("DG", lo, hi), OP.mult)
-            o = v(pb, 128, 152)
+            lst, abc, OH, Yn = "olist%d" % h, "pabc%d" % h, v("OH", lo, hi), v("Yn", lo, hi)
+            scan(v("av", lo, hi), v("NR"), v("val", lo, hi), OP.max, OP.min)
+            scan(v("SK", lo, hi), v("RSk"), bank("key", h), OP.min, OP.max, 31.0)
+            ts(last("KA", a, b), last("SK", a, b), 992, OP.bitwise_and)
+            hold("Dk", "KA", h)
+            if QUICK[h]:
+                tt(v("El", lo, hi), ind(v("KA", lo, hi), v("bcK", 0, 8)), v("DG"), OP.mult)
+            else:
+                alone(v("El", lo, hi), v("Dk", lo, hi), v("DG"))
+            o = bank("o", h, 0, 24)
             mms(o, [(v("IdH"), v("OB")), (v("El", lo, hi), v("BM32"))])
-            ts(v(lst), o, v("eO"), OP.add)
+            ts(v(lst), o, v("eQ" if QUICK[h] else "eO"), OP.add)
             for who, c0, c1 in YGATHER[h]:
                 (cp if who == "V" else act)(v(abc, 128 * c0, 128 * c1), ind(v("GD%d" % h), v(lst, 8 * c0, 8 * c1)))
-            y = v(pb, 256, 384)
-            mm(y, v("Ih"), v(abc, 0, 128), True, False)
-            nd = NDMA[h]
-            if nd:
-                mm(v(pb, 256, 256 + nd), v("Ih"), v(abc, 256, 256 + nd), False, False)
-            if nd < 128:
-                mm(v(pb, 256 + nd, 384), v("Ident"), v(abc, 256 + nd, 384), False, False)
-            mm(y, v("Ih"), v(abc, 128, 256), False, True)
-            yh = v("pb4", 256 + lo, 256 + hi)
-            ts(yh, y, 0.0, OP.min, -31.5, OP.max)
-            ts(v("Y", lo, hi), yh, -2.0, OP.mult)
-            mm(bank("u", 256 + a, 256 + b), v("Y", lo, hi), v("W8"))
-            tt(v("OH", lo, hi), bc("KA", h), v("i32s", 0, 128), OP.is_equal)
-            scan(v("sk", lo, hi), v("RS", lo, hi), v("OH", lo - 1, hi - 1), OP.mult, OP.add)
+            y = bank("y", h)
+            mms(y, [(v("Ih"), v(abc, 0, 128)), (v("Ih"), v(abc, 128, 256)), (v("Ident"), v(abc, 256, 384))])
+            ts(Yn, y, -192.0, OP.min, -223.5, OP.max)
+            move("Y", h, v("Y", lo, hi), Yn, -2.0, -384.0)
+            ts(OH, v("Dk", lo, hi), 32.0, OP.is_equal)
+            ts(v("sk", lo, hi), v("Dk", lo, hi), 64.0, OP.is_ge)
             scan(v("dd", lo, hi), v("val", lo, hi), v("sk", lo, hi), OP.add, OP.mult)
-            scan(v("ee", lo, hi), v("val", lo, hi), v("sk", lo, hi), OP.max, OP.min)
-            p = bank("PW", lo, hi, h)
-            mms(p, [(v("IdH"), v("V", lo, hi)), (v("In4k"), v("dd", lo, hi))])
-            line(v("PW", lo, hi), p, 1.0, 69632.0 + MID)
-            if MAXES:
-                p1, p2 = bank("P1", 256 + lo, 256 + hi, h), bank("P2", lo, hi, h)
-                mms(p1, [(v("IdH"), v("V", lo, hi)), (v("I8k"), v("OH", lo, hi))])
-                scan(v("m4", lo, hi), v("RSm", 0, 128), p1, OP.min, OP.max, -4097.0)
-                mms(p2, [(v("IdH"), v("VK", lo + 1, hi + 1)), (v("I8k"), v("OH", lo, hi))])
-                line(v("m3", lo, hi), p2, 1.0, -8192.0)
-                scan(v("m5", lo, hi), v("RSn", 0, 128), v("m3", lo, hi), OP.min, OP.max, -16384.0)
+            scan(v("ee%d" % h), v("val", lo, hi), v("sk", lo, hi), OP.max, OP.min)
+            mms(bank("PW", h), [(v("IdH"), v("V", lo, hi)), (v("In4k"), v("dd", lo, hi))])
+            move("PW", h, v("PW", lo, hi), bank("PW", h), 1.0, 69632.0 + MID)
+            alone(v("m2", lo, hi), v("V", lo, hi), OH)
+            alone(v("m3", lo, hi), v("VK", lo + 1, hi + 1), OH)
+            scan(v("m4", lo, hi), v("RS", 0, 128), v("m2", lo, hi), OP.mult, OP.add)
+            scan(v("m5", lo, hi), v("RS", 0, 128), v("m3", lo, hi), OP.mult, OP.add)
+            alone(v("i1", lo, hi), v("Cd", lo, hi), OH)
+            mms(bank("Cx", h), [(v("IdH"), v("Cd", lo, hi)), (v("IdH"), v("m3", lo, hi)), (v("InH"), v("i1", lo, hi))])
+
+        def hashed(h):
+            lo, hi, a, b = span(h)
+            for x in each(h):
+                mm(bank("u", x, 0, 8), v("Y", *span(x)[:2]), v("W8"))
+            move("Kp", h, v("Kp", a, b), last("m4", a, b), 1184.0, -1184.0 * MID)
+            move("UI", h, v("UI", a, b), bank("u", h, 0, 8))
+            ts(v("UI", a, b), v("UI", a, b), 4095, OP.bitwise_and)
+            if WHO["sq"][h % 2] == "V":
+                tt(v("sq", a, b), v("UI", a, b), v("UI", a, b), OP.mult)
             else:
-                tt(v("m2", lo, hi), v("OH", lo, hi), v("pb4", lo, hi), OP.mult)
-                tt(v("m3", lo, hi - 1), v("OH", lo, hi - 1), v("pb4", lo + 1, hi), OP.mult)
-                scan(v("m4", lo, hi), v("RS", lo, hi), v("m2", lo, hi), OP.mult, OP.add)
-                scan(v("m5", lo, hi), v("RS", lo, hi), v("m3", lo, hi), OP.mult, OP.add)
+                act(v("sq", a, b), v("UI", a, b), AF.Square)
+            tt(v("HI", a, b), v("sq", a, b), v("Kp", a, b), OP.add)
+            ts(v("HI", a, b), v("HI", a, b), 5, OP.arith_shift_right, 4095, OP.bitwise_and)
+            move("x", h, v("x", a, b), v("HI", a, b), 1.0, -MID)
+            tt(v("hh", a, b), v("x", a, b), v("s1", a, b), OP.max)
 
         def near(h):
             lo, hi = 128 * h, 128 * h + 128
-            pb, GV, EE = "pb" + BANK["z"][h], "GV%d" % h, "EE%d" % h
-            z = v(pb, 384, 512)
-            mm(z, v("ones"), v("LIM"), True, False)
-            mm(z, v("IZv"), v("val", lo, hi), False, False)
+            GV, EE = "GV%d" % h, "EE%d" % h
+            z = bank("z", h)
+            mm(z, v("IZv"), v("val", lo, hi), True, False)
             first = 2 + NABS[h]
             for s in range(first, 16):
-                mm(v(pb, 384 + s, 512, 16), v(GV, s, 2048, 16), v("GVw"), False, False)
+                mm(bank("z", h, s, 128, 16), v(GV, s, 2048, 16), v("GVw"), False, False)
+            mm(z, v("ones"), v("LIM"), False, False)
+            mm(z, v("IZv"), v("ee%d" % h, -1, 127), False, False)
             if first < 16:
                 mm(z, v("Y", lo, hi), v("Yw%d" % h), False, False)
-            mm(z, v("IZv"), v("ee", lo - 1, hi - 1), False, False)
-            nt = 2 + (NT if h == 0 else 0)
-            for s0 in range(2, nt, 4):
-                s1 = min(s0 + 4, nt)
-                for s in range(s0, s1):
-                    mms(bank("ET", 128 * (s - s0), 128 * (s - s0 + 1), (s0 // 4) % len(BANK["ET"])), [(v("Ident"), v(GV, s, 2048, 16)), (v("Ih"), v("Y", lo, hi))])
-                act(v(EE, 128 * s0 - 256, 128 * s1 - 256), bank("ET", 0, 128 * (s1 - s0), (s0 // 4) % len(BANK["ET"])), AF.Abs)
-            for s in range(nt, 16):
-                tt(v(EE, 128 * s - 256, 128 * s - 128), v(GV, s, 2048, 16), v("pb4", 256 + lo, 256 + hi), OP.subtract if s < first else OP.min)
-            for s0 in range(nt, first, NRUN):
-                e = v(EE, 128 * s0 - 256, 128 * min(s0 + NRUN, first) - 256)
-                act(e, e, AF.Abs)
             for s in range(2, 16):
-                mm(v(pb, 384 + s, 512, 16), v(EE, 128 * s - 256, 128 * s - 128), v("ABw" if s < first else "EEw"), False, s == 15)
+                scan(v(EE, 128 * s - 256, 128 * s - 128), v("Yn", lo, hi), v(GV, s, 2048, 16), OP.min, OP.subtract)
+            for s0 in range(2, first, NRUN[0]):
+                e = v(EE, 128 * s0 - 256, 128 * min(s0 + NRUN[0], first) - 256)
+                act(e, e, AF.Abs, 1.0, 96.0)
+            for s0 in range(first, 16, NRUN[1]):
+                e = v(EE, 128 * s0 - 256, 128 * min(s0 + NRUN[1], 16) - 256)
+                ts(e, e, -96.0, OP.max, 144.0, OP.add)
+            for s in range(2, 16):
+                mm(bank("z", h, s, 128, 16), v(EE, 128 * s - 256, 128 * s - 128), v("GVw" if s < first else "EEw"), False, s == 15)
             tt(v("m1", lo, hi), z, v("PW", lo, hi), OP.min)
-            scan(v("SM", lo, hi), v("RSm", 0, 128), v("m1", lo, hi), OP.min, OP.max, -4097.0)
+            scan(v("SM", lo, hi), v("RSm"), v("m1", lo, hi), OP.min, OP.max, -4097.0)
 
-        ts(v("s6"), last("cum"), 4.0, OP.is_lt, -8192.0, OP.mult)
-        tt(v("s1"), v("TRm"), v("s6"), OP.subtract)
-        message("K", ["VK"], t, FAR + 2.0)
-        ts(v("s7"), last("cum"), 4.0, OP.is_lt, 16.0, OP.mult)
-        tt(v("th2"), v("s7"), last("cum"), OP.subtract)
-        scan(v("av"), v("NR"), v("val"), OP.max, OP.min)
-        for part in PARTS.split():
-            {"b": bends, "g": gates, "k": key, "p": pick, "n": near}[part[0]](int(part[1]))
-        move("SB", v("SB", 16, 32), last("m5"))
-        move("Kp", v("Kp"), last("m4"), 1184.0, -1184.0 * (MID + 8192 * MAXES))
-        move("UI", v("UI"), bank("u", 256, 272))
-        ts(v("UI"), v("UI"), 4095, OP.bitwise_and)
-        if WHO["sq"] == "V":
-            tt(v("sq"), v("UI"), v("UI"), OP.mult)
-        else:
-            act(v("sq"), v("UI"), AF.Square)
-        tt(v("HI"), v("sq"), v("Kp"), OP.add)
-        ts(v("HI"), v("HI"), 5, OP.arith_shift_right, 4095, OP.bitwise_and)
-        move("x", v("x"), v("HI"), 1.0, -MID)
-        tt(v("hh"), v("x"), v("s1"), OP.max)
-        if MAXES:
-            mms(v("pb5", 0, 256), [(v("IdH"), v("Cd")), (v("In8k"), v("OH"))])
-            tt(v("pb5", 0, 256), v("pb5", 0, 256), v("m3"), OP.max)
-        else:
-            tt(v("i1"), v("OH"), v("pb5", 256, 512), OP.mult)
-            mms(v("pb5", 0, 256), [(v("IdH"), v("Cd")), (v("IdH"), v("m3")), (v("InH"), v("i1"))])
-        near(1 - int(PARTS[PARTS.index("n") + 1]))
-        ts(v("SB", 0, 16), last("SM"), 12, OP.logical_shift_right)
-        short = message("B", ["SB"], t, FAR)
-        tt(v("kn"), last("SM"), v("TR"), OP.min)
-        tt(v("zs", 1, 32, 2), v("kn"), v("hh"), OP.max)
-        tt(v("grow", 0, 16), last("SM"), v("s6"), OP.is_lt)
-        F = bank("F", 256, 512)
+        def closed(h):
+            a, b = span(h)[2:]
+            ts(v("SB", a, b), last("SM", a, b), 12, OP.logical_shift_right)
+            short[h] = message("B", h, v("SB", a, b), v(rB, a, b), t, FAR)
+            tt(v("kn", a, b), last("SM", a, b), v("TR", a, b), OP.min)
+            tt(last("zs1", a, b), v("kn", a, b), v("hh", a, b), OP.max)
+            tt(v("grow", 16 * a + 14, 16 * b, 16), last("SM", a, b), v("s6", a, b), OP.is_lt)
 
-        def gap1():
-            line(v("gw"), ind(v("grow"), v("bcG")), 1.0, 0.125)
-            act(v("sgm"), v("SM"), AF.Sign, 1.0, 0.5)
-            Z = bank("Z", 0, 256)
-            mms(Z, [(v("Za"), v("av")), (v("Zk"), v("sk")), (v("Zo"), v("OH")), (v("Zo"), v("sgm")), (v("Zg"), v("gw"))])
-            tt(v("Cp"), Z, v("Cd"), OP.max)
-            message("C", ["YC"], t, FAR + 1.5, [short])
-            act(v("Zs"), Z, AF.Abs, 1.0 / ZU, -8.625)
-            ts(v("FF"), v("Zs"), 9.25, OP.is_ge)
-            ts(v("Fu"), v("Zs"), 9.125, OP.is_equal)
-            mm(F, v("Ident"), v("FF"), True, False)
-            mm(F, v("Ident"), v("Fu", -1, 255), False, not KEEPF, True)
-            ts(v("mP"), v("Zs"), 6.125, OP.is_equal)
-            ts(v("Dn"), v("Zs"), 8.375, OP.is_equal)
-            ts(v("VM"), last("SM"), 4095, OP.bitwise_and)
-            move("s5", v("s5"), v("VM"), 1.0, -MID)
-            tt(v("s2"), v("s5"), v("zs", 1, 32, 2), OP.min)
-            act(v("xw"), bc("s2"))
-            if MAXES:
-                move("kc", v("kc"), v("kn"), 1.0, 8192.0)
-                tt(v("kc"), last("m4"), v("kc"), OP.max)
-                line(v("kw"), bc("kc"), 1.0, -8192.0)
+        def codes(h):
+            lo, hi, a, b = span(h)
+            Z, Zs = bank("Z", h), v("Zs", lo, hi)
+            if WHO["gw"][h % 2] == "S":
+                act(v("gw", lo, hi), ind(v("grow", lo, hi), v("bcG", 0, b - a)))
             else:
-                tt(v("kc"), last("m4"), v("kn"), OP.max)
-                act(v("kw"), bc("kc"))
-            tt(v("dz", 1, 32, 2), v("V0"), v(rK, 256, 272), OP.max)
-            tt(v("dz", 0, 32, 2), v(rB, 16, 32), v("dz", 1, 32, 2), OP.subtract)
+                hold("gw", "grow", h, 1, "RS2")
+            if WHO["sgm"][h % 2] == "S":
+                act(v("sgm", lo, hi), v("SM", lo, hi), AF.Sign, 1.0, 0.5)
+            else:
+                ts(v("sgm", lo, hi), v("SM", lo, hi), 0.0, OP.is_lt, -0.5, OP.add)
+            terms = [("ones", "CZ"), ("Za", "av"), ("Zk", "sk"), ("Zo", "OH"), ("Zo" if WHO["sgm"][h % 2] == "S" else "Zk", "sgm"), ("Zg", "gw")]
+            mms(Z, [(v(l, p=1), v(r, 0, hi - lo, p=1)) if r == "CZ" else (v(l), v(r, lo, hi)) for l, r in terms])
+            tt(v("Cp", lo, hi), Z, v("Cd", lo, hi), OP.max)
+            act(Zs, Z, AF.Abs, 1.0 / ZU, -8.625)
+            ts(v("FF", lo, hi), Zs, 9.25, OP.is_ge)
+            ts(v(pad("Fu", h)), Zs, 9.125, OP.is_equal)
+            mms(bank("F", h), [(v("Ident"), v("FF", lo, hi)), (v("Ident"), v(pad("Fu", h), -1, hi - lo - 1))])
+            ts(v(pad("mP", h)), Zs, 6.125, OP.is_equal)
+            ts(v("Dn", lo, hi), Zs, 8.375, OP.is_equal)
+            ts(v("VM", a, b), last("SM", a, b), 4095, OP.bitwise_and)
+            move("s5", h, v("s5", a, b), v("VM", a, b), 1.0, -MID)
+            if WHO["Fc"][h % 2] == "S":
+                act(v("Fc", lo, hi), Z, AF.Relu, -1.0 / ZU)
+            else:
+                ts(v("Fc", lo, hi), Zs, 9.5, OP.is_ge)
+            if WHO["xw"][h % 2] == "S":
+                tt(v("s2", a, b), v("s5", a, b), last("zs1", a, b), OP.min)
+                act(v("xw", lo, hi), bc("s2", h))
+            else:
+                tt(last("sx", a, b), v("s5", a, b), last("zs1", a, b), OP.min)
+                hold("xw", "sx", h)
 
-        def gap2():
-            tt(v("fxV"), F, v("xw"), OP.mult)
-            tt(v("fxC"), F, v("kw"), OP.mult)
-            for h in range(2):
-                lo, hi = 128 * h, 128 * h + 128
-                for b, x in (("pb4", "V"), ("pb5", "C")):
-                    tt(v("up" + x, lo + 1, hi), v("mP", lo, hi - 1), v(b, lo, hi - 1), OP.mult)
-                    tt(v("dn" + x, lo, hi - 1), v("Dn", lo, hi - 1), v(b, lo + 1, hi), OP.mult)
+        def moved(h):
+            lo, hi = 128 * h, 128 * h + 128
+            for old, x, new in (("old", "V", "xw"), ("Cx", "C", "m4")):
+                tt(v("fx" + x, lo, hi), bank("F", h), v(new, lo, hi), OP.mult)
+                tt(v("up" + x, lo + 1, hi), v(pad("mP", h), 0, 127), bank(old, h, 0, 127), OP.mult)
+                tt(v("dn" + x, lo, hi - 1), v("Dn", lo, hi - 1), bank(old, h, 1, 128), OP.mult)
+
+        def piece(h):
+            lo, hi = span(h)[:2]
+            message("C", h, v("Cp", lo, hi), v(rC, lo, hi), t, FAR + LATER * (hi - lo) / 256, [short.get(h, short.get(2, short.get(0)))])
+
+        def guess(h):
+            move("SB", 0, v("Vn"), last("m5"))
+            if h == 2:
+                message("Y", 0, v("VY"), v("rK%d" % t), t, FAR + 2 * LATER)
+            else:
+                message("Y", 0, v("YV"), v("rK%d" % t, 272, 544), t, FAR + LATER)
+            tt(v("dz", 2, 48, 3), v("V0"), v(rK, 256, 272), OP.max)
+            tt(v("dz", 1, 48, 3), v(rY, 256, 272), v("dz", 2, 48, 3), OP.subtract)
+
+        def shut(h):
             if not lastt:
                 act(v("s4"), last("SM"), AF.Sign, 1.0, 0.5, total=v("cs1"))
-                mm(bank("c", 0, 1), v("onesF"), v("cs1"))
-                move("cI", v("cI"), bank("c", 0, 1), 0.5, 1024.0)
+                mm(bank("c", h, 0, 1), v("onesF"), v("cs1"))
+                move("cI", h, v("cI"), bank("c", h, 0, 1), 0.5, 1024.0)
                 ts(v("cI"), v("cI"), 31, OP.bitwise_and)
                 line(v("lim"), v("cI"), v("eK"), v("thm"))
                 line(v("LIM"), v("blkl"), v("lim"), 0.0)
 
-        dedupe(gap1, gap2, ("Y",) if YS == 1 else ("Yb", "Yb"), "Ru1")
-        tt(v("take", 1, 32, 2), v(rB, 0, 16), v("th2"), OP.is_lt)
-        scan(v("zs"), v("take"), v("dz"), OP.mult, OP.add)
-        if not lastt:
-            tt(v("s3"), v("zs", 1, 32, 2), v("dz", 1, 32, 2), OP.subtract)
-            tt(v("V0"), v("V0"), v("s3"), OP.add)
-        tw = bank("tw", TW, TW + 256)
+        def takes(h):
+            a, b = span(h)[2:]
+            tt(third("take", h), v(rB, a, b), v("th2", a, b), OP.is_lt)
+            scan(third("zs2", h, 16), third("take", h, 16), v("dz", 3 * a, 3 * b), OP.mult, OP.add)
 
-        def gap3():
-            move("z16", v("z16"), v("zz"), 1.0, MID)
-            act(v("tw"), ind(v("take"), v("bcZ")))
-            if WHO["tw"] == "S":
-                act(tw, v("tw"))
+        def stays(h):
+            lo, hi, a, b = span(h)
+            if WHO["tw"][h % 2] == "S":
+                act(v("tw", lo, hi), ind(v("take", 3 * lo, 3 * hi), v("bcT", 0, b - a)))
             else:
-                mm(tw, v("Ident"), v("tw"))
-            if KEEPF:
-                for x, k in (("mP", 1), ("Dn", 0), ("tw", 0)):
-                    mm(F, v("Ident"), v(x, -k, 256 - k), False, x == "tw")
-                line(v("keep"), F, -1.0, 1.0)
-            else:
-                keep = bank("keep", 256, 512)
-                mms(keep, [(v("In1"), v(x, -k, 256 - k)) for x, k in (("FF", 0), ("Fu", 1), ("mP", 1), ("Dn", 0), ("tw", 0))])
-                line(v("keep"), keep, 1.0, 1.0)
-            if WHO["blend"] == "S":
-                act(v("BL"), ind(v("X"), v("z16")))
-                mms(bank("bl", 256, 512), [(v("IdH" if YS == 1 else "I2H"), v(rY)), (v("Ident"), v("BL"))])
-                if WHO["round"] == "V":
-                    ts(v("iw"), bank("bl", 256, 512), 0.5, OP.mult, -0.25, OP.add)
-                else:
-                    line(v("g1"), bank("bl", 256, 512), 0.5, 191.75)
-            else:
-                tt(v("BL"), ind(v("X"), v("z16")), v(rY), OP.add)
-                move("half", v("g1"), v("BL"), 0.5, 191.75)
+                hold("tw", "take", h, 3)
+            mm(bank("tw", h), v("Ident"), v("tw", lo, hi))
+            mms(bank("keep", h), [(v("In1"), x) for x in (v("FF", lo, hi), v(pad("Fu", h), -1, hi - lo - 1), v(pad("mP", h), -1, hi - lo - 1), v("Dn", lo, hi), v("tw", lo, hi))])
+            move("keep", h, v("keep", lo, hi), bank("keep", h), 1.0, 1.0)
 
         def taken(h):
             lo, hi = 128 * h, 128 * h + 128
-            for old, x, came in (("pb4", "V", rK), ("pb5", "C", rP)):
-                tt(v("kp" + x, lo, hi), v("keep", lo, hi), v(old, lo, hi), OP.mult)
-                tt(v("in" + x, lo, hi), bank("tw", TW + lo, TW + hi), v(came, lo, hi), OP.mult)
-            for k, (x, name, new) in enumerate((("V", "V", v("pb4", lo, hi)), ("C", "Cd", v("pb5", 256 + lo, 256 + hi)))):
-                mms(new, [(v("IdH"), v(p + x, lo, hi)) for p in ("up", "dn", "fx", "kp", "in")])
-                move(name, v(name, lo, hi), new)
+            for old, x, came in (("old", "V", v(rK, lo, hi)), ("Cx", "C", v(rC, lo, hi))):
+                tt(v("kp" + x, lo, hi), v("keep", lo, hi), bank(old, h), OP.mult)
+                tt(v("in" + x, lo, hi), bank("tw", h), came, OP.mult)
+            for k, (x, name, new) in enumerate((("V", "V", bank("old", h)), ("C", "Cd", bank("Cn", h)))):
+                mms(new, [(v("I8k"), v("Fc", lo, hi))] * k + [(v("IdH"), v(p + x, lo, hi)) for p in ("up", "dn", "fx", "kp", "in")])
+                move(name, h, v(name, lo, hi), new)
                 if not lastt:
-                    b = bank("list", 128 * k, 128 * k + 128, k)
+                    b = bank("list", h, 128 * k, 128 * k + 128)
                     mm(b, v(name, lo, hi), v("IdH"))
-                    ts(v("L" + x, lo, hi), b, MID, OP.add, float(W), OP.min)
+                    if k:
+                        ts(v("LC", lo, hi), b, MID, OP.add, float(W), OP.min)
+                    else:
+                        move("LV", h, v("LV", lo, hi), b, 1.0, MID)
             counts(h)
 
-        def gap4():
-            taken(0)
-            taken(1)
+        def grown(h):
+            cp(ind(v("X"), v("off1", 8 * h, 8 * h + 8)), v("Y", 128 * h, 128 * h + 128))
 
-        dedupe(gap3, gap4, ("iw",) if WHO["blend"] + WHO["round"] == "SV" else ("g1", "g2"), "Ru2")
-        if lastt:
+        def mixed(h):
+            lo, hi, a, b = span(h)
+            move("z16", h, v("z16", a, b), v("zz2", a, b), 1.0, MID)
+            move("blend", h, v("BL", lo, hi), ind(v("X"), v("z16", a, b)), 0.5, -0.25)
+            scan(v("g1", lo, hi), v("BL", lo, hi), v(rY, lo, hi), OP.min, OP.subtract, 64.0)
+
+        def blend(h):
+            lo, hi = 128 * h, 128 * h + 128
+            tt(ind(v("X"), v("off2", 8 * h, 8 * h + 8)), v("g1", lo, hi), v("g2", lo, hi), OP.add)
+
+        ts(v("s6"), last("cum"), 4.0, OP.is_lt, -8192.0, OP.mult)
+        tt(v("s1"), v("TRm"), v("s6"), OP.subtract)
+        if "y2" not in PARTS:
+            message("K", 0, v("VK"), v(rK, 0, 272), t, FAR + 2.0)
+        ts(v("s7"), last("cum"), 4.0, OP.is_lt, 16.0, OP.mult)
+        tt(v("th2"), v("s7"), last("cum"), OP.subtract)
+        for part[0] in PARTS.split():
+            {"b": bends, "g": gates, "k": key, "p": pick, "h": hashed, "n": near, "c": closed, "d": lambda h: dedupe("1", h), "z": codes,
+             "f": moved, "w": grown, "q": shut, "t": takes, "e": lambda h: dedupe("2", h), "s": stays, "r": taken, "l": mixed, "x": blend, "y": guess, "m": piece}[part[0][0]](int(part[0][1]))
+        part[0] = ""
+        if not lastt:
+            tt(v("s3"), v("zs2", 47, 768, 48), v("dz", 2, 48, 3), OP.subtract)
+            tt(v("V0"), v("V0"), v("s3"), OP.add)
+        else:
             dma("Y", T.yx[:, 0:half], T.X[:, 0:half], [v("X", 0, half)], [], LOAD)
             dma("S", T.yx[:, half:W], T.X[:, half:W], [v("X", half, W)], [], LOAD)
 
+    part[1] = ST
     for h in range(2):
         mm(v("pb1", 128 * h, 128 * h + 128, p=8), last("cum", 8 * h, 8 * h + 8), v("Ident"))
     act(v("LNF", p=8), v("pb1", 0, 256, p=8))
@@ -1008,39 +1047,43 @@ def rank_program(g, core, T, topo):
     halves = [(128 * h, 128 * h + 128) for h in range(2)]
     for lo, hi in halves:
         mm(v("pb6", lo, hi), v("cum", lo, hi), v("In1"))
-    line(v("g1"), v("pb6", 0, 256), 0.25, v("eH"))
+    line(v("rc"), v("pb6", 0, 256), 0.25, v("eH"))
     for lo, hi in halves:
         mm(v("pb6", 256 + lo, 256 + hi), v("cum", lo, hi), v("In1"), lo == 0, False)
         mm(v("pb6", 256 + lo, 256 + hi), v("val", lo, hi), v("I64"), False, False)
-    mm(v("pb6", 256, 512), v("In4"), v("g1"), False, True)
-    line(v("g2"), v("pb6", 256, 512), 1.0, v("eL"))
-    turn(("pb7", 0), "V")
-    turn(("pb7", 256), "Cd")
+    mm(v("pb6", 256, 512), v("In4"), v("rc"), False, True)
+    line(v("Dk"), v("pb6", 256, 512), 1.0, v("eL"))
+    turn(("pb3", 0), "V")
+    turn(("pb3", 256), "Cd")
     cp(v("nn"), last("cum"))
     tt(v("gw"), bc("nn"), v("QC"), OP.is_gt)
     masks = ("sgm", "keep", "Dn", "FF")
     for b in range(4):
-        ts(v(masks[b]), v("g2"), float(b), OP.is_equal)
+        ts(v(masks[b]), v("Dk"), float(b), OP.is_equal)
         mm(v("pb1", 0, 256), v("Ub%d" % b), v(masks[b]), b == 0, b == 3)
-        for old, part, new in ((("pb7", 0, 256), ("upV", "dnV", "fxV", "kpV"), "pb4"), (("pb7", 256, 512), ("upC", "dnC", "fxC", "kpC"), "pb5")):
-            tt(v(part[b]), v(masks[b]), v(*old), OP.mult)
-            mm(v(new, 0, 256), v("Uh%d" % b), v(part[b]), b == 0, b == 3)
+        for old, piece, new in ((("pb3", 0, 256), ("upV", "dnV", "fxV", "kpV"), "pb4"), (("pb3", 256, 512), ("upC", "dnC", "fxC", "kpC"), "pb5")):
+            tt(v(piece[b]), v(masks[b]), v(*old), OP.mult)
+            mm(v(new, 0, 256), v("Uh%d" % b), v(piece[b]), b == 0, b == 3)
     line(v("g3"), v("pb1", 0, 256), -1.0, v("eM"))
     for new in ("pb7", "pb6"):
         for lo, hi in halves:
             mm(v(new, lo, hi), v("gw", lo, hi), v("I2k"), lo == 0, False)
     masks = ("El", "Zs", "av", "sk")
     for a in range(4):
-        ts(v(masks[a]), v("g3"), 4.0 * a, OP.is_equal)
-        for old, part, new in (("pb4", ("inV", "i1", "Wz", "tV"), "pb7"), ("pb5", ("inC", "m3", "Ez", "tC"), "pb6")):
-            tt(v(part[a]), v(masks[a]), v(old, 0, 256), OP.mult)
-            mm(v(new, 0, 256), v("Uh%d" % (4 * a)), v(part[a]), False, a == 3)
+        if a:
+            ts(v(masks[a]), v("g3"), 4.0 * a, OP.is_equal)
+        for old, piece, new in (("pb4", ("inV", "i1", "Wz1", "tV"), "pb7"), ("pb5", ("inC", "m3", "Ez1", "tC"), "pb6")):
+            if a:
+                tt(v(piece[a]), v(masks[a]), v(old, 0, 256), OP.mult)
+            else:
+                act(v(piece[a]), v(old, 0, 256))
+            mm(v(new, 0, 256), v("Uh%d" % (4 * a)), v(piece[a]), False, a == 3)
     act(v("f1"), v("pb7", 0, 256))
     cp(v("f2"), v("pb6", 0, 256))
     dma("Y", T.yv[:], v("f1")[0], [v("f1")], [])
     dma("S", T.yc[:], v("f2")[0], [v("f2")], [])
     if "order" not in PLAN:
-        PLAN["order"] = order()
+        PLAN["order"] = order(OPS)
     for i in PLAN["order"]:
         OPS[i][1](OPS[i][2], OPS[i][3])
     for s in sorted(count):

@@ -1,4 +1,5 @@
 import numpy as np
+from concourse.bass import DstId, RemoteDMATransfer
 from concourse.mybir import AluOpType, AxisListType, ActivationFunctionType
 
 OP = AluOpType
@@ -10,33 +11,40 @@ F32, BF, I32, U16, F16 = "float32", "bfloat16", "int32", "uint16", "float16"
 RUNS = "SVM32 SVM64 SVM32|VVM16 SVM48 SVM64"
 SLOTS = ("A4 R5 R5", "T4 T4 A6")
 DIFF = "07"
-PARTS = "b1 b0 g1 k1 p1 h1 g0 k0 n1 p0 y2 c1 h0 d1 z1 f1 n0 w1 c0 t1 d0 e1 z0 m2 s1 r1 w0 f0 t0 q0 e0 l2 s0 r0 x1 x0"
-APART = ("Ru1", "Ru2")
+PARTS = "b1 b0 g1 k1 p1 g0 k0 n1 p0 y2 h2 c1 j1 d1 z1 f1 n0 w1 c0 j0 t1 d0 e1 z0 m2 s1 r1 w0 f0 t0 q0 e0 l1 l0 s0 r0 x1 x0"
 YGATHER = ((("S", 0, 3),), (("S", 0, 3),))
-WHO = {"Y": "SS", "SB": "VV", "sgm": "SS", "off1": "SS", "off2": "SS", "cI": "SS", "Ru1": "SS", "Ru2": "SS", "blend": "SS", "sq": "SS", "V": "SS", "Cd": "SS", "Kp": "SS", "zz1": "SS", "zz2": "SS", "x": "SS", "s5": "SS", "LV": "SS", "UI": "SS", "z16": "SS", "PW": "SS", "keep": "SS", "xw": "VS", "gw": "VS", "tw": "VS", "Fc": "SS"}
-QUICK = (1, 1)
+WHO = {"Y": "SS", "SB": "SS", "sgm": "SS", "off1": "SS", "off2": "SS", "cI": "SS", "Ru1": "SS", "Ru2": "PS", "blend": "SS", "sq": "SS", "V": "SS", "Cd": "SS", "Kp": "SS", "zz1": "PP", "zz2": "PP", "x": "SS", "s5": "SS", "LV": "SS", "UI": "SS", "z16": "SS", "PW": "SS", "keep": "SS", "xw": "VS", "gw": "VS", "tw": "VS", "Fc": "SS", "Cp": "VV", "val": "VV", "FF": "VV", "sk": "VV", "g1": "VV"}
+QUICK = 1
+AHEAD = 1
+REST = "TV"
+EARLY = (0, 0)
 NABS = (0, 7)
 NRUN = (4, 4)
-BANK = {"key": "23", "z": "16", "PW": "23", "u": "23", "Z": "16", "F": "54", "keep": "16", "tw": "54", "list": "16", "c": "77", "old": "54", "Cx": "54", "Cn": "54", "Ru1": "23", "Ru2": "07", "zU1": "23", "zU2": "07", "sum1": "23", "sum2": "07", "off1": "23", "off2": "07"}
-SPOT = {"key": (0, 0), "o": (128, 0), "y": (256, 0), "z": (384, 0), "PW": (384, 0), "u": (160, 8), "Z": (0, 0), "F": (256, 0), "keep": (128, 0), "tw": (384, 0), "list": (256, 0), "c": (0, 0), "old": (0, 0), "Cx": (128, 0), "Cn": (256, 0), "Ru1": (0, 0), "Ru2": (128, 0), "zU1": (448, 8), "zU2": (464, 8), "sum1": (256, 0), "sum2": (320, 0), "off1": (480, 8), "off2": (496, 8)}
+BANK = {"Kp": "0", "key": "23", "z": "16", "PW": "23", "u": "77", "Z": "16", "F": "54", "keep": "16", "tw": "54", "list": "16", "c": "77", "old": "54", "Cx": "54", "Cn": "54", "Ru1": "23", "Ru2": "27", "zU1": "07", "zU2": "23", "sum1": "23", "sum2": "07", "off1": "23", "off2": "07"}
+SPOT = {"bl": (0, 128), "key": (0, 0), "o": (128, 0), "y": (256, 0), "z": (384, 0), "PW": (384, 0), "u": (160, 8), "Z": (0, 0), "F": (256, 0), "keep": (128, 0), "tw": (384, 0), "list": (256, 0), "c": (0, 0), "old": (0, 0), "Cx": (128, 0), "Cn": (256, 0), "Ru1": (0, 0), "Ru2": (128, 0), "zU1": (448, 8), "zU2": (464, 8), "sum1": (256, 0), "sum2": (320, 0), "off1": (480, 8), "off2": (496, 8)}
 CYC, GATHER, SCATTER = 0.00083, 1.56, 3.8
 WAKE = 0.215
 TFIX = 0.006
 VFIX = 0.0
 ISSUE = 0.9
+FIRST = 2.0
 LOAD = 4.2
 SMALL = 1.8
 FAR = 2.5
 LATER = 0.8
 LONG = 2
-SEED = 1
-TURNS = 3500
-WARM = 0.3
-SLOW = (0.04, 0.5, 0.8, 0.4)
+SEED = 2
+TURNS = 8000
+POLISH = 1300
+DEAR = (1.66, 4.1, 0.97)
+WARM = 0.4
+LOCAL = 0.3
+ALONE = "cjdzfwtesrlxm"
+LUMP = {"V": 0.0, "T": 0.0}
 SHAKE = 0.3
 SHIFT = 1.0
 PLAN = {}
-XW = W + 2 * L
+XW = W + 4 * L
 GW = 2064
 KEYS = []
 for _r in RUNS.split("|"):
@@ -69,18 +77,18 @@ _add("AB0 AB1 CG0 CG1", 2048, BF)
 _add("DV0 DV1", 2048, F16)
 _add("EE0 EE1", 1792, BF)
 _add("EQ", 2048, BF)
-_pack("VY", "VK YV", 272, F16)
-ALIAS["V"], ALIAS["s1"] = ("VY", 0, 256, F16), ("VY", 256, 16, F16)
-ALIAS["Yn"], ALIAS["Vn"] = ("VY", 272, 256, F16), ("VY", 528, 16, F16)
-_pack("YN", "Cp Cd Y BL", 256, F16)
+_add("VK", 288, F16)
+_add("Yh", 288, BF)
+ALIAS["V"], ALIAS["s1"], ALIAS["Vn"] = ("VK", 0, 256, F16), ("VK", 256, 16, F16), ("VK", 272, 16, F16)
+_pack("YN", "Cp Cd BL", 256, F16)
 for _t in range(ST):
-    _add("rK%d" % _t, 544, F16)
-    ALIAS["rY%d" % _t] = ("rK%d" % _t, 272, 272, F16)
+    _add("rK%d" % _t, 288, F16)
+    _add("rY%d" % _t, 288, BF)
     _add("rC%d" % _t, 256, F16)
     _add("rB%d" % _t, 16, I32)
 _add("SB", 16, I32)
 _pack("MH", "Wz1 Ez1 Ru1 Wz2 Ez2 Ru2 xw kw i1 m2 m3 m4 m5 upV upC dnV dnC fxV fxC kpV kpC inV inC tV tC", 256, F16)
-_pack("MI", "IdH InH CQ Uh0 Uh1 Uh2 Uh3 Uh4 Uh8 Uh12", 128, F16)
+_pack("MI", "IdH InH Uh0 Uh1 Uh2 Uh3 Uh4 Uh8 Uh12", 128, F16)
 _add("blk8H", 8, F16)
 _pack("MP", "ee0 ee1 mP0 mP1 Fu0 Fu1", 128, BF, 16)
 if "z2" in PARTS:
@@ -90,25 +98,28 @@ if "z2" in PARTS:
 _pack("MZ", "zs1 sx", 256, F16)
 _add("zs2", 768, F16)
 _add("take", 768, BF)
-_pack("MF", "PW m1 QC f1 f2 LNF", 256, F32)
-_pack("MQ", "mm onesF PW2 G8 n3 n4 RSm RSk THR", 128, F32)
-_pack("MB", "val cum av sgp sk dd sgm gw tw keep Dn FF Fc Zs El Em1 Em2 rc Dk g1 g2 g3 grow OH RS RS2 CZ", 256, BF)
+_pack("MF", "PW QC f1 f2 LNF", 256, F32)
+_pack("MQ", "mm onesF PW2 G8 n3 n4 RSk THR", 128, F32)
+_pack("MB", "val cum av sgp sk dd sgm gw tw keep Dn FF Fc fit Zs El Em1 Em2 rc Dk g1 g2 g3 grow OH RS RS2 CZ", 256, BF)
 _add("pabc0 pabc1", 384, BF)
 _add("SK SM KA IV IC LNI", 256, I32)
 _add("LV LC", 256, U16)
-_pack("PLF", "nn V0 x kn Kp sq hh s2 s3 s4 s5 s6 s7 s8 th2 TR TRm oA1 oA2 zz1 zz2 t1", 16, F32)
+_pack("PLF", "nn V0 x kn Kp sq hh s2 s3 s4 s5 s9 th2 TR TRm oA1 oA2 zz1 zz2 t1", 16, F32)
 _add("dz", 48, F32)
 _pack("PLI", "UI HI VM", 16, I32)
 _pack("PLU", "off1 off2 z16 bcA bcG bcT bcK", 16, U16)
 _pack("OL", "olist0 olist1", 24, U16)
-_add("OB", 24, F16)
-_pack("PLB", "BM32 BMh", 24, BF)
-_pack("COF", "pcF pmF p4F thm lim cs1 e1 e2 e3 e4 e5 eK eO eQ eH eL eM wF wq wp", 1, F32)
+_add("OB", 24, F32)
+_add("BM32", 24, BF)
+_add("BMh", 16, F16)
+_add("OE", 24, F32)
+_pack("COF", "pcF pmF p4F thm lim cs1 e1 e2 e3 e4 e5 e6 e7 eK eO eH eL eM wF wq wp", 1, F32)
 _pack("COI", "pcI pmI p4I cI tI", 1, I32)
 _add("WI THI", 1, I32)
-_pack("IDS", "Ident In1 Za Zk Zo Zg Ih Ibig IZv In4k In4 I64 I2k I8k ones Yw0 Yw1 LIM blkw blkl CR zero two NR DG Ub0 Ub1 Ub2 Ub3", 128, BF)
-_pack("N8", "BKk BK2 BKn EEw GVw W8", 8, BF)
+_pack("IDS", "Ident In1 Za Zk Zo Zg Z2 RSs Ih Ibig IZv In4k In4 I64 I2k I8k I37 ones Yw0 Yw1 LIM blkw blkl CR zero two NR DG Ub0 Ub1 Ub2 Ub3", 128, BF)
+_pack("N8", "BKk BK2 BKn EEw GVw ABw W8 CP", 8, BF)
 _add("BW", 64, BF)
+_add("CK s7", 16, BF)
 _add("blk8F THF IdF", 8, F32)
 LOOPWISE = any(k[2] == "T" for r in KEYS for k in r)
 for _b in range(8):
@@ -173,12 +184,39 @@ def order(OPS):
     qs, cost, lat = [o[0] for o in OPS], [o[4] for o in OPS], [o[5] for o in OPS]
     banks = [sorted({a[0] for a in o[2] + o[3] if a[0].startswith("pb")}) for o in OPS]
     fwd = [[(j, cost[j] + (lat[j] + WAKE if k else 0.0)) for j, k in deps[i].items()] for i in range(n)]
+    PLAN["debug"] = (OPS, None, cost, None, fwd)
+    lump, at, heads, open_ = [], [], [], {}
+    for i, o in enumerate(OPS):
+        m = open_.get(qs[i])
+        h = heads[m][0] if m is not None else -1
+        if (h >= 0 and qs[i] in "VT" and OPS[h][9:] == o[9:] and OPS[h][3][0][0] == o[3][0][0] and banks[h] == banks[i] and heads[m][1] + cost[i] <= LUMP[qs[i]]
+                and all((lump[j] == m and not k) or above[h] >> j & 1 for j, k in deps[i].items())):
+            at.append(heads[m][1])
+            heads[m][1] += cost[i]
+        else:
+            m = open_[qs[i]] = len(heads)
+            heads.append([i, cost[i]])
+            at.append(0.0)
+        lump.append(m)
+    calls, n = n, len(heads)
+    edges, lat2 = [{} for _ in heads], [0.0] * n
+    for i in range(calls):
+        lat2[lump[i]] = max(lat2[lump[i]], at[i] + cost[i] + lat[i] - heads[lump[i]][1])
+        for j, w in fwd[i]:
+            if lump[j] != lump[i]:
+                edges[lump[i]][lump[j]] = max(edges[lump[i]].get(lump[j], -99.0), at[j] + w - at[i])
+    OPS = [OPS[h] for h, _c in heads]
+    qs, cost, lat, banks, deps = [qs[h] for h, _c in heads], [c for _h, c in heads], lat2, [banks[h] for h, _c in heads], edges
+    fwd = [list(e.items()) for e in edges]
     bwd = [[] for _ in OPS]
     for i in range(n):
         for j, w in fwd[i]:
             bwd[j].append((i, w - cost[j] + cost[i]))
 
+    wake = [WAKE]
+
     def fit(key, before, first, line):
+        gap = wake[0]
         for i in line:
             x = key[i]
             for j, _w in before[i]:
@@ -206,10 +244,10 @@ def order(OPS):
                 for b in banks[i]:
                     be, bs, bq = held[b]
                     m = len(be)
-                    while m and be[m - 1] > t - WAKE + 1e-9:
+                    while m and be[m - 1] > t - gap + 1e-9:
                         m -= 1
-                        if bq[m] != q and bs[m] < t + c + WAKE - 1e-9:
-                            t, moved = be[m] + WAKE, True
+                        if bq[m] != q and bs[m] < t + c + gap - 1e-9:
+                            t, moved = be[m] + gap, True
                             break
                 if not moved:
                     break
@@ -249,7 +287,7 @@ def order(OPS):
         for i in range(n):
             ends[(qs[i], round(st[i] + cost[i], 5))] = i
             for b in banks[i]:
-                ends[(b, round(st[i] + cost[i] + WAKE, 5))] = i
+                ends[(b, round(st[i] + cost[i] + wake[0], 5))] = i
         i = int((start + whole).argmax())
         while st[i] > 1e-6:
             j = [j for j, w in fwd[i] if abs(st[j] + w - st[i]) < 1e-6]
@@ -264,37 +302,33 @@ def order(OPS):
     for i in down:
         tail[i] = max([lat[i]] + [tail[j] + w for j, w in bwd[i]])
     PLAN["chain"] = max(tail[i] + cost[i] for i in range(n))
-    PLAN["debug"] = (OPS, tail, cost, bwd, fwd)
     kinds, parts = {}, {}
-    kind = np.array([kinds.setdefault((o[0], str(o[3]), str([a for a in o[2] if a[0][0] != "r"])), len(kinds)) for o in OPS])
-    part = np.array([parts.setdefault(o[9] + o[0], len(parts)) for o in OPS])
-    slow = [cost[i] + SLOW[1] * (lat[i] > 0 and qs[i] == "G") for i in range(n)]
-    late = [[(j, slow[j] + ((lat[j] + WAKE + SLOW[0] + SLOW[2] * (qs[j] == "G" and lat[j] > 0)) if k else 0.0)) for j, k in deps[i].items()] for i in range(n)]
-
-    def both(plan):
-        place = np.empty(n)
-        place[plan[2]] = np.arange(n)
-        start, free, held = [0.0] * n, dict.fromkeys("VSTGYF", 0.0), {}
-        for i in np.lexsort((place, np.round(plan[1], 6))).tolist():
-            q = qs[i]
-            t = free[q]
-            for j, w in late[i]:
-                if start[j] + w > t:
-                    t = start[j] + w
-            for b in banks[i]:
-                if b in held and held[b][0] != q and held[b][1] > t:
-                    t = held[b][1]
-            start[i] = t
-            free[q] = t = t + slow[i]
-            for b in banks[i]:
-                held[b] = (q, t + WAKE + SLOW[0])
-        return (1 - SLOW[3]) * plan[0] + SLOW[3] * float((np.array(start) + whole).max())
+    own = [o[10] == ST - 1 and o[9][:1] in ALONE for o in OPS]
+    kind = np.array([kinds.setdefault((o[0], str(o[3]), str([a for a in o[2] if a[0][0] != "r"]), own[i]), len(kinds)) for i, o in enumerate(OPS)])
+    part = np.array([parts.setdefault((o[9], o[0], own[i]), len(parts)) for i, o in enumerate(OPS)])
     rng = np.random.default_rng(SEED)
     best = now = again(forth(-np.array(tail) - took)[1])
-    least = mark = both(now)
     pairs = None
-    for k in range(TURNS):
-        how, s = rng.random(), now[1]
+    for k in range(TURNS + POLISH):
+        if k == TURNS:
+            lists = ("LV", "LC", "PLU", "OL")
+            was = list(cost)
+            for i, o in enumerate(OPS):
+                if qs[i] == "V" and o[3][0][0] == "X" and len(o[3]) > 1:
+                    cost[i] = 0.05 + (cost[i] - 0.05) * DEAR[1] / SCATTER
+                elif qs[i] in "VS" and lat[i] == 0 and o[3][0][0] not in lists and any(a[0] in lists for a in o[2]):
+                    cost[i] = 0.06 + (cost[i] - 0.06) * DEAR[0] / GATHER
+                lat[i] *= DEAR[2]
+            wake[0] *= DEAR[2]
+            fwd[:] = [[(j, cost[j] + (w - was[j]) * DEAR[2]) for j, w in e] for e in fwd]
+            bwd[:] = [[] for _ in OPS]
+            for i in range(n):
+                for j, w in fwd[i]:
+                    bwd[j].append((i, w - cost[j] + cost[i]))
+            took[:], whole[:] = np.array(cost), np.array(cost) + np.array(lat)
+            best = now = forth(best[1].copy())
+            pairs = None
+        how, s = rng.random() * (1.0 if k < TURNS else 0.5 + LOCAL), now[1]
         if how < 0.5:
             pairs = pairs or blocked(s)
             noise = np.zeros(len(kinds))
@@ -312,20 +346,23 @@ def order(OPS):
             new = forth(s + noise[kind])
             if now[0] - 1e-6 < new[0] < now[0] + 1.5:
                 new = min(new, again(new[1]), key=lambda r: r[0])
-        elif how < 0.75:
+        elif how < 0.5 + LOCAL:
+            at0 = rng.random() * now[0]
+            noise = np.zeros(len(kinds))
+            near = kind[(s > at0) & (s < at0 + 2.0)]
+            noise[near] = rng.normal(0.0, 2 * SHAKE, len(near))
+            new = forth(s + noise[kind]) if k % 2 else again(s - noise[kind])
+        elif how < 0.75 + LOCAL / 2:
             new = again(s - (rng.normal(0.0, SHIFT, len(parts)) * (rng.random(len(parts)) < 0.1))[part])
         else:
             new = again(s - (rng.normal(0.0, SHAKE, len(kinds)) * (rng.random(len(kinds)) < 0.2))[kind])
-        room = WARM * (1 - k / TURNS) * rng.random()
-        if new[0] < now[0] + room + 0.5:
-            x = both(new)
-            if x < mark + room:
-                now, pairs, mark = new, None, x
-                if x < least:
-                    best, least = now, x
-    PLAN["end"], PLAN["start"] = best[0], best[1].tolist()
-    place = {i: k for k, i in enumerate(best[2])}
-    return sorted(range(n), key=lambda i: (round(PLAN["start"][i], 6), place[i]))
+        if new[0] < now[0] + (WARM * (1 - k / TURNS) if k < TURNS else 0.03) * rng.random():
+            now, pairs = new, None
+            if now[0] < best[0]:
+                best = now
+    PLAN["end"], PLAN["lumps"] = best[0], n
+    place = {m: k for k, m in enumerate(best[2])}
+    return sorted(range(calls), key=lambda i: (round(float(best[1][lump[i]]) + at[i], 6), place[lump[i]], i))
 
 
 def rank_program(g, core, T, topo):
@@ -492,6 +529,12 @@ def rank_program(g, core, T, topo):
         else:
             line(out, a, scale, bias)
 
+    def step(who, h, out, a, edge, scale):
+        if WHO[who][h % 2] == "V":
+            ts(out, a, edge, OP.is_gt if scale > 0 else OP.is_lt)
+        else:
+            act(out, a, AF.Sigmoid, scale, -scale * edge)
+
     def mm(out, l, r, start=True, stop=True):
         c = TFIX + max(min(64, l[2]), r[2]) * CYC * (4 if SCRATCH[r[1][0][0]][2] == F32 else 1)
         OPS[op("T", lambda e: e.matmul(out[0], l[0], r[0], start, stop), [l, r], [out], c)][8] = (start, stop)
@@ -535,6 +578,9 @@ def rank_program(g, core, T, topo):
     def last(name, a0=0, a1=16):
         return v(name, a0 * 16 + 15, a1 * 16, 16)
 
+    def found(a0=0, a1=16):
+        return v("SM", a0 * 16 + 1, a1 * 16, 16)
+
     def third(x, h, step=48):
         return v(x, 3 * span(h)[0] + step - 1, 3 * span(h)[1], step)
 
@@ -573,15 +619,15 @@ def rank_program(g, core, T, topo):
     slots = [[0, 8], [1, 16]]
     for nm, c in (("ones", 1), ("zero", 0), ("onesF", 1), ("two", 2), ("g2", -192), ("dz", 0), ("KA", -32)):
         iota(v(nm), [[0, v(nm)[2]]], c, 0)
-    for x in (v("EQ"), v("take"), v("grow"), v("X", W, XW)):
+    for x in (v("EQ"), v("take"), v("grow"), v("X", W, XW), v("Yh", 256, 288)):
         fill(x, 0.0)
     cp(v("MZ"), v("take", 0, 512))
     cp(v("zs2"), v("take"))
-    iota(v("TR"), [[256, 2], [0, 8]], W // 2, 2)
-    iota(v("TRm"), [[256, 2], [0, 8]], W // 2 - 8192, 2)
+    iota(v("TR"), [[512, 2], [0, 8]], W // 2, 4)
+    iota(v("TRm"), [[512, 2], [0, 8]], W // 2 - 8192, 4)
     iota(v("OB", 0, 8), [[256, 8]], GW, 0)
     iota(v("OB", 8, 24), [[1, 2], [256, 8]], 0, 0)
-    iota(v("t1"), [[32, 16]], W + 2048, 0)
+    iota(v("t1"), [[512, 2], [0, 8]], W, 4)
     iota(v("f2", 0, 64), [[1, 8], [0, 8]], 0, 0)
     iota(v("f2", 64, 88), [[0, 3], [1, 8]], 0, 0)
     for nm in ("GV0", "GV1", "DC0", "DC1"):
@@ -593,7 +639,8 @@ def rank_program(g, core, T, topo):
     iota(last("CR", 0, 8), [[0, 8]], int(BIG), 0)
     iota(v("CZ"), [[0, 256]], int(2 * ZU), 0)
     iota(last("CZ"), [[0, 16]], int(10 * ZU), 0)
-    iota(v("CQ"), [[0, 8], [2, 16]], -W // 2, 0)
+    iota(v("CK"), [[0, 16]], -1184 * 2048, 0)
+    iota(v("CP", p=2), [[0, 8]], -75776, 75775)
     for lo in (0, 128):
         mask(v("RS", lo, lo + 128), v("ones"), slots, OP.is_gt, 0.0, 0, 0)
         mask(v("RS2", lo, lo + 128), v("ones"), slots, OP.is_ge, 0.0, -2, 0)
@@ -604,7 +651,7 @@ def rank_program(g, core, T, topo):
     mask(v("blkl"), v("blkw"), [[256, 8], [-1, 16]], OP.is_ge, 0.0, 241, -16)
     for h in range(2):
         if NABS[h] < 14:
-            line(v("Yw%d" % h), v("blkw"), -KZ, 0.0)
+            line(v("Yw%d" % h), v("blkw"), 2 * KZ, 0.0)
             mask(v("Yw%d" % h), v("Yw%d" % h), slots, OP.is_ge, 0.0, -2 - NABS[h], 0)
     ts(v("pmI"), v("pcI"), 15, OP.bitwise_and)
     ts(v("p4I"), v("pcI"), 4, OP.arith_shift_right)
@@ -619,37 +666,46 @@ def rank_program(g, core, T, topo):
         ts(v("bcG"), v("mm", 0, 16), 16.0, OP.mult, v("e5"), OP.add)
     ts(v("IdH"), v("mm"), v("pcF"), OP.is_equal)
     ts(v("IdF"), v("mm", 0, 8), v("pcF"), OP.is_equal)
-    for nm, c in (("Ident", 1.0), ("Ih", 0.5)):
+    for nm, c in (("Ident", 1.0), ("Ih", -0.5)):
         line(v(nm), v("IdH"), c, 0.0)
     ts(v("DG"), v("QC", 0, 128), v("pmF"), OP.is_equal)
-    line(v("RSm"), v("RS", 0, 128), 1048576.0, -4097.0)
+    line(v("RSs"), v("RS", 0, 128), 2.0, -1.0)
     line(v("RSk"), v("RS", 0, 128), BIG, 31.0)
-    ts(v("eO"), v("pmF"), 17.0, OP.mult, 1.0, OP.add)
-    if any(QUICK):
-        ts(v("eQ"), v("pmF"), 16.0, OP.mult, 16.0, OP.add)
+    if QUICK:
+        ts(v("eO"), v("pmF"), 16.0, OP.mult, 16.0, OP.add)
         ts(v("bcK"), v("mm", 0, 16), 16.0, OP.mult, 15.0, OP.add)
+    else:
+        ts(v("eO"), v("pmF"), 17.0, OP.mult, 1.0, OP.add)
+    ts(v("OE"), v("OB"), v("eO"), OP.add)
     ts(v("blk8F"), v("mm", 0, 8), v("p4F"), OP.is_equal)
     cp(v("blk8H"), v("blk8F"))
-    for nm, c in (("BKk", 2048.0), ("BK2", 4096.0), ("BKn", -2048.0), ("EEw", -4 * KZ), ("GVw", -2 * KZ)):
+    for nm, c in (("BKk", 2048.0), ("BK2", 4096.0), ("BKn", -2048.0), ("EEw", -4 * KZ), ("GVw", 2 * KZ), ("ABw", -2 * KZ)):
         line(v(nm), v("blk8F"), c, 0.0)
     ts(v("BM32"), v("f2", 64, 88), v("p4F"), OP.is_equal, -1.0 / 32, OP.mult)
     for h in range(2):
         tt(v("BMh", 8 * h, 8 * h + 8), v("t1", 8 * h, 8 * h + 8), v("blk8F"), OP.mult)
     cp(v("wF"), v("WI"))
-    ts(v("W8"), v("blk8F"), v("wF"), OP.mult)
+    ts(v("W8"), v("blk8F"), v("wF"), OP.mult, 2.0, OP.mult)
     line(v("eH"), v("pmF"), 0.25, 191.875)
     line(v("eL"), v("pmF"), 1.0, 768.0 + 1 - 64)
     line(v("eM"), v("pmF"), 1.0, 1.0 - 64)
-    for nm, c in (("Ibig", BIG), ("IZv", KZ * 2048), ("In4k", -4096.0), ("Za", -ZU / 4), ("Zk", -2 * ZU), ("Zo", ZU), ("Zg", 16 * ZU), ("In1", -1.0),
-                  ("InH", -1.0), ("I8k", 8192.0), ("In4", -4.0), ("I64", 64.0), ("I2k", MID)):
+    for nm, c in (("Ibig", BIG), ("IZv", KZ * 2048), ("In4k", -4096.0), ("Za", -ZU / 4), ("Zk", -2 * ZU), ("Zo", ZU), ("Zg", 16 * ZU), ("In1", -1.0)) + (("Z2", 2 * ZU),) * ("V" in WHO["sgm"]) + (
+                  ("InH", -1.0), ("I8k", 8192.0), ("I37", 1184.0)):
         select(v(nm), v("zero"), OP.not_equal, c, 0)
-    for k in (0, 1, 2, 3, 4, 8, 12):
-        select(v("Uh%d" % k), v("zero"), OP.not_equal, 1.0, k)
-        if k >= 4:
-            select(v("Uh%d" % k), v("Uh%d" % k), OP.not_equal, -1.0, 0)
-        else:
-            select(v("Ub%d" % k), v("blkw"), OP.is_ge, 0.0, k)
-            select(v("Ub%d" % k), v("Ub%d" % k), OP.not_equal, -63.0, k)
+
+    def shifts(after):
+        first = len(OPS)
+        for nm, c in (("In4", -4.0), ("I64", 64.0), ("I2k", MID)):
+            select(v(nm), v("zero"), OP.not_equal, c, 0)
+        for k in (0, 1, 2, 3, 4, 8, 12):
+            select(v("Uh%d" % k), v("zero"), OP.not_equal, 1.0, k)
+            if k >= 4:
+                select(v("Uh%d" % k), v("Uh%d" % k), OP.not_equal, -1.0, 0)
+            else:
+                select(v("Ub%d" % k), v("blkw"), OP.is_ge, 0.0, k)
+                select(v("Ub%d" % k), v("Ub%d" % k), OP.not_equal, -63.0, k)
+        for o in OPS[first:]:
+            o[7].append(after)
     scan(back("PW2", 0, 128), v("two"), v("zero"), OP.mult, OP.add, 2.0 ** -68)
     tt(v("n4", 0, 16), v("PW2", 0, 16), v("DG", 0, 16), OP.mult)
     total(v("wq"), v("n4", 0, 16))
@@ -660,10 +716,16 @@ def rank_program(g, core, T, topo):
     ts(v("THR"), v("n3"), v("wp"), OP.max)
     ts(v("BW"), v("f2", 0, 64), v("p4F"), OP.is_equal, v("wq"), OP.mult)
 
-    def counts(h):
+    def counts(h, final=False):
         lo, hi = 128 * h, 128 * h + 128
-        ts(v("val", lo, hi), v("Cd", lo, hi), MID, OP.is_lt)
-        scan(v("cum", lo, hi), v("RS", 0, 128), v("val", lo, hi), OP.mult, OP.add)
+        step("val", h, v("val", lo, hi), v("Cd", lo, hi), MID - 0.5, -256.0)
+        if final:
+            scan(v("cum", lo, hi), v("RS", 0, 128), v("val", lo, hi), OP.mult, OP.add)
+        else:
+            hold("rc", "val", h)
+
+    def rows(a0=0, a1=16):
+        return v("rc", 16 * a0, 16 * a1, 16)
 
     line(v("tV"), v("IV"), 1.0, -MID)
     line(v("tC"), v("IC"), 1.0, -MID)
@@ -702,23 +764,23 @@ def rank_program(g, core, T, topo):
             alone(v("Ez" + n, lo, hi), v("Wz" + n, lo, hi), v("DG"))
             mm(bank("zU" + n, x, 0, 8), v("Ez" + n, lo, hi), v("blk8H"))
             mm(bank(Ru, x), v("Wz" + n, lo, hi), v("IdH"))
-        for x in each(h) if Ru in APART else (h,):
-            move(Ru, x, v(Ru, *span(x)[:2]), bank(Ru, x))
-        move(zz, h, v(zz, *span(h)[2:]), bank("zU" + n, h, 0, 8))
-        for x in each(h):
-            lo, hi, a, b = span(x)
-            for k in range(8):
-                at = 128 * (a + k)
-                ts(v("EQ", at + 16 * k, at + 128), v(Ru, lo + 16 * k, hi), v(zz, a + k, a + k + 1), OP.is_equal, 2.0 ** (-16 * k), OP.mult)
-                mm(bank("sum" + n, x, 0, 64), v("EQ", at, at + 128), v("BW"), k == 0, k == 7)
-            for k in range(2):
-                out = v(Em, lo + k, hi, 2)
-                tt((out[0], v(Em, lo + 64 * k, lo + 64 * k + 64)[1]) + out[2:], bank("sum" + n, x, 0, 64), v("THR", k, 128, 2), OP.is_ge)
-            mms(bank("off" + n, x, 0, 8), [(v("CQ", p=1), v("ones", 0, 8, p=1)), (v(Em, lo, hi), v("BMh", a, b))])
-        for x in each(h) if "off" + n in APART else (h,):
-            a, b = span(x)[2:]
-            move("off" + n, x, v("oA" + n, a, b), v(zz, a, b), 1.0, MID)
-            tt(v("off" + n, a, b), bank("off" + n, x, 0, 8), v("oA" + n, a, b), OP.max)
+        lo, hi, a, b = span(h)
+        if WHO[Ru][h] != "P":
+            move(Ru, h, v(Ru, lo, hi), bank(Ru, h))
+        if WHO[zz][h] != "P":
+            move(zz, h, v(zz, a, b), bank("zU" + n, h, 0, 8))
+        for k in range(8):
+            at = 128 * (a + k)
+            names = bank(Ru, h, 16 * k) if WHO[Ru][h] == "P" else v(Ru, lo + 16 * k, hi)
+            name = bank("zU" + n, h, k, k + 1) if WHO[zz][h] == "P" else v(zz, a + k, a + k + 1)
+            ts(v("EQ", at + 16 * k, at + 128), names, name, OP.is_equal, 2.0 ** (-16 * k), OP.mult)
+            mm(bank("sum" + n, h, 0, 64), v("EQ", at, at + 128), v("BW"), k == 0, k == 7)
+        move("off" + n, h, v("oA" + n, a, b), bank("zU" + n, h, 0, 8) if WHO[zz][h] == "P" else v(zz, a, b), 1.0, MID)
+        for k in range(2):
+            out = v(Em, lo + k, hi, 2)
+            tt((out[0], v(Em, lo + 64 * k, lo + 64 * k + 64)[1]) + out[2:], bank("sum" + n, h, 0, 64), v("THR", k, 128, 2), OP.is_ge)
+        mm(bank("off" + n, h, 0, 8), v(Em, lo, hi), v("BMh", a, b))
+        tt(v("off" + n, a, b), bank("off" + n, h, 0, 8), v("oA" + n, a, b), OP.max)
 
     def message(m, h, out, land, t, cost, after=()):
         d = 1 + t % 3
@@ -728,17 +790,27 @@ def rank_program(g, core, T, topo):
 
         def emit(rd, wr):
             wait("G", need("G", rd, wr))
-            g.remote_dma(land[0], out[0], T.sem[asem], T.sem[lsem], pid, rid, topo.mask(core, dst))
+            if len(out) == 1:
+                g.remote_dma(land[0][0], out[0][0], T.sem[asem], T.sem[lsem], pid, rid, topo.mask(core, dst))
+            elif len(land) == 1:
+                g.remote_dma_fused([RemoteDMATransfer(dst_ids=[DstId(rid=rid, pnc=pid)], dma_engine_mask=topo.mask(core, dst), remote_sem=T.sem[asem],
+                                                      srcs=[x[0] for x in out], dsts=[land[0][0]], alu_op=2)], local_sem=T.sem[lsem])
+            else:
+                ways = topo.engines(core, dst)
+                ways = [ways[1::2], ways[0::2]] if len(out) == 2 else [ways[1::2], ways[0::4], ways[2::4]]
+                g.remote_dma_fused([RemoteDMATransfer(dst_ids=[DstId(rid=rid, pnc=pid)], dma_engine_mask=sum(1 << e for e in ways[k]),
+                                                      remote_sem=T.sem[asem], src=out[k][0], dst=land[k][0]) for k in range(len(out))], local_sem=T.sem[lsem])
             record("Gr", bump("G", lsem, len(topo.engines(core, dst))), rd, wr)
-        sent = add("G", emit, [out], [], ISSUE, cost)
+        sent = add("G", emit, out, [], ISSUE + FIRST * (m == "K" and t == 0), cost)
         OPS[sent][7] += after
 
         def came(rd, wr):
             n = len(topo.engines(src, core))
             count[asem] = n
             clock[(asem, n)] = {}
-            recs.setdefault(wr[0][0], []).append(wr[0][1:] + ((asem, n), "far", True))
-        add("F", came, [], [land], 0.0, 0.0, [sent])
+            for x in wr:
+                recs.setdefault(x[0], []).append(x[1:] + ((asem, n), "far", True))
+        add("F", came, [], land, 0.0, 0.0, [sent])
         return sent
 
     counts(0)
@@ -803,19 +875,22 @@ def rank_program(g, core, T, topo):
 
         def gates(h):
             lo, hi, a, b = 128 * h, 128 * h + 128, 8 * h, 8 * h + 8
-            hold("rc", "val", h)
             ts(v("sgp", lo, hi), v("rc", lo, hi), 3.0, OP.is_ge, -2.0, OP.add)
-            ts(last("sgp", a, b), last("cum", a, b), 4.0, OP.is_ge, -3.0, OP.mult)
+            if REST[h] == "V":
+                ts(last("sgp", a, b), rows(a, b), 4.0, OP.is_ge, -3.0, OP.mult)
+
 
         def key(h):
             lo, hi = 128 * h, 128 * h + 128
             k = bank("key", h)
             mm(k, v("ones", p=1), v("CR", p=1), True, False)
             mm(k, v("Ibig"), v("val", lo, hi), False, False)
+            if REST[h] == "T":
+                mm(bank("key", h, 15, 128, 16), v("Ibig"), v("s7", 8 * h, 8 * h + 8), False, False)
             whole = len(KEYS[h]) == 1
             if whole:
                 mm(k, v("Ibig"), v("sgp", lo, hi), False, False)
-            terms = []
+            terms, early = [], ([], [], [])
             for p0, p1, how in KEYS[h]:
                 for s in range(14):
                     out, kind = bank("key", h, s, 128, 16, (p0, p1)), how
@@ -825,9 +900,15 @@ def rank_program(g, core, T, topo):
                         at, kind = (128 * s, 128 * s + 128), "".join(c * n for c, n in SLOTS[h])[s]
                     else:
                         at = (16 * p0 + s, 16 * p1 - 15 + s, 16)
-                    if kind == "R":
-                        mm(out, v("DV%d" % h, *at), v("BKn"), False, False)
+                    if kind == "R" and how == "M" and EARLY[h]:
+                        early[0].append((out, v("GV%d" % h, s + 1, 2048, 16)))
+                        for x, (q0, q1) in enumerate(((0, EARLY[h]), (EARLY[h], 128))):
+                            early[1 + x].append((bank("key", h, s, 128, 16, (q0, q1)), v("DC%d" % h, 16 * q0 + s, 16 * q1, 16)))
+                    elif kind == "R":
+                        early[2].append((out, v("DV%d" % h, *at)))
                     terms.append((out, v("AB%d" % h, *at), v("BK2" if kind == "R" else "BKk")))
+            for o, l in early[0] + early[1] + early[2]:
+                mm(o, l, v("BKn"), False, False)
             for o, l, r in terms:
                 mm(o, l, r, False, whole and o is terms[-1][0])
             if not whole:
@@ -835,29 +916,35 @@ def rank_program(g, core, T, topo):
 
         def pick(h):
             lo, hi, a, b = 128 * h, 128 * h + 128, 8 * h, 8 * h + 8
-            lst, abc, OH, Yn = "olist%d" % h, "pabc%d" % h, v("OH", lo, hi), v("Yn", lo, hi)
+            lst, abc, OH, Yn = "olist%d" % h, "pabc%d" % h, v("OH", lo, hi), v("Yh", lo, hi)
             scan(v("av", lo, hi), v("NR"), v("val", lo, hi), OP.max, OP.min)
             scan(v("SK", lo, hi), v("RSk"), bank("key", h), OP.min, OP.max, 31.0)
             ts(last("KA", a, b), last("SK", a, b), 992, OP.bitwise_and)
             hold("Dk", "KA", h)
-            if QUICK[h]:
+            if QUICK:
                 tt(v("El", lo, hi), ind(v("KA", lo, hi), v("bcK", 0, 8)), v("DG"), OP.mult)
             else:
                 alone(v("El", lo, hi), v("Dk", lo, hi), v("DG"))
             o = bank("o", h, 0, 24)
-            mms(o, [(v("IdH"), v("OB")), (v("El", lo, hi), v("BM32"))])
-            ts(v(lst), o, v("eQ" if QUICK[h] else "eO"), OP.add)
+            mm(o, v("El", lo, hi), v("BM32"))
+            tt(v(lst), o, v("OE"), OP.add)
             for who, c0, c1 in YGATHER[h]:
-                (cp if who == "V" else act)(v(abc, 128 * c0, 128 * c1), ind(v("GD%d" % h), v(lst, 8 * c0, 8 * c1)))
+                out, src = v(abc, 128 * c0, 128 * c1), ind(v("GD%d" % h), v(lst, 8 * c0, 8 * c1))
+                if who == "V":
+                    ts(out, src, 96.0, OP.add)
+                else:
+                    line(out, src, 1.0, 96.0)
             y = bank("y", h)
-            mms(y, [(v("Ih"), v(abc, 0, 128)), (v("Ih"), v(abc, 128, 256)), (v("Ident"), v(abc, 256, 384))])
-            ts(Yn, y, -192.0, OP.min, -223.5, OP.max)
-            move("Y", h, v("Y", lo, hi), Yn, -2.0, -384.0)
+            mms(y, [(v("Ih"), v(abc, 0, 128)), (v("Ih"), v(abc, 128, 256)), (v("In1"), v(abc, 256, 384))])
+            ts(Yn, y, 31.5, OP.min, 0.0, OP.max)
             ts(OH, v("Dk", lo, hi), 32.0, OP.is_equal)
-            ts(v("sk", lo, hi), v("Dk", lo, hi), 64.0, OP.is_ge)
+            step("sk", h, v("sk", lo, hi), v("Dk", lo, hi), 48.0, 8.0)
             scan(v("dd", lo, hi), v("val", lo, hi), v("sk", lo, hi), OP.add, OP.mult)
             scan(v("ee%d" % h), v("val", lo, hi), v("sk", lo, hi), OP.max, OP.min)
-            mms(bank("PW", h), [(v("IdH"), v("V", lo, hi)), (v("In4k"), v("dd", lo, hi))])
+            mm(bank("PW", h), v("IdH"), v("V", lo, hi), True, False)
+            mm(bank("PW", h, 0, 128, 16), v("InH"), v("V", lo, hi, 16), False, False)
+            mm(bank("PW", h, 0, 128, 16), v("ones", p=2), v("CP", p=2), False, False)
+            mm(bank("PW", h), v("In4k"), v("dd", lo, hi), False, True)
             move("PW", h, v("PW", lo, hi), bank("PW", h), 1.0, 69632.0 + MID)
             alone(v("m2", lo, hi), v("V", lo, hi), OH)
             alone(v("m3", lo, hi), v("VK", lo + 1, hi + 1), OH)
@@ -869,15 +956,15 @@ def rank_program(g, core, T, topo):
         def hashed(h):
             lo, hi, a, b = span(h)
             for x in each(h):
-                mm(bank("u", x, 0, 8), v("Y", *span(x)[:2]), v("W8"))
-            move("Kp", h, v("Kp", a, b), last("m4", a, b), 1184.0, -1184.0 * MID)
+                mm(bank("u", x, 0, 8), v("Yh", *span(x)[:2]), v("W8"))
+            mms(v("pb" + BANK["Kp"], 192 + a, 192 + b), [(v("ones", p=1), v("CK", 0, b - a, p=1)), (v("I37"), last("m4", a, b))])
             move("UI", h, v("UI", a, b), bank("u", h, 0, 8))
             ts(v("UI", a, b), v("UI", a, b), 4095, OP.bitwise_and)
             if WHO["sq"][h % 2] == "V":
                 tt(v("sq", a, b), v("UI", a, b), v("UI", a, b), OP.mult)
             else:
                 act(v("sq", a, b), v("UI", a, b), AF.Square)
-            tt(v("HI", a, b), v("sq", a, b), v("Kp", a, b), OP.add)
+            tt(v("HI", a, b), v("pb" + BANK["Kp"], 192 + a, 192 + b), v("sq", a, b), OP.add)
             ts(v("HI", a, b), v("HI", a, b), 5, OP.arith_shift_right, 4095, OP.bitwise_and)
             move("x", h, v("x", a, b), v("HI", a, b), 1.0, -MID)
             tt(v("hh", a, b), v("x", a, b), v("s1", a, b), OP.max)
@@ -893,27 +980,36 @@ def rank_program(g, core, T, topo):
             mm(z, v("ones"), v("LIM"), False, False)
             mm(z, v("IZv"), v("ee%d" % h, -1, 127), False, False)
             if first < 16:
-                mm(z, v("Y", lo, hi), v("Yw%d" % h), False, False)
+                mm(z, v("Yh", lo, hi), v("Yw%d" % h), False, False)
             for s in range(2, 16):
-                scan(v(EE, 128 * s - 256, 128 * s - 128), v("Yn", lo, hi), v(GV, s, 2048, 16), OP.min, OP.subtract)
+                scan(v(EE, 128 * s - 256, 128 * s - 128), v("Yh", lo, hi), v(GV, s, 2048, 16), OP.max, OP.add)
             for s0 in range(2, first, NRUN[0]):
                 e = v(EE, 128 * s0 - 256, 128 * min(s0 + NRUN[0], first) - 256)
                 act(e, e, AF.Abs, 1.0, 96.0)
             for s0 in range(first, 16, NRUN[1]):
                 e = v(EE, 128 * s0 - 256, 128 * min(s0 + NRUN[1], 16) - 256)
-                ts(e, e, -96.0, OP.max, 144.0, OP.add)
+                ts(e, e, -96.0, OP.max, 48.0, OP.add)
             for s in range(2, 16):
-                mm(bank("z", h, s, 128, 16), v(EE, 128 * s - 256, 128 * s - 128), v("GVw" if s < first else "EEw"), False, s == 15)
-            tt(v("m1", lo, hi), z, v("PW", lo, hi), OP.min)
-            scan(v("SM", lo, hi), v("RSm"), v("m1", lo, hi), OP.min, OP.max, -4097.0)
+                mm(bank("z", h, s, 128, 16), v(EE, 128 * s - 256, 128 * s - 128), v("ABw" if s < first else "EEw"), False, s == 15)
+            scan(back("SM", lo, hi), back("pb" + BANK["z"][h], SPOT["z"][0], SPOT["z"][0] + 128), back("PW", lo, hi), OP.max, OP.min, -4097.0)
+            if WHO["sgm"][h] == "S":
+                act(v("fit", lo, hi), z, AF.Sign)
+            else:
+                ts(v("fit", lo, hi), z, 0.0, OP.is_gt, -0.5, OP.add)
+            scan(v("sgm", lo, hi), v("RSs"), v("fit", lo, hi), OP.min, OP.max, -1.0)
 
         def closed(h):
             a, b = span(h)[2:]
-            ts(v("SB", a, b), last("SM", a, b), 12, OP.logical_shift_right)
-            short[h] = message("B", h, v("SB", a, b), v(rB, a, b), t, FAR)
-            tt(v("kn", a, b), last("SM", a, b), v("TR", a, b), OP.min)
+            ts(v("SB", a, b), found(a, b), 12, OP.logical_shift_right)
+            short[h] = message("B", h, [v("SB", a, b)], [v(rB, a, b)], t, FAR)
+            tt(v("grow", 16 * a + 14, 16 * b, 16), found(a, b), v("s9", a, b), OP.is_lt)
+
+        def named(h):
+            a, b = span(h)[2:]
+            tt(v("kn", a, b), found(a, b), v("TR", a, b), OP.min)
             tt(last("zs1", a, b), v("kn", a, b), v("hh", a, b), OP.max)
-            tt(v("grow", 16 * a + 14, 16 * b, 16), last("SM", a, b), v("s6", a, b), OP.is_lt)
+            ts(v("VM", a, b), found(a, b), 4095, OP.bitwise_and)
+            move("s5", h, v("s5", a, b), v("VM", a, b), 1.0, -MID)
 
         def codes(h):
             lo, hi, a, b = span(h)
@@ -922,21 +1018,18 @@ def rank_program(g, core, T, topo):
                 act(v("gw", lo, hi), ind(v("grow", lo, hi), v("bcG", 0, b - a)))
             else:
                 hold("gw", "grow", h, 1, "RS2")
-            if WHO["sgm"][h % 2] == "S":
-                act(v("sgm", lo, hi), v("SM", lo, hi), AF.Sign, 1.0, 0.5)
-            else:
-                ts(v("sgm", lo, hi), v("SM", lo, hi), 0.0, OP.is_lt, -0.5, OP.add)
-            terms = [("ones", "CZ"), ("Za", "av"), ("Zk", "sk"), ("Zo", "OH"), ("Zo" if WHO["sgm"][h % 2] == "S" else "Zk", "sgm"), ("Zg", "gw")]
+            terms = [("ones", "CZ"), ("Za", "av"), ("Zk", "sk"), ("Zo", "OH"), ("Zo" if WHO["sgm"][h % 2] == "S" else "Z2", "sgm"), ("Zg", "gw")]
             mms(Z, [(v(l, p=1), v(r, 0, hi - lo, p=1)) if r == "CZ" else (v(l), v(r, lo, hi)) for l, r in terms])
-            tt(v("Cp", lo, hi), Z, v("Cd", lo, hi), OP.max)
+            if WHO["Cp"][h] == "S":
+                act(v("Cp", lo, hi), Z)
+            else:
+                tt(v("Cp", lo, hi), Z, v("Cd", lo, hi), OP.max)
             act(Zs, Z, AF.Abs, 1.0 / ZU, -8.625)
-            ts(v("FF", lo, hi), Zs, 9.25, OP.is_ge)
+            step("FF", h, v("FF", lo, hi), Zs, 9.25, 1024.0)
             ts(v(pad("Fu", h)), Zs, 9.125, OP.is_equal)
             mms(bank("F", h), [(v("Ident"), v("FF", lo, hi)), (v("Ident"), v(pad("Fu", h), -1, hi - lo - 1))])
             ts(v(pad("mP", h)), Zs, 6.125, OP.is_equal)
             ts(v("Dn", lo, hi), Zs, 8.375, OP.is_equal)
-            ts(v("VM", a, b), last("SM", a, b), 4095, OP.bitwise_and)
-            move("s5", h, v("s5", a, b), v("VM", a, b), 1.0, -MID)
             if WHO["Fc"][h % 2] == "S":
                 act(v("Fc", lo, hi), Z, AF.Relu, -1.0 / ZU)
             else:
@@ -957,20 +1050,20 @@ def rank_program(g, core, T, topo):
 
         def piece(h):
             lo, hi = span(h)[:2]
-            message("C", h, v("Cp", lo, hi), v(rC, lo, hi), t, FAR + LATER * (hi - lo) / 256, [short.get(h, short.get(2, short.get(0)))])
+            short["C"] = message("C", h, [v("Cp", lo, hi)] + [v("Cd", lo, hi)] * ("S" in WHO["Cp"]), [v(rC, lo, hi)], t, FAR + LATER * (hi - lo) / 256, [short.get(h, short.get(2, short.get(0)))])
 
         def guess(h):
             move("SB", 0, v("Vn"), last("m5"))
-            if h == 2:
-                message("Y", 0, v("VY"), v("rK%d" % t), t, FAR + 2 * LATER)
+            if t < AHEAD:
+                message("Y", 0, [v("VK", 144), v("Yh", 0, 144), v("Yh", 144)], [v(rK, 144), v(rY, 0, 144), v(rY, 144)], t, FAR + 1.5 * LATER)
             else:
-                message("Y", 0, v("YV"), v("rK%d" % t, 272, 544), t, FAR + LATER)
+                message("Y", 0, [v("VK"), v("Yh")], [v(rK), v(rY)], t, FAR + 2 * LATER)
             tt(v("dz", 2, 48, 3), v("V0"), v(rK, 256, 272), OP.max)
-            tt(v("dz", 1, 48, 3), v(rY, 256, 272), v("dz", 2, 48, 3), OP.subtract)
+            tt(v("dz", 1, 48, 3), v(rK, 272, 288), v("dz", 2, 48, 3), OP.subtract)
 
         def shut(h):
             if not lastt:
-                act(v("s4"), last("SM"), AF.Sign, 1.0, 0.5, total=v("cs1"))
+                act(v("s4"), found(), AF.Sign, 1.0, 0.5, total=v("cs1"))
                 mm(bank("c", h, 0, 1), v("onesF"), v("cs1"))
                 move("cI", h, v("cI"), bank("c", h, 0, 1), 0.5, 1024.0)
                 ts(v("cI"), v("cI"), 31, OP.bitwise_and)
@@ -1007,31 +1100,33 @@ def rank_program(g, core, T, topo):
                         ts(v("LC", lo, hi), b, MID, OP.add, float(W), OP.min)
                     else:
                         move("LV", h, v("LV", lo, hi), b, 1.0, MID)
-            counts(h)
+            counts(h, lastt)
 
         def grown(h):
-            cp(ind(v("X"), v("off1", 8 * h, 8 * h + 8)), v("Y", 128 * h, 128 * h + 128))
+            tt(ind(v("X"), v("off1", 8 * h, 8 * h + 8)), v("Yh", 128 * h, 128 * h + 128), v("Yh", 128 * h, 128 * h + 128), OP.add)
 
         def mixed(h):
             lo, hi, a, b = span(h)
-            move("z16", h, v("z16", a, b), v("zz2", a, b), 1.0, MID)
-            move("blend", h, v("BL", lo, hi), ind(v("X"), v("z16", a, b)), 0.5, -0.25)
-            scan(v("g1", lo, hi), v("BL", lo, hi), v(rY, lo, hi), OP.min, OP.subtract, 64.0)
+            move("z16", h, v("z16", a, b), v("oA2", a, b))
+            move("blend", h, v("BL", lo, hi), ind(v("X"), v("z16", a, b)), 0.5, 191.75)
+            scan(v("g1", lo, hi), v(rY, lo, hi), v("BL", lo, hi), OP.min, OP.add, 64.0)
 
         def blend(h):
             lo, hi = 128 * h, 128 * h + 128
             tt(ind(v("X"), v("off2", 8 * h, 8 * h + 8)), v("g1", lo, hi), v("g2", lo, hi), OP.add)
 
-        ts(v("s6"), last("cum"), 4.0, OP.is_lt, -8192.0, OP.mult)
-        tt(v("s1"), v("TRm"), v("s6"), OP.subtract)
-        if "y2" not in PARTS:
-            message("K", 0, v("VK"), v(rK, 0, 272), t, FAR + 2.0)
-        ts(v("s7"), last("cum"), 4.0, OP.is_lt, 16.0, OP.mult)
-        tt(v("th2"), v("s7"), last("cum"), OP.subtract)
+        ts(v("s9"), rows(), 4.0, OP.is_lt, -8192.0, OP.mult)
+        tt(v("s1"), v("TRm"), v("s9"), OP.subtract)
+        if t < AHEAD:
+            message("K", 0, [v("VK", 0, 144)], [v(rK, 0, 144)], t, FAR + 6.0)
+        ts(v("s7"), rows(), 4.0, OP.is_lt, 16.0, OP.mult)
+        tt(v("th2"), v("s7"), rows(), OP.subtract)
         for part[0] in PARTS.split():
             {"b": bends, "g": gates, "k": key, "p": pick, "h": hashed, "n": near, "c": closed, "d": lambda h: dedupe("1", h), "z": codes,
-             "f": moved, "w": grown, "q": shut, "t": takes, "e": lambda h: dedupe("2", h), "s": stays, "r": taken, "l": mixed, "x": blend, "y": guess, "m": piece}[part[0][0]](int(part[0][1]))
+             "f": moved, "w": grown, "q": shut, "t": takes, "e": lambda h: dedupe("2", h), "s": stays, "r": taken, "l": mixed, "x": blend, "y": guess, "m": piece, "j": named}[part[0][0]](int(part[0][1]))
         part[0] = ""
+        if t == 0:
+            shifts(short["C"])
         if not lastt:
             tt(v("s3"), v("zs2", 47, 768, 48), v("dz", 2, 48, 3), OP.subtract)
             tt(v("V0"), v("V0"), v("s3"), OP.add)

import numpy as np
from concourse.bass import DstId, RemoteDMATransfer
from concourse.mybir import AluOpType, AxisListType, ActivationFunctionType

OP = AluOpType
AF = ActivationFunctionType
W, L, S, ST = 4096, 256, 16, 5
BIG, KZ, MID, ZU = 4194304.0, 262144.0, 2048.0, 3072.0
F32, BF, I32, U16, F16 = "float32", "bfloat16", "int32", "uint16", "float16"

RUNS = "SVM32 SVM64 SVM32|VVM16 SVM48 SVM64"
SLOTS = ("A4 R5 R5", "T4 T4 A6")
DIFF = "07"
PARTS = "b1 b0 g1 k1 p1 g0 k0 n1 p0 y2 h2 c1 j1 d1 z1 f1 n0 w1 c0 j0 t1 d0 e1 z0 m2 s1 r1 w0 f0 t0 q0 e0 l1 l0 s0 r0 x1 x0"
YGATHER = ((("S", 0, 3),), (("S", 0, 3),))
WHO = {"Y": "SS", "SB": "SS", "sgm": "SS", "off1": "SS", "off2": "SS", "cI": "SS", "Ru1": "SS", "Ru2": "PS", "blend": "SS", "sq": "SS", "V": "SS", "Cd": "SS", "Kp": "SS", "zz1": "PP", "zz2": "PP", "x": "SS", "s5": "SS", "LV": "SS", "UI": "SS", "z16": "SS", "PW": "SS", "keep": "SS", "xw": "VS", "gw": "VS", "tw": "VS", "Fc": "SS", "Cp": "VV", "val": "VV", "FF": "VV", "sk": "VV", "g1": "VV"}
QUICK = 1
AHEAD = 1
REST = "TV"
EARLY = (0, 0)
NABS = (0, 7)
NRUN = (4, 4)
BANK = {"Kp": "0", "key": "23", "z": "16", "PW": "23", "u": "77", "Z": "16", "F": "54", "keep": "16", "tw": "54", "list": "16", "c": "77", "old": "54", "Cx": "54", "Cn": "54", "Ru1": "23", "Ru2": "27", "zU1": "07", "zU2": "23", "sum1": "23", "sum2": "07", "off1": "23", "off2": "07"}
SPOT = {"bl": (0, 128), "key": (0, 0), "o": (128, 0), "y": (256, 0), "z": (384, 0), "PW": (384, 0), "u": (160, 8), "Z": (0, 0), "F": (256, 0), "keep": (128, 0), "tw": (384, 0), "list": (256, 0), "c": (0, 0), "old": (0, 0), "Cx": (128, 0), "Cn": (256, 0), "Ru1": (0, 0), "Ru2": (128, 0), "zU1": (448, 8), "zU2": (464, 8), "sum1": (256, 0), "sum2": (320, 0), "off1": (480, 8), "off2": (496, 8)}
CYC, GATHER, SCATTER = 0.00083, 1.56, 3.8
WAKE = 0.215
TFIX = 0.006
VFIX = 0.0
ISSUE = 0.9
FIRST = 2.0
LOAD = 4.2
SMALL = 1.8
FAR = 2.5
LATER = 0.8
LONG = 2
SEED = 2
TURNS = 8000
POLISH = 1300
DEAR = (1.66, 4.1, 0.97)
WARM = 0.4
LOCAL = 0.3
ALONE = "cjdzfwtesrlxm"
LUMP = {"V": 0.0, "T": 0.0}
SHAKE = 0.3
SHIFT = 1.0
PLAN = {}
XW = W + 4 * L
GW = 2064
KEYS = []
for _r in RUNS.split("|"):
    KEYS.append([])
    for _k in _r.split("/"):
        _p = KEYS[-1][-1][1] if KEYS[-1] else 0
        KEYS[-1].append((_p, _p + sum(int(x[3:]) for x in _k.split()), _k.split()[0][2]))
RUNS = [[(x[:2], x[2], int(x[3:])) for x in r.split() if x != "/"] for r in RUNS.split("|")]
SLOTS = [[(x[0], int(x[1:])) for x in r.split()] for r in SLOTS]
SCRATCH = {"X": ("sbuf", [128, XW], BF)}
ALIAS = {}


def _pack(buf, names, cols, d, pad=0):
    names = names.split()
    for k, n in enumerate(names):
        ALIAS[n] = (buf, k * (cols + pad) + pad, cols, d)
    SCRATCH[buf] = ("sbuf", [128, len(names) * (cols + pad)], d)


def _add(names, cols, d):
    for n in names.split():
        SCRATCH[n] = ("sbuf", [128, cols], d)


for _h in "01":
    SCRATCH["GD" + _h] = ("sbuf", [128, 2 * GW], BF)
    ALIAS["GV" + _h], ALIAS["DC" + _h] = ("GD" + _h, 0, GW, BF), ("GD" + _h, GW, GW, BF)
_add("AB0 AB1 CG0 CG1", 2048, BF)
_add("DV0 DV1", 2048, F16)
_add("EE0 EE1", 1792, BF)
_add("EQ", 2048, BF)
_add("VK", 288, F16)
_add("Yh", 288, BF)
ALIAS["V"], ALIAS["s1"], ALIAS["Vn"] = ("VK", 0, 256, F16), ("VK", 256, 16, F16), ("VK", 272, 16, F16)
_pack("YN", "Cp Cd BL", 256, F16)
for _t in range(ST):
    _add("rK%d" % _t, 288, F16)
    _add("rY%d" % _t, 288, BF)
    _add("rC%d" % _t, 256, F16)
    _add("rB%d" % _t, 16, I32)
_add("SB", 16, I32)
_pack("MH", "Wz1 Ez1 Ru1 Wz2 Ez2 Ru2 xw kw i1 m2 m3 m4 m5 upV upC dnV dnC fxV fxC kpV kpC inV inC tV tC", 256, F16)
_pack("MI", "IdH InH Uh0 Uh1 Uh2 Uh3 Uh4 Uh8 Uh12", 128, F16)
_add("blk8H", 8, F16)
_pack("MP", "ee0 ee1 mP0 mP1 Fu0 Fu1", 128, BF, 16)
if "z2" in PARTS:
    for _n in ("mP", "Fu"):
        _at = ALIAS[_n + "0"][1]
        ALIAS[_n + "1"], ALIAS[_n + "2"] = ("MP", _at + 128, 128, BF), ("MP", _at, 256, BF)
_pack("MZ", "zs1 sx", 256, F16)
_add("zs2", 768, F16)
_add("take", 768, BF)
_pack("MF", "PW QC f1 f2 LNF", 256, F32)
_pack("MQ", "mm onesF PW2 G8 n3 n4 RSk THR", 128, F32)
_pack("MB", "val cum av sgp sk dd sgm gw tw keep Dn FF Fc fit Zs El Em1 Em2 rc Dk g1 g2 g3 grow OH RS RS2 CZ", 256, BF)
_add("pabc0 pabc1", 384, BF)
_add("SK SM KA IV IC LNI", 256, I32)
_add("LV LC", 256, U16)
_pack("PLF", "nn V0 x kn Kp sq hh s2 s3 s4 s5 s9 th2 TR TRm oA1 oA2 zz1 zz2 t1", 16, F32)
_add("dz", 48, F32)
_pack("PLI", "UI HI VM", 16, I32)
_pack("PLU", "off1 off2 z16 bcA bcG bcT bcK", 16, U16)
_pack("OL", "olist0 olist1", 24, U16)
_add("OB", 24, F32)
_add("BM32", 24, BF)
_add("BMh", 16, F16)
_add("OE", 24, F32)
_pack("COF", "pcF pmF p4F thm lim cs1 e1 e2 e3 e4 e5 e6 e7 eK eO eH eL eM wF wq wp", 1, F32)
_pack("COI", "pcI pmI p4I cI tI", 1, I32)
_add("WI THI", 1, I32)
_pack("IDS", "Ident In1 Za Zk Zo Zg Z2 RSs Ih Ibig IZv In4k In4 I64 I2k I8k I37 ones Yw0 Yw1 LIM blkw blkl CR zero two NR DG Ub0 Ub1 Ub2 Ub3", 128, BF)
_pack("N8", "BKk BK2 BKn EEw GVw ABw W8 CP", 8, BF)
_add("BW", 64, BF)
_add("CK s7", 16, BF)
_add("blk8F THF IdF", 8, F32)
LOOPWISE = any(k[2] == "T" for r in KEYS for k in r)
for _b in range(8):
    SCRATCH["pb%d" % _b] = ("psum", [128, 32, 16] if str(_b) in DIFF and LOOPWISE else [128, 512], F32)

MAIL = ("K0", "Y0", "B0", "B1", "C0", "C1")
SEMAPHORES = ["sV", "sS", "sT", "sG"] + ["l" + m for m in MAIL] + ["a%s%d" % (m, t) for m in MAIL for t in range(ST)]
SEMAPHORES += ["d%d" % k for k in range(12)]


def order(OPS):
    n = len(OPS)
    seen, deps = {}, []
    for i, o in enumerate(OPS):
        q, dp = o[0], {}
        for j in o[7]:
            dp[j] = 0
        for j in o[6]:
            dp[j] = 1
        for acc, wr in [(a, 0) for a in o[2]] + [(a, 1) for a in o[3]]:
            name, lo, hi = acc
            for (l2, h2, j, q2, w2) in seen.get(name, []):
                if lo < h2 and l2 < hi and (wr or w2):
                    dp[j] = max(dp.get(j, 0), 0 if q == q2 == "T" else 1)
        for acc, wr in [(a, 0) for a in o[2]] + [(a, 1) for a in o[3]]:
            name, lo, hi = acc
            old = seen.get(name, [])
            if wr:
                old = [r for r in old if not (lo <= r[0] and r[1] <= hi)]
            seen[name] = old + [(lo, hi, i, q, wr)]
        dp.pop(i, None)
        deps.append(dp)
    sums, opened = [], {}
    for i, o in enumerate(OPS):
        if o[8]:
            b = o[3][0][0]
            if o[8][0]:
                opened[b] = [b, i]
                sums.append(opened[b])
            else:
                deps[i].setdefault(opened[b][1], 0)
                opened[b].append(i)
            if o[8][1]:
                for j in opened[b][1:-1]:
                    deps[i].setdefault(j, 0)
    lastof = {}
    for s in sums:
        for e in reversed(lastof.setdefault(s[0], [])):
            if len(s) > LONG or len(e) > LONG:
                deps[s[1]].setdefault(e[-1], 0)
            if len(e) > LONG:
                break
        lastof[s[0]].append(s)
    above = []
    for i in range(n):
        m = 0
        for j in sorted(deps[i], reverse=True):
            if m >> j & 1 and any(deps[i][k] >= deps[i][j] and above[k] >> j & 1 and OPS[j][5] == 0 for k in deps[i]):
                del deps[i][j]
            m |= above[j] | (1 << j)
        above.append(m)
    qs, cost, lat = [o[0] for o in OPS], [o[4] for o in OPS], [o[5] for o in OPS]
    banks = [sorted({a[0] for a in o[2] + o[3] if a[0].startswith("pb")}) for o in OPS]
    fwd = [[(j, cost[j] + (lat[j] + WAKE if k else 0.0)) for j, k in deps[i].items()] for i in range(n)]
    PLAN["debug"] = (OPS, None, cost, None, fwd)
    lump, at, heads, open_ = [], [], [], {}
    for i, o in enumerate(OPS):
        m = open_.get(qs[i])
        h = heads[m][0] if m is not None else -1
        if (h >= 0 and qs[i] in "VT" and OPS[h][9:] == o[9:] and OPS[h][3][0][0] == o[3][0][0] and banks[h] == banks[i] and heads[m][1] + cost[i] <= LUMP[qs[i]]
                and all((lump[j] == m and not k) or above[h] >> j & 1 for j, k in deps[i].items())):
            at.append(heads[m][1])
            heads[m][1] += cost[i]
        else:
            m = open_[qs[i]] = len(heads)
            heads.append([i, cost[i]])
            at.append(0.0)
        lump.append(m)
    calls, n = n, len(heads)
    edges, lat2 = [{} for _ in heads], [0.0] * n
    for i in range(calls):
        lat2[lump[i]] = max(lat2[lump[i]], at[i] + cost[i] + lat[i] - heads[lump[i]][1])
        for j, w in fwd[i]:
            if lump[j] != lump[i]:
                edges[lump[i]][lump[j]] = max(edges[lump[i]].get(lump[j], -99.0), at[j] + w - at[i])
    OPS = [OPS[h] for h, _c in heads]
    qs, cost, lat, banks, deps = [qs[h] for h, _c in heads], [c for _h, c in heads], lat2, [banks[h] for h, _c in heads], edges
    fwd = [list(e.items()) for e in edges]
    bwd = [[] for _ in OPS]
    for i in range(n):
        for j, w in fwd[i]:
            bwd[j].append((i, w - cost[j] + cost[i]))

    wake = [WAKE]

    def fit(key, before, first, line):
        gap = wake[0]
        for i in line:
            x = key[i]
            for j, _w in before[i]:
                if key[j] >= x:
                    x = key[j] + 1e-7
            key[i] = x
        line = np.argsort(key, kind="stable").tolist()
        start, busy = [0.0] * n, {q: ([], []) for q in "VSTGYF"}
        held = {"pb%d" % b: ([], [], []) for b in range(8)}
        for i in line:
            q, c, t = qs[i], cost[i], first[i]
            for j, w in before[i]:
                if start[j] + w > t:
                    t = start[j] + w
            s, e = busy[q]
            k = len(e)
            while k and e[k - 1] > t + 1e-9:
                k -= 1
            while True:
                while k < len(s) and s[k] < t + c - 1e-9:
                    if e[k] > t:
                        t = e[k]
                    k += 1
                moved = False
                for b in banks[i]:
                    be, bs, bq = held[b]
                    m = len(be)
                    while m and be[m - 1] > t - gap + 1e-9:
                        m -= 1
                        if bq[m] != q and bs[m] < t + c + gap - 1e-9:
                            t, moved = be[m] + gap, True
                            break
                if not moved:
                    break
            start[i] = t
            if k and e[k - 1] >= t - 1e-9:
                if k < len(s) and s[k] <= t + c + 1e-9:
                    e[k - 1] = e[k]
                    del s[k], e[k]
                else:
                    e[k - 1] = t + c
            elif k < len(s) and s[k] <= t + c + 1e-9:
                s[k] = t
            else:
                s.insert(k, t)
                e.insert(k, t + c)
            for b in banks[i]:
                be, bs, bq = held[b]
                m = len(be)
                while m and be[m - 1] > t + c:
                    m -= 1
                be.insert(m, t + c)
                bs.insert(m, t)
                bq.insert(m, q)
        return np.array(start), line
    none, up, down = [0.0] * n, range(n), range(n - 1, -1, -1)
    took, whole = np.array(cost), np.array(cost) + np.array(lat)

    def forth(key):
        start, line = fit(key.tolist(), fwd, none, up)
        return float((start + whole).max()), start, line

    def again(start):
        return forth(-fit((-start - took).tolist(), bwd, lat, down)[0] - took)

    def blocked(start):
        st, ends, out = start.tolist(), {}, []
        for i in range(n):
            ends[(qs[i], round(st[i] + cost[i], 5))] = i
            for b in banks[i]:
                ends[(b, round(st[i] + cost[i] + wake[0], 5))] = i
        i = int((start + whole).argmax())
        while st[i] > 1e-6:
            j = [j for j, w in fwd[i] if abs(st[j] + w - st[i]) < 1e-6]
            if not j:
                j = [ends[c] for c in [(x, round(st[i], 5)) for x in [qs[i]] + banks[i]] if ends.get(c, i) != i]
                if not j:
                    break
                out.append((j[0], i))
            i = j[0]
        return out
    tail = [0.0] * n
    for i in down:
        tail[i] = max([lat[i]] + [tail[j] + w for j, w in bwd[i]])
    PLAN["chain"] = max(tail[i] + cost[i] for i in range(n))
    kinds, parts = {}, {}
    own = [o[10] == ST - 1 and o[9][:1] in ALONE for o in OPS]
    kind = np.array([kinds.setdefault((o[0], str(o[3]), str([a for a in o[2] if a[0][0] != "r"]), own[i]), len(kinds)) for i, o in enumerate(OPS)])
    part = np.array([parts.setdefault((o[9], o[0], own[i]), len(parts)) for i, o in enumerate(OPS)])
    rng = np.random.default_rng(SEED)
    best = now = again(forth(-np.array(tail) - took)[1])
    pairs = None
    for k in range(TURNS + POLISH):
        if k == TURNS:
            lists = ("LV", "LC", "PLU", "OL")
            was = list(cost)
            for i, o in enumerate(OPS):
                if qs[i] == "V" and o[3][0][0] == "X" and len(o[3]) > 1:
                    cost[i] = 0.05 + (cost[i] - 0.05) * DEAR[1] / SCATTER
                elif qs[i] in "VS" and lat[i] == 0 and o[3][0][0] not in lists and any(a[0] in lists for a in o[2]):
                    cost[i] = 0.06 + (cost[i] - 0.06) * DEAR[0] / GATHER
                lat[i] *= DEAR[2]
            wake[0] *= DEAR[2]
            fwd[:] = [[(j, cost[j] + (w - was[j]) * DEAR[2]) for j, w in e] for e in fwd]
            bwd[:] = [[] for _ in OPS]
            for i in range(n):
                for j, w in fwd[i]:
                    bwd[j].append((i, w - cost[j] + cost[i]))
            took[:], whole[:] = np.array(cost), np.array(cost) + np.array(lat)
            best = now = forth(best[1].copy())
            pairs = None
        how, s = rng.random() * (1.0 if k < TURNS else 0.5 + LOCAL), now[1]
        if how < 0.5:
            pairs = pairs or blocked(s)
            noise = np.zeros(len(kinds))
            for _ in range(1 + int(rng.integers(3))):
                j, i = pairs[int(rng.integers(len(pairs)))]
                if rng.random() < 0.5:
                    noise[kind[j]] = s[i] - s[j] + 0.01 + rng.random() * 0.5
                else:
                    goal, todo = s[j] - 0.01, [i]
                    while todo:
                        x = todo.pop()
                        if s[x] + noise[kind[x]] > goal:
                            noise[kind[x]] = goal - s[x]
                            todo += deps[x]
            new = forth(s + noise[kind])
            if now[0] - 1e-6 < new[0] < now[0] + 1.5:
                new = min(new, again(new[1]), key=lambda r: r[0])
        elif how < 0.5 + LOCAL:
            at0 = rng.random() * now[0]
            noise = np.zeros(len(kinds))
            near = kind[(s > at0) & (s < at0 + 2.0)]
            noise[near] = rng.normal(0.0, 2 * SHAKE, len(near))
            new = forth(s + noise[kind]) if k % 2 else again(s - noise[kind])
        elif how < 0.75 + LOCAL / 2:
            new = again(s - (rng.normal(0.0, SHIFT, len(parts)) * (rng.random(len(parts)) < 0.1))[part])
        else:
            new = again(s - (rng.normal(0.0, SHAKE, len(kinds)) * (rng.random(len(kinds)) < 0.2))[kind])
        if new[0] < now[0] + (WARM * (1 - k / TURNS) if k < TURNS else 0.03) * rng.random():
            now, pairs = new, None
            if now[0] < best[0]:
                best = now
    PLAN["end"], PLAN["lumps"] = best[0], n
    place = {m: k for k, m in enumerate(best[2])}
    return sorted(range(calls), key=lambda i: (round(float(best[1][lump[i]]) + at[i], 6), place[lump[i]], i))


def rank_program(g, core, T, topo):
    rank = T.rank_of(core)
    if rank is None:
        return
    queues = {"V": g.vector, "S": g.scalar, "T": g.tensor, "G": g, "Y": g.sync}
    count = {}
    known = {q: {} for q in queues}
    clock = {}
    recs = {}
    ndma = [0]
    part = ["", -1]

    def v(name, lo=0, hi=None, step=1, p=None):
        if name in ALIAS:
            name, at, width, _d = ALIAS[name]
            hi = at + (width if hi is None else hi)
            lo += at
        t = T[name]
        if len(SCRATCH[name][1]) == 3:
            hi = SCRATCH[name][1][1] * 16 if hi is None else hi
            a, b, s = lo // 16, (hi + 15) // 16, lo % 16
            p1 = p or 128
            if step < 0:
                return (t[:, a:b, s:s + 14], [(name, lo, hi)], (b - a) * 14, False)
            if hi - lo < 16:
                return (t[0:p1, a, s:s + hi - lo], [(name, lo, hi)], hi - lo, False)
            return (t[0:p1, a:b, :] if step == 1 else t[0:p1, a:b, s], [(name, lo, hi)], (hi - lo + step - 1) // step, False)
        hi = SCRATCH[name][1][1] if hi is None else hi
        sl = slice(lo, hi, step) if step != 1 else slice(lo, hi)
        p0, p1 = p if isinstance(p, tuple) else (0, p or 128)
        return (t[p0:p1, sl], [(name, lo, hi)], (hi - lo + step - 1) // step, False)

    def back(name, lo, hi, step=1):
        x = v(name, lo, hi, step)
        name, lo, hi = x[1][0]
        return (T[name][:, hi - 1:(lo - 1 if lo else None):-step],) + x[1:]

    def ind(win, off):
        return (win[0].indirect(off[0]), win[1] + off[1], off[2] * 16, True)

    def need(q, reads, writes):
        toks = []
        for acc, wr in [(a, False) for a in reads] + [(a, True) for a in writes]:
            name, lo, hi = acc
            bank = name.startswith("pb")
            for (l2, h2, tok, q2, w2) in recs.get(name, []):
                if bank and q2 != q:
                    toks.append(tok)
                elif lo < h2 and l2 < hi and (wr or w2):
                    if q2 == q and q == "T":
                        continue
                    toks.append(tok)
        return toks

    def wait(q, toks):
        best = {}
        for s, n in toks:
            best[s] = max(best.get(s, 0), n)
        kn = known[q]
        todo = sorted(best.items(), key=lambda a: -len(clock.get(a, {})))
        for s, n in todo:
            if kn.get(s, 0) >= n:
                continue
            if any(clock.get((s2, n2), {}).get(s, 0) >= n for s2, n2 in todo if s2 != s and kn.get(s2, 0) < n2):
                continue
            queues[q].wait_ge(T.sem[s], n)
            for s3, n3 in clock.get((s, n), {}).items():
                kn[s3] = max(kn.get(s3, 0), n3)
            kn[s] = max(kn.get(s, 0), n)

    def record(q, tok, reads, writes):
        for acc, wr in [(a, False) for a in reads] + [(a, True) for a in writes]:
            name, lo, hi = acc
            old = recs.get(name, [])
            if name.startswith("pb"):
                old = [r for r in old if r[3] == q]
            if wr:
                old = [r for r in old if not (lo <= r[0] and r[1] <= hi)]
            else:
                old = [r for r in old if r[4] or r[3] != q or (r[0], r[1]) != (lo, hi)]
            old.append((lo, hi, tok, q, wr))
            recs[name] = old

    def bump(q, sem, n):
        count[sem] = count.get(sem, 0) + n
        tok = (sem, count[sem])
        clock[tok] = dict(known[q])
        return tok

    OPS = []

    def add(q, emit, reads, writes, cost, lat=0.0, after=()):
        OPS.append([q, emit, [a for x in reads for a in x[1]], [a for x in writes for a in x[1]], cost, lat, list(after), [], None, part[0], part[1]])
        return len(OPS) - 1

    def op(q, fn, reads, writes, cost=0.06):
        def emit(rd, wr):
            wait(q, need(q, rd, wr))
            sem = "s" + q
            fn(queues[q]).then_inc(T.sem[sem], 1)
            record(q, bump(q, sem, 1), rd, wr)
        return add(q, emit, reads, writes, cost + VFIX * (q == "V"))

    def dma(q, out, in_, reads=(), writes=(), lat=SMALL):
        sem = "d%d" % ndma[0]
        ndma[0] += 1

        def emit(rd, wr):
            wait(q, need(q, rd, wr))
            queues[q].dma_start(out, in_).then_inc(T.sem[sem], 16)
            record(q + "d", bump(q, sem, 16), rd, wr)
        return add(q, emit, reads, writes, 0.1, lat)

    def vcost(out, a, b=None):
        views = [x for x in (out, a, b) if x is not None]
        if out[3]:
            return 0.05 + SCATTER * CYC * out[2]
        if any(x[3] for x in views):
            return 0.05 + GATHER * CYC * out[2]
        n = max(out[2], a[2])
        psum = any(x[1][0][0].startswith("pb") for x in views[1:])
        small = all(SCRATCH[x[1][0][0]][2] in (BF, U16, F16) for x in views)
        if b is not None:
            n *= 1 if psum else 2
        elif small:
            n *= 0.5
        return max(64, n) * CYC

    def tt(out, a, b, o):
        op("V", lambda e: e.tensor_tensor(out[0], a[0], b[0], o), [a, b], [out], vcost(out, a, b))

    def ts(out, a, s1, o0, s2=None, o1=None):
        rd = [a] + [x for x in (s1, s2) if isinstance(x, tuple)]
        x1 = s1[0] if isinstance(s1, tuple) else s1
        x2 = s2[0] if isinstance(s2, tuple) else s2
        if o1 is None:
            op("V", lambda e: e.tensor_scalar(out[0], a[0], x1, None, o0), rd, [out], vcost(out, a))
        else:
            op("V", lambda e: e.tensor_scalar(out[0], a[0], x1, x2, o0, o1), rd, [out], vcost(out, a))

    def cp(out, a):
        op("V", lambda e: e.tensor_copy(out[0], a[0]), [a], [out], vcost(out, a))

    def act(out, a, f=AF.Copy, scale=1.0, bias=0.0, total=None):
        c = (0.07 + GATHER * CYC * out[2]) if a[3] else 0.12 + CYC * max(64, out[2])
        rd = [a] + [x for x in (scale, bias) if isinstance(x, tuple)]
        sc = scale[0] if isinstance(scale, tuple) else scale
        bi = bias[0] if isinstance(bias, tuple) else bias
        if total is None:
            op("S", lambda e: e.activation(out[0], a[0], f, bias=bi, scale=sc), rd, [out], c)
        else:
            op("S", lambda e: e.activation(out[0], a[0], f, bias=bi, scale=sc, accum_out=total[0]), rd, [out, total], c + 0.02)

    def line(dst, x, scale, bias):
        act(dst, x, AF.Identity, scale, bias)

    def move(who, h, out, a, scale=None, bias=None):
        if scale is None:
            (cp if WHO[who][h % 2] == "V" else act)(out, a)
        elif WHO[who][h % 2] == "V":
            ts(out, a, scale, OP.mult, bias, OP.add)
        else:
            line(out, a, scale, bias)

    def step(who, h, out, a, edge, scale):
        if WHO[who][h % 2] == "V":
            ts(out, a, edge, OP.is_gt if scale > 0 else OP.is_lt)
        else:
            act(out, a, AF.Sigmoid, scale, -scale * edge)

    def mm(out, l, r, start=True, stop=True):
        c = TFIX + max(min(64, l[2]), r[2]) * CYC * (4 if SCRATCH[r[1][0][0]][2] == F32 else 1)
        OPS[op("T", lambda e: e.matmul(out[0], l[0], r[0], start, stop), [l, r], [out], c)][8] = (start, stop)

    def mms(out, terms):
        for k, (l, r) in enumerate(terms):
            mm(out, l, r, k == 0, k == len(terms) - 1)

    def scan(out, d0, d1, o0, o1, init=0.0):
        small = all(SCRATCH[x[1][0][0]][2] in (BF, F16) for x in (out, d0, d1))
        op("V", lambda e: e.tensor_tensor_scan(out[0], d0[0], d1[0], init, o0, o1), [d0, d1], [out], max(64, out[2] * (0.5 if small else 1)) * CYC)

    def alone(out, a, ones):
        scan(out, a, ones, OP.add, OP.mult)

    def hold(out, x, h, step=1, keep="RS"):
        lo, hi = span(h)[:2]
        scan(back(out, lo, hi), v(keep, 0, hi - lo), back(x, lo * step, hi * step, step), OP.mult, OP.add)

    def total(out, a):
        op("V", lambda e: e.tensor_reduce(out[0], a[0], AxisListType.X, OP.add), [a], [out], max(64, a[2]) * CYC)

    def fill(out, c):
        op("V", lambda e: e.memset(out[0], c), [], [out], max(64, out[2] * 0.5) * CYC)

    def iota(out, pat, base, cm):
        if SCRATCH[out[1][0][0]][2] == I32:
            op("G", lambda e: e.iota(out[0], pat, base, cm), [], [out], 0.13 + 2 * CYC * out[2])
        else:
            op("G", lambda e: e.iota(out[0], pat, base, cm, allow_small_or_imprecise_dtypes=True), [], [out], 0.13 + 2 * CYC * out[2])

    def mask(out, a, pat, cmp, other, base, cm):
        op("G", lambda e: e.affine_select(out[0], a[0], pat, cmp, other, base, cm), [a], [out], 0.17 + 2 * CYC * out[2])

    def select(out, a, cmp, other, k):
        mask(out, a, [[1, out[2]]], cmp, other, k, -1)

    def bc(x, h=None):
        return ind(v(x), v("bcA")) if h in (None, 2) else ind(v(x, 8 * h, 8 * h + 8), v("bcA", 0, 8))

    def last(name, a0=0, a1=16):
        return v(name, a0 * 16 + 15, a1 * 16, 16)

    def found(a0=0, a1=16):
        return v("SM", a0 * 16 + 1, a1 * 16, 16)

    def third(x, h, step=48):
        return v(x, 3 * span(h)[0] + step - 1, 3 * span(h)[1], step)

    def pad(name, h):
        return name + str(h)

    def turn(dst, src):
        for h in range(2):
            mm(v(dst[0], dst[1] + 128 * h, dst[1] + 128 * h + 128), v(src, 128 * h, 128 * h + 128), v("IdH"))

    def bank(name, h, lo=0, hi=128, step=1, p=None):
        at, width = SPOT[name]
        if h == 2:
            assert BANK[name][0] == BANK[name][1] and width
            h, hi = 0, hi + width
        return v("pb" + BANK[{"o": "key", "y": "key"}.get(name, name)][h], at + h * width + lo, at + h * width + hi, step, p)

    def span(h):
        return (0, 256, 0, 16) if h == 2 else (128 * h, 128 * h + 128, 8 * h, 8 * h + 8)

    def each(h):
        return (1, 0) if h == 2 else (h,)

    half = W // 2
    dma("Y", T.IV[:], T.vl[:], [], [v("IV")])
    dma("S", T.IC[:], T.cl[:], [], [v("IC")])
    dma("Y", T.X[:, 0:half], T.xc[:, 0:half], [], [v("X", 0, half)], LOAD)
    dma("S", T.X[:, half:W], T.xc[:, half:W], [], [v("X", half, W)], LOAD)
    dma("Y", T.LNI[0:8, :], T.ln[:], [], [v("LNI")])
    dma("S", T.WI[:], T.wt[:], [], [v("WI")])
    dma("Y", T.THI[0:8, :], T.th[:], [], [v("THI")])

    iota(v("pcI"), [[0, 1]], 0, 1)
    iota(v("mm"), [[1, 128]], 0, 0)
    iota(v("QC"), [[0, 16], [1, 16]], 0, 0)
    slots = [[0, 8], [1, 16]]
    for nm, c in (("ones", 1), ("zero", 0), ("onesF", 1), ("two", 2), ("g2", -192), ("dz", 0), ("KA", -32)):
        iota(v(nm), [[0, v(nm)[2]]], c, 0)
    for x in (v("EQ"), v("take"), v("grow"), v("X", W, XW), v("Yh", 256, 288)):
        fill(x, 0.0)
    cp(v("MZ"), v("take", 0, 512))
    cp(v("zs2"), v("take"))
    iota(v("TR"), [[512, 2], [0, 8]], W // 2, 4)
    iota(v("TRm"), [[512, 2], [0, 8]], W // 2 - 8192, 4)
    iota(v("OB", 0, 8), [[256, 8]], GW, 0)
    iota(v("OB", 8, 24), [[1, 2], [256, 8]], 0, 0)
    iota(v("t1"), [[512, 2], [0, 8]], W, 4)
    iota(v("f2", 0, 64), [[1, 8], [0, 8]], 0, 0)
    iota(v("f2", 64, 88), [[0, 3], [1, 8]], 0, 0)
    for nm in ("GV0", "GV1", "DC0", "DC1"):
        iota(v(nm, 2048, GW), [[0, GW - 2048]], 0, 0)
    iota(v("MP", 15, 6 * 144, 144), [[0, 6]], 0, 0)
    iota(v("upV", 0, 512, 128), [[0, 4]], 0, 0)
    iota(v("dnV", 127, 512, 128), [[0, 4]], 0, 0)
    iota(v("CR"), [[0, 8], [-32, 16]], 512, 0)
    iota(last("CR", 0, 8), [[0, 8]], int(BIG), 0)
    iota(v("CZ"), [[0, 256]], int(2 * ZU), 0)
    iota(last("CZ"), [[0, 16]], int(10 * ZU), 0)
    iota(v("CK"), [[0, 16]], -1184 * 2048, 0)
    iota(v("CP", p=2), [[0, 8]], -75776, 75775)
    for lo in (0, 128):
        mask(v("RS", lo, lo + 128), v("ones"), slots, OP.is_gt, 0.0, 0, 0)
        mask(v("RS2", lo, lo + 128), v("ones"), slots, OP.is_ge, 0.0, -2, 0)
    mask(v("NR"), v("zero"), slots, OP.is_gt, 1.0, 0, 0)
    mask(v("G8", p=8), v("onesF", p=8), [[-1, 8], [0, 16]], OP.is_equal, 0.0, 0, 1)
    mask(v("blkw"), v("ones"), [[-16, 8], [0, 16]], OP.is_ge, 0.0, 0, 1)
    mask(v("blkw"), v("blkw"), [[16, 8], [0, 16]], OP.is_ge, 0.0, 15, -1)
    mask(v("blkl"), v("blkw"), [[256, 8], [-1, 16]], OP.is_ge, 0.0, 241, -16)
    for h in range(2):
        if NABS[h] < 14:
            line(v("Yw%d" % h), v("blkw"), 2 * KZ, 0.0)
            mask(v("Yw%d" % h), v("Yw%d" % h), slots, OP.is_ge, 0.0, -2 - NABS[h], 0)
    ts(v("pmI"), v("pcI"), 15, OP.bitwise_and)
    ts(v("p4I"), v("pcI"), 4, OP.arith_shift_right)
    cp(v("COF", 0, 3), v("COI", 0, 3))
    cp(v("LV"), v("IV"))
    cp(v("LC"), v("IC"))
    cp(v("bcA"), v("mm", 0, 16))
    if "S" in WHO["tw"]:
        ts(v("bcT"), v("mm", 0, 16), 48.0, OP.mult, 47.0, OP.add)
    if "S" in WHO["gw"]:
        ts(v("e5"), v("pmF"), 15.0, OP.is_equal, 14.0, OP.add)
        ts(v("bcG"), v("mm", 0, 16), 16.0, OP.mult, v("e5"), OP.add)
    ts(v("IdH"), v("mm"), v("pcF"), OP.is_equal)
    ts(v("IdF"), v("mm", 0, 8), v("pcF"), OP.is_equal)
    for nm, c in (("Ident", 1.0), ("Ih", -0.5)):
        line(v(nm), v("IdH"), c, 0.0)
    ts(v("DG"), v("QC", 0, 128), v("pmF"), OP.is_equal)
    line(v("RSs"), v("RS", 0, 128), 2.0, -1.0)
    line(v("RSk"), v("RS", 0, 128), BIG, 31.0)
    if QUICK:
        ts(v("eO"), v("pmF"), 16.0, OP.mult, 16.0, OP.add)
        ts(v("bcK"), v("mm", 0, 16), 16.0, OP.mult, 15.0, OP.add)
    else:
        ts(v("eO"), v("pmF"), 17.0, OP.mult, 1.0, OP.add)
    ts(v("OE"), v("OB"), v("eO"), OP.add)
    ts(v("blk8F"), v("mm", 0, 8), v("p4F"), OP.is_equal)
    cp(v("blk8H"), v("blk8F"))
    for nm, c in (("BKk", 2048.0), ("BK2", 4096.0), ("BKn", -2048.0), ("EEw", -4 * KZ), ("GVw", 2 * KZ), ("ABw", -2 * KZ)):
        line(v(nm), v("blk8F"), c, 0.0)
    ts(v("BM32"), v("f2", 64, 88), v("p4F"), OP.is_equal, -1.0 / 32, OP.mult)
    for h in range(2):
        tt(v("BMh", 8 * h, 8 * h + 8), v("t1", 8 * h, 8 * h + 8), v("blk8F"), OP.mult)
    cp(v("wF"), v("WI"))
    ts(v("W8"), v("blk8F"), v("wF"), OP.mult, 2.0, OP.mult)
    line(v("eH"), v("pmF"), 0.25, 191.875)
    line(v("eL"), v("pmF"), 1.0, 768.0 + 1 - 64)
    line(v("eM"), v("pmF"), 1.0, 1.0 - 64)
    for nm, c in (("Ibig", BIG), ("IZv", KZ * 2048), ("In4k", -4096.0), ("Za", -ZU / 4), ("Zk", -2 * ZU), ("Zo", ZU), ("Zg", 16 * ZU), ("In1", -1.0)) + (("Z2", 2 * ZU),) * ("V" in WHO["sgm"]) + (
                  ("InH", -1.0), ("I8k", 8192.0), ("I37", 1184.0)):
        select(v(nm), v("zero"), OP.not_equal, c, 0)

    def shifts(after):
        first = len(OPS)
        for nm, c in (("In4", -4.0), ("I64", 64.0), ("I2k", MID)):
            select(v(nm), v("zero"), OP.not_equal, c, 0)
        for k in (0, 1, 2, 3, 4, 8, 12):
            select(v("Uh%d" % k), v("zero"), OP.not_equal, 1.0, k)
            if k >= 4:
                select(v("Uh%d" % k), v("Uh%d" % k), OP.not_equal, -1.0, 0)
            else:
                select(v("Ub%d" % k), v("blkw"), OP.is_ge, 0.0, k)
                select(v("Ub%d" % k), v("Ub%d" % k), OP.not_equal, -63.0, k)
        for o in OPS[first:]:
            o[7].append(after)
    scan(back("PW2", 0, 128), v("two"), v("zero"), OP.mult, OP.add, 2.0 ** -68)
    tt(v("n4", 0, 16), v("PW2", 0, 16), v("DG", 0, 16), OP.mult)
    total(v("wq"), v("n4", 0, 16))
    tt(v("n4", 16, 24), v("PW2", 0, 128, 16), v("blk8F"), OP.mult)
    total(v("wp"), v("n4", 16, 24))
    ts(v("wp"), v("wp"), v("wq"), OP.mult, 2.5 * 2.0 ** -60, OP.mult)
    line(v("n3"), v("DG"), -2.0 ** 90, 2.0 ** 90)
    ts(v("THR"), v("n3"), v("wp"), OP.max)
    ts(v("BW"), v("f2", 0, 64), v("p4F"), OP.is_equal, v("wq"), OP.mult)

    def counts(h, final=False):
        lo, hi = 128 * h, 128 * h + 128
        step("val", h, v("val", lo, hi), v("Cd", lo, hi), MID - 0.5, -256.0)
        if final:
            scan(v("cum", lo, hi), v("RS", 0, 128), v("val", lo, hi), OP.mult, OP.add)
        else:
            hold("rc", "val", h)

    def rows(a0=0, a1=16):
        return v("rc", 16 * a0, 16 * a1, 16)

    line(v("tV"), v("IV"), 1.0, -MID)
    line(v("tC"), v("IC"), 1.0, -MID)
    turn(("pb7", 0), "tC")
    for h in range(2):
        mm(bank("old", h), v("tV", 128 * h, 128 * h + 128), v("IdH"))
        act(v("V", 128 * h, 128 * h + 128), bank("old", h))
    act(v("LNF", p=8), v("LNI", p=8))
    cp(v("THF", 0, 1, p=8), v("THI", p=8))
    for h in range(2):
        mm(v("pb2", 8 * h, 8 * h + 8), v("LNF", 128 * h, 128 * h + 128, p=8), v("IdF", p=8))
    cp(v("nn"), v("pb2", 0, 16))
    tt(v("m4"), bc("nn"), v("QC"), OP.is_le)
    line(v("m5"), v("m4"), 4096.0, -MID)
    tt(v("Cd"), v("pb7", 0, 256), v("m5"), OP.max)
    ts(v("s3"), v("nn"), 1.0, OP.min, -8192.0, OP.mult)
    tt(v("s2"), v("s3"), v("TR"), OP.add)
    tt(v("V0"), v("V", 0, 256, 16), v("s2"), OP.max)
    mm(v("pb3", 0, 1), v("G8", p=8), v("THF", 0, 1, p=8))
    cp(v("tI"), v("pb3", 0, 1))
    ts(v("tI"), v("tI"), 31, OP.bitwise_and)
    ts(v("e1"), v("pmF"), 0.0, OP.is_equal, KZ, OP.mult)
    ts(v("eK"), v("pmF"), 1.0, OP.is_equal, KZ, OP.mult)
    ts(v("e4"), v("pmF"), 15.0, OP.is_equal, -4096 * KZ, OP.mult)
    tt(v("e2"), v("pb3", 0, 1), v("tI"), OP.subtract)
    ts(v("e2"), v("e2"), -4096.0, OP.add, v("e1"), OP.mult)
    ts(v("e3"), v("tI"), 0.5, OP.add, v("eK"), OP.mult)
    ts(v("thm"), v("e2"), v("e3"), OP.add, v("e4"), OP.add)
    ts(v("LIM"), v("blkl"), v("thm"), OP.mult)

    def dedupe(n, h):
        zz, Ru, Em = "zz" + n, "Ru" + n, "Em" + n
        for x in each(h):
            lo, hi, a, b = span(x)
            hold("Wz" + n, "zs" + n, x, 1 if n == "1" else 3)
            alone(v("Ez" + n, lo, hi), v("Wz" + n, lo, hi), v("DG"))
            mm(bank("zU" + n, x, 0, 8), v("Ez" + n, lo, hi), v("blk8H"))
            mm(bank(Ru, x), v("Wz" + n, lo, hi), v("IdH"))
        lo, hi, a, b = span(h)
        if WHO[Ru][h] != "P":
            move(Ru, h, v(Ru, lo, hi), bank(Ru, h))
        if WHO[zz][h] != "P":
            move(zz, h, v(zz, a, b), bank("zU" + n, h, 0, 8))
        for k in range(8):
            at = 128 * (a + k)
            names = bank(Ru, h, 16 * k) if WHO[Ru][h] == "P" else v(Ru, lo + 16 * k, hi)
            name = bank("zU" + n, h, k, k + 1) if WHO[zz][h] == "P" else v(zz, a + k, a + k + 1)
            ts(v("EQ", at + 16 * k, at + 128), names, name, OP.is_equal, 2.0 ** (-16 * k), OP.mult)
            mm(bank("sum" + n, h, 0, 64), v("EQ", at, at + 128), v("BW"), k == 0, k == 7)
        move("off" + n, h, v("oA" + n, a, b), bank("zU" + n, h, 0, 8) if WHO[zz][h] == "P" else v(zz, a, b), 1.0, MID)
        for k in range(2):
            out = v(Em, lo + k, hi, 2)
            tt((out[0], v(Em, lo + 64 * k, lo + 64 * k + 64)[1]) + out[2:], bank("sum" + n, h, 0, 64), v("THR", k, 128, 2), OP.is_ge)
        mm(bank("off" + n, h, 0, 8), v(Em, lo, hi), v("BMh", a, b))
        tt(v("off" + n, a, b), bank("off" + n, h, 0, 8), v("oA" + n, a, b), OP.max)

    def message(m, h, out, land, t, cost, after=()):
        d = 1 + t % 3
        dst, src = T.cores[(rank + d) % 4], T.cores[(rank - d) % 4]
        rid, pid, _se = topo.addr(dst)
        asem, lsem = "a%s%d%d" % (m, h % 2, t), "l%s%d" % (m, h % 2)

        def emit(rd, wr):
            wait("G", need("G", rd, wr))
            if len(out) == 1:
                g.remote_dma(land[0][0], out[0][0], T.sem[asem], T.sem[lsem], pid, rid, topo.mask(core, dst))
            elif len(land) == 1:
                g.remote_dma_fused([RemoteDMATransfer(dst_ids=[DstId(rid=rid, pnc=pid)], dma_engine_mask=topo.mask(core, dst), remote_sem=T.sem[asem],
                                                      srcs=[x[0] for x in out], dsts=[land[0][0]], alu_op=2)], local_sem=T.sem[lsem])
            else:
                ways = topo.engines(core, dst)
                ways = [ways[1::2], ways[0::2]] if len(out) == 2 else [ways[1::2], ways[0::4], ways[2::4]]
                g.remote_dma_fused([RemoteDMATransfer(dst_ids=[DstId(rid=rid, pnc=pid)], dma_engine_mask=sum(1 << e for e in ways[k]),
                                                      remote_sem=T.sem[asem], src=out[k][0], dst=land[k][0]) for k in range(len(out))], local_sem=T.sem[lsem])
            record("Gr", bump("G", lsem, len(topo.engines(core, dst))), rd, wr)
        sent = add("G", emit, out, [], ISSUE + FIRST * (m == "K" and t == 0), cost)
        OPS[sent][7] += after

        def came(rd, wr):
            n = len(topo.engines(src, core))
            count[asem] = n
            clock[(asem, n)] = {}
            for x in wr:
                recs.setdefault(x[0], []).append(x[1:] + ((asem, n), "far", True))
        add("F", came, [], land, 0.0, 0.0, [sent])
        return sent

    counts(0)
    counts(1)
    for t in range(ST):
        rK, rC, rB, rY = "rK%d" % t, "rC%d" % t, "rB%d" % t, "rY%d" % t
        lastt = t == ST - 1
        turns, short, part[1] = [0], {}, t

        def diff(n):
            turns[0] += 1
            return "pb" + DIFF[(turns[0] - 1) % len(DIFF)], 0, n

        def bends(h):
            GV, DC, DV, AB, at = "GV%d" % h, "DC%d" % h, "DV%d" % h, "AB%d" % h, 0
            for who, how, n in RUNS[h]:
                lo, hi, lst = 16 * at, 16 * (at + n), (128 * h + at, 128 * h + at + n)
                src = ind(v("X", 0, W), v("LV", *lst))
                if who[0] == "S":
                    line(v(GV, lo, hi), src, -0.5, -96.0)
                else:
                    ts(v(GV, lo, hi), src, -0.5, OP.mult, -96.0, OP.add)
                at += n
            at = 0
            for who, how, n in RUNS[h]:
                lo, hi, lst = 16 * at, 16 * (at + n), (128 * h + at, 128 * h + at + n)
                src = ind(v("X", 0, XW if t else W), v("LC", *lst))
                if who[1] == "S":
                    act(v("CG%d" % h, lo, hi), src)
                    scan(v(DC, lo, hi), v("CG%d" % h, lo, hi), v(GV, lo, hi), OP.max, OP.add)
                else:
                    tt(v(DC, lo, hi), src, v(GV, lo, hi), OP.add)
                if how == "T":
                    pb = diff(hi - lo)
                    mms(v(*pb), [(v("Ident"), v(GV, lo + 1, hi + 1)), (v("Ident"), v(DC, lo, hi))])
                    ab = 2 * max(k[0] for k in KEYS[h] if k[0] <= at) + 14 * at
                    act(v(AB, ab, ab + 14 * n), v(*pb, -1), AF.Abs, 1.0, 192.0)
                elif how != "M":
                    scan(v(DV, lo, hi - 2), v(GV, lo + 1, hi - 1), v(DC, lo, hi - 2), OP.max, OP.add, -256.0)
                    size(how, v(AB, lo, hi - 2), v(DV, lo, hi - 2))
                at += n
            if how == "M":
                at = 0
                for how, n in SLOTS[h]:
                    out = v(AB, 128 * at, 128 * (at + n))
                    pb = diff(128 * n) if how == "T" else None
                    for s in range(at, at + n):
                        a, b = v(GV, s + 1, 2048, 16), v(DC, s, 2048, 16)
                        if pb:
                            for k, x in enumerate((a, b)):
                                mm(v(pb[0], 128 * (s - at), 128 * (s - at + 1)), v("Ident"), x, s == at and k == 0, s == at + n - 1 and k == 1)
                        else:
                            scan(v(DV, 128 * s, 128 * s + 128), a, b, OP.max, OP.add, -256.0)
                    size(how, out, v(*pb) if pb else v(DV, 128 * at, 128 * (at + n)))
                    at += n

        def size(how, out, a):
            if how == "R":
                ts(out, a, -192.0, OP.max, 96.0, OP.add)
            else:
                act(out, a, AF.Abs, 1.0, 192.0)

        def gates(h):
            lo, hi, a, b = 128 * h, 128 * h + 128, 8 * h, 8 * h + 8
            ts(v("sgp", lo, hi), v("rc", lo, hi), 3.0, OP.is_ge, -2.0, OP.add)
            if REST[h] == "V":
                ts(last("sgp", a, b), rows(a, b), 4.0, OP.is_ge, -3.0, OP.mult)


        def key(h):
            lo, hi = 128 * h, 128 * h + 128
            k = bank("key", h)
            mm(k, v("ones", p=1), v("CR", p=1), True, False)
            mm(k, v("Ibig"), v("val", lo, hi), False, False)
            if REST[h] == "T":
                mm(bank("key", h, 15, 128, 16), v("Ibig"), v("s7", 8 * h, 8 * h + 8), False, False)
            whole = len(KEYS[h]) == 1
            if whole:
                mm(k, v("Ibig"), v("sgp", lo, hi), False, False)
            terms, early = [], ([], [], [])
            for p0, p1, how in KEYS[h]:
                for s in range(14):
                    out, kind = bank("key", h, s, 128, 16, (p0, p1)), how
                    if how == "T":
                        at = (16 * p0 + s, 16 * p0 + 14 * (p1 - p0), 14)
                    elif how == "M":
                        at, kind = (128 * s, 128 * s + 128), "".join(c * n for c, n in SLOTS[h])[s]
                    else:
                        at = (16 * p0 + s, 16 * p1 - 15 + s, 16)
                    if kind == "R" and how == "M" and EARLY[h]:
                        early[0].append((out, v("GV%d" % h, s + 1, 2048, 16)))
                        for x, (q0, q1) in enumerate(((0, EARLY[h]), (EARLY[h], 128))):
                            early[1 + x].append((bank("key", h, s, 128, 16, (q0, q1)), v("DC%d" % h, 16 * q0 + s, 16 * q1, 16)))
                    elif kind == "R":
                        early[2].append((out, v("DV%d" % h, *at)))
                    terms.append((out, v("AB%d" % h, *at), v("BK2" if kind == "R" else "BKk")))
            for o, l in early[0] + early[1] + early[2]:
                mm(o, l, v("BKn"), False, False)
            for o, l, r in terms:
                mm(o, l, r, False, whole and o is terms[-1][0])
            if not whole:
                mm(k, v("Ibig"), v("sgp", lo, hi), False, True)

        def pick(h):
            lo, hi, a, b = 128 * h, 128 * h + 128, 8 * h, 8 * h + 8
            lst, abc, OH, Yn = "olist%d" % h, "pabc%d" % h, v("OH", lo, hi), v("Yh", lo, hi)
            scan(v("av", lo, hi), v("NR"), v("val", lo, hi), OP.max, OP.min)
            scan(v("SK", lo, hi), v("RSk"), bank("key", h), OP.min, OP.max, 31.0)
            ts(last("KA", a, b), last("SK", a, b), 992, OP.bitwise_and)
            hold("Dk", "KA", h)
            if QUICK:
                tt(v("El", lo, hi), ind(v("KA", lo, hi), v("bcK", 0, 8)), v("DG"), OP.mult)
            else:
                alone(v("El", lo, hi), v("Dk", lo, hi), v("DG"))
            o = bank("o", h, 0, 24)
            mm(o, v("El", lo, hi), v("BM32"))
            tt(v(lst), o, v("OE"), OP.add)
            for who, c0, c1 in YGATHER[h]:
                out, src = v(abc, 128 * c0, 128 * c1), ind(v("GD%d" % h), v(lst, 8 * c0, 8 * c1))
                if who == "V":
                    ts(out, src, 96.0, OP.add)
                else:
                    line(out, src, 1.0, 96.0)
            y = bank("y", h)
            mms(y, [(v("Ih"), v(abc, 0, 128)), (v("Ih"), v(abc, 128, 256)), (v("In1"), v(abc, 256, 384))])
            ts(Yn, y, 31.5, OP.min, 0.0, OP.max)
            ts(OH, v("Dk", lo, hi), 32.0, OP.is_equal)
            step("sk", h, v("sk", lo, hi), v("Dk", lo, hi), 48.0, 8.0)
            scan(v("dd", lo, hi), v("val", lo, hi), v("sk", lo, hi), OP.add, OP.mult)
            scan(v("ee%d" % h), v("val", lo, hi), v("sk", lo, hi), OP.max, OP.min)
            mm(bank("PW", h), v("IdH"), v("V", lo, hi), True, False)
            mm(bank("PW", h, 0, 128, 16), v("InH"), v("V", lo, hi, 16), False, False)
            mm(bank("PW", h, 0, 128, 16), v("ones", p=2), v("CP", p=2), False, False)
            mm(bank("PW", h), v("In4k"), v("dd", lo, hi), False, True)
            move("PW", h, v("PW", lo, hi), bank("PW", h), 1.0, 69632.0 + MID)
            alone(v("m2", lo, hi), v("V", lo, hi), OH)
            alone(v("m3", lo, hi), v("VK", lo + 1, hi + 1), OH)
            scan(v("m4", lo, hi), v("RS", 0, 128), v("m2", lo, hi), OP.mult, OP.add)
            scan(v("m5", lo, hi), v("RS", 0, 128), v("m3", lo, hi), OP.mult, OP.add)
            alone(v("i1", lo, hi), v("Cd", lo, hi), OH)
            mms(bank("Cx", h), [(v("IdH"), v("Cd", lo, hi)), (v("IdH"), v("m3", lo, hi)), (v("InH"), v("i1", lo, hi))])

        def hashed(h):
            lo, hi, a, b = span(h)
            for x in each(h):
                mm(bank("u", x, 0, 8), v("Yh", *span(x)[:2]), v("W8"))
            mms(v("pb" + BANK["Kp"], 192 + a, 192 + b), [(v("ones", p=1), v("CK", 0, b - a, p=1)), (v("I37"), last("m4", a, b))])
            move("UI", h, v("UI", a, b), bank("u", h, 0, 8))
            ts(v("UI", a, b), v("UI", a, b), 4095, OP.bitwise_and)
            if WHO["sq"][h % 2] == "V":
                tt(v("sq", a, b), v("UI", a, b), v("UI", a, b), OP.mult)
            else:
                act(v("sq", a, b), v("UI", a, b), AF.Square)
            tt(v("HI", a, b), v("pb" + BANK["Kp"], 192 + a, 192 + b), v("sq", a, b), OP.add)
            ts(v("HI", a, b), v("HI", a, b), 5, OP.arith_shift_right, 4095, OP.bitwise_and)
            move("x", h, v("x", a, b), v("HI", a, b), 1.0, -MID)
            tt(v("hh", a, b), v("x", a, b), v("s1", a, b), OP.max)

        def near(h):
            lo, hi = 128 * h, 128 * h + 128
            GV, EE = "GV%d" % h, "EE%d" % h
            z = bank("z", h)
            mm(z, v("IZv"), v("val", lo, hi), True, False)
            first = 2 + NABS[h]
            for s in range(first, 16):
                mm(bank("z", h, s, 128, 16), v(GV, s, 2048, 16), v("GVw"), False, False)
            mm(z, v("ones"), v("LIM"), False, False)
            mm(z, v("IZv"), v("ee%d" % h, -1, 127), False, False)
            if first < 16:
                mm(z, v("Yh", lo, hi), v("Yw%d" % h), False, False)
            for s in range(2, 16):
                scan(v(EE, 128 * s - 256, 128 * s - 128), v("Yh", lo, hi), v(GV, s, 2048, 16), OP.max, OP.add)
            for s0 in range(2, first, NRUN[0]):
                e = v(EE, 128 * s0 - 256, 128 * min(s0 + NRUN[0], first) - 256)
                act(e, e, AF.Abs, 1.0, 96.0)
            for s0 in range(first, 16, NRUN[1]):
                e = v(EE, 128 * s0 - 256, 128 * min(s0 + NRUN[1], 16) - 256)
                ts(e, e, -96.0, OP.max, 48.0, OP.add)
            for s in range(2, 16):
                mm(bank("z", h, s, 128, 16), v(EE, 128 * s - 256, 128 * s - 128), v("ABw" if s < first else "EEw"), False, s == 15)
            scan(back("SM", lo, hi), back("pb" + BANK["z"][h], SPOT["z"][0], SPOT["z"][0] + 128), back("PW", lo, hi), OP.max, OP.min, -4097.0)
            if WHO["sgm"][h] == "S":
                act(v("fit", lo, hi), z, AF.Sign)
            else:
                ts(v("fit", lo, hi), z, 0.0, OP.is_gt, -0.5, OP.add)
            scan(v("sgm", lo, hi), v("RSs"), v("fit", lo, hi), OP.min, OP.max, -1.0)

        def closed(h):
            a, b = span(h)[2:]
            ts(v("SB", a, b), found(a, b), 12, OP.logical_shift_right)
            short[h] = message("B", h, [v("SB", a, b)], [v(rB, a, b)], t, FAR)
            tt(v("grow", 16 * a + 14, 16 * b, 16), found(a, b), v("s9", a, b), OP.is_lt)

        def named(h):
            a, b = span(h)[2:]
            tt(v("kn", a, b), found(a, b), v("TR", a, b), OP.min)
            tt(last("zs1", a, b), v("kn", a, b), v("hh", a, b), OP.max)
            ts(v("VM", a, b), found(a, b), 4095, OP.bitwise_and)
            move("s5", h, v("s5", a, b), v("VM", a, b), 1.0, -MID)

        def codes(h):
            lo, hi, a, b = span(h)
            Z, Zs = bank("Z", h), v("Zs", lo, hi)
            if WHO["gw"][h % 2] == "S":
                act(v("gw", lo, hi), ind(v("grow", lo, hi), v("bcG", 0, b - a)))
            else:
                hold("gw", "grow", h, 1, "RS2")
            terms = [("ones", "CZ"), ("Za", "av"), ("Zk", "sk"), ("Zo", "OH"), ("Zo" if WHO["sgm"][h % 2] == "S" else "Z2", "sgm"), ("Zg", "gw")]
            mms(Z, [(v(l, p=1), v(r, 0, hi - lo, p=1)) if r == "CZ" else (v(l), v(r, lo, hi)) for l, r in terms])
            if WHO["Cp"][h] == "S":
                act(v("Cp", lo, hi), Z)
            else:
                tt(v("Cp", lo, hi), Z, v("Cd", lo, hi), OP.max)
            act(Zs, Z, AF.Abs, 1.0 / ZU, -8.625)
            step("FF", h, v("FF", lo, hi), Zs, 9.25, 1024.0)
            ts(v(pad("Fu", h)), Zs, 9.125, OP.is_equal)
            mms(bank("F", h), [(v("Ident"), v("FF", lo, hi)), (v("Ident"), v(pad("Fu", h), -1, hi - lo - 1))])
            ts(v(pad("mP", h)), Zs, 6.125, OP.is_equal)
            ts(v("Dn", lo, hi), Zs, 8.375, OP.is_equal)
            if WHO["Fc"][h % 2] == "S":
                act(v("Fc", lo, hi), Z, AF.Relu, -1.0 / ZU)
            else:
                ts(v("Fc", lo, hi), Zs, 9.5, OP.is_ge)
            if WHO["xw"][h % 2] == "S":
                tt(v("s2", a, b), v("s5", a, b), last("zs1", a, b), OP.min)
                act(v("xw", lo, hi), bc("s2", h))
            else:
                tt(last("sx", a, b), v("s5", a, b), last("zs1", a, b), OP.min)
                hold("xw", "sx", h)

        def moved(h):
            lo, hi = 128 * h, 128 * h + 128
            for old, x, new in (("old", "V", "xw"), ("Cx", "C", "m4")):
                tt(v("fx" + x, lo, hi), bank("F", h), v(new, lo, hi), OP.mult)
                tt(v("up" + x, lo + 1, hi), v(pad("mP", h), 0, 127), bank(old, h, 0, 127), OP.mult)
                tt(v("dn" + x, lo, hi - 1), v("Dn", lo, hi - 1), bank(old, h, 1, 128), OP.mult)

        def piece(h):
            lo, hi = span(h)[:2]
            short["C"] = message("C", h, [v("Cp", lo, hi)] + [v("Cd", lo, hi)] * ("S" in WHO["Cp"]), [v(rC, lo, hi)], t, FAR + LATER * (hi - lo) / 256, [short.get(h, short.get(2, short.get(0)))])

        def guess(h):
            move("SB", 0, v("Vn"), last("m5"))
            if t < AHEAD:
                message("Y", 0, [v("VK", 144), v("Yh", 0, 144), v("Yh", 144)], [v(rK, 144), v(rY, 0, 144), v(rY, 144)], t, FAR + 1.5 * LATER)
            else:
                message("Y", 0, [v("VK"), v("Yh")], [v(rK), v(rY)], t, FAR + 2 * LATER)
            tt(v("dz", 2, 48, 3), v("V0"), v(rK, 256, 272), OP.max)
            tt(v("dz", 1, 48, 3), v(rK, 272, 288), v("dz", 2, 48, 3), OP.subtract)

        def shut(h):
            if not lastt:
                act(v("s4"), found(), AF.Sign, 1.0, 0.5, total=v("cs1"))
                mm(bank("c", h, 0, 1), v("onesF"), v("cs1"))
                move("cI", h, v("cI"), bank("c", h, 0, 1), 0.5, 1024.0)
                ts(v("cI"), v("cI"), 31, OP.bitwise_and)
                line(v("lim"), v("cI"), v("eK"), v("thm"))
                line(v("LIM"), v("blkl"), v("lim"), 0.0)

        def takes(h):
            a, b = span(h)[2:]
            tt(third("take", h), v(rB, a, b), v("th2", a, b), OP.is_lt)
            scan(third("zs2", h, 16), third("take", h, 16), v("dz", 3 * a, 3 * b), OP.mult, OP.add)

        def stays(h):
            lo, hi, a, b = span(h)
            if WHO["tw"][h % 2] == "S":
                act(v("tw", lo, hi), ind(v("take", 3 * lo, 3 * hi), v("bcT", 0, b - a)))
            else:
                hold("tw", "take", h, 3)
            mm(bank("tw", h), v("Ident"), v("tw", lo, hi))
            mms(bank("keep", h), [(v("In1"), x) for x in (v("FF", lo, hi), v(pad("Fu", h), -1, hi - lo - 1), v(pad("mP", h), -1, hi - lo - 1), v("Dn", lo, hi), v("tw", lo, hi))])
            move("keep", h, v("keep", lo, hi), bank("keep", h), 1.0, 1.0)

        def taken(h):
            lo, hi = 128 * h, 128 * h + 128
            for old, x, came in (("old", "V", v(rK, lo, hi)), ("Cx", "C", v(rC, lo, hi))):
                tt(v("kp" + x, lo, hi), v("keep", lo, hi), bank(old, h), OP.mult)
                tt(v("in" + x, lo, hi), bank("tw", h), came, OP.mult)
            for k, (x, name, new) in enumerate((("V", "V", bank("old", h)), ("C", "Cd", bank("Cn", h)))):
                mms(new, [(v("I8k"), v("Fc", lo, hi))] * k + [(v("IdH"), v(p + x, lo, hi)) for p in ("up", "dn", "fx", "kp", "in")])
                move(name, h, v(name, lo, hi), new)
                if not lastt:
                    b = bank("list", h, 128 * k, 128 * k + 128)
                    mm(b, v(name, lo, hi), v("IdH"))
                    if k:
                        ts(v("LC", lo, hi), b, MID, OP.add, float(W), OP.min)
                    else:
                        move("LV", h, v("LV", lo, hi), b, 1.0, MID)
            counts(h, lastt)

        def grown(h):
            tt(ind(v("X"), v("off1", 8 * h, 8 * h + 8)), v("Yh", 128 * h, 128 * h + 128), v("Yh", 128 * h, 128 * h + 128), OP.add)

        def mixed(h):
            lo, hi, a, b = span(h)
            move("z16", h, v("z16", a, b), v("oA2", a, b))
            move("blend", h, v("BL", lo, hi), ind(v("X"), v("z16", a, b)), 0.5, 191.75)
            scan(v("g1", lo, hi), v(rY, lo, hi), v("BL", lo, hi), OP.min, OP.add, 64.0)

        def blend(h):
            lo, hi = 128 * h, 128 * h + 128
            tt(ind(v("X"), v("off2", 8 * h, 8 * h + 8)), v("g1", lo, hi), v("g2", lo, hi), OP.add)

        ts(v("s9"), rows(), 4.0, OP.is_lt, -8192.0, OP.mult)
        tt(v("s1"), v("TRm"), v("s9"), OP.subtract)
        if t < AHEAD:
            message("K", 0, [v("VK", 0, 144)], [v(rK, 0, 144)], t, FAR + 6.0)
        ts(v("s7"), rows(), 4.0, OP.is_lt, 16.0, OP.mult)
        tt(v("th2"), v("s7"), rows(), OP.subtract)
        for part[0] in PARTS.split():
            {"b": bends, "g": gates, "k": key, "p": pick, "h": hashed, "n": near, "c": closed, "d": lambda h: dedupe("1", h), "z": codes,
             "f": moved, "w": grown, "q": shut, "t": takes, "e": lambda h: dedupe("2", h), "s": stays, "r": taken, "l": mixed, "x": blend, "y": guess, "m": piece, "j": named}[part[0][0]](int(part[0][1]))
        part[0] = ""
        if t == 0:
            shifts(short["C"])
        if not lastt:
            tt(v("s3"), v("zs2", 47, 768, 48), v("dz", 2, 48, 3), OP.subtract)
            tt(v("V0"), v("V0"), v("s3"), OP.add)
        else:
            dma("Y", T.yx[:, 0:half], T.X[:, 0:half], [v("X", 0, half)], [], LOAD)
            dma("S", T.yx[:, half:W], T.X[:, half:W], [v("X", half, W)], [], LOAD)

    part[1] = ST
    for h in range(2):
        mm(v("pb1", 128 * h, 128 * h + 128, p=8), last("cum", 8 * h, 8 * h + 8), v("Ident"))
    act(v("LNF", p=8), v("pb1", 0, 256, p=8))
    dma("Y", T.yn[:], v("LNF", p=8)[0], [v("LNF")], [])
    halves = [(128 * h, 128 * h + 128) for h in range(2)]
    for lo, hi in halves:
        mm(v("pb6", lo, hi), v("cum", lo, hi), v("In1"))
    line(v("rc"), v("pb6", 0, 256), 0.25, v("eH"))
    for lo, hi in halves:
        mm(v("pb6", 256 + lo, 256 + hi), v("cum", lo, hi), v("In1"), lo == 0, False)
        mm(v("pb6", 256 + lo, 256 + hi), v("val", lo, hi), v("I64"), False, False)
    mm(v("pb6", 256, 512), v("In4"), v("rc"), False, True)
    line(v("Dk"), v("pb6", 256, 512), 1.0, v("eL"))
    turn(("pb3", 0), "V")
    turn(("pb3", 256), "Cd")
    cp(v("nn"), last("cum"))
    tt(v("gw"), bc("nn"), v("QC"), OP.is_gt)
    masks = ("sgm", "keep", "Dn", "FF")
    for b in range(4):
        ts(v(masks[b]), v("Dk"), float(b), OP.is_equal)
        mm(v("pb1", 0, 256), v("Ub%d" % b), v(masks[b]), b == 0, b == 3)
        for old, piece, new in ((("pb3", 0, 256), ("upV", "dnV", "fxV", "kpV"), "pb4"), (("pb3", 256, 512), ("upC", "dnC", "fxC", "kpC"), "pb5")):
            tt(v(piece[b]), v(masks[b]), v(*old), OP.mult)
            mm(v(new, 0, 256), v("Uh%d" % b), v(piece[b]), b == 0, b == 3)
    line(v("g3"), v("pb1", 0, 256), -1.0, v("eM"))
    for new in ("pb7", "pb6"):
        for lo, hi in halves:
            mm(v(new, lo, hi), v("gw", lo, hi), v("I2k"), lo == 0, False)
    masks = ("El", "Zs", "av", "sk")
    for a in range(4):
        if a:
            ts(v(masks[a]), v("g3"), 4.0 * a, OP.is_equal)
        for old, piece, new in (("pb4", ("inV", "i1", "Wz1", "tV"), "pb7"), ("pb5", ("inC", "m3", "Ez1", "tC"), "pb6")):
            if a:
                tt(v(piece[a]), v(masks[a]), v(old, 0, 256), OP.mult)
            else:
                act(v(piece[a]), v(old, 0, 256))
            mm(v(new, 0, 256), v("Uh%d" % (4 * a)), v(piece[a]), False, a == 3)
    act(v("f1"), v("pb7", 0, 256))
    cp(v("f2"), v("pb6", 0, 256))
    dma("Y", T.yv[:], v("f1")[0], [v("f1")], [])
    dma("S", T.yc[:], v("f2")[0], [v("f2")], [])
    if "order" not in PLAN:
        PLAN["order"] = order(OPS)
    for i in PLAN["order"]:
        OPS[i][1](OPS[i][2], OPS[i][3])
    for s in sorted(count):
        if known["G"].get(s, 0) < count[s]:
            g.wait_ge(T.sem[s], count[s])
